import numpy as np, ml_dtypes
CORES = [16,18,20,22]
N = 4
BF = ml_dtypes.bfloat16
LN, B, SQ, KN, RO, SH = 256, 4, 128, 16, 6, 5
KS = KN * SQ; W = B * KS
def draw(rng):
    fe = np.clip(rng.integers(-6, 10, (N, 8, 16, 1, 1, 1), dtype=np.int8) + rng.integers(-3, 4, (N, 8, 1, 1, KN, 1), dtype=np.int8) + rng.integers(-9, 10, (N, 8, 16, B, KN, SQ), dtype=np.int8), -15, 15)
    kind = rng.integers(1, KN, (N, 8, 16, LN)); sq = rng.integers(0, SQ, (N, 8, 16, LN)); gone = rng.random((N, 8, 16, LN)) < 0.2
    near = (rng.integers(0, SQ, (1, 8, LN)) + rng.integers(0, 3, (N, 8, LN))) & (SQ - 1)
    sq[:, :, 0] = np.where(rng.random((N, 8, LN)) < 0.7, near, sq[:, :, 0])
    st = rng.integers(1, SQ, (N, 8, 16)); u = rng.integers(-127, 128, (N, 8, 16, 16)); v = rng.integers(-127, 128, (N, 8, 16, 16))
    u[..., 0] = np.where(rng.random((N, 8, 1)) < 0.5, np.abs(u[..., 0]), u[..., 0])
    return fe, kind, sq, gone, st, u, v
def pack(fe, kind, sq, gone, st, u, v):
    fe = fe.copy(); fe[:, :, :, :, 0] = 0
    po = np.where(gone & (np.arange(16) > 0)[None, None, :, None], 0, kind * SQ + sq)
    return {"feat": fe.reshape(N, 128, W).astype(np.float32).astype(BF), "pos": np.ascontiguousarray(po.reshape(N, 128, LN)).astype(np.int32), "step": np.ascontiguousarray(st.reshape(N, 128, 1)).astype(np.int32),
            "u": u.reshape(N, 128, 16).astype(np.float32).astype(BF), "v": v.reshape(N, 128, 16).astype(np.float32).astype(BF)}
def setup_inputs(rng):
    return pack(*draw(rng))
def setup_inputs_ends(rng):
    fe, kind, sq, gone, st, u, v = draw(rng); mode = np.array([0, 1, 2, 0, 1, 2, 1, 2])
    fe = (30 * rng.integers(0, 2, (N, 8, 16, B, KN, SQ), dtype=np.int8) - 15).astype(np.int8)
    fe[:, mode == 1] = (30 * rng.integers(0, 2, (N, 3, 1, B, KN, SQ)) - 15).astype(np.int8)
    kind[:] = KN - 1; sq[:] = SQ - 1; gone = rng.random(gone.shape) < 0.5
    low = rng.random((N, 8, LN)) < 0.5; kind[:, :, 0] = np.where(low, 1, KN - 1); sq[:, :, 0] = np.where(low, 0, SQ - 1)
    st = np.where(rng.random(st.shape) < 0.5, 1, SQ - 1); st[:, 0, 0] = 1; st[:, 0, 1] = SQ - 1
    u = 254 * rng.integers(0, 2, u.shape) - 127; v = 254 * rng.integers(0, 2, v.shape) - 127
    u[:, mode == 1] = 254 * rng.integers(0, 2, (N, 3, 1, 16)) - 127; v[:, mode == 1] = 254 * rng.integers(0, 2, (N, 3, 1, 16)) - 127
    for q in range(N):
        for g in (2, 5, 7):
            mine = KN - 1 - (q & 1); other = KN - 2 + (q & 1)
            fe[q, g, :, :, mine] = -15; fe[q, g, :, :, other] = 15; fe[q, g, :, :, KN - 3] = 14
            kind[q, g, :, 3::4] = mine; sq[q, g, :, 3::4] = SQ - 1 - (q & 1); gone[q, g, :, 3::4] = False
            w = np.arange(3, LN, 8); w = w[(((w >> 3) + q) & 1) == 1]; kind[q, g, 0, w] = KN - 3
            sq[q, g, 0, 15::16] = SQ - 1 if q == N - 2 else (B - 1) << SH if q == N - 1 else 1 << (SH - 1)
            st[q, g, 0] = SQ - 1
            u[q, g] = -127; u[q, g][:, [5, 10, 15, int(rng.integers(1, 15))]] = 127
            v[q, g] = 254 * rng.integers(0, 2, (1, 16)) - 127; v[q, g, :, 0] = -127; v[q, g][:, [7, 15]] = 127
    return pack(fe, kind, sq, gone, st, u, v)
def setup_inputs_corners(rng):
    fe, kind, sq, gone, st, u, v = draw(rng); i = np.arange(LN); c = i % 8
    st[:, 1::2] = st[:, 1::2, 0:1]
    edge = ((rng.integers(0, B, (N, 8, 1, LN)) << SH) - rng.integers(0, 2, (N, 8, 1, LN))) & (SQ - 1)
    k0 = np.where(c == 3, edge, sq[:, :, 0:1]); s0 = st[:, :, 0][:, :, None, None]; q = sq[:, :, 1:].copy()
    sm = np.take_along_axis(st, rng.integers(0, 16, (N, 8, 15 * LN)), 2).reshape(N, 8, 15, LN)
    q = np.where((c == 1) | (c == 6), k0, q); q = np.where(c == 2, k0 + s0, q)
    q = np.where(c == 4, k0 + s0 * rng.integers(0, 2, q.shape), q); q = np.where(c == 5, k0 - sm, q)
    sq = np.concatenate([k0, q & (SQ - 1)], axis=2)
    but = (c == 2) & ((i >> 3) % 2 == 1); sq[:, :, 15] = np.where(but, (sq[:, :, 15] + 1) & (SQ - 1), sq[:, :, 15])
    kind = np.where(c == 6, kind[:, :, 0:1], kind)
    gone = np.where(c == 0, True, np.where((c == 3) | (c == 7), gone, False))
    fe[:, 4] = -np.abs(fe[:, 4]); fe[:, 6] = np.abs(fe[:, 6])
    u[:, 0:2] = np.minimum(u[:, 0:2], 126); u[:, 0:2, :, 0] = 127
    u[:, 7, :, 8:] = u[:, 7, :, :8]; v[:, 7, :, 8:] = v[:, 7, :, :8]; v[:, 2, :, 8:] = v[:, 2, :, :8]
    return pack(fe, kind, sq, gone, st, u, v)
def setup_inputs_calm(rng):
    fe, kind, sq, gone, st, u, v = draw(rng); i = np.arange(LN)
    kind[:, :, 0] = 1; kind[:, :, 1:] = rng.integers(2, np.where(i % 2 == 0, 9, KN), (N, 8, 15, LN))
    sq = np.moveaxis(np.argsort(rng.random((N, 8, LN, SQ)), axis=-1)[..., :16], 3, 2)
    sq = (sq - sq[:, :, 0:1] + rng.integers(0, SQ, (1, 8, 1, LN)) + rng.integers(0, 3, (N, 8, 1, LN))) & (SQ - 1)
    gone[:, 4:] = False
    fe = rng.integers(-1, 2, (N, 8, 16, B, KN, SQ), dtype=np.int8); fe[:, :, :, :, :9] = 0; fe[:, 4:] += 8
    a = (np.arange(N)[:, None] + np.arange(8)) & 3; brim = (np.arange(8) >= 4)[None, :, None]; half = (np.arange(16) < 8)[None, None, :]
    fe[:, :, :, :, 1, :] = np.where(half, a[:, :, None] + np.where(brim, 6, 0), np.where(brim, 7, 2)).astype(np.int8)[..., None, None]
    t1 = rng.integers(0, 2, (N, 8, 1, 16)); t1[..., 1] = 1 - t1[..., 0]; t2 = rng.integers(0, 2, (N, 8, 1, 16)); t2[..., 1] = 1 - t2[..., 0]
    h = (np.arange(16) < 8)[:, None]
    u = np.where(h, 1 - t1, t1) * rng.integers(1, 16, (N, 8, 1, 1)); v = np.where(h, 1 - t2, t2) * rng.integers(1, 16, (N, 8, 1, 1))
    return pack(fe, kind, sq, gone, st, u, v)
def setup_inputs_spread(rng):
    fe, kind, sq, gone, st, u, v = draw(rng)
    lim = np.array([0, 1, 3, 7, 15], np.int8)[rng.integers(0, 5, (N, 8, 1, B, KN, SQ))]
    fe = np.clip(rng.integers(-15, 16, (N, 8, 16, B, KN, SQ), dtype=np.int8), -lim, lim)
    big = np.array([1, 15, 60, 127])
    lu = big[rng.integers(0, 4, (N, 8, 1, 16))]; lv = big[rng.integers(0, 4, (N, 8, 1, 16))]
    u = np.clip(rng.integers(-127, 128, u.shape), -lu, lu); v = np.clip(rng.integers(-127, 128, v.shape), -lv, lv)
    st = np.minimum(np.exp2(rng.random(st.shape) * (SQ.bit_length() - 1)).astype(np.int64), SQ - 1)
    kind = np.minimum(1 + ((KN - 1) * rng.random(kind.shape) ** 3).astype(np.int64), KN - 1)
    sq[:, ::2] = np.minimum((SQ * rng.random((N, 4, 16, LN)) ** 2).astype(np.int64), SQ - 1)
    gone = rng.random(gone.shape) < rng.random((N, 8, 1, LN))
    return pack(fe, kind, sq, gone, st, u, v)
def steepness(rng, neg):
    t = np.argsort(rng.random((N, 8, 16, 12)), axis=2) & 1
    w = np.concatenate([rng.integers(110, 116, (N, 8, 16, 4)), rng.integers(119, 127, (N, 8, 16, 1)) + t], axis=3)
    return w - np.where(neg, 237, 0)[None, :, None, None]
def setup_inputs_steep(rng):
    fe, kind, sq, gone, st, u, v = draw(rng); g = np.arange(8)
    fe = rng.integers(5, 11, (N, 8, 16, B, KN, SQ), dtype=np.int8); gone = rng.random(gone.shape) < 0.03
    st = 1 + np.argsort(rng.random((N, 8, SQ - 1)), axis=-1)[..., :16]
    u = steepness(rng, (g >> 1) % 2 == 1); v = steepness(rng, g % 2 == 1)
    u[:, 6:] = np.roll(u[:, 6:], -4, axis=3)
    return pack(fe, kind, sq, gone, st, u, v)
def check_inputs(d):
    bad = []
    for k, lo, hi in (("feat", -15, 15), ("pos", 0, KS - 1), ("step", 1, SQ - 1), ("u", -127, 127), ("v", -127, 127)):
        x = np.asarray(d[k]).astype(np.float32)
        if not (np.min(x) >= lo and np.max(x) <= hi): bad.append("range of " + k)
        elif not np.all(x == np.rint(x)): bad.append("whole numbers in " + k)
    p = np.asarray(d["pos"])
    if np.any((p > 0) & (p < SQ)): bad.append("piece numbers of kind 0 in pos")
    if np.any(p[:, ::16] < SQ): bad.append("an empty row 0 in pos")
    if np.any(np.asarray(d["feat"]).reshape(N, 128, B, KN, SQ)[:, :, :, 0].astype(np.float32) != 0): bad.append("columns of kind 0 in feat")
    return bad
def reference(feat, pos, step, u, v):
    fe = feat.astype(np.float32).astype(np.int32).reshape(N, 8, 16, W); st = step.astype(np.int64).reshape(N, 8, 16)
    ut = np.swapaxes(u.astype(np.float32).astype(np.int64).reshape(N, 8, 16, 16), 2, 3); vt = np.swapaxes(v.astype(np.float32).astype(np.int64).reshape(N, 8, 16, 16), 2, 3)
    cur = pos.astype(np.int64).reshape(N, 8, 16, LN)
    cl = np.zeros((N, 8, 16, LN, B), np.int64); ca = np.zeros((N, 8, 16, LN, B), np.int64); row = np.arange(16)[None, None, :, None]
    for t in range(RO):
        if t > 0: cur = np.roll(cur, 1, axis=0)
        b = (cur[:, :, 0] & (SQ - 1)) >> SH
        ix = np.broadcast_to(b[:, :, None, :, None], (N, 8, 16, LN, 1))
        o = np.take_along_axis(cl, ix, 4)[..., 0]; a = np.take_along_axis(ca, ix, 4)[..., 0]; ne = o != cur
        for k in range(16):
            w = np.take_along_axis(fe, (b * KS + o[:, :, k])[:, :, None, :], 3)
            a = np.where(ne[:, :, k][:, :, None, :], np.maximum(a - w, 0), a)
        for k in range(16):
            w = np.take_along_axis(fe, (b * KS + cur[:, :, k])[:, :, None, :], 3)
            a = np.where(ne[:, :, k][:, :, None, :], np.maximum(a + w, 0), a)
        np.put_along_axis(cl, ix, cur[..., None], 4); np.put_along_axis(ca, ix, a[..., None], 4)
        y = np.minimum(a, 127)
        k = np.argmax(np.where(cur > 0, np.matmul(ut, y), -2 ** 40), axis=2); m = np.argmax(np.matmul(vt, y), axis=2)
        old = np.take_along_axis(cur, k[:, :, None, :], 2)[:, :, 0]; s = old & (SQ - 1)
        new = (s + np.take_along_axis(st, m, 2)) & (SQ - 1)
        me = row == k[:, :, None, :]
        hit = (cur > 0) & (row > 0) & ((cur & (SQ - 1)) == new[:, :, None, :])
        cur = np.where(me, (old - s + new)[:, :, None, :], np.where(hit, 0, cur))
    return {"yl": cur.reshape(N, 128, LN).astype(np.float32), "ya": ca.reshape(N, 128, LN * B).astype(np.float32), "yc": cl.reshape(N, 128, LN * B).astype(np.float32)}

@@ -1,0 +1,741 @@
+from concourse.bass import DstId, RemoteDMATransfer
+from concourse.mybir import AluOpType as A, ActivationFunctionType as F
+
+NR, LN, RO = 4, 256, 6
+NCH = 4
+n = LN // NCH
+HS = 7 * n
+DEAD = -16384.0
+GONE = -2.0 ** 50
+OFS = 240.0
+
+P = {"vcols": 4, "spieces": 3, "vc0_0": 40, "vc0_1": 32, "vc0_2": 0, "vc0_3": 8, "spieces0": 3,
+     "vc1_0": 56, "vc1_1": 8, "vc5_0": 8, "vc5_1": 0, "vc5_2": 8, "vc5_3": 40, "rp": 1, "nowr": 0,
+     "e_lrelu": "V", "e_og": "V", "e_zz": "V", "e_mn": "V", "nep": 0, "neg": "SSSS", "e_f0": "V", "e_f1": "G", "e_f2": "V", "e_f3": "G",
+     "e_hist": "G", "e_hist5": "S", "e_ms": "G", "e_yc": "S", "e_ya": "S", "e_yl": "V", "delta": 0.0,
+     "g": 1.56, "f": 1.25, "pe": 0.5, "hop": 0.1, "rlat": 2.5, "riss": 0.6, "klat": 10.0, "bw": 250.0, "fix": 0.02,
+     "tq": 2.0, "short": 4.0, "scp": 2, "vp": 1, "seed": 0, "jit": 0.0, "off": {}, "fbi": 6}
+
+P.update({"spieces": 2, "e_hist5": "V", "vc5_3": 32, "vc5_2": 16, "vc5_1": 8, "tq": 4, "seed": 49, "jit": 0.2})
+
+BF, F32, I32, U16 = "bfloat16", "float32", "int32", "uint16"
+SCRATCH = {
+    "tab": ("sbuf", [128, 16384], BF),
+    "xb": ("sbuf", [128, 32 * LN], BF), "so": ("sbuf", [128, 2 * 32 * n], BF),
+    "d1": ("sbuf", [128, 2 * 32 * n], BF),
+    "hl": ("sbuf", [128, NCH * HS], F32), "ha": ("sbuf", [128, NCH * HS], BF),
+    "posi": ("sbuf", [128, LN], I32), "ki": ("sbuf", [128, LN], I32), "si": ("sbuf", [128, LN], I32), "dd": ("sbuf", [128, LN], F32),
+    "kall": ("sbuf", [128, NR * LN], BF), "sin": ("sbuf", [128, RO * LN], BF), "sout": ("sbuf", [128, RO * LN], BF),
+    "ub": ("sbuf", [128, 16], BF), "vb": ("sbuf", [128, 16], BF), "stepi": ("sbuf", [128, 4], I32),
+    "mt": ("sbuf", [128, RO * LN], BF), "dg": ("sbuf", [128, LN], F32), "poff": ("sbuf", [128, 16 * NCH], U16),
+    "og": ("sbuf", [128, LN], F32), "ne": ("sbuf", [128, LN], BF), "off": ("sbuf", [128, 2 * LN], U16),
+    "tt": ("sbuf", [128, LN], BF), "yb": ("sbuf", [128, 9 * n], BF),
+    "km": ("sbuf", [128, 128 * NCH], F32), "ri": ("sbuf", [128, 8 * NCH], I32), "ix": ("sbuf", [128, 32 * NCH], BF),
+    "ft": ("sbuf", [128, 128 * NCH], BF), "mo": ("sbuf", [128, 2 * LN], BF), "wr": ("sbuf", [128, LN], BF),
+    "ht": ("sbuf", [128, LN], BF), "h2": ("sbuf", [128, LN], BF), "mn": ("sbuf", [128, LN], BF),
+    "fm": ("sbuf", [128, 2 * LN], BF), "foff": ("sbuf", [128, 16 * NCH], U16),
+    "oyl": ("sbuf", [128, LN], F32), "oya": ("sbuf", [128, 4 * LN], F32), "oyc": ("sbuf", [128, 4 * LN], F32),
+    "ci": ("sbuf", [128, 16], I32), "col": ("sbuf", [128, 64], F32), "thr": ("sbuf", [128, 8], F32), "gm": ("sbuf", [128, 8], F32),
+    "i2t": ("sbuf", [128, 8], F32), "cg": ("sbuf", [128, 128], BF), "pw": ("sbuf", [128, 128], BF), "dw": ("sbuf", [128, 144], BF),
+    "tie": ("sbuf", [128, 128], BF), "c4": ("sbuf", [128, 16], BF), "rs": ("sbuf", [128, 128], BF), "cd": ("sbuf", [128, n], BF),
+    "cmp": ("sbuf", [128, 8], F32), "wfw": ("sbuf", [128, 144], BF), "ws": ("sbuf", [128, RO * 128], BF),
+    "tmp": ("sbuf", [128, n], F32),
+}
+for _m in ("bm", "eye", "neye", "selk", "wp", "wb", "wst", "uu", "vv", "penu", "tiev", "ee", "n16", "n24"):
+    SCRATCH[_m] = ("sbuf", [128, 128], BF)
+SCRATCH["eyef"] = ("sbuf", [128, 128], F32)
+for _b in range(8):
+    SCRATCH["pb%d" % _b] = ("psum", [128, 512], F32)
+
+SEMAPHORES = ["sV", "sS", "sP", "sG", "karr", "sent", "outs", "lpos", "lu", "lv", "lstep"] + ["lf%d" % i for i in range(4)] \
+    + ["ar%d_%d" % (t, c) for t in range(1, RO) for c in range(NCH)]
+
+
+def build(p):
+    ops = []
+    lastw, readers, bank = {}, {}, {}
+    tag = [None]
+
+    def add(eng, fn, r, w, cost, bk=None, sem=None, lat=None):
+        k = len(ops)
+        deps = set()
+        for x in r:
+            if x in lastw:
+                deps.add(lastw[x])
+        for x in w:
+            if x in lastw:
+                deps.add(lastw[x])
+            deps.update(readers.get(x, ()))
+        for x in r:
+            readers.setdefault(x, []).append(k)
+        for x in w:
+            lastw[x] = k
+            readers[x] = []
+        if bk is not None:
+            e0, run, prev = bank.get(bk, (None, [], []))
+            if e0 == eng:
+                deps.update(prev)
+                if eng == "P":
+                    deps.add(run[-1])
+                run.append(k)
+            else:
+                deps.update(run)
+                bank[bk] = (eng, [k], run)
+        deps.discard(k)
+        ops.append({"eng": eng, "fn": fn, "deps": deps, "cost": cost, "sem": sem, "lat": lat, "tag": tag[0],
+                    "cls": ("s" if tag[0] is None else "abbbbc"[tag[0] // NCH]) + str(eng) + "".join([x for x in (list(w) + ["y"])[0] if x.isalpha()])})
+        return k
+
+    def ts(out, in0, s1, s2, o0, o1, r, w, m, bk=None):
+        if o1 is None:
+            add("V", lambda q, T, X: q.tensor_scalar(out(T), in0(T), s1(T), None, o0), r, w, ("c", m), bk)
+        else:
+            add("V", lambda q, T, X: q.tensor_scalar(out(T), in0(T), s1(T), s2(T), o0, o1), r, w, ("c", m), bk)
+
+    def tt(out, a, b, o, r, w, m, bk=None, kind="c"):
+        add("V", lambda q, T, X: q.tensor_tensor(out(T), a(T), b(T), o), r, w, (kind, m), bk)
+
+    def cp(out, a, r, w, m, bk=None, kind="c"):
+        add("V", lambda q, T, X: q.tensor_copy(out(T), a(T)), r, w, (kind, m), bk)
+
+    def ms(out, v, w, m, r=()):
+        add("V", lambda q, T, X: q.memset(out(T), v), r, w, ("c", m))
+
+    def act(out, a, f, r, w, m, bk=None, kind="c", bias=None, scale=None):
+        def fn(q, T, X):
+            kw = {}
+            if bias is not None:
+                kw["bias"] = bias(T)
+            if scale is not None:
+                kw["scale"] = scale(T)
+            return q.activation(out(T), a(T), f, **kw)
+        add("S", fn, r, w, (kind, m), bk)
+
+    def relu(e, out, a, r, w, m, bk, bias=None):
+        if e == "S":
+            act(out, a, F.Relu, r, w, m, bk, bias=bias)
+        elif bias is None:
+            ts(out, a, num(0.0), None, A.max, None, r, w, m, bk)
+        else:
+            ts(out, a, bias, num(0.0), A.add, A.max, r, w, m, bk)
+
+    def mm(out, lh, rh, st, sp, r, w, m, bk):
+        add("P", lambda q, T, X: q.matmul(out(T), lh(T), rh(T), st, sp), r, w, ("p", m), bk)
+
+    def group(out, key, bk, terms):
+        for i, x in enumerate(terms):
+            mm(x[4] if len(x) > 4 else out, x[0], x[1], i == 0, i == len(terms) - 1, x[2], [key], x[3], bk)
+
+    def iota(out, pat, base, cm, w, m, flag=True):
+        if flag:
+            add("G", lambda q, T, X: q.iota(out(T), pat, base, cm, allow_small_or_imprecise_dtypes=True), [], w, ("gi", m))
+        else:
+            add("G", lambda q, T, X: q.iota(out(T), pat, base, cm), [], w, ("gi", m))
+
+    def num(v):
+        return lambda T: v
+
+    def ap(name, a=None, b=None, s=None, p1=None):
+        if a is None:
+            return lambda T: T[name][:]
+        if p1 is not None:
+            return lambda T: T[name][0:p1, a:b]
+        if s is None:
+            return lambda T: T[name][:, a:b]
+        return lambda T: T[name][:, a:b:s]
+
+    def ind(name, a, b, oname, c, d):
+        return lambda T: T[name][:, a:b].indirect(T[oname][:, c:d])
+
+    def dma(eng, out, a, r, w, sem, nbytes, slow=False):
+        if slow:
+            add(eng, lambda q, T, X: q.dma_start(out(T), a(T), allow_slow_non_contiguous=True), r, w, ("d", 0), None, sem, ("dl", nbytes))
+        else:
+            add(eng, lambda q, T, X: q.dma_start(out(T), a(T)), r, w, ("d", 0), None, sem, ("dl", nbytes))
+
+    dma("Y", ap("posi"), ap("pos"), [], ["posi"], "lpos", 131072)
+    for i in range(4):
+        dma("Y", ap("tab", 2048 * i, 2048 * i + 2048), ap("feat", 2048 * i, 2048 * i + 2048), [], ["tab%d" % i], "lf%d" % i,
+            131072 + 524288 * (i + 1))
+    dma("S", ap("ub"), ap("u"), [], ["ub"], "lu", 4096)
+    dma("S", ap("vb"), ap("v"), [], ["vb"], "lv", 4096)
+
+    names = {}
+
+    def C(name):
+        j = names.setdefault(name, len(names))
+        return ap("col", j, j + 1)
+
+    def cs(name, src, s1, s2, o0, o1=None):
+        r = ["c_" + x for x in (src, s1, s2) if isinstance(x, str)]
+        f = [C(x) if isinstance(x, str) else num(x) for x in (src, s1, s2)]
+        ts(C(name), f[0], f[1], f[2], o0, o1, r, ["c_" + name], 64)
+
+    iota(ap("ci", 0, 1), [[0, 1]], 0, 1, ["ci0"], 1, False)
+    iota(ap("dw"), [[1, 144]], -16, 0, ["dw"], 144)
+    iota(ap("cg"), [[1, 8], [0, 16]], 0, 0, ["cg"], 128)
+    iota(ap("i2t"), [[2, 8]], 0, 0, ["i2t"], 8)
+    iota(ap("tie"), [[0, 8], [-2, 16]], 15, 0, ["tie"], 128)
+    iota(ap("pw"), [[1, 64], [0, 2]], 0, 0, ["pw"], 128)
+    iota(ap("c4"), [[4, 16]], 0, 0, ["c4"], 16)
+    dma("S", ap("stepi", 0, 1), ap("step"), [], ["stepi"], "lstep", 512)
+
+    C("p")
+    for j, (nm, op, v) in enumerate((("k", A.bitwise_and, 15), ("g", A.arith_shift_right, 4), ("odd", A.bitwise_and, 1),
+                                     ("ph", A.arith_shift_right, 1))):
+        C(nm)
+        ts(ap("ci", j + 1, j + 2), ap("ci", 0, 1), num(v), None, op, None, ["ci0"], ["ci%d" % (j + 1)], 64)
+    cp(ap("col", 0, 5), ap("ci", 0, 5), ["ci%d" % j for j in range(5)], ["c_p", "c_k", "c_g", "c_odd", "c_ph"], 64)
+    cs("king", "k", 0.0, None, A.is_equal)
+    cs("ab", "k", 13.0, 2048.0, A.is_ge, A.mult)
+    cs("big12", "k", 12.0, 1.0e6, A.is_le, A.mult)
+    cs("o32", "odd", 32.0, None, A.mult)
+    cs("b0", "k", -12.0, 32.0, A.add, A.mult)
+    cs("base", "b0", "o32", None, A.max)
+    ts(ap("gm"), ap("i2t"), C("k"), C("big12"), A.is_le, A.mult, ["i2t", "c_k", "c_big12"], ["gm"], 64)
+    ts(ap("thr"), ap("gm"), C("base"), None, A.add, None, ["gm", "c_base"], ["thr"], 64)
+    ts(ap("gm"), ap("dw", 16, 24), C("g"), None, A.is_equal, None, ["dw", "c_g"], ["gm"], 64)
+
+    def blk(name, c):
+        ts(ap(name), ap("cg"), C("g"), C(c), A.is_equal, A.mult, ["cg", "c_g", "c_" + c], [name], 64)
+
+    def diag(name, v, m=64):
+        r = ["dw", "c_p"] + (["c_" + v] if isinstance(v, str) else [])
+        ts(ap(name), ap("dw", 16, 144), C("p"), C(v) if isinstance(v, str) else num(v), A.is_equal, A.mult, r, [name], m)
+
+    diag("eye", 1.0)
+    blk("selk", "king")
+    blk("wb", "ab")
+    ts(ap("ki"), ap("posi"), num(1920), None, A.bitwise_and, None, ["posi"], ["ki"], 256)
+    ts(ap("si"), ap("posi"), num(127), None, A.bitwise_and, None, ["posi"], ["si"], 256)
+    ts(ap("dd"), ap("posi"), num(0.0), num(GONE), A.is_equal, A.mult, ["posi"], ["dd"], 256)
+    cp(ap("kall", 0, LN), ap("ki"), ["ki"], ["kall0"], 256)
+    tt(ap("sin", 0, LN), ap("si"), ap("dd"), A.add, ["si", "dd"], ["sin0_%d" % c for c in range(NCH)], 512)
+
+    def sendk(q, T, X):
+        tr = RemoteDMATransfer(dst_ids=[DstId(rid=X["addr"][j][0], pnc=X["addr"][j][1]) for j in range(1, NR)],
+                               dma_engine_mask=X["mask"], remote_sem=T.sem["karr"], srcs=[T["kall"][:, 0:LN]],
+                               dsts=[T["kall"][:, j * LN:(j + 1) * LN] for j in range(1, NR)])
+        return q.remote_dma_fused([tr], local_sem=T.sem["sent"])
+    add("G", sendk, ["kall0"], ["ksent"], ("r", 0), None, "sent")
+    add(None, None, ["ksent"], ["kall1", "kall2", "kall3"], ("a", 1), None, "karr")
+
+    ms(ap("rs"), 0.0, ["rs"], 64)
+    ms(ap("rs", 0, 128, 16), -float(2 ** 30), ["rs"], 64)
+    def fill(e, name, a, b, v, w):
+        if e == "V":
+            ms(ap(name, a, b), v, w, (b - a) // 2)
+        else:
+            iota(ap(name, a, b), [[0, b - a]], int(v), 0, w, b - a)
+
+    def sel(out, a, pat, op, v, base, cm, r, w, m):
+        add("G", lambda q, T, X: q.affine_select(out(T), a(T), pat, op, v, base, cm), r, w, ("ga", m))
+
+    fill(p["e_f0"], "yb", 0, 9 * n, 0.0, ["yb%d" % c for c in range(NCH)])
+    for par in range(2):
+        for i in range(4):
+            fill(p["e_f1"] if i < 2 else p["e_f2"], "d1", (32 * par + 8 * i) * n, (32 * par + 8 * i + 8) * n, -OFS, ["d1f%d_%d" % (par, i)])
+    ms(ap("ix"), 0.0, ["ix%d" % c for c in range(NCH)], 64)
+    for gi in range(8):
+        for src, dst in (("ub", "uu"), ("vb", "vv")):
+            act(ap(dst, 16 * gi, 16 * gi + 16), ap(src), F.Copy, [src, "gm"], ["%s%d" % (dst, gi)], 64, scale=ap("gm", gi, gi + 1))
+    UU = ["uu%d" % i for i in range(8)]
+    VV = ["vv%d" % i for i in range(8)]
+    cs("chit", "king", 9998.0, 1.0, A.mult, A.add)
+    ts(ap("tiev"), ap("tie"), num(1.0 / 32), None, A.mult, None, ["tie"], ["tiev"], 64)
+    diag("penu", 2.0 ** -28)
+    diag("neye", -1.0)
+    ts(ap("bm"), ap("cg"), C("g"), None, A.is_equal, None, ["cg", "c_g"], ["bm"], 64)
+    cp(C("step"), ap("stepi", 0, 1), ["stepi"], ["c_step"], 64)
+    blk("wst", "step")
+    cs("sg", "odd", -2.0, 1.0, A.mult, A.add)
+    cs("a1", "odd", -64.0, 32.0, A.mult, A.add)
+    cs("kt", "k", -2.0, 15.0, A.mult, A.add)
+    cs("kq", "kt", "kt", -64.0, A.mult, A.mult)
+    cs("b33", "kq", 65.0, None, A.add)
+    cs("b32", "kq", 64.0, None, A.add)
+    if p["nowr"]:
+        cs("w129", "kq", -1.0, 65.0, A.mult, A.add)
+        cs("chi2", "chit", 128.0, None, A.add)
+    ts(ap("ee"), ap("tie"), C("a1"), num(-32.0), A.mult, A.add, ["tie", "c_a1"], ["ee"], 64)
+    sel(ap("ee"), ap("ee"), [[-2, 8], [0, 16]], A.is_ge, 0.0, 0, 1, ["ee"], ["ee"], 128)
+    sel(ap("ee"), ap("ee"), [[2, 8], [0, 16]], A.is_ge, 0.0, 1, -1, ["ee"], ["ee"], 128)
+
+    def negate(i, r):
+        a = 2048 * i
+        if p["neg"][i] in "Ss":
+            act(ap("tab", 8192 + a, 10240 + a), ap("tab", a, a + 2048), F.Copy, ["tab%d" % i] + r, ["neg%d" % i], 2048, scale=num(-1.0))
+        else:
+            ts(ap("tab", 8192 + a, 10240 + a), ap("tab", a, a + 2048), num(-1.0), None, A.mult, None, ["tab%d" % i] + r, ["neg%d" % i], 1024)
+    for i in range(4):
+        if p["neg"][i] in "SV":
+            negate(i, [])
+    for c in range(NCH):
+        fill(p["e_f3"], "hl", c * HS, c * HS + n, 0.0, ["hl%d_0" % c])
+        fill(p["e_f3"], "ha", c * HS, c * HS + n, -OFS, ["ha%d_0" % c])
+    cs("le12", "k", 12.0, "sg", A.is_le, A.mult)
+    cs("s1", "k", "odd", 0.5 * n, A.subtract, A.mult)
+    cs("af", "s1", float(n), None, A.add)
+    cs("apx", "af", "le12", None, A.mult)
+    cs("ath", "ab", -1.0 / 64, None, A.mult)
+    cs("aw", "le12", -256.0, "ath", A.mult, A.add)
+    cs("th2", "ab", 1.0 / 4096, None, A.mult)
+    cs("q0", "g", 8.0, "ph", A.mult, A.subtract)
+    cs("q1", "q0", "th2", 2.0, A.mult, A.mult)
+    cs("q2", "q1", "ph", None, A.add)
+    ts(ap("cmp"), ap("i2t"), C("th2"), C("q2"), A.mult, A.add, ["i2t", "c_th2", "c_q2"], ["cmp"], 64)
+    blk("wp", "apx")
+    for s in range(RO):
+        ts(ap("ws", 128 * s, 128 * s + 128), ap("pw"), ap("cmp", s, s + 1), C("aw"), A.is_equal, A.mult, ["pw", "cmp", "c_aw"], ["ws%d" % s], 64)
+    ts(ap("tmp"), ap("tie", 0, n), C("kt"), num(DEAD), A.not_equal, A.mult, ["tie", "c_kt"], ["tmp5"], 64)
+    tt(ap("cd"), ap("tmp"), ap("dw", 16, 16 + n), A.add, ["tmp5", "dw"], ["cd"], 128)
+    diag("eyef", 1.0, 128)
+    diag("n16", 16384.0)
+    diag("n24", 24576.0)
+    cs("g16o", "g", 16.0, "odd", A.mult, A.add)
+    cs("ge12", "k", 12.0, 1.0e6, A.is_ge, A.mult)
+    cs("cf0", "ge12", "o32", None, A.subtract)
+    cs("cf1", "cf0", -64.0, None, A.add)
+    ts(ap("ci", 8, 9), ap("ci", 1, 2), num(2), None, A.arith_shift_right, None, ["ci1"], ["ci8"], 64)
+    cp(C("rf"), ap("ci", 8, 9), ["ci8"], ["c_rf"], 64)
+    ts(ap("wfw"), ap("dw"), C("g16o"), C("af"), A.is_equal, A.mult, ["dw", "c_g16o", "c_af"], ["wfw"], 72)
+
+    TAB = ["tab%d" % i for i in range(4)]
+    NEG = ["neg%d" % i for i in range(4)]
+    eye, neye = ap("eye"), ap("neye")
+
+    def ply(t, c):
+        ba, bb = 2 * c, 2 * c + 1
+        pa, pb = "pb%d" % ba, "pb%d" % bb
+        cn, h0, par = c * n, c * HS, c % 2
+        S, sk = ap("sin", t * LN + cn, t * LN + cn + n), "sin%d_%d" % (t, c)
+        K, kk = ap("kall", (t % NR) * LN + cn, (t % NR) * LN + cn + n), "kall%d" % (t % NR)
+
+        def Mt(s):
+            return ap("mt", s * LN + cn, s * LN + cn + n)
+
+        def mk(s):
+            return "mt%d_%d" % (s, c)
+
+        def k(x):
+            return "%s%d" % (x, c)
+
+        def loc(name, w=1):
+            return ap(name, w * cn, w * cn + w * n)
+        HL = ["hl%d_%d" % (c, s) for s in range(t + 1)]
+        HA = ["ha%d_%d" % (c, s) for s in range(t + 1)]
+        Lh, lk = ap("hl", h0 + (t + 1) * n, h0 + (t + 2) * n), "hl%d_%d" % (c, t + 1)
+        group(ap(pa, 0, n), k("z"), ba, [(ap("ws", 128 * s, 128 * s + 128), Mt(s), ["ws%d" % s, mk(s)], n) for s in range(t)]
+              + [(ap("selk"), S, ["selk", sk], n)])
+        nep = p["nep"] and t > 0
+        Lp, lb = (ap(pa, 448, 448 + n), ba) if nep else (ap(pb, 0, n), bb)
+        group(Lp, k("nq" if nep else "L"), lb, [(eye, K, ["eye", kk], n), (eye, S, ["eye", sk], n)])
+        ts(Mt(t), ap(pa, 0, n), ap("thr", t, t + 1), None, A.is_ge, None, [k("z"), "thr"], [mk(t)], n, ba)
+        if not nep:
+            relu(p["e_lrelu"], Lh, Lp, [k("L")], [lk], n, bb)
+        st = 32 if t else 16
+        x0 = 32 * cn
+        if t:
+            group(ap(pa, n, 2 * n), k("pt"), ba, [(eye, ap("cd"), ["eye", "cd"], n), (ap("wp"), Mt(t), ["wp", mk(t)], n)])
+            add("V", lambda q, T, X: q.tensor_tensor_scan(T["dg"][:, cn:cn + n], T["rs"][:, 0:n], T[pa][:, n:2 * n], 0.0, A.add, A.max),
+                ["rs", k("pt")], [k("dg")], ("c", n), ba)
+            nc = n // 16
+            cp(ap("poff", 16 * c, 16 * c + nc), ap("dg", cn + 15, cn + n, 16), [k("dg")], [k("poff")], 64)
+            src = ind("hl", h0, h0 + (t + 1) * n, "poff", 16 * c, 16 * c + nc)
+            if p["e_og"] == "S":
+                act(loc("og"), src, F.Copy, HL + [k("poff")], [k("og")], n, kind="gs")
+            else:
+                cp(loc("og"), src, HL + [k("poff")], [k("og")], n, kind="gv")
+            if nep:
+                relu("V", Lh, Lp, [k("nq")], [lk], n, ba)
+                tt(loc("ne"), loc("og"), Lp, A.not_equal, [k("og"), k("nq")], [k("ne")], n, ba)
+            else:
+                tt(loc("ne"), loc("og"), Lh, A.not_equal, [k("og"), lk], [k("ne")], 2 * n)
+            group(ap(pa, 2 * n, 3 * n), k("pl"), ba, [(eye, K, ["eye", kk], n), (eye, S, ["eye", sk], n), (ap("wb"), Mt(t), ["wb", mk(t)], n),
+                                                      (ap("n16"), loc("ne"), ["n16", k("ne")], n)])
+            group(ap(pb, n, 2 * n), k("po"), bb, [(ap("wb"), Mt(t), ["wb", mk(t)], n), (ap("eyef"), loc("og"), ["eyef", k("og")], 4 * n),
+                                                  (ap("n24"), loc("ne"), ["n24", k("ne")], n)])
+            ts(ap("off", 2 * cn + 1, 2 * cn + 2 * n, 2), ap(pa, 2 * n, 3 * n), num(DEAD), num(0.0), A.add, A.max, [k("pl")], [k("offl")], n, ba)
+            ts(ap("off", 2 * cn, 2 * cn + 2 * n, 2), ap(pb, n, 2 * n), num(DEAD), num(0.0), A.add, A.max, [k("po")], [k("offo")], n, bb)
+            vc = p.get("vc%d_%d" % (t, c), p["vcols"])
+            ncol, sp, win, wk = 2 * n, p["spieces"], 16384, TAB + NEG
+        else:
+            group(ap(pa, 2 * n, 3 * n), k("pl"), ba, [(eye, K, ["eye", kk], n), (eye, S, ["eye", sk], n), (ap("wb"), Mt(t), ["wb", mk(t)], n)])
+            ts(ap("off", 2 * cn, 2 * cn + n), ap(pa, 2 * n, 3 * n), num(0.0), None, A.max, None, [k("pl")], [k("offl"), k("offo")], n, ba)
+            ncol, vc, sp, win, wk = n, p["vc0_%d" % c], p["spieces0"], 8192, TAB
+        sc = ncol - vc
+        cuts = [2 * ((sc * i // sp) // 2) for i in range(sp)] + [sc]
+        vp = p["vp"] if vc else 0
+        cuts += [sc + 2 * ((vc * (i + 1) // vp) // 2) for i in range(vp)]
+        XK = ["x%d_%d" % (c, i) for i in range(64)]
+        ok = wk + [k("offl"), k("offo")]
+        for i in range(sp + vp):
+            a, b = cuts[i], cuts[i + 1]
+            dst, src = ap("xb", x0 + 16 * a, x0 + 16 * b), ind("tab", 0, win, "off", 2 * cn + a, 2 * cn + b)
+            if i < sp:
+                act(dst, src, F.Copy, ok, XK[a // 2:b // 2], 16 * (b - a), kind="gs")
+            else:
+                cp(dst, src, ok, XK[a // 2:b // 2], 16 * (b - a), kind="gv")
+        if t == 0 and c == NCH - 1:
+            for i in range(4):
+                if p["neg"][i] in "sv":
+                    negate(i, XK[:1])
+        if t == RO - 1:
+            final(c)
+            outs(c, "yc", "hl", p["e_yc"], 0.0)
+        dn = "d1"
+        d0 = par * 32 * n
+        DK = ["d1_%d_%d" % (par, i) for i in range(8)]
+        df = ["d1f%d_%d" % (par, i) for i in range(st // 8)]
+        if t == 1 and c < 2:
+            ms(ap(dn, d0 + 16, d0 + 16 * n, 32), -OFS, DK[:4], 64)
+        rp = p.get("rp%d_%d" % (t, c), p["rp"]) if t else 1
+        h = n // rp
+        for i in range(rp):
+            a, b = st * h * i, st * h * (i + 1)
+            xf, xk, dk = ap("xb", x0 + a, x0 + b, st), XK[a // 32:b // 32], DK[a // 256:b // 256]
+            if t:
+                tb = ap("tt", cn + h * i, cn + h * i + h)
+                tt(tb, ind("ha", h0, h0 + (t + 1) * n, "poff", 16 * c + h * i // 16, 16 * c + (h * i + h) // 16), xf, A.add,
+                   HA + xk + [k("poff")], [k("tt%d_" % i)], h, kind="gv")
+                ts(ap(dn, d0 + a, d0 + b, st), tb, num(-OFS), None, A.max, None, [k("tt%d_" % i)] + df, dk, 64)
+            else:
+                ts(ap(dn, d0 + a, d0 + b, st), xf, num(-OFS), num(-OFS), A.add, A.max, xk + df, dk, 64)
+            if p["e_ms"] == "V":
+                ms(xf, -1024.0, xk, 64)
+            else:
+                iota(xf, [[0, h]], -1024, 0, xk, h)
+        s0 = par * 32 * n
+        sok = ["so%d_%d" % (par, i) for i in range(8)]
+        scp = max(rp, p["scp"] * st // 32)
+        w = st * n // scp
+
+        def scan(i):
+            add("V", lambda q, T, X: q.tensor_tensor_scan(T["so"][:, s0 + i * w:s0 + i * w + w], T["xb"][:, x0 + i * w:x0 + i * w + w],
+                                                          T[dn][:, d0 + i * w:d0 + i * w + w], 0.0, A.add, A.max),
+                XK[i * w // 32:(i * w + w) // 32] + DK[i * w // 256:(i * w + w) // 256], sok[i * w // 256:(i * w + w) // 256], ("c", w // 2))
+        for i in range(scp):
+            scan(i)
+        fin = ap("so", s0 + st - 1, s0 + st * n, st)
+        ts(ap("yb", 2 * cn + n, 2 * cn + 2 * n), fin, num(OFS), num(127.0), A.add, A.min, sok, [k("yb")], 64)
+        Ah, ak = ap("ha", h0 + (t + 1) * n, h0 + (t + 2) * n), "ha%d_%d" % (c, t + 1)
+        eh = p["e_hist5"] if (t, c) == (RO - 1, NCH - 1) else p["e_hist"]
+        if eh == "G":
+            sel(Ah, fin, [[0, n]], A.is_ge, 0.0, 0, 0, sok, [ak], n)
+        elif eh == "S":
+            act(Ah, fin, F.Copy, sok, [ak], n)
+        else:
+            cp(Ah, fin, sok, [ak], 64)
+        lo, hi = (2 * cn + n, 2 * cn + 3 * n), (2 * cn, 2 * cn + 2 * n)
+        group(ap(pb, 128, 256, p1=2 * n), k("key"), bb,
+              [(eye, ap("tiev"), ["eye", "tiev"], 128), (S, ap("penu"), [sk, "penu"], 128, ap(pb, 128, 256, p1=n)),
+               (ap("yb", *lo), ap("uu"), [k("yb")] + UU, 128), (ap("yb", *hi), ap("vv"), [k("yb")] + VV, 128)])
+        add("V", lambda q, T, X: q.tensor_tensor_scan(T["km"][:, 128 * c:128 * c + 128], T["rs"][:], T[pb][:, 128:256], 0.0, A.add, A.max),
+            ["rs", k("key")], [k("km")], ("c", 128), bb)
+        best = ap("km", 128 * c + 15, 128 * c + 128, 16)
+        cp(ap("ri", 8 * c, 8 * c + 8), best, [k("km")], [k("ri")], 64)
+        tt(ap("ix", 32 * c + 1, 32 * c + 17, 2), best, ap("ri", 8 * c, 8 * c + 8), A.subtract, [k("km"), k("ri")], [k("ix")], 64)
+        group(ap(pa, 256, 384, p1=16), k("tr"), ba, [(ap("ix", 32 * c + 1, 32 * c + 17), eye, [k("ix"), "eye"], 128),
+                                                     (ap("ix", 32 * c, 32 * c + 16), eye, [k("ix"), "eye"], 128)])
+        sq = names["sg"]
+        act(ap("ft", 128 * c, 128 * c + 128, p1=16), ap(pa, 256, 384, p1=16), F.Square, [k("tr"), "c_sg"], [k("ft")], 128, ba,
+            bias=ap("col", sq, sq + 1, p1=16), scale=num(32.0))
+        ee, fu, fv = ap("ee", 0, 128, p1=16), ap("ft", 128 * c, 128 * c + n, p1=16), ap("ft", 128 * c + n, 128 * c + 2 * n, p1=16)
+        group(ap(pb, 256, 256 + n), k("zu"), bb, [(eye, S, ["eye", sk], n), (ee, fu, ["ee", k("ft")], n)])
+        group(ap(pb, 256 + n, 256 + 2 * n), k("zv"), bb, [(ee, fv, ["ee", k("ft")], n)])
+        relu(p["e_zz"], loc("mo", 2), ap(pb, 256, 256 + 2 * n), [k("zu"), k("zv"), "c_b33"], [k("mo")], 2 * n, bb, C("b33"))
+        msq, oh = ap("mo", 2 * cn, 2 * cn + n), ap("mo", 2 * cn + n, 2 * cn + 2 * n)
+        pre = [(ap("bm"), msq, ["bm", k("mo")], n), (ap("wst"), oh, ["wst", k("mo")], n)]
+        wrap = [(neye, loc("wr"), ["neye", k("wr")], n)]
+        s2 = [(eye, S, ["eye", sk], n), (neye, msq, ["neye", k("mo")], n)]
+        last = [(eye, loc("mn"), ["eye", k("mn")], n)]
+        if p["nowr"]:
+            group(ap(pa, 448, 448 + n), k("nq"), ba, [(ee, fu, ["ee", k("ft")], n)] + pre)
+            group(ap(pb, 384, 384 + n), k("e"), bb, [(neye, S, ["neye", sk], n)] + pre)
+            relu("V", loc("mn"), ap(pa, 448, 448 + n), [k("nq"), "c_b32"], [k("mn")], n, ba, C("b32"))
+            ts(loc("wr"), ap(pa, 448, 448 + n), C("w129"), num(128.0), A.is_ge, A.mult, [k("nq"), "c_w129"], [k("wr")], n, ba)
+            ts(loc("h2"), ap(pb, 384, 384 + n), C("chi2"), num(GONE), A.is_equal, A.mult, [k("e"), "c_chi2"], [k("h2")], n, bb)
+            ts(loc("ht"), ap(pb, 384, 384 + n), C("chit"), num(GONE), A.is_equal, A.mult, [k("e"), "c_chit"], [k("ht")], n, bb)
+            last += wrap + [(eye, loc("h2"), ["eye", k("h2")], n)]
+        else:
+            group(ap(pa, 384, 384 + n), k("pre"), ba, pre)
+            ts(loc("wr"), ap(pa, 384, 384 + n), num(129.0), num(128.0), A.is_ge, A.mult, [k("pre")], [k("wr")], n, ba)
+            group(ap(pb, 384, 384 + n), k("e"), bb, [(neye, S, ["neye", sk], n)] + pre + wrap)
+            group(ap(pa, 448, 448 + n), k("nq"), ba, [(ee, fu, ["ee", k("ft")], n)] + pre + wrap)
+            ts(loc("ht"), ap(pb, 384, 384 + n), C("chit"), num(GONE), A.is_equal, A.mult, [k("e"), "c_chit"], [k("ht")], n, bb)
+            relu(p["e_mn"], loc("mn"), ap(pa, 448, 448 + n), [k("nq"), "c_b32"], [k("mn")], n, ba, C("b32"))
+        if t < RO - 1:
+            group(ap(pa, 0, n), k("z"), ba, s2 + last)
+            o = t * LN + cn
+            tt(ap("sout", o, o + n), ap(pa, 0, n), loc("ht"), A.add, [k("z"), k("ht")], ["su%d_%d" % (t, c)], n, ba)
+            an = "ar%d_%d" % (t + 1, c)
+            add("G", lambda q, T, X: q.remote_dma(T["sin"][:, o + LN:o + LN + n], T["sout"][:, o:o + n], T.sem[an], T.sem["sent"],
+                                                  X["addr"][1][1], X["addr"][1][0], X["mask"]),
+                ["su%d_%d" % (t, c)], ["st%d_%d" % (t, c)], ("r", 0), None, "sent")
+            add(None, None, ["st%d_%d" % (t, c)], ["sin%d_%d" % (t + 1, c)], ("a", 0), None, an)
+        else:
+            group(ap(pa, 0, n), k("z"), ba, s2 + [(eye, K, ["eye", kk], n), (eye, loc("ht"), ["eye", k("ht")], n)] + last)
+            relu(p["e_yl"], loc("oyl"), ap(pa, 0, n), [k("z")], [k("oyl")], n, ba)
+            dma("Y", ap("yl", cn, cn + n), loc("oyl"), [k("oyl")], [], "outs", 32768)
+
+    def final(c):
+        ba, bb = 2 * c, 2 * c + 1
+        pb = "pb%d" % bb
+        cn, h0, nc = c * n, c * HS, n // 4
+        group(ap(pb, 448, 448 + n), "zf%d" % c, bb,
+              [(ap("ws", 128 * s, 128 * s + 128), ap("mt", s * LN + cn, s * LN + cn + n), ["ws%d" % s, "mt%d_%d" % (s, c)], n) for s in range(RO)])
+        for h in range(2):
+            ts(ap("fm", 2 * cn + h * n, 2 * cn + h * n + n), ap(pb, 448, 448 + n), C("cf%d" % h), None, A.is_equal, None,
+               ["zf%d" % c, "c_cf%d" % h], ["fm%d_%d" % (c, h)], n, bb)
+        terms = [(eye, ap("c4", 0, nc), ["eye", "c4"], 64)]
+        for h in range(2):
+            for r in range(4):
+                d = 4 * r + 2 * h
+                terms.append((ap("wfw", 16 - d, 144 - d), ap("fm", 2 * cn + h * n + r, 2 * cn + h * n + n, 4), ["wfw", "fm%d_%d" % (c, h)], 64))
+        group(ap(pb, 448, 448 + nc), "zf%d" % c, bb, terms)
+        ts(ap("foff", 16 * c, 16 * c + nc), ap(pb, 448, 448 + nc), C("rf"), None, A.add, None, ["zf%d" % c, "c_rf"], ["foff%d" % c], 64, bb)
+
+    def outs(c, nm, hn, e, bias):
+        cn, h0, nc = c * n, c * HS, n // 4
+        src = ind(hn, h0, h0 + HS, "foff", 16 * c, 16 * c + nc)
+        r = ["%s%d_%d" % (hn, c, s) for s in range(7)] + ["foff%d" % c]
+        dst = ap("o" + nm, 4 * cn, 4 * cn + 4 * n)
+        if e == "S":
+            act(dst, src, F.Identity, r, ["o%s%d" % (nm, c)], 4 * n, kind="gs", bias=num(bias))
+        else:
+            add("V", lambda q, T, X: q.tensor_scalar(dst(T), src(T), bias, None, A.add), r, ["o%s%d" % (nm, c)], ("gv", 4 * n))
+        dma("Y", ap(nm, 4 * cn, 4 * cn + 4 * n), dst, ["o%s%d" % (nm, c)], [], "outs", 131072)
+
+    for t in range(RO):
+        for c in range(NCH):
+            tag[0] = t * NCH + c
+            ply(t, c)
+            if t == RO - 1:
+                outs(c, "ya", "ha", p["e_ya"], OFS)
+    return ops
+
+
+def times(op, p):
+    kind, m = op["cost"]
+    cy = 0.00083 * p["f"]
+    if kind == "c":
+        d = max(64, m) * cy + p["fix"]
+    elif kind == "p":
+        d = max(64, m) * cy * p["pe"]
+    elif kind == "gv":
+        d = 0.05 + m * cy * p["g"]
+    elif kind == "gs":
+        d = 0.065 + m * cy * p["g"]
+    elif kind == "gi":
+        d = 0.13 + 2 * m * cy
+    elif kind == "ga":
+        d = 0.17 + 2 * m * cy
+    elif kind == "r":
+        d = p["riss"]
+    elif kind == "a":
+        return 0.0, p["rlat"] + p["klat"] * m
+    else:
+        return (1.0 if op["eng"] == "G" else 0.1), 2.0 + op["lat"][1] / p["bw"] / 1000.0
+    return d, d
+
+
+def schedule(ops, p):
+    N = len(ops)
+    tm = [times(o, p) for o in ops]
+    succ = [[] for _ in range(N)]
+    for k, o in enumerate(ops):
+        for d in o["deps"]:
+            succ[d].append(k)
+    pr = [0.0] * N
+    z = p["seed"] * 7919 + 1
+    for k in range(N - 1, -1, -1):
+        own = -p["tq"] * ops[k]["tag"] if ops[k]["tag"] is not None else -1.0e3
+        pr[k] = tm[k][1] + max([pr[s] + p["hop"] for s in succ[k]] + [own])
+    for k in range(N):
+        pr[k] += p["off"].get(ops[k]["cls"], 0.0) - p["short"] * tm[k][0]
+    if p["jit"]:
+        for k in range(N):
+            z = (z * 1103515245 + 12345) % 2147483648
+            pr[k] += p["jit"] * (z / 2147483648.0)
+    left = [len(o["deps"]) for o in ops]
+    rdy = [0.0] * N
+    free, order, ready = {}, {}, {}
+    stack = [k for k in range(N) if not left[k]]
+    done = 0
+    while done < N:
+        while stack:
+            k = stack.pop()
+            e = ops[k]["eng"]
+            if e is None:
+                done += 1
+                for s in succ[k]:
+                    rdy[s] = max(rdy[s], rdy[k] + tm[k][1])
+                    left[s] -= 1
+                    if not left[s]:
+                        stack.append(s)
+            else:
+                ready.setdefault(e, []).append(k)
+        be, bt = None, 0.0
+        for e, l in ready.items():
+            if l:
+                t0 = max(free.get(e, 0.0), min([rdy[k] for k in l]))
+                if be is None or t0 < bt:
+                    be, bt = e, t0
+        if be is None:
+            break
+        k = max([k for k in ready[be] if rdy[k] <= bt + p["delta"]], key=lambda j: (pr[j], -j))
+        ready[be].remove(k)
+        st = max(bt, rdy[k])
+        free[be] = st + tm[k][0]
+        order.setdefault(be, []).append(k)
+        done += 1
+        for s in succ[k]:
+            hop = 0.0 if (be == "P" and ops[s]["eng"] == "P") else p["hop"]
+            rdy[s] = max(rdy[s], st + tm[k][1] + hop)
+            left[s] -= 1
+            if not left[s]:
+                stack.append(s)
+    return improve(ops, p, order)
+
+
+def place(ops, tm, pred, key, hop):
+    N = len(ops)
+    start, busy = [0.0] * N, {}
+    for k in sorted(range(N), key=lambda j: key[j]):
+        e = ops[k]["eng"]
+        t0 = 0.0
+        for d, w in pred[k]:
+            t0 = max(t0, start[d] + w)
+        if e is not None:
+            l, du = busy.setdefault(e, []), tm[k][0]
+            i = len(l)
+            while i > 0 and l[i - 1][1] > t0:
+                i -= 1
+            while i < len(l) and l[i][0] < t0 + du - 1e-9:
+                t0 = max(t0, l[i][1])
+                i += 1
+            l.insert(i, (t0, t0 + du))
+        start[k] = t0
+    return start
+
+
+def improve(ops, p, order):
+    N = len(ops)
+    tm = [times(o, p) for o in ops]
+    fw, bw = [[] for _ in range(N)], [[] for _ in range(N)]
+    for k, o in enumerate(ops):
+        for d in o["deps"]:
+            h = 0.0 if (ops[d]["eng"] is None or (o["eng"] == "P" and ops[d]["eng"] == "P")) else p["hop"]
+            fw[k].append((d, tm[d][1] + h))
+            bw[d].append((k, tm[k][0] + h + tm[d][1] - tm[d][0]))
+    key = [0.0] * N
+    nxt = {e: 0 for e in order}
+    fin, free = [None] * N, {e: 0.0 for e in order}
+    todo = [k for k in range(N) if ops[k]["eng"] is None]
+    moved = True
+    while moved:
+        moved = False
+        for k in todo:
+            if fin[k] is None and all([fin[d] is not None for d, w in fw[k]]):
+                fin[k] = max([fin[d] + w for d, w in fw[k]])
+                moved = True
+        for e, l in order.items():
+            while nxt[e] < len(l) and all([fin[d] is not None for d, w in fw[l[nxt[e]]]]):
+                k = l[nxt[e]]
+                fin[k] = max([free[e]] + [fin[d] + w for d, w in fw[k]])
+                free[e] = fin[k] + tm[k][0]
+                nxt[e] += 1
+                moved = True
+    st = fin
+    best, bo = max([st[k] + tm[k][1] for k in range(N)]), order
+    for it in range(p["fbi"]):
+        sb = place(ops, tm, bw, [(-round(st[k] + tm[k][0], 6), -k) for k in range(N)], p["hop"])
+        st = place(ops, tm, fw, [(-round(sb[k] + tm[k][0], 6), k) for k in range(N)], p["hop"])
+        end = max([st[k] + tm[k][1] for k in range(N)])
+        if end < best:
+            best, bo = end, {}
+            for k in sorted(range(N), key=lambda j: (round(st[j], 6), j)):
+                if ops[k]["eng"] is not None:
+                    bo.setdefault(ops[k]["eng"], []).append(k)
+    return bo
+
+
+PLAN = {}
+
+
+def plan():
+    if not PLAN:
+        ops = build(P)
+        PLAN["ops"] = ops
+        PLAN["order"] = schedule(ops, P)
+    return PLAN["ops"], PLAN["order"]
+
+
+def rank_program(g, core, T, topo):
+    rank = T.rank_of(core)
+    if rank is None:
+        return
+    ops, order = plan()
+    peers = [T.cores[(rank + j) % NR] for j in range(NR)]
+    mask = topo.mask(core, peers[1])
+    for c in peers[2:]:
+        mask &= topo.mask(core, c)
+    ne = bin(mask).count("1")
+    X = {"addr": [topo.addr(c) for c in peers], "mask": mask}
+    queue = {"V": g.vector, "S": g.scalar, "P": g.tensor, "G": g, "Y": g.sync}
+    pos = {}
+    for e, l in order.items():
+        for i, k in enumerate(l):
+            pos[k] = i
+    waits, needed = {}, set()
+    for e, l in order.items():
+        seen = {}
+        for k in l:
+            top = {}
+            for d in ops[k]["deps"]:
+                o = ops[d]
+                if o["sem"] is not None:
+                    top[("x", d)] = d
+                elif not (e == "P" and o["eng"] == "P"):
+                    f = o["eng"]
+                    if f not in top or pos[d] > pos[top[f]]:
+                        top[f] = d
+            w = []
+            for f, d in top.items():
+                if ops[d]["sem"] is not None:
+                    if f not in seen:
+                        seen[f] = 1
+                        w.append(d)
+                elif seen.get(f, -1) < pos[d]:
+                    seen[f] = pos[d]
+                    w.append(d)
+                    needed.add(d)
+            waits[k] = sorted(w)
+    token, total = {}, {}
+    for e, l in order.items():
+        for k in l:
+            if k in needed:
+                total["s" + e] = total.get("s" + e, 0) + 1
+                token[k] = ("s" + e, total["s" + e])
+    for k, o in enumerate(ops):
+        if o["eng"] is None:
+            token[k] = (o["sem"], ne * (NR - 1 if o["sem"] == "karr" else 1))
+        elif o["cost"][0] == "d":
+            token[k] = (o["sem"], 16)
+    nout = nsent = 0
+    for e, l in order.items():
+        q = queue[e]
+        for k in l:
+            for d in waits[k]:
+                q.wait_ge(T.sem[token[d][0]], token[d][1])
+            o = ops[k]
+            ins = o["fn"](q, T, X)
+            if o["cost"][0] == "d":
+                ins.then_inc(T.sem[o["sem"]], 16)
+                nout += 16 if o["sem"] == "outs" else 0
+            elif o["cost"][0] == "r":
+                nsent += ne
+            elif k in needed:
+                ins.then_inc(T.sem["s" + e], 1)
+    g.wait_ge(T.sem["sent"], nsent)
+    g.sync.wait_ge(T.sem["outs"], nout)

@@ -16,11 +16,16 @@ P = {"vcols": 4, "spieces": 3, "vc0_0": 40, "vc0_1": 32, "vc0_2": 0, "vc0_3": 8,
      "g": 1.56, "f": 1.25, "pe": 0.5, "hop": 0.1, "rlat": 2.5, "riss": 0.6, "klat": 10.0, "bw": 250.0, "fix": 0.02,
      "tq": 2.0, "short": 4.0, "scp": 2, "vp": 1, "seed": 0, "jit": 0.0, "off": {}, "fbi": 6}
 
-P.update({"spieces": 2, "e_hist5": "V", "vc5_3": 32, "vc5_2": 16, "vc5_1": 8, "tq": 4, "seed": 49, "jit": 0.2})
+P.update({"spieces": 2, "e_hist5": "V", "vc5_3": 32, "vc5_2": 16, "vc5_1": 8, "tq": 4, "seed": 49, "jit": 0.0,
+          "x0": 1, "neg2": 1, "e_sg": "V", "nowr": 1, "scp": 4, "e_ms": "V",
+          "hop": 0.22, "rlat": 2.8, "riss": 0.8, "f": 1.2, "g": 1.6})
+P.update({"vcols": 12, "spieces": 3, "spieces0": 2, "e_f0": "G", "e_f2": "G", "vc0_1": 16, "vc0_3": 0, "vc1_1": 24, "vc5_3": 16,
+          "vc5_2": 32, "vc5_1": 16, "vc5_0": 0, "scp": 2, "g": 1.9, "pe": 0.7})
+P.update({"e_hist5": "G", "vc0_3": 8, "vc1_0": 40, "hop": 0.23})
 
 BF, F32, I32, U16 = "bfloat16", "float32", "int32", "uint16"
 SCRATCH = {
-    "tab": ("sbuf", [128, 16384], BF),
+    "tab": ("sbuf", [128, 16400], BF),
     "xb": ("sbuf", [128, 32 * LN], BF), "so": ("sbuf", [128, 2 * 32 * n], BF),
     "d1": ("sbuf", [128, 2 * 32 * n], BF),
     "hl": ("sbuf", [128, NCH * HS], F32), "ha": ("sbuf", [128, NCH * HS], BF),
@@ -30,8 +35,10 @@ SCRATCH = {
     "mt": ("sbuf", [128, RO * LN], BF), "dg": ("sbuf", [128, LN], F32), "poff": ("sbuf", [128, 16 * NCH], U16),
     "og": ("sbuf", [128, LN], F32), "ne": ("sbuf", [128, LN], BF), "off": ("sbuf", [128, 2 * LN], U16),
     "tt": ("sbuf", [128, LN], BF), "yb": ("sbuf", [128, 9 * n], BF),
-    "km": ("sbuf", [128, 128 * NCH], F32), "ri": ("sbuf", [128, 8 * NCH], I32), "ix": ("sbuf", [128, 32 * NCH], BF),
-    "ft": ("sbuf", [128, 128 * NCH], BF), "mo": ("sbuf", [128, 2 * LN], BF), "wr": ("sbuf", [128, LN], BF),
+    "km": ("sbuf", [128, 128 * NCH], F32), "lastc": ("sbuf", [128, 8], U16),
+    "selkf": ("sbuf", [128, 128], F32), "cd2": ("sbuf", [128, n], BF), "dg2": ("sbuf", [128, LN], F32),
+    "xoff": ("sbuf", [128, 16 * NCH], U16), "sg": ("sbuf", [128, LN], BF),
+    "ft": ("sbuf", [128, 128 * NCH], BF), "kc": ("sbuf", [128, 128 * NCH], F32), "mo": ("sbuf", [128, 2 * LN], BF), "wr": ("sbuf", [128, LN], BF),
     "ht": ("sbuf", [128, LN], BF), "h2": ("sbuf", [128, LN], BF), "mn": ("sbuf", [128, LN], BF),
     "fm": ("sbuf", [128, 2 * LN], BF), "foff": ("sbuf", [128, 16 * NCH], U16),
     "oyl": ("sbuf", [128, LN], F32), "oya": ("sbuf", [128, 4 * LN], F32), "oyc": ("sbuf", [128, 4 * LN], F32),
@@ -41,7 +48,7 @@ SCRATCH = {
     "cmp": ("sbuf", [128, 8], F32), "wfw": ("sbuf", [128, 144], BF), "ws": ("sbuf", [128, RO * 128], BF),
     "tmp": ("sbuf", [128, n], F32),
 }
-for _m in ("bm", "eye", "neye", "selk", "wp", "wb", "wst", "uu", "vv", "penu", "tiev", "ee", "n16", "n24"):
+for _m in ("bm", "eye", "neye", "selk", "wp", "wb", "wst", "uu", "vv", "penu", "tiev", "ee", "selk24", "n16", "n24"):
     SCRATCH[_m] = ("sbuf", [128, 128], BF)
 SCRATCH["eyef"] = ("sbuf", [128, 128], F32)
 for _b in range(8):
@@ -235,7 +242,6 @@ def build(p):
     for par in range(2):
         for i in range(4):
             fill(p["e_f1"] if i < 2 else p["e_f2"], "d1", (32 * par + 8 * i) * n, (32 * par + 8 * i + 8) * n, -OFS, ["d1f%d_%d" % (par, i)])
-    ms(ap("ix"), 0.0, ["ix%d" % c for c in range(NCH)], 64)
     for gi in range(8):
         for src, dst in (("ub", "uu"), ("vb", "vv")):
             act(ap(dst, 16 * gi, 16 * gi + 16), ap(src), F.Copy, [src, "gm"], ["%s%d" % (dst, gi)], 64, scale=ap("gm", gi, gi + 1))
@@ -249,17 +255,22 @@ def build(p):
     cp(C("step"), ap("stepi", 0, 1), ["stepi"], ["c_step"], 64)
     blk("wst", "step")
     cs("sg", "odd", -2.0, 1.0, A.mult, A.add)
-    cs("a1", "odd", -64.0, 32.0, A.mult, A.add)
     cs("kt", "k", -2.0, 15.0, A.mult, A.add)
-    cs("kq", "kt", "kt", -64.0, A.mult, A.mult)
-    cs("b33", "kq", 65.0, None, A.add)
-    cs("b32", "kq", 64.0, None, A.add)
+    cs("b33", "king", 0.0, -255.0, A.mult, A.add)
+    cs("b32", "king", 0.0, -256.0, A.mult, A.add)
     if p["nowr"]:
-        cs("w129", "kq", -1.0, 65.0, A.mult, A.add)
-        cs("chi2", "chit", 128.0, None, A.add)
-    ts(ap("ee"), ap("tie"), C("a1"), num(-32.0), A.mult, A.add, ["tie", "c_a1"], ["ee"], 64)
-    sel(ap("ee"), ap("ee"), [[-2, 8], [0, 16]], A.is_ge, 0.0, 0, 1, ["ee"], ["ee"], 128)
-    sel(ap("ee"), ap("ee"), [[2, 8], [0, 16]], A.is_ge, 0.0, 1, -1, ["ee"], ["ee"], 128)
+        cs("w129", "king", 0.0, 385.0, A.mult, A.add)
+        cs("chi2", "king", 9998.0, 129.0, A.mult, A.add)
+    diag("ee", 256.0)
+    iota(ap("ci", 8, 16), [[16, 8]], 15, 0, ["ci9"], 8, False)
+    cp(ap("lastc"), ap("ci", 8, 16), ["ci9"], ["lastc"], 64)
+    if p["x0"]:
+        cs("k16", "king", 16384.0, None, A.mult)
+        ts(ap("selkf"), ap("cg"), C("g"), C("king"), A.is_equal, A.mult, ["cg", "c_g", "c_king"], ["selkf"], 128)
+        cs("k24", "king", 24576.0, None, A.mult)
+        blk("selk24", "k24")
+        ts(ap("cd2"), ap("tie", 0, n), C("kt"), num(-131072.0), A.not_equal, A.mult, ["tie", "c_kt"], ["cd2"], 64)
+        ms(ap("tab", 16384, 16400), -1024.0, ["tabx"], 64)
 
     def negate(i, r):
         a = 2048 * i
@@ -296,8 +307,8 @@ def build(p):
     cs("ge12", "k", 12.0, 1.0e6, A.is_ge, A.mult)
     cs("cf0", "ge12", "o32", None, A.subtract)
     cs("cf1", "cf0", -64.0, None, A.add)
-    ts(ap("ci", 8, 9), ap("ci", 1, 2), num(2), None, A.arith_shift_right, None, ["ci1"], ["ci8"], 64)
-    cp(C("rf"), ap("ci", 8, 9), ["ci8"], ["c_rf"], 64)
+    ts(ap("ci", 6, 7), ap("ci", 1, 2), num(2), None, A.arith_shift_right, None, ["ci1"], ["ci8"], 64)
+    cp(C("rf"), ap("ci", 6, 7), ["ci8"], ["c_rf"], 64)
     ts(ap("wfw"), ap("dw"), C("g16o"), C("af"), A.is_equal, A.mult, ["dw", "c_g16o", "c_af"], ["wfw"], 72)
 
     TAB = ["tab%d" % i for i in range(4)]
@@ -349,6 +360,8 @@ def build(p):
             if nep:
                 relu("V", Lh, Lp, [k("nq")], [lk], n, ba)
                 tt(loc("ne"), loc("og"), Lp, A.not_equal, [k("og"), k("nq")], [k("ne")], n, ba)
+            elif p["neg2"]:
+                tt(loc("ne"), src, Lh, A.not_equal, HL + [k("poff"), lk], [k("ne")], n, kind="gv")
             else:
                 tt(loc("ne"), loc("og"), Lh, A.not_equal, [k("og"), lk], [k("ne")], 2 * n)
             group(ap(pa, 2 * n, 3 * n), k("pl"), ba, [(eye, K, ["eye", kk], n), (eye, S, ["eye", sk], n), (ap("wb"), Mt(t), ["wb", mk(t)], n),
@@ -356,9 +369,24 @@ def build(p):
             group(ap(pb, n, 2 * n), k("po"), bb, [(ap("wb"), Mt(t), ["wb", mk(t)], n), (ap("eyef"), loc("og"), ["eyef", k("og")], 4 * n),
                                                   (ap("n24"), loc("ne"), ["n24", k("ne")], n)])
             ts(ap("off", 2 * cn + 1, 2 * cn + 2 * n, 2), ap(pa, 2 * n, 3 * n), num(DEAD), num(0.0), A.add, A.max, [k("pl")], [k("offl")], n, ba)
-            ts(ap("off", 2 * cn, 2 * cn + 2 * n, 2), ap(pb, n, 2 * n), num(DEAD), num(0.0), A.add, A.max, [k("po")], [k("offo")], n, bb)
             vc = p.get("vc%d_%d" % (t, c), p["vcols"])
             ncol, sp, win, wk = 2 * n, p["spieces"], 16384, TAB + NEG
+            if p["x0"]:
+                ts(ap("off", 2 * cn, 2 * cn + 2 * n, 2), ap(pb, n, 2 * n), num(DEAD), C("k16"), A.add, A.max, [k("po"), "c_k16"], [k("offo")], n, bb)
+                group(ap(pb, 256, 256 + n), k("xk"), bb,
+                      [(eye, ap("cd2"), ["eye", "cd2"], n), (ap("wb"), Mt(t), ["wb", mk(t)], n), (ap("selkf"), loc("og"), ["selkf", k("og")], 4 * n),
+                       (ap("selk24"), loc("ne"), ["selk24", k("ne")], n)])
+                add("V", lambda q, T, X: q.tensor_tensor_scan(T["dg2"][:, cn:cn + n], T["rs"][:, 0:n], T[pb][:, 256:256 + n], 0.0, A.add, A.max),
+                    ["rs", k("xk")], [k("dgx")], ("c", n), bb)
+                ts(ap("xoff", 16 * c, 16 * c + nc), ap("dg2", cn + 15, cn + n, 16), num(DEAD), num(0.0), A.add, A.max, [k("dgx")], [k("xoff")], 64)
+                src = ind("ha", h0, h0 + (t + 1) * n, "poff", 16 * c, 16 * c + nc)
+                if p["e_sg"] == "S":
+                    act(loc("sg"), src, F.Copy, HA + [k("poff")], [k("sg")], n, kind="gs")
+                else:
+                    cp(loc("sg"), src, HA + [k("poff")], [k("sg")], n, kind="gv")
+                win, wk = 16400, wk + ["tabx"]
+            else:
+                ts(ap("off", 2 * cn, 2 * cn + 2 * n, 2), ap(pb, n, 2 * n), num(DEAD), num(0.0), A.add, A.max, [k("po")], [k("offo")], n, bb)
         else:
             group(ap(pa, 2 * n, 3 * n), k("pl"), ba, [(eye, K, ["eye", kk], n), (eye, S, ["eye", sk], n), (ap("wb"), Mt(t), ["wb", mk(t)], n)])
             ts(ap("off", 2 * cn, 2 * cn + n), ap(pa, 2 * n, 3 * n), num(0.0), None, A.max, None, [k("pl")], [k("offl"), k("offo")], n, ba)
@@ -391,6 +419,10 @@ def build(p):
             ms(ap(dn, d0 + 16, d0 + 16 * n, 32), -OFS, DK[:4], 64)
         rp = p.get("rp%d_%d" % (t, c), p["rp"]) if t else 1
         h = n // rp
+        if t and p["x0"]:
+            rp = 0
+            tt(loc("tt"), ind("tab", 0, 16384, "xoff", 16 * c, 16 * c + n // 16), loc("sg"), A.add, wk + [k("xoff"), k("sg")], [k("tt")], n, kind="gv")
+            ts(ap(dn, d0, d0 + st * n, st), loc("tt"), num(-OFS), None, A.max, None, [k("tt")] + df, DK, 64)
         for i in range(rp):
             a, b = st * h * i, st * h * (i + 1)
             xf, xk, dk = ap("xb", x0 + a, x0 + b, st), XK[a // 32:b // 32], DK[a // 256:b // 256]
@@ -407,7 +439,7 @@ def build(p):
                 iota(xf, [[0, h]], -1024, 0, xk, h)
         s0 = par * 32 * n
         sok = ["so%d_%d" % (par, i) for i in range(8)]
-        scp = max(rp, p["scp"] * st // 32)
+        scp = max(1, rp, p["scp"] * st // 32)
         w = st * n // scp
 
         def scan(i):
@@ -432,36 +464,32 @@ def build(p):
                (ap("yb", *lo), ap("uu"), [k("yb")] + UU, 128), (ap("yb", *hi), ap("vv"), [k("yb")] + VV, 128)])
         add("V", lambda q, T, X: q.tensor_tensor_scan(T["km"][:, 128 * c:128 * c + 128], T["rs"][:], T[pb][:, 128:256], 0.0, A.add, A.max),
             ["rs", k("key")], [k("km")], ("c", 128), bb)
-        best = ap("km", 128 * c + 15, 128 * c + 128, 16)
-        cp(ap("ri", 8 * c, 8 * c + 8), best, [k("km")], [k("ri")], 64)
-        tt(ap("ix", 32 * c + 1, 32 * c + 17, 2), best, ap("ri", 8 * c, 8 * c + 8), A.subtract, [k("km"), k("ri")], [k("ix")], 64)
-        group(ap(pa, 256, 384, p1=16), k("tr"), ba, [(ap("ix", 32 * c + 1, 32 * c + 17), eye, [k("ix"), "eye"], 128),
-                                                     (ap("ix", 32 * c, 32 * c + 16), eye, [k("ix"), "eye"], 128)])
-        sq = names["sg"]
-        act(ap("ft", 128 * c, 128 * c + 128, p1=16), ap(pa, 256, 384, p1=16), F.Square, [k("tr"), "c_sg"], [k("ft")], 128, ba,
-            bias=ap("col", sq, sq + 1, p1=16), scale=num(32.0))
-        ee, fu, fv = ap("ee", 0, 128, p1=16), ap("ft", 128 * c, 128 * c + n, p1=16), ap("ft", 128 * c + n, 128 * c + 2 * n, p1=16)
-        group(ap(pb, 256, 256 + n), k("zu"), bb, [(eye, S, ["eye", sk], n), (ee, fu, ["ee", k("ft")], n)])
-        group(ap(pb, 256 + n, 256 + 2 * n), k("zv"), bb, [(ee, fv, ["ee", k("ft")], n)])
-        relu(p["e_zz"], loc("mo", 2), ap(pb, 256, 256 + 2 * n), [k("zu"), k("zv"), "c_b33"], [k("mo")], 2 * n, bb, C("b33"))
+        cp(ap("kc", 128 * c, 128 * c + 128), ap(pb, 128, 256), [k("key")], [k("kc")], 128, bb)
+        hh = ap("ft", 128 * c, 128 * c + 128)
+        tt(hh, ind("km", 128 * c, 128 * c + 128, "lastc", 0, 8), ap("kc", 128 * c, 128 * c + 128),
+           A.is_equal, [k("km"), k("kc"), "lastc"], [k("ft")], 128, kind="gv")
+        group(ap(pa, 256, 256 + n), k("zu"), ba, [(eye, S, ["eye", sk], n), (hh, ap("ee", 0, n), ["ee", k("ft")], n)])
+        group(ap(pa, 256 + n, 256 + 2 * n), k("zv"), ba, [(hh, ap("ee", n, 2 * n), ["ee", k("ft")], n)])
+        relu(p["e_zz"], loc("mo", 2), ap(pa, 256, 256 + 2 * n), [k("zu"), k("zv"), "c_b33"], [k("mo")], 2 * n, ba, C("b33"))
+        win1 = [(hh, ap("ee", 0, n), ["ee", k("ft")], n)]
         msq, oh = ap("mo", 2 * cn, 2 * cn + n), ap("mo", 2 * cn + n, 2 * cn + 2 * n)
         pre = [(ap("bm"), msq, ["bm", k("mo")], n), (ap("wst"), oh, ["wst", k("mo")], n)]
         wrap = [(neye, loc("wr"), ["neye", k("wr")], n)]
         s2 = [(eye, S, ["eye", sk], n), (neye, msq, ["neye", k("mo")], n)]
         last = [(eye, loc("mn"), ["eye", k("mn")], n)]
         if p["nowr"]:
-            group(ap(pa, 448, 448 + n), k("nq"), ba, [(ee, fu, ["ee", k("ft")], n)] + pre)
-            group(ap(pb, 384, 384 + n), k("e"), bb, [(neye, S, ["neye", sk], n)] + pre)
-            relu("V", loc("mn"), ap(pa, 448, 448 + n), [k("nq"), "c_b32"], [k("mn")], n, ba, C("b32"))
-            ts(loc("wr"), ap(pa, 448, 448 + n), C("w129"), num(128.0), A.is_ge, A.mult, [k("nq"), "c_w129"], [k("wr")], n, ba)
-            ts(loc("h2"), ap(pb, 384, 384 + n), C("chi2"), num(GONE), A.is_equal, A.mult, [k("e"), "c_chi2"], [k("h2")], n, bb)
-            ts(loc("ht"), ap(pb, 384, 384 + n), C("chit"), num(GONE), A.is_equal, A.mult, [k("e"), "c_chit"], [k("ht")], n, bb)
+            group(ap(pb, 0, n), k("L"), bb, win1 + pre)
+            group(ap(pa, 384, 384 + n), k("e"), ba, [(neye, S, ["neye", sk], n)] + pre)
+            relu("V", loc("mn"), ap(pb, 0, n), [k("L"), "c_b32"], [k("mn")], n, bb, C("b32"))
+            ts(loc("wr"), ap(pb, 0, n), C("w129"), num(128.0), A.is_ge, A.mult, [k("L"), "c_w129"], [k("wr")], n, bb)
+            ts(loc("h2"), ap(pa, 384, 384 + n), C("chi2"), num(GONE), A.is_equal, A.mult, [k("e"), "c_chi2"], [k("h2")], n, ba)
+            ts(loc("ht"), ap(pa, 384, 384 + n), C("chit"), num(GONE), A.is_equal, A.mult, [k("e"), "c_chit"], [k("ht")], n, ba)
             last += wrap + [(eye, loc("h2"), ["eye", k("h2")], n)]
         else:
             group(ap(pa, 384, 384 + n), k("pre"), ba, pre)
             ts(loc("wr"), ap(pa, 384, 384 + n), num(129.0), num(128.0), A.is_ge, A.mult, [k("pre")], [k("wr")], n, ba)
             group(ap(pb, 384, 384 + n), k("e"), bb, [(neye, S, ["neye", sk], n)] + pre + wrap)
-            group(ap(pa, 448, 448 + n), k("nq"), ba, [(ee, fu, ["ee", k("ft")], n)] + pre + wrap)
+            group(ap(pa, 448, 448 + n), k("nq"), ba, win1 + pre + wrap)
             ts(loc("ht"), ap(pb, 384, 384 + n), C("chit"), num(GONE), A.is_equal, A.mult, [k("e"), "c_chit"], [k("ht")], n, bb)
             relu(p["e_mn"], loc("mn"), ap(pa, 448, 448 + n), [k("nq"), "c_b32"], [k("mn")], n, ba, C("b32"))
         if t < RO - 1:

@@ -21,7 +21,9 @@ P.update({"spieces": 2, "e_hist5": "V", "vc5_3": 32, "vc5_2": 16, "vc5_1": 8, "t
           "hop": 0.22, "rlat": 2.8, "riss": 0.8, "f": 1.2, "g": 1.6})
 P.update({"vcols": 12, "spieces": 3, "spieces0": 2, "e_f0": "G", "e_f2": "G", "vc0_1": 16, "vc0_3": 0, "vc1_1": 24, "vc5_3": 16,
           "vc5_2": 32, "vc5_1": 16, "vc5_0": 0, "scp": 2, "g": 1.9, "pe": 0.7})
-P.update({"e_hist5": "G", "vc0_3": 8, "vc1_0": 40, "hop": 0.23})
+P.update({"e_hist5": "G", "vc0_3": 8, "vc1_0": 40, "hop": 0.23, "iters": 3000, "temp": 0.0003, "e_kc": "V", "dgp": 0})
+P.update({"vcols": 8, "spieces": 4, "vc1_1": 32, "vc5_3": 40, "vc5_2": 24, "vc5_1": 24, "vc5_0": 16, "vp": 2, "e_sg": "S"})
+P.update({"vcols": 16, "e_f3": "V", "vc0_1": 24, "vc1_1": 16, "vc5_1": 0, "e_ms": "G", "rlat": 2.6, "fix": 0.0, "bw": 450.0, "iters": 0})
 
 BF, F32, I32, U16 = "bfloat16", "float32", "int32", "uint16"
 SCRATCH = {
@@ -45,10 +47,10 @@ SCRATCH = {
     "ci": ("sbuf", [128, 16], I32), "col": ("sbuf", [128, 64], F32), "thr": ("sbuf", [128, 8], F32), "gm": ("sbuf", [128, 8], F32),
     "i2t": ("sbuf", [128, 8], F32), "cg": ("sbuf", [128, 128], BF), "pw": ("sbuf", [128, 128], BF), "dw": ("sbuf", [128, 144], BF),
     "tie": ("sbuf", [128, 128], BF), "c4": ("sbuf", [128, 16], BF), "rs": ("sbuf", [128, 128], BF), "cd": ("sbuf", [128, n], BF),
-    "cmp": ("sbuf", [128, 8], F32), "wfw": ("sbuf", [128, 144], BF), "ws": ("sbuf", [128, RO * 128], BF),
+    "cmp": ("sbuf", [128, 8], F32), "wfw": ("sbuf", [128, 144], BF), "wpw": ("sbuf", [128, 144], BF), "ws": ("sbuf", [128, RO * 128], BF),
     "tmp": ("sbuf", [128, n], F32),
 }
-for _m in ("bm", "eye", "neye", "selk", "wp", "wb", "wst", "uu", "vv", "penu", "tiev", "ee", "selk24", "n16", "n24"):
+for _m in ("bm", "eye", "neye", "selk", "wp", "wb", "wst", "uu", "vv", "penu", "tiev", "ee", "e4", "selk24", "n16", "n24"):
     SCRATCH[_m] = ("sbuf", [128, 128], BF)
 SCRATCH["eyef"] = ("sbuf", [128, 128], F32)
 for _b in range(8):
@@ -295,11 +297,17 @@ def build(p):
     cs("q1", "q0", "th2", 2.0, A.mult, A.mult)
     cs("q2", "q1", "ph", None, A.add)
     ts(ap("cmp"), ap("i2t"), C("th2"), C("q2"), A.mult, A.add, ["i2t", "c_th2", "c_q2"], ["cmp"], 64)
-    blk("wp", "apx")
+    if p["dgp"]:
+        cs("g16", "g", 16.0, None, A.mult)
+        ts(ap("wpw"), ap("dw"), C("g16"), C("apx"), A.is_equal, A.mult, ["dw", "c_g16", "c_apx"], ["wpw"], 72)
+        diag("e4", 4.0)
+    else:
+        blk("wp", "apx")
     for s in range(RO):
         ts(ap("ws", 128 * s, 128 * s + 128), ap("pw"), ap("cmp", s, s + 1), C("aw"), A.is_equal, A.mult, ["pw", "cmp", "c_aw"], ["ws%d" % s], 64)
-    ts(ap("tmp"), ap("tie", 0, n), C("kt"), num(DEAD), A.not_equal, A.mult, ["tie", "c_kt"], ["tmp5"], 64)
-    tt(ap("cd"), ap("tmp"), ap("dw", 16, 16 + n), A.add, ["tmp5", "dw"], ["cd"], 128)
+    if not p["dgp"]:
+        ts(ap("tmp"), ap("tie", 0, n), C("kt"), num(DEAD), A.not_equal, A.mult, ["tie", "c_kt"], ["tmp5"], 64)
+        tt(ap("cd"), ap("tmp"), ap("dw", 16, 16 + n), A.add, ["tmp5", "dw"], ["cd"], 128)
     diag("eyef", 1.0, 128)
     diag("n16", 16384.0)
     diag("n24", 24576.0)
@@ -347,11 +355,17 @@ def build(p):
         st = 32 if t else 16
         x0 = 32 * cn
         if t:
-            group(ap(pa, n, 2 * n), k("pt"), ba, [(eye, ap("cd"), ["eye", "cd"], n), (ap("wp"), Mt(t), ["wp", mk(t)], n)])
-            add("V", lambda q, T, X: q.tensor_tensor_scan(T["dg"][:, cn:cn + n], T["rs"][:, 0:n], T[pa][:, n:2 * n], 0.0, A.add, A.max),
-                ["rs", k("pt")], [k("dg")], ("c", n), ba)
             nc = n // 16
-            cp(ap("poff", 16 * c, 16 * c + nc), ap("dg", cn + 15, cn + n, 16), [k("dg")], [k("poff")], 64)
+            if p["dgp"]:
+                m0 = t * LN + cn
+                group(ap(pa, n, n + nc), k("pt"), ba, [(ap("e4"), ap("c4", 0, nc), ["e4", "c4"], 64)]
+                      + [(ap("wpw", 16 - r, 144 - r), ap("mt", m0 + r, m0 + n, 16), ["wpw", mk(t)], 64) for r in range(16)])
+                ts(ap("poff", 16 * c, 16 * c + nc), ap(pa, n, n + nc), C("k"), None, A.add, None, [k("pt"), "c_k"], [k("poff")], 64, ba)
+            else:
+                group(ap(pa, n, 2 * n), k("pt"), ba, [(eye, ap("cd"), ["eye", "cd"], n), (ap("wp"), Mt(t), ["wp", mk(t)], n)])
+                add("V", lambda q, T, X: q.tensor_tensor_scan(T["dg"][:, cn:cn + n], T["rs"][:, 0:n], T[pa][:, n:2 * n], 0.0, A.add, A.max),
+                    ["rs", k("pt")], [k("dg")], ("c", n), ba)
+                cp(ap("poff", 16 * c, 16 * c + nc), ap("dg", cn + 15, cn + n, 16), [k("dg")], [k("poff")], 64)
             src = ind("hl", h0, h0 + (t + 1) * n, "poff", 16 * c, 16 * c + nc)
             if p["e_og"] == "S":
                 act(loc("og"), src, F.Copy, HL + [k("poff")], [k("og")], n, kind="gs")
@@ -464,7 +478,13 @@ def build(p):
                (ap("yb", *lo), ap("uu"), [k("yb")] + UU, 128), (ap("yb", *hi), ap("vv"), [k("yb")] + VV, 128)])
         add("V", lambda q, T, X: q.tensor_tensor_scan(T["km"][:, 128 * c:128 * c + 128], T["rs"][:], T[pb][:, 128:256], 0.0, A.add, A.max),
             ["rs", k("key")], [k("km")], ("c", 128), bb)
-        cp(ap("kc", 128 * c, 128 * c + 128), ap(pb, 128, 256), [k("key")], [k("kc")], 128, bb)
+        if p["e_kc"] == "S":
+            group(ap(pa, 128, 256), k("pl"), ba,
+                  [(eye, ap("tiev"), ["eye", "tiev"], 128), (S, ap("penu"), [sk, "penu"], 128, ap(pa, 128, 256, p1=n)),
+                   (ap("yb", *lo), ap("uu"), [k("yb")] + UU, 128), (ap("yb", *hi), ap("vv"), [k("yb")] + VV, 128)])
+            act(ap("kc", 128 * c, 128 * c + 128), ap(pa, 128, 256), F.Copy, [k("pl")], [k("kc")], 128, ba)
+        else:
+            cp(ap("kc", 128 * c, 128 * c + 128), ap(pb, 128, 256), [k("key")], [k("kc")], 128, bb)
         hh = ap("ft", 128 * c, 128 * c + 128)
         tt(hh, ind("km", 128 * c, 128 * c + 128, "lastc", 0, 8), ap("kc", 128 * c, 128 * c + 128),
            A.is_equal, [k("km"), k("kc"), "lastc"], [k("ft")], 128, kind="gv")
@@ -688,6 +708,102 @@ def improve(ops, p, order):
     return bo
 
 
+CASES = [{"g": 1.2, "f": 1.0, "hop": 0.26, "rlat": 2.5, "pe": 0.5, "fix": 0.0, "riss": 0.8, "bw": 350.0, "klat": 5.0, "base": 98.8},
+         {"g": 2.0, "f": 1.45, "hop": 0.25, "rlat": 2.2, "pe": 0.5, "fix": 0.0, "riss": 1.2, "bw": 250.0, "klat": 5.0, "base": 135.1},
+         {"g": 1.3, "f": 1.45, "hop": 0.22, "rlat": 2.9, "pe": 0.6, "fix": 0.01, "riss": 0.6, "bw": 300.0, "klat": 5.0, "base": 119.1},
+         {"g": 1.9, "f": 1.1, "hop": 0.24, "rlat": 2.6, "pe": 0.5, "fix": 0.01, "riss": 1.0, "bw": 400.0, "klat": 5.0, "base": 107.9}]
+
+
+def polish(ops, p, order):
+    N = len(ops)
+    eng = [o["eng"] for o in ops]
+    succ = [[] for _ in range(N)]
+    for k, o in enumerate(ops):
+        for d in o["deps"]:
+            succ[d].append(k)
+    data = []
+    for c in CASES:
+        q = dict(p)
+        q.update(c)
+        tm = [times(o, q) for o in ops]
+        pred = [[(d, tm[d][1] + (0.0 if (eng[d] is None or (eng[k] == "P" and eng[d] == "P")) else q["hop"])) for d in ops[k]["deps"]]
+                for k in range(N)]
+        data.append(([x[0] for x in tm], [x[1] for x in tm], pred, c["base"]))
+
+    def run(seq, i, keep):
+        du, la, pred, base = data[i]
+        st, free, last, par = [0.0] * N, {}, {}, [None] * N
+        end, ek = 0.0, 0
+        for k in seq:
+            e = eng[k]
+            t0, w = free.get(e, 0.0), last.get(e)
+            for d, x in pred[k]:
+                x += st[d]
+                if x > t0:
+                    t0, w = x, d
+            st[k], par[k] = t0, w
+            if e is not None:
+                free[e], last[e] = t0 + du[k], k
+            if t0 + la[k] > end:
+                end, ek = t0 + la[k], k
+        keep.append((st, par, ek))
+        return end / base
+
+    def score(seq):
+        keep = []
+        r = [run(seq, i, keep) for i in range(len(data))]
+        return max(r) + sum(r) / len(r), keep
+
+    nxt, placed, seq = {e: 0 for e in order}, [False] * N, []
+    while len(seq) < N:
+        for k in range(N):
+            if not placed[k] and (eng[k] is None or order[eng[k]][nxt[eng[k]]] == k) and all([placed[d] for d in ops[k]["deps"]]):
+                placed[k] = True
+                seq.append(k)
+                if eng[k] is not None:
+                    nxt[eng[k]] += 1
+    cur, keep = score(seq)
+    best, bseq = cur, seq
+    z = 12345 + p["seed"]
+    for it in range(p["iters"]):
+        z = (z * 1103515245 + 12345) % 2147483648
+        st, par, k = keep[(z >> 8) % len(data)]
+        pos = [0] * N
+        for i, j in enumerate(seq):
+            pos[j] = i
+        seq = sorted(seq, key=lambda j: (st[j], pos[j]))
+        for i, j in enumerate(seq):
+            pos[j] = i
+        pairs = []
+        while par[k] is not None:
+            if eng[k] is not None and eng[par[k]] == eng[k] and par[k] not in ops[k]["deps"]:
+                pairs.append((par[k], k))
+            k = par[k]
+        if not pairs:
+            continue
+        z = (z * 1103515245 + 12345) % 2147483648
+        a, b = pairs[(z >> 8) % len(pairs)]
+        new = None
+        early = max([pos[d] for d in ops[b]["deps"]], default=-1) < pos[a]
+        late = min([pos[s] for s in succ[a]], default=N) > pos[b]
+        if early and (not late or (z >> 20) & 1):
+            new = seq[:pos[a]] + [b] + seq[pos[a]:pos[b]] + seq[pos[b] + 1:]
+        elif late:
+            new = seq[:pos[a]] + seq[pos[a] + 1:pos[b] + 1] + [a] + seq[pos[b] + 1:]
+        if new is None:
+            continue
+        s, kp = score(new)
+        if s <= cur + p["temp"] * (1.0 - it / p["iters"]) * ((z >> 4) % 16) / 16.0:
+            cur, keep, seq = s, kp, new
+            if s < best:
+                best, bseq = s, new
+    out = {}
+    for k in bseq:
+        if eng[k] is not None:
+            out.setdefault(eng[k], []).append(k)
+    return out
+
+
 PLAN = {}
 
 
@@ -695,7 +811,7 @@ def plan():
     if not PLAN:
         ops = build(P)
         PLAN["ops"] = ops
-        PLAN["order"] = schedule(ops, P)
+        PLAN["order"] = polish(ops, P, schedule(ops, P))
     return PLAN["ops"], PLAN["order"]
 
 
@@ -715,30 +831,41 @@ def rank_program(g, core, T, topo):
     for e, l in order.items():
         for i, k in enumerate(l):
             pos[k] = i
-    waits, needed = {}, set()
-    for e, l in order.items():
-        seen = {}
-        for k in l:
-            top = {}
-            for d in ops[k]["deps"]:
-                o = ops[d]
-                if o["sem"] is not None:
-                    top[("x", d)] = d
-                elif not (e == "P" and o["eng"] == "P"):
-                    f = o["eng"]
-                    if f not in top or pos[d] > pos[top[f]]:
-                        top[f] = d
-            w = []
-            for f, d in top.items():
-                if ops[d]["sem"] is not None:
-                    if f not in seen:
-                        seen[f] = 1
-                        w.append(d)
-                elif seen.get(f, -1) < pos[d]:
-                    seen[f] = pos[d]
+    waits, needed, known = {}, set(), {}
+    seen, nxt = {e: {} for e in order}, {e: 0 for e in order}
+    moved = True
+    while moved:
+        moved = False
+        for e, l in order.items():
+            while nxt[e] < len(l) and all([ops[d]["eng"] is None or d in known for d in ops[l[nxt[e]]]["deps"]]):
+                k = l[nxt[e]]
+                top = {}
+                for d in ops[k]["deps"]:
+                    o = ops[d]
+                    if o["sem"] is not None:
+                        top[("x", d)] = d
+                    elif not (e == "P" and o["eng"] == "P"):
+                        f = o["eng"]
+                        if f not in top or pos[d] > pos[top[f]]:
+                            top[f] = d
+                w = []
+                for f, d in top.items():
+                    at = 0 if ops[d]["sem"] is not None else pos[d]
+                    if seen[e].get(f, -1) >= at:
+                        continue
+                    if any([d2 != d and known.get(d2, {}).get(f, -1) >= at for d2 in top.values()]):
+                        continue
                     w.append(d)
-                    needed.add(d)
-            waits[k] = sorted(w)
+                for f, d in top.items():
+                    at = 0 if ops[d]["sem"] is not None else pos[d]
+                    seen[e][f] = max(seen[e].get(f, -1), at)
+                    for f2, a2 in known.get(d, {}).items():
+                        seen[e][f2] = max(seen[e].get(f2, -1), a2)
+                needed.update([d for d in w if ops[d]["sem"] is None])
+                waits[k] = sorted(w)
+                known[k] = dict(seen[e])
+                nxt[e] += 1
+                moved = True
     token, total = {}, {}
     for e, l in order.items():
         for k in l:

@@ -5,69 +5,109 @@ NR, LN, RO = 4, 256, 6
 NCH = 4
 n = LN // NCH
 HS = 7 * n
+NU = NCH + 2
+TW = 16400
+KW = 2 * LN + 48
 DEAD = -16384.0
-GONE = -2.0 ** 50
+GONE = -2.0 ** 90
 OFS = 240.0
+BIG = 2.0 ** 18
 
-P = {"vcols": 4, "spieces": 3, "vc0_0": 40, "vc0_1": 32, "vc0_2": 0, "vc0_3": 8, "spieces0": 3,
-     "vc1_0": 56, "vc1_1": 8, "vc5_0": 8, "vc5_1": 0, "vc5_2": 8, "vc5_3": 40, "rp": 1, "nowr": 0,
-     "e_lrelu": "V", "e_og": "V", "e_zz": "V", "e_mn": "V", "nep": 0, "neg": "SSSS", "e_f0": "V", "e_f1": "G", "e_f2": "V", "e_f3": "G",
-     "e_hist": "G", "e_hist5": "S", "e_ms": "G", "e_yc": "S", "e_ya": "S", "e_yl": "V", "delta": 0.0,
-     "g": 1.56, "f": 1.25, "pe": 0.5, "hop": 0.1, "rlat": 2.5, "riss": 0.6, "klat": 10.0, "bw": 250.0, "fix": 0.02,
-     "tq": 2.0, "short": 4.0, "scp": 2, "vp": 1, "seed": 0, "jit": 0.0, "off": {}, "fbi": 6}
+P = {"sk": ((0, 2, 1, 3), (1, 3, 0, 2)), "pair": 1, "hf": 1, "nd1": 2, "neg2": "VVVV", "tlate": 1, "x0": 1, "q2": 0, "mv": 1, "neg": "SSSS",
+     "vcols": 16, "spieces": 4, "spieces0": 2, "vp": 2, "scp": 8, "rp": 1,
+     "vc0": 32, "vc1": 24, "vc5": 24,
+     "e_lh": "V", "e_og": "V", "e_sg": "S", "e_msq": "V", "e_ost": "V", "e_su": "S", "e_hist": "G", "e_ms": "G",
+     "e_yc": "S", "e_ya": "S", "e_yl": "V", "e_f0": "G", "e_f1": "G", "e_f2": "G", "e_f3": "V",
+     "g": 1.75, "f": 1.2, "pe": 0.7, "hop": 0.23, "rlat": 2.3, "riss": 0.8, "klat": 5.0, "bw": 350.0, "fix": 0.0,
+     "tq": 4.0, "short": 2.0, "fbi": 6}
 
-P.update({"spieces": 2, "e_hist5": "V", "vc5_3": 32, "vc5_2": 16, "vc5_1": 8, "tq": 4, "seed": 49, "jit": 0.0,
-          "x0": 1, "neg2": 1, "e_sg": "V", "nowr": 1, "scp": 4, "e_ms": "V",
-          "hop": 0.22, "rlat": 2.8, "riss": 0.8, "f": 1.2, "g": 1.6})
-P.update({"vcols": 12, "spieces": 3, "spieces0": 2, "e_f0": "G", "e_f2": "G", "vc0_1": 16, "vc0_3": 0, "vc1_1": 24, "vc5_3": 16,
-          "vc5_2": 32, "vc5_1": 16, "vc5_0": 0, "scp": 2, "g": 1.9, "pe": 0.7})
-P.update({"e_hist5": "G", "vc0_3": 8, "vc1_0": 40, "hop": 0.23, "iters": 3000, "temp": 0.0003, "e_kc": "V", "dgp": 0})
-P.update({"vcols": 8, "spieces": 4, "vc1_1": 32, "vc5_3": 40, "vc5_2": 24, "vc5_1": 24, "vc5_0": 16, "vp": 2, "e_sg": "S"})
-P.update({"vcols": 16, "e_f3": "V", "vc0_1": 24, "vc1_1": 16, "vc5_1": 0, "e_ms": "G", "rlat": 2.6, "fix": 0.0, "bw": 450.0, "iters": 0})
+P.update({"sk": ((0, 1, 2, 3), (0, 1, 2, 3)), "pair": 0, "spieces0": 3, "e_ms": "V", "e_f3": "G",
+          "up": {}, "klate": 1, "x00": 1, "bor": (99, 0), "xka": 0, "tail": 0, "e_mn": "V", "m1r": 1, "t1": 2, "nship": 1, "ogh": 1, "nep": 0, "lp": ((0, 1), (1, 2), (2, 3), (3, 4))})
+
+P.update({'vcols': 20, 'spieces0': 1, 'vc0': 16, 'vc1': 16, 'vc5': 32, 'e_su': 'V', 'e_f0': 'V', 'e_f2': 'V', 'riss': 1.0, 'bw': 450.0,
+          'fbi': 2, 'lp': ((0, 1), (1, 4)),
+          'up': {'dgx0': 1, 'og0': -8, 'dg0': -1, 'so2': 2, 'poff0': 4, 'tt0': 1, 'x4': 2, 'x2': 1, 'rq0': -1, 'sg0': -1, 'tq0': -2,
+                 'x5': -1, 'so6': -1, 'so0': -8, 'ne0': -4, 'so1': -2, 'offo0': 4, 'h0': 4, 'hl0': 2, 'mn0': 8, 'd0': -2}})
+
+P.update({'up': {}, 'mv': 2, 'spieces': 3, 'vp': 1, 'scp': 4, 'vc0': 24, 'vc5': 24, 'e_sg': 'V', 'e_ms': 'G', 'e_f1': 'V', 'e_f2': 'G',
+          'g': 1.6, 'f': 1.3, 'hop': 0.19, 'bw': 350.0, 'fix': 0.015, 'm1r': 0})
+
+P.update({'mv': 1, 'neg': 'SVSV', 'spieces': 4, 'vp': 2, 'scp': 8, 'vc0': 16, 'vc5': 32, 'e_sg': 'S', 'e_su': 'S', 'e_f1': 'G', 'e_f2': 'S',
+          'g': 1.75, 'f': 1.2, 'hop': 0.23, 'riss': 0.6, 'bw': 300.0, 'fix': 0.0,
+          'up': {'dgx0': 4, 'og0': -8, 'dg0': -1, 'so2': 2, 'poff0': 4, 'tt0': 1, 'x4': 2, 'x2': 1, 'rq0': -1, 'sg0': -1, 'tq0': -2, 'x5': -1,
+                 'so6': 4, 'so0': -8, 'ne0': -4, 'so1': -2, 'offo0': 4, 'h0': -1, 'hl0': 2, 'mn0': 8, 'd0': -2, 'ht0': -4, 'M0': 1, 'suu': -8,
+                 'sws': -1, 'ax': -8, 'ad': 4}})
+
+P.update({'spieces0': 3, 'e_f0': 'S', 'e_f1': 'S', 'e_f2': 'G', 'tq': 6.0, 'bor': (4, 19), 'm1r': 1, 'vc0_1': 8,
+          'up': {'dgx0': 4, 'og0': -8, 'dg0': -1, 'so2': -2, 'tt0': 8, 'x4': 2, 'x2': 1, 'rq0': -2, 'sg0': -1, 'tq0': 1, 'x5': -1, 'so6': 4,
+                 'so0': -8, 'ne0': -4, 'so1': -2, 'offo0': 4, 'h0': -1, 'mn0': 8, 'd0': -2, 'ht0': -8, 'M0': 1, 'suu': -8, 'sws': -1, 'ad': -1,
+                 'so5': 8, 'wr0': -8, 'asu': -8, 'so4': -8, 'dM': -4, 'cfoff': -4, 'so7': -2, 'ost0': -2, 'yb0': -2, 'so3': -2, 'su0': 4}})
+
+P.update({'neg': 'SSSV', 'vcols': 24, 'spieces': 3, 'vc0': 8, 'vc1': 24, 'e_su': 'V', 'e_f0': 'G', 'f': 1.1, 'bw': 450.0, 'bor': (5, 23),
+          'nep': 1, 'vc0_0': 32,
+          'up': {'ahl': -8, 'ost0': 2, 'so5': -4, 'coyc': 8, 'dgx0': -4, 'coya': -4, 'msq0': -4, 'x4': 1, 'xoff0': 4, 'sng': 8, 'ax': -2,
+                 'sws': 8, 'cx': -4, 'so6': -2}})
 
 BF, F32, I32, U16 = "bfloat16", "float32", "int32", "uint16"
 SCRATCH = {
-    "tab": ("sbuf", [128, 16400], BF),
-    "xb": ("sbuf", [128, 32 * LN], BF), "so": ("sbuf", [128, 2 * 32 * n], BF),
-    "d1": ("sbuf", [128, 2 * 32 * n], BF),
-    "hl": ("sbuf", [128, NCH * HS], F32), "ha": ("sbuf", [128, NCH * HS], BF),
+    "tab": ("sbuf", [128, 2 * TW], BF),
+    "xb": ("sbuf", [128, 32 * LN], BF), "so": ("sbuf", [128, 32 * LN], BF), "d1": ("sbuf", [128, 32 * LN], BF),
+    "hl": ("sbuf", [128, NU * HS], F32), "ha": ("sbuf", [128, NU * HS], F32),
     "posi": ("sbuf", [128, LN], I32), "ki": ("sbuf", [128, LN], I32), "si": ("sbuf", [128, LN], I32), "dd": ("sbuf", [128, LN], F32),
-    "kall": ("sbuf", [128, NR * LN], BF), "sin": ("sbuf", [128, RO * LN], BF), "sout": ("sbuf", [128, RO * LN], BF),
-    "ub": ("sbuf", [128, 16], BF), "vb": ("sbuf", [128, 16], BF), "stepi": ("sbuf", [128, 4], I32),
-    "mt": ("sbuf", [128, RO * LN], BF), "dg": ("sbuf", [128, LN], F32), "poff": ("sbuf", [128, 16 * NCH], U16),
+    "kall": ("sbuf", [128, NR * KW], BF), "sin": ("sbuf", [128, NU * RO * 2 * n], BF), "sout": ("sbuf", [128, NU * RO * 2 * n], BF),
+    "stepi": ("sbuf", [128, 4], I32), "du": ("sbuf", [128, 64], BF),
+    "dg": ("sbuf", [128, LN], F32), "poff": ("sbuf", [128, 16 * NCH], U16),
     "og": ("sbuf", [128, LN], F32), "ne": ("sbuf", [128, LN], BF), "off": ("sbuf", [128, 2 * LN], U16),
     "tt": ("sbuf", [128, LN], BF), "yb": ("sbuf", [128, 9 * n], BF),
-    "km": ("sbuf", [128, 128 * NCH], F32), "lastc": ("sbuf", [128, 8], U16),
-    "selkf": ("sbuf", [128, 128], F32), "cd2": ("sbuf", [128, n], BF), "dg2": ("sbuf", [128, LN], F32),
+    "selkf": ("sbuf", [128, 128], F32), "eyef": ("sbuf", [128, 128], F32), "cd2": ("sbuf", [128, n], BF), "dg2": ("sbuf", [128, LN], F32),
     "xoff": ("sbuf", [128, 16 * NCH], U16), "sg": ("sbuf", [128, LN], BF),
-    "ft": ("sbuf", [128, 128 * NCH], BF), "kc": ("sbuf", [128, 128 * NCH], F32), "mo": ("sbuf", [128, 2 * LN], BF), "wr": ("sbuf", [128, LN], BF),
+    "rq": ("sbuf", [128, 128 * NCH], BF), "tq": ("sbuf", [128, 128 * NCH], BF),
+    "msq": ("sbuf", [128, LN], BF), "ost": ("sbuf", [128, LN], BF), "wr": ("sbuf", [128, LN], BF),
     "ht": ("sbuf", [128, LN], BF), "h2": ("sbuf", [128, LN], BF), "mn": ("sbuf", [128, LN], BF),
     "fm": ("sbuf", [128, 2 * LN], BF), "foff": ("sbuf", [128, 16 * NCH], U16),
     "oyl": ("sbuf", [128, LN], F32), "oya": ("sbuf", [128, 4 * LN], F32), "oyc": ("sbuf", [128, 4 * LN], F32),
     "ci": ("sbuf", [128, 16], I32), "col": ("sbuf", [128, 64], F32), "thr": ("sbuf", [128, 8], F32), "gm": ("sbuf", [128, 8], F32),
-    "i2t": ("sbuf", [128, 8], F32), "cg": ("sbuf", [128, 128], BF), "pw": ("sbuf", [128, 128], BF), "dw": ("sbuf", [128, 144], BF),
-    "tie": ("sbuf", [128, 128], BF), "c4": ("sbuf", [128, 16], BF), "rs": ("sbuf", [128, 128], BF), "cd": ("sbuf", [128, n], BF),
-    "cmp": ("sbuf", [128, 8], F32), "wfw": ("sbuf", [128, 144], BF), "wpw": ("sbuf", [128, 144], BF), "ws": ("sbuf", [128, RO * 128], BF),
-    "tmp": ("sbuf", [128, n], F32),
+    "i2t": ("sbuf", [128, 8], F32), "dw": ("sbuf", [128, 160], BF), "c4": ("sbuf", [128, 16], BF), "cd": ("sbuf", [128, n], BF),
+    "cmp": ("sbuf", [128, 8], F32), "wfw": ("sbuf", [128, 144], BF), "ws": ("sbuf", [128, RO * 128], BF),
+    "ogh": ("sbuf", [128, LN], "float16"), "eyeh": ("sbuf", [128, 128], "float16"), "selkh": ("sbuf", [128, 128], "float16"),
+    "tmp": ("sbuf", [128, n], F32), "one": ("sbuf", [128, n], BF),
 }
-for _m in ("bm", "eye", "neye", "selk", "wp", "wb", "wst", "uu", "vv", "penu", "tiev", "ee", "e4", "selk24", "n16", "n24"):
+for _m in ("cg", "pw", "tie", "rs", "bmq", "bmh", "eye2", "selk2", "nhalf", "eye", "neye", "selk", "nselk", "wp", "wb", "ee", "ee2", "selk24", "n16", "n24",
+           "dc", "dc2", "eps", "zr", "cp", "cn", "gd"):
     SCRATCH[_m] = ("sbuf", [128, 128], BF)
-SCRATCH["eyef"] = ("sbuf", [128, 128], F32)
+for _m in ("uu0", "vv0", "uu1", "vv1", "pen", "pen2"):
+    SCRATCH[_m] = ("sbuf", [128, 144], BF)
 for _b in range(8):
     SCRATCH["pb%d" % _b] = ("psum", [128, 512], F32)
 
 SEMAPHORES = ["sV", "sS", "sP", "sG", "karr", "sent", "outs", "lpos", "lu", "lv", "lstep"] + ["lf%d" % i for i in range(4)] \
-    + ["ar%d_%d" % (t, c) for t in range(1, RO) for c in range(NCH)]
+    + ["ar%d_%d" % (t, c) for t in range(1, RO) for c in range(NCH)] + ["tf%d" % i for i in range(4)] \
+    + [x + str(c) for x in ("h0_", "h4_", "mn_") for c in range(NCH)]
 
 
 def build(p):
     ops = []
     lastw, readers, bank = {}, {}, {}
-    tag = [None]
+    tag, me, cur, count = [None], [0], [None], {}
+    kinds = 1 + p["pair"]
 
-    def add(eng, fn, r, w, cost, bk=None, sem=None, lat=None):
+    def kind(eng, nm, rd):
+        if cur[0] is None:
+            return "s" + nm
+        x = "adbbbc"[cur[0][0]] + "".join([ch for ch in nm if ch.isalpha()]).replace("sin", "").replace("sout", "")
+        if eng in ("V", "S", "G"):
+            i = count[me[0], cur[0], x] = count.get((me[0], cur[0], x), -1) + 1
+            x += str(i)
+        elif eng == "P":
+            x += "." + "".join([ch for ch in rd[0][1] + rd[1][1][:3] if ch.isalpha()]).replace("sin", "").replace("sou", "")
+        return x
+
+    def add(eng, fn, r, w, cost, bk=None, sem=None, lat=None, to=None):
         k = len(ops)
         deps = set()
+        at = me[0] if to is None else to
+        nm = (list(w) + [""])[0]
+        r, w = [(me[0], x) for x in r], [(at, x) for x in w]
         for x in r:
             if x in lastw:
                 deps.add(lastw[x])
@@ -81,6 +121,7 @@ def build(p):
             lastw[x] = k
             readers[x] = []
         if bk is not None:
+            bk = (at, bk)
             e0, run, prev = bank.get(bk, (None, [], []))
             if e0 == eng:
                 deps.update(prev)
@@ -91,8 +132,8 @@ def build(p):
                 deps.update(run)
                 bank[bk] = (eng, [k], run)
         deps.discard(k)
-        ops.append({"eng": eng, "fn": fn, "deps": deps, "cost": cost, "sem": sem, "lat": lat, "tag": tag[0],
-                    "cls": ("s" if tag[0] is None else "abbbbc"[tag[0] // NCH]) + str(eng) + "".join([x for x in (list(w) + ["y"])[0] if x.isalpha()])})
+        ops.append({"eng": eng and eng + str(at), "fn": fn, "deps": deps, "cost": cost, "sem": sem, "lat": lat, "tag": tag[0],
+                    "w": nm, "core": at, "unit": cur[0], "ty": kind(eng, nm, r)})
         return k
 
     def ts(out, in0, s1, s2, o0, o1, r, w, m, bk=None):
@@ -109,6 +150,9 @@ def build(p):
 
     def ms(out, v, w, m, r=()):
         add("V", lambda q, T, X: q.memset(out(T), v), r, w, ("c", m))
+
+    def scan(out, a, b, o0, o1, r, w, m, bk=None):
+        add("V", lambda q, T, X: q.tensor_tensor_scan(out(T), a(T), b(T), 0.0, o0, o1), r, w, ("c", m), bk)
 
     def act(out, a, f, r, w, m, bk=None, kind="c", bias=None, scale=None):
         def fn(q, T, X):
@@ -128,12 +172,16 @@ def build(p):
         else:
             ts(out, a, bias, num(0.0), A.add, A.max, r, w, m, bk)
 
-    def mm(out, lh, rh, st, sp, r, w, m, bk):
-        add("P", lambda q, T, X: q.matmul(out(T), lh(T), rh(T), st, sp), r, w, ("p", m), bk)
+    def copy(e, out, a, r, w, m, bk=None, gather=False):
+        if e == "S":
+            act(out, a, F.Copy, r, w, m, bk, kind="gs" if gather else "c")
+        else:
+            cp(out, a, r, w, m, bk, kind="gv" if gather else "c")
 
-    def group(out, key, bk, terms):
+    def group(out, key, bk, terms, first=True, last=True):
         for i, x in enumerate(terms):
-            mm(x[4] if len(x) > 4 else out, x[0], x[1], i == 0, i == len(terms) - 1, x[2], [key], x[3], bk)
+            o, lh, rh, st, sp = x[4] if len(x) > 4 else out, x[0], x[1], first and i == 0, last and i == len(terms) - 1
+            add("P", lambda q, T, X, o=o, lh=lh, rh=rh, st=st, sp=sp: q.matmul(o(T), lh(T), rh(T), st, sp), x[2], [key], ("p", x[3]), bk)
 
     def iota(out, pat, base, cm, w, m, flag=True):
         if flag:
@@ -153,21 +201,31 @@ def build(p):
             return lambda T: T[name][:, a:b]
         return lambda T: T[name][:, a:b:s]
 
+    def back(name, a, b):
+        return (lambda T: T[name][:, b - 1:a - 1:-1]) if a else (lambda T: T[name][:, b - 1::-1])
+
     def ind(name, a, b, oname, c, d):
         return lambda T: T[name][:, a:b].indirect(T[oname][:, c:d])
 
-    def dma(eng, out, a, r, w, sem, nbytes, slow=False):
-        if slow:
-            add(eng, lambda q, T, X: q.dma_start(out(T), a(T), allow_slow_non_contiguous=True), r, w, ("d", 0), None, sem, ("dl", nbytes))
-        else:
-            add(eng, lambda q, T, X: q.dma_start(out(T), a(T)), r, w, ("d", 0), None, sem, ("dl", nbytes))
+    def dma(eng, out, a, r, w, sem, nbytes):
+        add(eng, lambda q, T, X: q.dma_start(out(T), a(T)), r, w, ("d", 0), None, sem, ("dl", nbytes))
 
-    dma("Y", ap("posi"), ap("pos"), [], ["posi"], "lpos", 131072)
-    for i in range(4):
-        dma("Y", ap("tab", 2048 * i, 2048 * i + 2048), ap("feat", 2048 * i, 2048 * i + 2048), [], ["tab%d" % i], "lf%d" % i,
-            131072 + 524288 * (i + 1))
-    dma("S", ap("ub"), ap("u"), [], ["ub"], "lu", 4096)
-    dma("S", ap("vb"), ap("v"), [], ["vb"], "lv", 4096)
+    def send(dst, pieces, rd, wr, sem, cost=("a", 0), mask="all", name=None):
+        d = (dst - me[0]) % NR
+
+        def fn(q, T, X):
+            rid, pid = X["addr"][d][0], X["addr"][d][1]
+            if len(pieces) == 1:
+                b, i, b2, o, w = pieces[0]
+                return q.remote_dma(T[b2][:, o:o + w], T[b][:, i:i + w], T.sem[sem], T.sem["sent"], pid, rid, X[mask])
+            return q.remote_dma_fused([RemoteDMATransfer(dst_ids=[DstId(rid=rid, pnc=pid)], dma_engine_mask=m, remote_sem=T.sem[sem],
+                                                         srcs=[T[b][:, i:i + w]], dsts=[T[b2][:, o:o + w]])
+                                       for (b, i, b2, o, w), m in zip(pieces, X["parts"][len(pieces)])], local_sem=T.sem["sent"])
+        add("G", fn, rd, ["st" + (name or sem)], ("r", 0), None, "sent", mask)
+        add(None, None, ["st" + (name or sem)], wr, cost, None, sem, mask, to=dst % kinds)
+
+    def mat(name, rhs, r, m=n):
+        return (ap(name, 0, 128), rhs, [name] + r, m)
 
     names = {}
 
@@ -180,372 +238,487 @@ def build(p):
         f = [C(x) if isinstance(x, str) else num(x) for x in (src, s1, s2)]
         ts(C(name), f[0], f[1], f[2], o0, o1, r, ["c_" + name], 64)
 
-    iota(ap("ci", 0, 1), [[0, 1]], 0, 1, ["ci0"], 1, False)
-    iota(ap("dw"), [[1, 144]], -16, 0, ["dw"], 144)
-    iota(ap("cg"), [[1, 8], [0, 16]], 0, 0, ["cg"], 128)
-    iota(ap("i2t"), [[2, 8]], 0, 0, ["i2t"], 8)
-    iota(ap("tie"), [[0, 8], [-2, 16]], 15, 0, ["tie"], 128)
-    iota(ap("pw"), [[1, 64], [0, 2]], 0, 0, ["pw"], 128)
-    iota(ap("c4"), [[4, 16]], 0, 0, ["c4"], 16)
-    dma("S", ap("stepi", 0, 1), ap("step"), [], ["stepi"], "lstep", 512)
-
-    C("p")
-    for j, (nm, op, v) in enumerate((("k", A.bitwise_and, 15), ("g", A.arith_shift_right, 4), ("odd", A.bitwise_and, 1),
-                                     ("ph", A.arith_shift_right, 1))):
-        C(nm)
-        ts(ap("ci", j + 1, j + 2), ap("ci", 0, 1), num(v), None, op, None, ["ci0"], ["ci%d" % (j + 1)], 64)
-    cp(ap("col", 0, 5), ap("ci", 0, 5), ["ci%d" % j for j in range(5)], ["c_p", "c_k", "c_g", "c_odd", "c_ph"], 64)
-    cs("king", "k", 0.0, None, A.is_equal)
-    cs("ab", "k", 13.0, 2048.0, A.is_ge, A.mult)
-    cs("big12", "k", 12.0, 1.0e6, A.is_le, A.mult)
-    cs("o32", "odd", 32.0, None, A.mult)
-    cs("b0", "k", -12.0, 32.0, A.add, A.mult)
-    cs("base", "b0", "o32", None, A.max)
-    ts(ap("gm"), ap("i2t"), C("k"), C("big12"), A.is_le, A.mult, ["i2t", "c_k", "c_big12"], ["gm"], 64)
-    ts(ap("thr"), ap("gm"), C("base"), None, A.add, None, ["gm", "c_base"], ["thr"], 64)
-    ts(ap("gm"), ap("dw", 16, 24), C("g"), None, A.is_equal, None, ["dw", "c_g"], ["gm"], 64)
-
     def blk(name, c):
-        ts(ap(name), ap("cg"), C("g"), C(c), A.is_equal, A.mult, ["cg", "c_g", "c_" + c], [name], 64)
+        r = ["cg", "c_g"] + (["c_" + c] if isinstance(c, str) else [])
+        ts(ap(name), ap("cg"), C("g"), C(c) if isinstance(c, str) else num(c), A.is_equal, A.mult, r, [name], 64)
 
-    def diag(name, v, m=64):
+    def diag(name, v, m=64, at=16, w=128):
         r = ["dw", "c_p"] + (["c_" + v] if isinstance(v, str) else [])
-        ts(ap(name), ap("dw", 16, 144), C("p"), C(v) if isinstance(v, str) else num(v), A.is_equal, A.mult, r, [name], m)
+        ts(ap(name, 0, w), ap("dw", at, at + w), C("p"), C(v) if isinstance(v, str) else num(v), A.is_equal, A.mult, r, [name], m)
 
-    diag("eye", 1.0)
-    blk("selk", "king")
-    blk("wb", "ab")
-    ts(ap("ki"), ap("posi"), num(1920), None, A.bitwise_and, None, ["posi"], ["ki"], 256)
-    ts(ap("si"), ap("posi"), num(127), None, A.bitwise_and, None, ["posi"], ["si"], 256)
-    ts(ap("dd"), ap("posi"), num(0.0), num(GONE), A.is_equal, A.mult, ["posi"], ["dd"], 256)
-    cp(ap("kall", 0, LN), ap("ki"), ["ki"], ["kall0"], 256)
-    tt(ap("sin", 0, LN), ap("si"), ap("dd"), A.add, ["si", "dd"], ["sin0_%d" % c for c in range(NCH)], 512)
+    def marks(name, v, at, w):
+        ms(ap(name), v, [name], 64)
+        ms(ap(name, at, 128, 16), w, [name], 64)
 
-    def sendk(q, T, X):
-        tr = RemoteDMATransfer(dst_ids=[DstId(rid=X["addr"][j][0], pnc=X["addr"][j][1]) for j in range(1, NR)],
-                               dma_engine_mask=X["mask"], remote_sem=T.sem["karr"], srcs=[T["kall"][:, 0:LN]],
-                               dsts=[T["kall"][:, j * LN:(j + 1) * LN] for j in range(1, NR)])
-        return q.remote_dma_fused([tr], local_sem=T.sem["sent"])
-    add("G", sendk, ["kall0"], ["ksent"], ("r", 0), None, "sent")
-    add(None, None, ["ksent"], ["kall1", "kall2", "kall3"], ("a", 1), None, "karr")
-
-    ms(ap("rs"), 0.0, ["rs"], 64)
-    ms(ap("rs", 0, 128, 16), -float(2 ** 30), ["rs"], 64)
-    def fill(e, name, a, b, v, w):
+    def fill(e, name, a, b, v, w, half=2):
         if e == "V":
-            ms(ap(name, a, b), v, w, (b - a) // 2)
+            ms(ap(name, a, b), v, w, (b - a) // half)
+        elif e == "S":
+            act(ap(name, a, b), ap("tab", 64, 64 + b - a), F.Identity, ["tab0_0"], w, b - a, bias=num(v), scale=num(0.0))
         else:
             iota(ap(name, a, b), [[0, b - a]], int(v), 0, w, b - a)
 
-    def sel(out, a, pat, op, v, base, cm, r, w, m):
-        add("G", lambda q, T, X: q.affine_select(out(T), a(T), pat, op, v, base, cm), r, w, ("ga", m))
+    def weights(w, slot):
+        for i, x in enumerate("uv"):
+            a, b, dst = slot * KW + 2 * LN + 16 * i, 32 * w + 16 * i, "%s%s%d" % (x, x, w)
+            ms(ap("du", b, b + 1), 0.0, [dst + "z"], 64)
+            tt(ap("du", b + 1, b + 16), ap("kall", a, a + 15), ap("kall", a + 1, a + 16), A.subtract, [x + str(slot)], [dst + "d"], 64)
+            if p["q2"]:
+                ms(ap(dst, 128, 144), 0.0, [dst + "_8"], 64)
+            for gi in range(8):
+                act(ap(dst, 16 * gi, 16 * gi + 16), ap("du", b, b + 16), F.Copy, [dst + "z", dst + "d", "gm"], ["%s_%d" % (dst, gi)], 64,
+                    scale=ap("gm", gi, gi + 1))
 
-    fill(p["e_f0"], "yb", 0, 9 * n, 0.0, ["yb%d" % c for c in range(NCH)])
-    for par in range(2):
+    negs = []
+
+    def negate(w, engs):
         for i in range(4):
-            fill(p["e_f1"] if i < 2 else p["e_f2"], "d1", (32 * par + 8 * i) * n, (32 * par + 8 * i + 8) * n, -OFS, ["d1f%d_%d" % (par, i)])
-    for gi in range(8):
-        for src, dst in (("ub", "uu"), ("vb", "vv")):
-            act(ap(dst, 16 * gi, 16 * gi + 16), ap(src), F.Copy, [src, "gm"], ["%s%d" % (dst, gi)], 64, scale=ap("gm", gi, gi + 1))
-    UU = ["uu%d" % i for i in range(8)]
-    VV = ["vv%d" % i for i in range(8)]
-    cs("chit", "king", 9998.0, 1.0, A.mult, A.add)
-    ts(ap("tiev"), ap("tie"), num(1.0 / 32), None, A.mult, None, ["tie"], ["tiev"], 64)
-    diag("penu", 2.0 ** -28)
-    diag("neye", -1.0)
-    ts(ap("bm"), ap("cg"), C("g"), None, A.is_equal, None, ["cg", "c_g"], ["bm"], 64)
-    cp(C("step"), ap("stepi", 0, 1), ["stepi"], ["c_step"], 64)
-    blk("wst", "step")
-    cs("sg", "odd", -2.0, 1.0, A.mult, A.add)
-    cs("kt", "k", -2.0, 15.0, A.mult, A.add)
-    cs("b33", "king", 0.0, -255.0, A.mult, A.add)
-    cs("b32", "king", 0.0, -256.0, A.mult, A.add)
-    if p["nowr"]:
-        cs("w129", "king", 0.0, 385.0, A.mult, A.add)
-        cs("chi2", "king", 9998.0, 129.0, A.mult, A.add)
-    diag("ee", 256.0)
-    iota(ap("ci", 8, 16), [[16, 8]], 15, 0, ["ci9"], 8, False)
-    cp(ap("lastc"), ap("ci", 8, 16), ["ci9"], ["lastc"], 64)
-    if p["x0"]:
-        cs("k16", "king", 16384.0, None, A.mult)
-        ts(ap("selkf"), ap("cg"), C("g"), C("king"), A.is_equal, A.mult, ["cg", "c_g", "c_king"], ["selkf"], 128)
-        cs("k24", "king", 24576.0, None, A.mult)
-        blk("selk24", "k24")
-        ts(ap("cd2"), ap("tie", 0, n), C("kt"), num(-131072.0), A.not_equal, A.mult, ["tie", "c_kt"], ["cd2"], 64)
-        ms(ap("tab", 16384, 16400), -1024.0, ["tabx"], 64)
+            a = w * TW + 2048 * i
+            src, dst, rd, wr = ap("tab", a, a + 2048), ap("tab", 8192 + a, 10240 + a), ["tab%d_%d" % (w, i), "low"], ["neg%d_%d" % (w, i)]
+            if engs[i] == "S":
+                act(dst, src, F.Copy, rd, wr, 2048, scale=num(-1.0))
+            else:
+                for b in range(a, a + 2048, 512):
+                    ts(ap("tab", 8192 + b, 8704 + b), ap("tab", b, b + 512), num(-1.0), None, A.mult, None, rd, ["ng%d" % b], 256)
+                    negs.append("ng%d" % b)
 
-    def negate(i, r):
-        a = 2048 * i
-        if p["neg"][i] in "Ss":
-            act(ap("tab", 8192 + a, 10240 + a), ap("tab", a, a + 2048), F.Copy, ["tab%d" % i] + r, ["neg%d" % i], 2048, scale=num(-1.0))
+    def setup(r):
+        dma("Y", ap("posi"), ap("pos"), [], ["posi"], "lpos", 131072)
+        for i, (a, b) in enumerate(p["lp"]):
+            dma("Y", ap("tab", 2048 * a, 2048 * b), ap("feat", 2048 * a, 2048 * b), [], ["tab0_%d" % j for j in range(a, b)], "lf%d" % i,
+                131072 + 524288 * b + 100000 * (i + 2))
+        dma("S", ap("kall", 2 * LN, 2 * LN + 16), ap("u"), [], ["u0"], "lu", 4096)
+        dma("S", ap("kall", 2 * LN + 16, 2 * LN + 32), ap("v"), [], ["v0"], "lv", 4096)
+        iota(ap("ci", 0, 1), [[0, 1]], 0, 1, ["ci0"], 1, False)
+        iota(ap("dw"), [[1, 160]], -16, 0, ["dw"], 160)
+        iota(ap("cg"), [[1, 8], [0, 16]], 0, 0, ["cg"], 128)
+        iota(ap("i2t"), [[2, 8]], 0, 0, ["i2t"], 8)
+        iota(ap("tie"), [[0, 8], [-2, 16]], 15, 0, ["tie"], 128)
+        iota(ap("pw"), [[1, 64], [0, 2]], 0, 0, ["pw"], 128)
+        iota(ap("c4"), [[4, 16]], 0, 0, ["c4"], 16)
+        dma("S", ap("stepi", 0, 1), ap("step"), [], ["stepi"], "lstep", 512)
+
+        C("p")
+        for j, (nm, op, v) in enumerate((("k", A.bitwise_and, 15), ("g", A.arith_shift_right, 4), ("odd", A.bitwise_and, 1),
+                                         ("ph", A.arith_shift_right, 1))):
+            C(nm)
+            ts(ap("ci", j + 1, j + 2), ap("ci", 0, 1), num(v), None, op, None, ["ci0"], ["ci%d" % (j + 1)], 64)
+        cp(ap("col", 0, 5), ap("ci", 0, 5), ["ci%d" % j for j in range(5)], ["c_p", "c_k", "c_g", "c_odd", "c_ph"], 64)
+        cs("king", "k", 0.0, None, A.is_equal)
+        cs("ab", "k", 13.0, 2048.0, A.is_ge, A.mult)
+        cs("big12", "k", 12.0, 1.0e6, A.is_le, A.mult)
+        cs("o32", "odd", 32.0, None, A.mult)
+        cs("b0", "k", -12.0, 32.0, A.add, A.mult)
+        cs("base", "b0", "o32", None, A.max)
+        ts(ap("gm"), ap("i2t"), C("k"), C("big12"), A.is_le, A.mult, ["i2t", "c_k", "c_big12"], ["gm"], 64)
+        ts(ap("thr"), ap("gm"), C("base"), num(128.0), A.add, A.add, ["gm", "c_base"], ["thr"], 64)
+        ts(ap("gm"), ap("dw", 16, 24), C("g"), None, A.is_equal, None, ["dw", "c_g"], ["gm"], 64)
+        diag("eye", 1.0)
+        diag("eye2", 2.0)
+        blk("selk", "king")
+        cs("king2", "king", 2.0, None, A.mult)
+        blk("selk2", "king2")
+        blk("wb", "ab")
+        ts(ap("ki"), ap("posi"), num(1920), None, A.bitwise_and, None, ["posi"], ["ki"], 256)
+        ts(ap("si"), ap("posi"), num(127), None, A.bitwise_and, None, ["posi"], ["si"], 256)
+        ts(ap("dd"), ap("posi"), num(0.0), num(GONE), A.is_equal, A.mult, ["posi"], ["dd"], 256)
+        ts(ap("kall", 0, LN), ap("ki"), num(-128.0), None, A.add, None, ["ki"], ["kall0"], 256)
+        ts(ap("og"), ap("si"), num(0.5), num(64.0), A.mult, A.add, ["si"], ["og%d" % j for j in range(NCH)], 256)
+        tt(ap("kall", LN, 2 * LN), ap("og"), ap("dd"), A.add, ["og0", "og1", "og2", "og3", "dd"], ["sall0"], 512)
+        ms(ap("zr"), 0.0, ["zr"], 64)
+        cp(C("step"), ap("stepi", 0, 1), ["stepi"], ["c_step"], 64)
+        ts(ap("kall", 2 * LN + 32, KW), ap("zr", 0, 16), C("step"), num(128.0), A.add, A.add, ["zr", "c_step"], ["step0"], 64)
+
+        def sendk(q, T, X):
+            kw = KW if p["pair"] else 2 * LN
+            tr = RemoteDMATransfer(dst_ids=[DstId(rid=X["addr"][j][0], pnc=X["addr"][j][1]) for j in range(1, NR)],
+                                   dma_engine_mask=X["mask"], remote_sem=T.sem["karr"], srcs=[T["kall"][:, 0:kw]],
+                                   dsts=[T["kall"][:, j * KW:j * KW + kw] for j in range(1, NR)])
+            return q.remote_dma_fused([tr], local_sem=T.sem["sent"])
+        add("G", sendk, ["kall0", "sall0"] + ["tab0_%d" % i for i in range(4 * p["klate"])] + (["u0", "v0", "step0"] if p["pair"] else []), ["ksent"], ("r", 0), None, "sent")
+        add(None, None, ["ksent"], [x + str(j) for x in ("kall", "sall", "u", "v", "step") for j in range(1, NR)], ("a", 1), None, "karr",
+            to=(r + 1) % kinds)
+        if p["pair"] and not p["nship"]:
+            for i in range(4):
+                send(r ^ 1, [("tab", 2048 * i, "tab", TW + 2048 * i, 2048)],
+                     ["tab0_%d" % j for j in (range(4) if p["tlate"] else [i])] + ["sttf%d" % (i - 1)],
+                     ["tab1_%d" % i], "tf%d" % i, ("b", 524288 * (i + 1)))
+
+        marks("rs", 0.0, 0, -2.0 ** 30)
+        fill(p["e_f0"], "yb", 0, 9 * n, 0.0, ["yb%d" % c for c in range(NCH)])
+        for par in range(p["nd1"]):
+            for i in range(4):
+                fill(p["e_f1"] if i < 2 else p["e_f2"], "d1", (32 * par + 8 * i) * n, (32 * par + 8 * i + 8) * n, -OFS, ["d1f%d_%d" % (par, i)])
+        weights(0, 0)
+        diag("pen", -2.0 ** -71, 72, 16, 144)
+        diag("pen2", 2.0 ** -71, 72, 15, 144)
+        tt(ap("pen"), ap("pen"), ap("pen2"), A.add, ["pen", "pen2"], ["pen"], 288)
+        marks("dc", 1.0 / 16, 0, -2.0 ** 22)
+        if p["q2"]:
+            marks("dc2", 1.0 / 16, 15, 2.0 ** 22)
         else:
-            ts(ap("tab", 8192 + a, 10240 + a), ap("tab", a, a + 2048), num(-1.0), None, A.mult, None, ["tab%d" % i] + r, ["neg%d" % i], 1024)
-    for i in range(4):
-        if p["neg"][i] in "SV":
-            negate(i, [])
-    for c in range(NCH):
-        fill(p["e_f3"], "hl", c * HS, c * HS + n, 0.0, ["hl%d_0" % c])
-        fill(p["e_f3"], "ha", c * HS, c * HS + n, -OFS, ["ha%d_0" % c])
-    cs("le12", "k", 12.0, "sg", A.is_le, A.mult)
-    cs("s1", "k", "odd", 0.5 * n, A.subtract, A.mult)
-    cs("af", "s1", float(n), None, A.add)
-    cs("apx", "af", "le12", None, A.mult)
-    cs("ath", "ab", -1.0 / 64, None, A.mult)
-    cs("aw", "le12", -256.0, "ath", A.mult, A.add)
-    cs("th2", "ab", 1.0 / 4096, None, A.mult)
-    cs("q0", "g", 8.0, "ph", A.mult, A.subtract)
-    cs("q1", "q0", "th2", 2.0, A.mult, A.mult)
-    cs("q2", "q1", "ph", None, A.add)
-    ts(ap("cmp"), ap("i2t"), C("th2"), C("q2"), A.mult, A.add, ["i2t", "c_th2", "c_q2"], ["cmp"], 64)
-    if p["dgp"]:
-        cs("g16", "g", 16.0, None, A.mult)
-        ts(ap("wpw"), ap("dw"), C("g16"), C("apx"), A.is_equal, A.mult, ["dw", "c_g16", "c_apx"], ["wpw"], 72)
-        diag("e4", 4.0)
-    else:
+            marks("eps", -2.0 ** -9, 0, 2.0 ** 30)
+        diag("ee", -BIG)
+        diag("ee2", BIG / 2)
+        diag("neye", -1.0)
+        diag("nhalf", -0.5)
+        cs("nking", "king", -1.0, None, A.mult)
+        blk("nselk", "nking")
+        cs("sg", "odd", -2.0, 1.0, A.mult, A.add)
+        cs("kt", "k", -2.0, 15.0, A.mult, A.add)
+        blk("bmq", -0.25)
+        blk("bmh", 0.5)
+        ms(ap("one"), 1.0, ["one"], 64)
+        ms(ap("cp"), 1.5 * 2.0 ** 22, ["cp"], 64)
+        ms(ap("cn"), -1.5 * 2.0 ** 22, ["cn"], 64)
+        cs("gone", "k", 1.0, GONE, A.is_ge, A.mult)
+        diag("gd", "gone")
+        if p["x00"]:
+            ms(ap("tab", 16, 32), -1024.0, ["low"], 64, ["tab0_0"])
+            cs("rest", "k", 1.0, None, A.is_ge)
+            cs("k1", "king", 16.0, None, A.mult)
+        if p["x0"]:
+            cs("k16", "king", 16384.0, None, A.mult)
+            blk("selkh" if p["ogh"] else "selkf", "king")
+            cs("k24", "king", 24576.0, None, A.mult)
+            blk("selk24", "k24")
+            ts(ap("cd2"), ap("tie", 0, n), C("kt"), num(-131072.0), A.not_equal, A.mult, ["tie", "c_kt"], ["cd2"], 64)
+            for w in range(1 + (p["pair"] and not p["nship"])):
+                ms(ap("tab", w * TW + 16384, w * TW + TW), -1024.0, ["tabx%d" % w], 64)
+
+        negate(0, p["neg"])
+        if p["pair"] and p["nship"]:
+            send(r ^ 1, [("tab", 0, "tab", TW, 8192)], ["tab0_%d" % j for j in range(4)], ["tab1_%d" % j for j in range(4)], "tf0",
+                 ("b", 2 * 2097152), "low")
+            send(r ^ 1, [("tab", 8192, "tab", TW + 8192, TW - 8192)], ["neg0_%d" % j for j in range(4)] + ["tabx0", "sttf0"],
+                 ["neg1_%d" % j for j in range(4)] + ["tabx1"], "tf1", ("b", 3 * 2097152), "low")
+        for u in range(NU if p["pair"] else NCH):
+            fill(p["e_f3"], "hl", u * HS, u * HS + n, 0.0, ["hl%d_0" % u], 1)
+            fill(p["e_f3"], "ha", u * HS, u * HS + n, -OFS, ["ha%d_0" % u], 1)
+        cs("le12", "k", 12.0, "sg", A.is_le, A.mult)
+        cs("s1", "k", "odd", 0.5 * n, A.subtract, A.mult)
+        cs("af", "s1", float(n), None, A.add)
+        cs("apx", "af", "le12", None, A.mult)
+        cs("ath", "ab", -1.0 / 64, None, A.mult)
+        cs("aw", "le12", -256.0, "ath", A.mult, A.add)
+        cs("th2", "ab", 1.0 / 4096, None, A.mult)
+        cs("q0", "g", 8.0, "ph", A.mult, A.subtract)
+        cs("q1", "q0", "th2", 2.0, A.mult, A.mult)
+        cs("q2", "q1", "ph", None, A.add)
+        ts(ap("cmp"), ap("i2t"), C("th2"), C("q2"), A.mult, A.add, ["i2t", "c_th2", "c_q2"], ["cmp"], 64)
         blk("wp", "apx")
-    for s in range(RO):
-        ts(ap("ws", 128 * s, 128 * s + 128), ap("pw"), ap("cmp", s, s + 1), C("aw"), A.is_equal, A.mult, ["pw", "cmp", "c_aw"], ["ws%d" % s], 64)
-    if not p["dgp"]:
+        for s in range(RO):
+            ts(ap("ws", 128 * s, 128 * s + 128), ap("pw"), ap("cmp", s, s + 1), C("aw"), A.is_equal, A.mult, ["pw", "cmp", "c_aw"],
+               ["ws%d" % s], 64)
         ts(ap("tmp"), ap("tie", 0, n), C("kt"), num(DEAD), A.not_equal, A.mult, ["tie", "c_kt"], ["tmp5"], 64)
         tt(ap("cd"), ap("tmp"), ap("dw", 16, 16 + n), A.add, ["tmp5", "dw"], ["cd"], 128)
-    diag("eyef", 1.0, 128)
-    diag("n16", 16384.0)
-    diag("n24", 24576.0)
-    cs("g16o", "g", 16.0, "odd", A.mult, A.add)
-    cs("ge12", "k", 12.0, 1.0e6, A.is_ge, A.mult)
-    cs("cf0", "ge12", "o32", None, A.subtract)
-    cs("cf1", "cf0", -64.0, None, A.add)
-    ts(ap("ci", 6, 7), ap("ci", 1, 2), num(2), None, A.arith_shift_right, None, ["ci1"], ["ci8"], 64)
-    cp(C("rf"), ap("ci", 6, 7), ["ci8"], ["c_rf"], 64)
-    ts(ap("wfw"), ap("dw"), C("g16o"), C("af"), A.is_equal, A.mult, ["dw", "c_g16o", "c_af"], ["wfw"], 72)
+        diag("eyeh" if p["ogh"] else "eyef", 1.0, 128)
+        diag("n16", 16384.0)
+        diag("n24", 24576.0)
+        cs("g16o", "g", 16.0, "odd", A.mult, A.add)
+        cs("ge12", "k", 12.0, 1.0e6, A.is_ge, A.mult)
+        cs("cf0", "ge12", "o32", None, A.subtract)
+        cs("cf1", "cf0", -64.0, None, A.add)
+        ts(ap("ci", 6, 7), ap("ci", 1, 2), num(2), None, A.arith_shift_right, None, ["ci1"], ["ci8"], 64)
+        cp(C("rf"), ap("ci", 6, 7), ["ci8"], ["c_rf"], 64)
+        ts(ap("wfw"), ap("dw", 0, 144), C("g16o"), C("af"), A.is_equal, A.mult, ["dw", "c_g16o", "c_af"], ["wfw"], 72)
 
-    TAB = ["tab%d" % i for i in range(4)]
-    NEG = ["neg%d" % i for i in range(4)]
-    eye, neye = ap("eye"), ap("neye")
+    nc = n // 16
 
-    def ply(t, c):
-        ba, bb = 2 * c, 2 * c + 1
+    t1 = p["t1"]
+
+    def away(q, c):
+        return (q - q % 2 + (c // 2 ^ p["hf"])) % NR if p["pair"] else q % NR
+
+    def proc(q, c, t):
+        return away(q, c) if t1 <= t < RO - 1 else q % NR
+
+    def unit(r, q, c):
+        return c if q % NR == r % NR else NCH + c % 2
+
+    slots = {}
+    for t in range(RO):
+        for r in range(NR):
+            here = [(q, c) for c in range(NCH) for q in range(NR) if proc(q, c, t) == r]
+            for q, c in here:
+                if t and proc(q - 1, c, t - 1) == r:
+                    slots[t, q, c] = slots[t - 1, (q - 1) % NR, c]
+            left = [j for j in range(NCH) if j not in [slots.get((t, q, c)) for q, c in here]]
+            for q, c in here:
+                if (t, q, c) not in slots:
+                    slots[t, q, c] = left.pop(0)
+
+    def pay(buf, u, s):
+        return (u * RO + s) * 2 * n
+
+    def flags(buf, u, s):
+        o = pay(buf, u, s) + n
+        return ap(buf, o, o + n), "%sM%d_%d" % (buf, u, s)
+
+    def nextflags(r, q, c, s):
+        if proc(q + 1, c, s) == r:
+            return flags("sin", unit(r, q + 1, c), s)
+        return flags("sout", unit(r, q, c), s)
+
+    def struck(fl):
+        return [(ap("ws", 128 * s, 128 * s + 128), x[0], ["ws%d" % s, x[1]], n) for s, x in enumerate(fl)]
+
+    def partner(r):
+        sl = (r - (r ^ 1)) % NR
+        weights(1, sl)
+        if not p["nship"]:
+            negate(1, p["neg2"])
+        for c in range(NCH):
+            if away(r ^ 1, c) == r and t1 == 1:
+                u, j = unit(r, r ^ 1, c), slots[1, r ^ 1, c]
+                a = sl * KW + c * n
+                group(ap("pb%d" % (2 * j), 448, 448 + n), "l0%d" % j, 2 * j,
+                      [mat("eye", ap("kall", a, a + n), ["kall%d" % sl]), mat("eye", ap("kall", LN + a, LN + a + n), ["sall%d" % sl])])
+                relu("S", ap("hl", u * HS + n, u * HS + 2 * n), ap("pb%d" % (2 * j), 448, 448 + n), ["l0%d" % j], ["hl%d_1" % u], n, 2 * j)
+
+    uses = {}
+
+    def ply(t, r, q, c):
+        u, j, tw = unit(r, q, c), slots[t, q, c], int(q % NR != r)
+        ba, bb = 2 * j, 2 * j + 1
         pa, pb = "pb%d" % ba, "pb%d" % bb
-        cn, h0, par = c * n, c * HS, c % 2
-        S, sk = ap("sin", t * LN + cn, t * LN + cn + n), "sin%d_%d" % (t, c)
-        K, kk = ap("kall", (t % NR) * LN + cn, (t % NR) * LN + cn + n), "kall%d" % (t % NR)
-
-        def Mt(s):
-            return ap("mt", s * LN + cn, s * LN + cn + n)
-
-        def mk(s):
-            return "mt%d_%d" % (s, c)
+        cn, h0, t0 = j * n, u * HS, tw * TW
+        par = uses.get(r, 0) % p["nd1"]
+        uses[r] = uses.get(r, 0) + 1
+        o = pay("sin", u, t)
+        S, sk = (ap("sin", o, o + n), "sinS%d_%d" % (u, t)) if t else (ap("kall", LN + c * n, LN + c * n + n), "sall0")
+        ks, ws_ = (r - q + t) % NR, (r - q) % NR
+        K, kk = ap("kall", ks * KW + c * n, ks * KW + c * n + n), "kall%d" % ks
+        step = ap("kall", ws_ * KW + 2 * LN + 32, ws_ * KW + 2 * LN + 33)
+        M, mk = flags("sin", u, t)
+        TAB = ["tab%d_%d" % (tw, i) for i in range(4)]
+        NEG = ["neg%d_%d" % (tw, i) for i in range(4)] + negs
 
         def k(x):
-            return "%s%d" % (x, c)
+            return "%s%d" % (x, j)
 
         def loc(name, w=1):
             return ap(name, w * cn, w * cn + w * n)
-        HL = ["hl%d_%d" % (c, s) for s in range(t + 1)]
-        HA = ["ha%d_%d" % (c, s) for s in range(t + 1)]
-        Lh, lk = ap("hl", h0 + (t + 1) * n, h0 + (t + 2) * n), "hl%d_%d" % (c, t + 1)
-        group(ap(pa, 0, n), k("z"), ba, [(ap("ws", 128 * s, 128 * s + 128), Mt(s), ["ws%d" % s, mk(s)], n) for s in range(t)]
-              + [(ap("selk"), S, ["selk", sk], n)])
-        nep = p["nep"] and t > 0
-        Lp, lb = (ap(pa, 448, 448 + n), ba) if nep else (ap(pb, 0, n), bb)
-        group(Lp, k("nq" if nep else "L"), lb, [(eye, K, ["eye", kk], n), (eye, S, ["eye", sk], n)])
-        ts(Mt(t), ap(pa, 0, n), ap("thr", t, t + 1), None, A.is_ge, None, [k("z"), "thr"], [mk(t)], n, ba)
-        if not nep:
-            relu(p["e_lrelu"], Lh, Lp, [k("L")], [lk], n, bb)
+
+        def on(name, x):
+            return mat(name, loc(x), [k(x)])
+        HL = ["hl%d_%d" % (u, s) for s in range(t + 1)]
+        HA = ["ha%d_%d" % (u, s) for s in range(t + 1)]
+        Lh, lk = ap("hl", h0 + (t + 1) * n, h0 + (t + 2) * n), "hl%d_%d" % (u, t + 1)
+        KS = [mat("eye", K, [kk]), mat("eye2", S, [sk])]
+        if t <= p["m1r"]:
+            group(ap(pa, 384, 384 + n), k("z0"), ba, struck([flags("sin", u, s) for s in range(t)]) + [mat("selk2", S, [sk])])
+            ts(M, ap(pa, 384, 384 + n), ap("thr", t, t + 1), None, A.is_ge, None, [k("z0"), "thr"], [mk], n, ba)
+        group(ap(pb, 0, n), k("L"), bb, KS)
+        relu(p["e_lh"], Lh, ap(pb, 0, n), [k("L")], [lk], n, bb)
         st = 32 if t else 16
         x0 = 32 * cn
         if t:
-            nc = n // 16
-            if p["dgp"]:
-                m0 = t * LN + cn
-                group(ap(pa, n, n + nc), k("pt"), ba, [(ap("e4"), ap("c4", 0, nc), ["e4", "c4"], 64)]
-                      + [(ap("wpw", 16 - r, 144 - r), ap("mt", m0 + r, m0 + n, 16), ["wpw", mk(t)], 64) for r in range(16)])
-                ts(ap("poff", 16 * c, 16 * c + nc), ap(pa, n, n + nc), C("k"), None, A.add, None, [k("pt"), "c_k"], [k("poff")], 64, ba)
+            group(ap(pa, 0, n), k("pt"), ba, [mat("eye", ap("cd"), ["cd"]), mat("wp", M, [mk])])
+            scan(loc("dg"), ap("rs", 0, n), ap(pa, 0, n), A.add, A.max, ["rs", k("pt")], [k("dg")], n, ba)
+            cp(ap("poff", 16 * j, 16 * j + nc), ap("dg", cn + 15, cn + n, 16), [k("dg")], [k("poff")], 64)
+            src = ind("hl", h0, h0 + (t + 1) * n, "poff", 16 * j, 16 * j + nc)
+            og, om = (loc("ogh"), n) if p["ogh"] else (loc("og"), 4 * n)
+            sfx = "h" if p["ogh"] else "f"
+            copy(p["e_og"], og, src, HL + [k("poff")], [k("og")], n, gather=True)
+            if p["nep"]:
+                tt(loc("ne"), og, ap(pb, 0, n), A.not_equal, [k("og"), k("L")], [k("ne")], n, bb)
             else:
-                group(ap(pa, n, 2 * n), k("pt"), ba, [(eye, ap("cd"), ["eye", "cd"], n), (ap("wp"), Mt(t), ["wp", mk(t)], n)])
-                add("V", lambda q, T, X: q.tensor_tensor_scan(T["dg"][:, cn:cn + n], T["rs"][:, 0:n], T[pa][:, n:2 * n], 0.0, A.add, A.max),
-                    ["rs", k("pt")], [k("dg")], ("c", n), ba)
-                cp(ap("poff", 16 * c, 16 * c + nc), ap("dg", cn + 15, cn + n, 16), [k("dg")], [k("poff")], 64)
-            src = ind("hl", h0, h0 + (t + 1) * n, "poff", 16 * c, 16 * c + nc)
-            if p["e_og"] == "S":
-                act(loc("og"), src, F.Copy, HL + [k("poff")], [k("og")], n, kind="gs")
-            else:
-                cp(loc("og"), src, HL + [k("poff")], [k("og")], n, kind="gv")
-            if nep:
-                relu("V", Lh, Lp, [k("nq")], [lk], n, ba)
-                tt(loc("ne"), loc("og"), Lp, A.not_equal, [k("og"), k("nq")], [k("ne")], n, ba)
-            elif p["neg2"]:
                 tt(loc("ne"), src, Lh, A.not_equal, HL + [k("poff"), lk], [k("ne")], n, kind="gv")
-            else:
-                tt(loc("ne"), loc("og"), Lh, A.not_equal, [k("og"), lk], [k("ne")], 2 * n)
-            group(ap(pa, 2 * n, 3 * n), k("pl"), ba, [(eye, K, ["eye", kk], n), (eye, S, ["eye", sk], n), (ap("wb"), Mt(t), ["wb", mk(t)], n),
-                                                      (ap("n16"), loc("ne"), ["n16", k("ne")], n)])
-            group(ap(pb, n, 2 * n), k("po"), bb, [(ap("wb"), Mt(t), ["wb", mk(t)], n), (ap("eyef"), loc("og"), ["eyef", k("og")], 4 * n),
-                                                  (ap("n24"), loc("ne"), ["n24", k("ne")], n)])
-            ts(ap("off", 2 * cn + 1, 2 * cn + 2 * n, 2), ap(pa, 2 * n, 3 * n), num(DEAD), num(0.0), A.add, A.max, [k("pl")], [k("offl")], n, ba)
-            vc = p.get("vc%d_%d" % (t, c), p["vcols"])
+            group(ap(pa, n, 2 * n), k("pl"), ba, KS + [mat("wb", M, [mk]), on("n16", "ne")])
+            group(ap(pb, n, 2 * n), k("po"), bb, [mat("wb", M, [mk]), mat("eye" + sfx, og, [k("og")], om), on("n24", "ne")])
+            xterms = [mat("eye", ap("cd2"), ["cd2"]), mat("wb", M, [mk]), mat("selk" + sfx, og, [k("og")], om), on("selk24", "ne")]
+            px, bx = (pa, ba) if p["xka"] else (pb, bb)
+            if p["x0"] and not p["xka"]:
+                group(ap(px, 256, 256 + n), k("xk"), bx, xterms)
+            ts(ap("off", 2 * cn + 1, 2 * cn + 2 * n, 2), ap(pa, n, 2 * n), num(DEAD), num(0.0), A.add, A.max, [k("pl")], [k("offl")], n, ba)
+            if p["x0"] and p["xka"]:
+                group(ap(px, 256, 256 + n), k("xk"), bx, xterms)
+            vc = p.get("vc%d" % t, p["vcols"])
             ncol, sp, win, wk = 2 * n, p["spieces"], 16384, TAB + NEG
             if p["x0"]:
                 ts(ap("off", 2 * cn, 2 * cn + 2 * n, 2), ap(pb, n, 2 * n), num(DEAD), C("k16"), A.add, A.max, [k("po"), "c_k16"], [k("offo")], n, bb)
-                group(ap(pb, 256, 256 + n), k("xk"), bb,
-                      [(eye, ap("cd2"), ["eye", "cd2"], n), (ap("wb"), Mt(t), ["wb", mk(t)], n), (ap("selkf"), loc("og"), ["selkf", k("og")], 4 * n),
-                       (ap("selk24"), loc("ne"), ["selk24", k("ne")], n)])
-                add("V", lambda q, T, X: q.tensor_tensor_scan(T["dg2"][:, cn:cn + n], T["rs"][:, 0:n], T[pb][:, 256:256 + n], 0.0, A.add, A.max),
-                    ["rs", k("xk")], [k("dgx")], ("c", n), bb)
-                ts(ap("xoff", 16 * c, 16 * c + nc), ap("dg2", cn + 15, cn + n, 16), num(DEAD), num(0.0), A.add, A.max, [k("dgx")], [k("xoff")], 64)
-                src = ind("ha", h0, h0 + (t + 1) * n, "poff", 16 * c, 16 * c + nc)
-                if p["e_sg"] == "S":
-                    act(loc("sg"), src, F.Copy, HA + [k("poff")], [k("sg")], n, kind="gs")
-                else:
-                    cp(loc("sg"), src, HA + [k("poff")], [k("sg")], n, kind="gv")
-                win, wk = 16400, wk + ["tabx"]
+                scan(loc("dg2"), ap("rs", 0, n), ap(px, 256, 256 + n), A.add, A.max, ["rs", k("xk")], [k("dgx")], n, bx)
+                ts(ap("xoff", 16 * j, 16 * j + nc), ap("dg2", cn + 15, cn + n, 16), num(DEAD), num(0.0), A.add, A.max, [k("dgx")], [k("xoff")], 64)
+                copy(p["e_sg"], loc("sg"), ind("ha", h0, h0 + (t + 1) * n, "poff", 16 * j, 16 * j + nc), HA + [k("poff")], [k("sg")], n, gather=True)
+                win, wk = TW, wk + ["tabx%d" % tw]
             else:
                 ts(ap("off", 2 * cn, 2 * cn + 2 * n, 2), ap(pb, n, 2 * n), num(DEAD), num(0.0), A.add, A.max, [k("po")], [k("offo")], n, bb)
         else:
-            group(ap(pa, 2 * n, 3 * n), k("pl"), ba, [(eye, K, ["eye", kk], n), (eye, S, ["eye", sk], n), (ap("wb"), Mt(t), ["wb", mk(t)], n)])
-            ts(ap("off", 2 * cn, 2 * cn + n), ap(pa, 2 * n, 3 * n), num(0.0), None, A.max, None, [k("pl")], [k("offl"), k("offo")], n, ba)
-            ncol, vc, sp, win, wk = n, p["vc0_%d" % c], p["spieces0"], 8192, TAB
+            group(ap(pa, n, 2 * n), k("pl"), ba, KS + [mat("wb", M, [mk])])
+            ncol, vc, sp, win, wk = n, p.get("vc0_%d" % c, p["vc0"]), p["spieces0"], 8192, TAB
+            if p["x00"]:
+                ts(ap("off", 2 * cn, 2 * cn + n), ap(pa, n, 2 * n), C("rest"), C("k1"), A.mult, A.max, [k("pl"), "c_rest", "c_k1"],
+                   [k("offl"), k("offo")], n, ba)
+                group(ap(pb, 256, 256 + n), k("xk"), bb, [mat("eye", ap("cd2"), ["cd2"]), mat("wb", M, [mk]), mat("selk", K, [kk]), mat("selk2", S, [sk])])
+                scan(loc("dg2"), ap("rs", 0, n), ap(pb, 256, 256 + n), A.add, A.max, ["rs", k("xk")], [k("dgx")], n, bb)
+                cp(ap("xoff", 16 * j, 16 * j + nc), ap("dg2", cn + 15, cn + n, 16), [k("dgx")], [k("xoff")], 64)
+                wk = wk + ["low"]
+            else:
+                ts(ap("off", 2 * cn, 2 * cn + n), ap(pa, n, 2 * n), num(0.0), None, A.max, None, [k("pl")], [k("offl"), k("offo")], n, ba)
+        if t == p["m1r"]:
+            a = 3 * KW + LN + c * n
+            kings = [(ap("kall", a, a + n), "sall3"), (ap("sout", pay("sout", u, 1), pay("sout", u, 1) + n), "su%d_1" % u)]
+            for s in range(t + 1):
+                fl = [nextflags(r, q, c, i) for i in range(s + 1)]
+                group(ap(pa, 448, 448 + n), k("l0"), ba, struck(fl[:s]) + [mat("selk2", kings[s][0], [kings[s][1]])])
+                ts(fl[s][0], ap(pa, 448, 448 + n), ap("thr", s, s + 1), None, A.is_ge, None, [k("l0"), "thr"], [fl[s][1]], n, ba)
         sc = ncol - vc
         cuts = [2 * ((sc * i // sp) // 2) for i in range(sp)] + [sc]
+        if t and p["tail"]:
+            e = (sc - p["tail"]) // 16 * 16
+            cuts = [2 * ((e * i // (sp - 1)) // 2) for i in range(sp)] + [sc]
         vp = p["vp"] if vc else 0
         cuts += [sc + 2 * ((vc * (i + 1) // vp) // 2) for i in range(vp)]
-        XK = ["x%d_%d" % (c, i) for i in range(64)]
+        XK = ["x%d_%d" % (j, i) for i in range(64)]
         ok = wk + [k("offl"), k("offo")]
         for i in range(sp + vp):
             a, b = cuts[i], cuts[i + 1]
-            dst, src = ap("xb", x0 + 16 * a, x0 + 16 * b), ind("tab", 0, win, "off", 2 * cn + a, 2 * cn + b)
-            if i < sp:
-                act(dst, src, F.Copy, ok, XK[a // 2:b // 2], 16 * (b - a), kind="gs")
-            else:
-                cp(dst, src, ok, XK[a // 2:b // 2], 16 * (b - a), kind="gv")
-        if t == 0 and c == NCH - 1:
-            for i in range(4):
-                if p["neg"][i] in "sv":
-                    negate(i, XK[:1])
+            if a < b:
+                copy("S" if i < sp else "V", ap("xb", x0 + 16 * a, x0 + 16 * b), ind("tab", t0, t0 + win, "off", 2 * cn + a, 2 * cn + b),
+                     ok, XK[a // 2:b // 2], 16 * (b - a), gather=True)
         if t == RO - 1:
-            final(c)
+            final(c, bb)
             outs(c, "yc", "hl", p["e_yc"], 0.0)
-        dn = "d1"
         d0 = par * 32 * n
         DK = ["d1_%d_%d" % (par, i) for i in range(8)]
         df = ["d1f%d_%d" % (par, i) for i in range(st // 8)]
-        if t == 1 and c < 2:
-            ms(ap(dn, d0 + 16, d0 + 16 * n, 32), -OFS, DK[:4], 64)
-        rp = p.get("rp%d_%d" % (t, c), p["rp"]) if t else 1
+        if t == 1 and uses[r] <= NCH + p["nd1"]:
+            ms(ap("d1", d0 + 16, d0 + 16 * n, 32), -OFS, DK[:4], 64, df)
+        rp = p["rp"] if t else 1
         h = n // rp
+        if t == 0 and p["x00"]:
+            rp = 0
+            add("V", lambda q, T, X: q.tensor_scalar(T["d1"][:, d0:d0 + st * n:st], T["tab"][:, 0:8192].indirect(T["xoff"][:, 16 * j:16 * j + nc]),
+                                                     -OFS, -OFS, A.add, A.max), wk + [k("xoff")] + df, DK, ("gv", n))
         if t and p["x0"]:
             rp = 0
-            tt(loc("tt"), ind("tab", 0, 16384, "xoff", 16 * c, 16 * c + n // 16), loc("sg"), A.add, wk + [k("xoff"), k("sg")], [k("tt")], n, kind="gv")
-            ts(ap(dn, d0, d0 + st * n, st), loc("tt"), num(-OFS), None, A.max, None, [k("tt")] + df, DK, 64)
+            tt(loc("tt"), ind("tab", t0, t0 + 16384, "xoff", 16 * j, 16 * j + nc), loc("sg"), A.add, wk + [k("xoff"), k("sg")], [k("tt")], n,
+               kind="gv")
+            ts(ap("d1", d0, d0 + st * n, st), loc("tt"), num(-OFS), None, A.max, None, [k("tt")] + df, DK, 64)
         for i in range(rp):
             a, b = st * h * i, st * h * (i + 1)
             xf, xk, dk = ap("xb", x0 + a, x0 + b, st), XK[a // 32:b // 32], DK[a // 256:b // 256]
             if t:
                 tb = ap("tt", cn + h * i, cn + h * i + h)
-                tt(tb, ind("ha", h0, h0 + (t + 1) * n, "poff", 16 * c + h * i // 16, 16 * c + (h * i + h) // 16), xf, A.add,
+                tt(tb, ind("ha", h0, h0 + (t + 1) * n, "poff", 16 * j + h * i // 16, 16 * j + (h * i + h) // 16), xf, A.add,
                    HA + xk + [k("poff")], [k("tt%d_" % i)], h, kind="gv")
-                ts(ap(dn, d0 + a, d0 + b, st), tb, num(-OFS), None, A.max, None, [k("tt%d_" % i)] + df, dk, 64)
+                ts(ap("d1", d0 + a, d0 + b, st), tb, num(-OFS), None, A.max, None, [k("tt%d_" % i)] + df, dk, 64)
             else:
-                ts(ap(dn, d0 + a, d0 + b, st), xf, num(-OFS), num(-OFS), A.add, A.max, xk + df, dk, 64)
+                ts(ap("d1", d0 + a, d0 + b, st), xf, num(-OFS), num(-OFS), A.add, A.max, xk + df, dk, 64)
             if p["e_ms"] == "V":
                 ms(xf, -1024.0, xk, 64)
             else:
                 iota(xf, [[0, h]], -1024, 0, xk, h)
-        s0 = par * 32 * n
-        sok = ["so%d_%d" % (par, i) for i in range(8)]
+        sok = ["so%d_%d" % (j, i) for i in range(8)]
         scp = max(1, rp, p["scp"] * st // 32)
         w = st * n // scp
-
-        def scan(i):
-            add("V", lambda q, T, X: q.tensor_tensor_scan(T["so"][:, s0 + i * w:s0 + i * w + w], T["xb"][:, x0 + i * w:x0 + i * w + w],
-                                                          T[dn][:, d0 + i * w:d0 + i * w + w], 0.0, A.add, A.max),
-                XK[i * w // 32:(i * w + w) // 32] + DK[i * w // 256:(i * w + w) // 256], sok[i * w // 256:(i * w + w) // 256], ("c", w // 2))
         for i in range(scp):
-            scan(i)
-        fin = ap("so", s0 + st - 1, s0 + st * n, st)
+            a = i * w
+            scan(ap("so", x0 + a, x0 + a + w), ap("xb", x0 + a, x0 + a + w), ap("d1", d0 + a, d0 + a + w), A.add, A.max,
+                 XK[a // 32:(a + w) // 32] + DK[a // 256:(a + w) // 256], sok[a // 256:(a + w) // 256], w // 2)
+        fin = ap("so", x0 + st - 1, x0 + st * n, st)
         ts(ap("yb", 2 * cn + n, 2 * cn + 2 * n), fin, num(OFS), num(127.0), A.add, A.min, sok, [k("yb")], 64)
-        Ah, ak = ap("ha", h0 + (t + 1) * n, h0 + (t + 2) * n), "ha%d_%d" % (c, t + 1)
-        eh = p["e_hist5"] if (t, c) == (RO - 1, NCH - 1) else p["e_hist"]
-        if eh == "G":
-            sel(Ah, fin, [[0, n]], A.is_ge, 0.0, 0, 0, sok, [ak], n)
-        elif eh == "S":
-            act(Ah, fin, F.Copy, sok, [ak], n)
+        Ah, ak = ap("ha", h0 + (t + 1) * n, h0 + (t + 2) * n), "ha%d_%d" % (u, t + 1)
+        if p["e_hist"] == "G":
+            add("G", lambda q, T, X: q.affine_select(Ah(T), fin(T), [[0, n]], A.is_ge, 0.0, 0, 0), sok, [ak], ("ga", n))
         else:
-            cp(Ah, fin, sok, [ak], 64)
-        lo, hi = (2 * cn + n, 2 * cn + 3 * n), (2 * cn, 2 * cn + 2 * n)
-        group(ap(pb, 128, 256, p1=2 * n), k("key"), bb,
-              [(eye, ap("tiev"), ["eye", "tiev"], 128), (S, ap("penu"), [sk, "penu"], 128, ap(pb, 128, 256, p1=n)),
-               (ap("yb", *lo), ap("uu"), [k("yb")] + UU, 128), (ap("yb", *hi), ap("vv"), [k("yb")] + VV, 128)])
-        add("V", lambda q, T, X: q.tensor_tensor_scan(T["km"][:, 128 * c:128 * c + 128], T["rs"][:], T[pb][:, 128:256], 0.0, A.add, A.max),
-            ["rs", k("key")], [k("km")], ("c", 128), bb)
-        if p["e_kc"] == "S":
-            group(ap(pa, 128, 256), k("pl"), ba,
-                  [(eye, ap("tiev"), ["eye", "tiev"], 128), (S, ap("penu"), [sk, "penu"], 128, ap(pa, 128, 256, p1=n)),
-                   (ap("yb", *lo), ap("uu"), [k("yb")] + UU, 128), (ap("yb", *hi), ap("vv"), [k("yb")] + VV, 128)])
-            act(ap("kc", 128 * c, 128 * c + 128), ap(pa, 128, 256), F.Copy, [k("pl")], [k("kc")], 128, ba)
-        else:
-            cp(ap("kc", 128 * c, 128 * c + 128), ap(pb, 128, 256), [k("key")], [k("kc")], 128, bb)
-        hh = ap("ft", 128 * c, 128 * c + 128)
-        tt(hh, ind("km", 128 * c, 128 * c + 128, "lastc", 0, 8), ap("kc", 128 * c, 128 * c + 128),
-           A.is_equal, [k("km"), k("kc"), "lastc"], [k("ft")], 128, kind="gv")
-        group(ap(pa, 256, 256 + n), k("zu"), ba, [(eye, S, ["eye", sk], n), (hh, ap("ee", 0, n), ["ee", k("ft")], n)])
-        group(ap(pa, 256 + n, 256 + 2 * n), k("zv"), ba, [(hh, ap("ee", n, 2 * n), ["ee", k("ft")], n)])
-        relu(p["e_zz"], loc("mo", 2), ap(pa, 256, 256 + 2 * n), [k("zu"), k("zv"), "c_b33"], [k("mo")], 2 * n, ba, C("b33"))
-        win1 = [(hh, ap("ee", 0, n), ["ee", k("ft")], n)]
-        msq, oh = ap("mo", 2 * cn, 2 * cn + n), ap("mo", 2 * cn + n, 2 * cn + 2 * n)
-        pre = [(ap("bm"), msq, ["bm", k("mo")], n), (ap("wst"), oh, ["wst", k("mo")], n)]
-        wrap = [(neye, loc("wr"), ["neye", k("wr")], n)]
-        s2 = [(eye, S, ["eye", sk], n), (neye, msq, ["neye", k("mo")], n)]
-        last = [(eye, loc("mn"), ["eye", k("mn")], n)]
-        if p["nowr"]:
-            group(ap(pb, 0, n), k("L"), bb, win1 + pre)
-            group(ap(pa, 384, 384 + n), k("e"), ba, [(neye, S, ["neye", sk], n)] + pre)
-            relu("V", loc("mn"), ap(pb, 0, n), [k("L"), "c_b32"], [k("mn")], n, bb, C("b32"))
-            ts(loc("wr"), ap(pb, 0, n), C("w129"), num(128.0), A.is_ge, A.mult, [k("L"), "c_w129"], [k("wr")], n, bb)
-            ts(loc("h2"), ap(pa, 384, 384 + n), C("chi2"), num(GONE), A.is_equal, A.mult, [k("e"), "c_chi2"], [k("h2")], n, ba)
-            ts(loc("ht"), ap(pa, 384, 384 + n), C("chit"), num(GONE), A.is_equal, A.mult, [k("e"), "c_chit"], [k("ht")], n, ba)
-            last += wrap + [(eye, loc("h2"), ["eye", k("h2")], n)]
-        else:
-            group(ap(pa, 384, 384 + n), k("pre"), ba, pre)
-            ts(loc("wr"), ap(pa, 384, 384 + n), num(129.0), num(128.0), A.is_ge, A.mult, [k("pre")], [k("wr")], n, ba)
-            group(ap(pb, 384, 384 + n), k("e"), bb, [(neye, S, ["neye", sk], n)] + pre + wrap)
-            group(ap(pa, 448, 448 + n), k("nq"), ba, win1 + pre + wrap)
-            ts(loc("ht"), ap(pb, 384, 384 + n), C("chit"), num(GONE), A.is_equal, A.mult, [k("e"), "c_chit"], [k("ht")], n, bb)
-            relu(p["e_mn"], loc("mn"), ap(pa, 448, 448 + n), [k("nq"), "c_b32"], [k("mn")], n, ba, C("b32"))
-        if t < RO - 1:
-            group(ap(pa, 0, n), k("z"), ba, s2 + last)
-            o = t * LN + cn
-            tt(ap("sout", o, o + n), ap(pa, 0, n), loc("ht"), A.add, [k("z"), k("ht")], ["su%d_%d" % (t, c)], n, ba)
-            an = "ar%d_%d" % (t + 1, c)
-            add("G", lambda q, T, X: q.remote_dma(T["sin"][:, o + LN:o + LN + n], T["sout"][:, o:o + n], T.sem[an], T.sem["sent"],
-                                                  X["addr"][1][1], X["addr"][1][0], X["mask"]),
-                ["su%d_%d" % (t, c)], ["st%d_%d" % (t, c)], ("r", 0), None, "sent")
-            add(None, None, ["st%d_%d" % (t, c)], ["sin%d_%d" % (t + 1, c)], ("a", 0), None, an)
-        else:
-            group(ap(pa, 0, n), k("z"), ba, s2 + [(eye, K, ["eye", kk], n), (eye, loc("ht"), ["eye", k("ht")], n)] + last)
-            relu(p["e_yl"], loc("oyl"), ap(pa, 0, n), [k("z")], [k("oyl")], n, ba)
-            dma("Y", ap("yl", cn, cn + n), loc("oyl"), [k("oyl")], [], "outs", 32768)
+            copy(p["e_hist"], Ah, fin, sok, [ak], 64)
+        if t == t1 - 1 and away(q, c) != r:
+            u2 = unit(away(q, c), q, c)
+            hs = ("ha", "hl") if t else ("ha",)
+            send(away(q, c), [(x, h0 + n, x, u2 * HS + n, t1 * n) for x in hs], [ak, lk] + HL[1:] + HA[1:],
+                 ["%s%d_%d" % (x, u2, s) for x in hs for s in range(1, t1 + 1)], "h0_%d" % c)
+        if t == RO - 2 and q % NR != r:
+            a, m = (t1 + 1) * n, (RO - 1 - t1) * n
+            send(q, [("hl", h0 + a, "hl", c * HS + a, m), ("ha", h0 + a, "ha", c * HS + a, m),
+                     ("sin", pay("sin", u, t1), "sin", pay("sin", c, t1), 2 * m)],
+                 [x % (u, s) for s in range(t1, 5) for x in ("sinS%d_%d", "sinM%d_%d")] + HL[t1 + 1:] + HA[t1 + 1:] + [lk, ak],
+                 [x % (c, s) for s in range(t1 + 1, 6) for x in ("hl%d_%d", "ha%d_%d")] + ["sinM%d_%d" % (c, s) for s in range(t1, 5)],
+                 "h4_%d" % c, ("b", 1536 * m))
+        lo, hi = ap("yb", 2 * cn + n, 2 * cn + 3 * n), ap("yb", 2 * cn, 2 * cn + 2 * n)
+        uu, vv = "uu%d" % tw, "vv%d" % tw
 
-    def final(c):
-        ba, bb = 2 * c, 2 * c + 1
+        def keys(pb, bb, at, key, const, sh):
+            group(ap(pb, at, at + 128), key, bb,
+                  [mat("eye", ap(const), [const], 128), (S, ap("pen", sh, sh + 128), [sk, "pen"], 128, ap(pb, at, at + 128, p1=n)),
+                   (lo, ap(uu, sh, sh + 128), [k("yb")] + ["%s_%d" % (uu, i) for i in range(9)], 128),
+                   (hi, ap(vv, sh, sh + 128), [k("yb")] + ["%s_%d" % (vv, i) for i in range(9)], 128)])
+        q0 = 128 * j
+        rq, tq = ap("rq", q0, q0 + 128), ap("tq", q0, q0 + 128)
+        keys(pb, bb, 128, k("key"), "dc", 0)
+        if p["q2"]:
+            keys(pa, ba, 0, k("kez"), "dc2", 1)
+        scan(rq, ap(pb, 128, 256), ap("zr"), A.add, A.max, [k("key"), "zr"], [k("rq")], 128, bb)
+        if p["q2"]:
+            scan(back("tq", q0, q0 + 128), back(pa, 0, 128), ap("zr"), A.add, A.min, [k("kez"), "zr"], [k("tq")], 128, ba)
+        else:
+            scan(back("tq", q0, q0 + 128), ap("eps"), back("rq", q0, q0 + 128), A.add, A.min, [k("rq"), "eps"], [k("tq")], 64)
+
+        def lost(a):
+            return [(rq, ap("ee", a, a + n), ["ee", k("rq")], n), (tq, ap("ee2", a, a + n), ["ee2", k("tq")], n)]
+        group(ap(pa, 192, 192 + n), k("zu"), ba, [mat("eye2", S, [sk])] + lost(0))
+        group(ap(pb, 320, 320 + n), k("zv"), bb, lost(n))
+        relu(p["e_msq"], loc("msq"), ap(pa, 192, 192 + n), [k("zu")], [k("msq")], n, ba)
+        relu(p["e_ost"], loc("ost"), ap(pb, 320, 320 + n), [k("zv"), "step%d" % ws_], [k("ost")], n, bb, step)
+        if p["m1r"] <= t < RO - 1:
+            group(ap(pb, 384, 384 + n), k("zn"), bb,
+                  struck([nextflags(r, q, c, s) for s in range(t + 1)]) + [mat("selk2", S, [sk]), on("nselk", "msq")], last=False)
+        b1 = (ba - 2) % 8 if p["bor"][0] <= t * NCH + c <= p["bor"][1] else ba
+        w1 = ap("pb%d" % b1, 256, 256 + n)
+        group(w1, k("w1"), b1, [on("bmq", "msq"), on("bmq", "ost"), mat("cp", ap("one"), ["one"]), mat("cn", ap("one"), ["one"]),
+                                on("bmh", "msq"), on("bmh", "ost")])
+        tt(loc("mn"), w1, loc("msq"), A.min, [k("w1"), k("msq")], [k("mn")], n, b1)
+        tt(loc("ht"), w1, S, A.is_equal, [k("w1"), sk], [k("ht")], n, b1)
+        king = [on("selk2", "mn")]
+        last = [on("eye", "mn"), on("gd", "ht")]
+        s2 = [mat("eye", S, [sk]), on("nhalf", "msq")]
+        if t < RO - 1:
+            r2 = proc(q + 1, c, t + 1)
+            u2 = unit(r2, q + 1, c)
+            Mn, mnk = nextflags(r, q, c, t + 1)
+            o2 = pay("sin", u2, t + 1)
+            buf, o1, su = ("sin", o2, "sinS%d_%d" % (u2, t + 1)) if r2 == r else ("sout", pay("sout", u, t + 1), "su%d_%d" % (u, t + 1))
+            if t >= p["m1r"]:
+                group(ap(pb, 384, 384 + n), k("zn"), bb, king, first=False)
+            group(ap(pa, 320, 320 + n), k("fin"), ba, s2 + last)
+            if t >= p["m1r"]:
+                ts(Mn, ap(pb, 384, 384 + n), ap("thr", t + 1, t + 2), None, A.is_ge, None, [k("zn"), "thr"], [mnk], n, bb)
+            copy(p["e_su"], ap(buf, o1, o1 + n), ap(pa, 320, 320 + n), [k("fin")], [su], n, ba)
+            if t < p["m1r"]:
+                send(r2, [("sout", o1, "sin", o2, n)], [su], ["sinS%d_%d" % (u2, t + 1)], "ar%d_%d" % (t + 1, c), name=su)
+            elif r2 != r:
+                send(r2, [("sout", o1, "sin", o2, 2 * n)], [su, mnk], ["sinS%d_%d" % (u2, t + 1), "sinM%d_%d" % (u2, t + 1)],
+                     "ar%d_%d" % (t + 1, slots[t + 1, (q + 1) % NR, c]), mask="high" if p["pair"] and p["nship"] and t < 2 else "all", name=su)
+            r3 = proc(q, c, t1)
+            if t == t1 - 1 and r3 != r and r3 != r2:
+                u3 = unit(r3, q, c)
+                send(r3, [("sout", pay("sout", u, 0) + n, "sout", pay("sout", u3, 0) + n, (2 * t1 + 1) * n)],
+                     ["su%d_%d" % (u, s) for s in range(1, t1 + 1)] + ["soutM%d_%d" % (u, s) for s in range(t1 + 1)],
+                     ["soutM%d_%d" % (u3, s) for s in range(t1 + 1)], "mn_%d" % c)
+        else:
+            group(ap(pa, 320, 320 + n), k("fin"), ba, KS + [on("neye", "msq"), on("eye2", "mn"), on("gd", "ht")])
+            relu(p["e_yl"], loc("oyl"), ap(pa, 320, 320 + n), [k("fin")], [k("oyl")], n, ba)
+            dma("Y", ap("yl", c * n, c * n + n), loc("oyl"), [k("oyl")], [], "outs", 32768)
+
+    def final(c, bb):
         pb = "pb%d" % bb
-        cn, h0, nc = c * n, c * HS, n // 4
-        group(ap(pb, 448, 448 + n), "zf%d" % c, bb,
-              [(ap("ws", 128 * s, 128 * s + 128), ap("mt", s * LN + cn, s * LN + cn + n), ["ws%d" % s, "mt%d_%d" % (s, c)], n) for s in range(RO)])
+        cn, n4 = c * n, n // 4
+        group(ap(pb, 448, 448 + n), "zf%d" % c, bb, struck([flags("sin", c, s) for s in range(RO)]))
         for h in range(2):
             ts(ap("fm", 2 * cn + h * n, 2 * cn + h * n + n), ap(pb, 448, 448 + n), C("cf%d" % h), None, A.is_equal, None,
                ["zf%d" % c, "c_cf%d" % h], ["fm%d_%d" % (c, h)], n, bb)
-        terms = [(eye, ap("c4", 0, nc), ["eye", "c4"], 64)]
+        terms = [mat("eye", ap("c4", 0, n4), ["c4"], 64)]
         for h in range(2):
             for r in range(4):
                 d = 4 * r + 2 * h
                 terms.append((ap("wfw", 16 - d, 144 - d), ap("fm", 2 * cn + h * n + r, 2 * cn + h * n + n, 4), ["wfw", "fm%d_%d" % (c, h)], 64))
-        group(ap(pb, 448, 448 + nc), "zf%d" % c, bb, terms)
-        ts(ap("foff", 16 * c, 16 * c + nc), ap(pb, 448, 448 + nc), C("rf"), None, A.add, None, ["zf%d" % c, "c_rf"], ["foff%d" % c], 64, bb)
+        group(ap(pb, 448, 448 + n4), "zf%d" % c, bb, terms)
+        ts(ap("foff", 16 * c, 16 * c + n4), ap(pb, 448, 448 + n4), C("rf"), None, A.add, None, ["zf%d" % c, "c_rf"], ["foff%d" % c], 64, bb)
 
     def outs(c, nm, hn, e, bias):
-        cn, h0, nc = c * n, c * HS, n // 4
-        src = ind(hn, h0, h0 + HS, "foff", 16 * c, 16 * c + nc)
+        cn, h0, n4 = c * n, c * HS, n // 4
+        src = ind(hn, h0, h0 + HS, "foff", 16 * c, 16 * c + n4)
         r = ["%s%d_%d" % (hn, c, s) for s in range(7)] + ["foff%d" % c]
         dst = ap("o" + nm, 4 * cn, 4 * cn + 4 * n)
         if e == "S":
@@ -554,12 +727,26 @@ def build(p):
             add("V", lambda q, T, X: q.tensor_scalar(dst(T), src(T), bias, None, A.add), r, ["o%s%d" % (nm, c)], ("gv", 4 * n))
         dma("Y", ap(nm, 4 * cn, 4 * cn + 4 * n), dst, ["o%s%d" % (nm, c)], [], "outs", 131072)
 
+    for r in range(kinds):
+        me[0] = r
+        setup(r)
     for t in range(RO):
+        if t == 1 and p["pair"]:
+            tag[0] = cur[0] = None
+            for r in range(2):
+                me[0] = r
+                partner(r)
         for c in range(NCH):
             tag[0] = t * NCH + c
-            ply(t, c)
-            if t == RO - 1:
-                outs(c, "ya", "ha", p["e_ya"], OFS)
+            for r in range(kinds):
+                me[0] = r
+                for q in (r, r ^ 1):
+                    if proc(q, c, t) == r:
+                        tag[0] = t * NCH + p["sk"][(q - t) % 2][c]
+                        cur[0] = (t, (q - t) % 2 if p["pair"] else 0, c)
+                        ply(t, r, q, c)
+                        if t == RO - 1:
+                            outs(c, "ya", "ha", p["e_ya"], OFS)
     return ops
 
 
@@ -582,8 +769,10 @@ def times(op, p):
         d = p["riss"]
     elif kind == "a":
         return 0.0, p["rlat"] + p["klat"] * m
+    elif kind == "b":
+        return 0.0, p["rlat"] + m / p["bw"] / 1000.0
     else:
-        return (1.0 if op["eng"] == "G" else 0.1), 2.0 + op["lat"][1] / p["bw"] / 1000.0
+        return 0.1, 2.0 + op["lat"][1] / p["bw"] / 1000.0
     return d, d
 
 
@@ -595,16 +784,11 @@ def schedule(ops, p):
         for d in o["deps"]:
             succ[d].append(k)
     pr = [0.0] * N
-    z = p["seed"] * 7919 + 1
     for k in range(N - 1, -1, -1):
         own = -p["tq"] * ops[k]["tag"] if ops[k]["tag"] is not None else -1.0e3
         pr[k] = tm[k][1] + max([pr[s] + p["hop"] for s in succ[k]] + [own])
     for k in range(N):
-        pr[k] += p["off"].get(ops[k]["cls"], 0.0) - p["short"] * tm[k][0]
-    if p["jit"]:
-        for k in range(N):
-            z = (z * 1103515245 + 12345) % 2147483648
-            pr[k] += p["jit"] * (z / 2147483648.0)
+        pr[k] += p["up"].get(ops[k]["ty"][1:], 0.0) + p["up"].get(ops[k]["ty"].rstrip("0123456789_"), 0.0) - p["short"] * tm[k][0]
     left = [len(o["deps"]) for o in ops]
     rdy = [0.0] * N
     free, order, ready = {}, {}, {}
@@ -631,22 +815,26 @@ def schedule(ops, p):
                     be, bt = e, t0
         if be is None:
             break
-        k = max([k for k in ready[be] if rdy[k] <= bt + p["delta"]], key=lambda j: (pr[j], -j))
+        k = max([k for k in ready[be] if rdy[k] <= bt], key=lambda j: (pr[j], -j))
         ready[be].remove(k)
         st = max(bt, rdy[k])
         free[be] = st + tm[k][0]
         order.setdefault(be, []).append(k)
         done += 1
         for s in succ[k]:
-            hop = 0.0 if (be == "P" and ops[s]["eng"] == "P") else p["hop"]
+            hop = 0.0 if (be[0] == "P" and ops[s]["eng"] == be) else p["hop"]
             rdy[s] = max(rdy[s], st + tm[k][1] + hop)
             left[s] -= 1
             if not left[s]:
                 stack.append(s)
-    return improve(ops, p, order)
+    order = improve(ops, p, order)
+    for e, l in order.items():
+        if e[0] == "Y":
+            order[e] = sorted([k for k in l if not ops[k]["deps"]]) + [k for k in l if ops[k]["deps"]]
+    return order
 
 
-def place(ops, tm, pred, key, hop):
+def place(ops, tm, pred, key):
     N = len(ops)
     start, busy = [0.0] * N, {}
     for k in sorted(range(N), key=lambda j: key[j]):
@@ -673,10 +861,9 @@ def improve(ops, p, order):
     fw, bw = [[] for _ in range(N)], [[] for _ in range(N)]
     for k, o in enumerate(ops):
         for d in o["deps"]:
-            h = 0.0 if (ops[d]["eng"] is None or (o["eng"] == "P" and ops[d]["eng"] == "P")) else p["hop"]
+            h = 0.0 if (ops[d]["eng"] is None or (o["eng"] == ops[d]["eng"] and o["eng"][0] == "P")) else p["hop"]
             fw[k].append((d, tm[d][1] + h))
             bw[d].append((k, tm[k][0] + h + tm[d][1] - tm[d][0]))
-    key = [0.0] * N
     nxt = {e: 0 for e in order}
     fin, free = [None] * N, {e: 0.0 for e in order}
     todo = [k for k in range(N) if ops[k]["eng"] is None]
@@ -697,8 +884,8 @@ def improve(ops, p, order):
     st = fin
     best, bo = max([st[k] + tm[k][1] for k in range(N)]), order
     for it in range(p["fbi"]):
-        sb = place(ops, tm, bw, [(-round(st[k] + tm[k][0], 6), -k) for k in range(N)], p["hop"])
-        st = place(ops, tm, fw, [(-round(sb[k] + tm[k][0], 6), k) for k in range(N)], p["hop"])
+        sb = place(ops, tm, bw, [(-round(st[k] + tm[k][0], 6), -k) for k in range(N)])
+        st = place(ops, tm, fw, [(-round(sb[k] + tm[k][0], 6), k) for k in range(N)])
         end = max([st[k] + tm[k][1] for k in range(N)])
         if end < best:
             best, bo = end, {}
@@ -708,102 +895,6 @@ def improve(ops, p, order):
     return bo
 
 
-CASES = [{"g": 1.2, "f": 1.0, "hop": 0.26, "rlat": 2.5, "pe": 0.5, "fix": 0.0, "riss": 0.8, "bw": 350.0, "klat": 5.0, "base": 98.8},
-         {"g": 2.0, "f": 1.45, "hop": 0.25, "rlat": 2.2, "pe": 0.5, "fix": 0.0, "riss": 1.2, "bw": 250.0, "klat": 5.0, "base": 135.1},
-         {"g": 1.3, "f": 1.45, "hop": 0.22, "rlat": 2.9, "pe": 0.6, "fix": 0.01, "riss": 0.6, "bw": 300.0, "klat": 5.0, "base": 119.1},
-         {"g": 1.9, "f": 1.1, "hop": 0.24, "rlat": 2.6, "pe": 0.5, "fix": 0.01, "riss": 1.0, "bw": 400.0, "klat": 5.0, "base": 107.9}]
-
-
-def polish(ops, p, order):
-    N = len(ops)
-    eng = [o["eng"] for o in ops]
-    succ = [[] for _ in range(N)]
-    for k, o in enumerate(ops):
-        for d in o["deps"]:
-            succ[d].append(k)
-    data = []
-    for c in CASES:
-        q = dict(p)
-        q.update(c)
-        tm = [times(o, q) for o in ops]
-        pred = [[(d, tm[d][1] + (0.0 if (eng[d] is None or (eng[k] == "P" and eng[d] == "P")) else q["hop"])) for d in ops[k]["deps"]]
-                for k in range(N)]
-        data.append(([x[0] for x in tm], [x[1] for x in tm], pred, c["base"]))
-
-    def run(seq, i, keep):
-        du, la, pred, base = data[i]
-        st, free, last, par = [0.0] * N, {}, {}, [None] * N
-        end, ek = 0.0, 0
-        for k in seq:
-            e = eng[k]
-            t0, w = free.get(e, 0.0), last.get(e)
-            for d, x in pred[k]:
-                x += st[d]
-                if x > t0:
-                    t0, w = x, d
-            st[k], par[k] = t0, w
-            if e is not None:
-                free[e], last[e] = t0 + du[k], k
-            if t0 + la[k] > end:
-                end, ek = t0 + la[k], k
-        keep.append((st, par, ek))
-        return end / base
-
-    def score(seq):
-        keep = []
-        r = [run(seq, i, keep) for i in range(len(data))]
-        return max(r) + sum(r) / len(r), keep
-
-    nxt, placed, seq = {e: 0 for e in order}, [False] * N, []
-    while len(seq) < N:
-        for k in range(N):
-            if not placed[k] and (eng[k] is None or order[eng[k]][nxt[eng[k]]] == k) and all([placed[d] for d in ops[k]["deps"]]):
-                placed[k] = True
-                seq.append(k)
-                if eng[k] is not None:
-                    nxt[eng[k]] += 1
-    cur, keep = score(seq)
-    best, bseq = cur, seq
-    z = 12345 + p["seed"]
-    for it in range(p["iters"]):
-        z = (z * 1103515245 + 12345) % 2147483648
-        st, par, k = keep[(z >> 8) % len(data)]
-        pos = [0] * N
-        for i, j in enumerate(seq):
-            pos[j] = i
-        seq = sorted(seq, key=lambda j: (st[j], pos[j]))
-        for i, j in enumerate(seq):
-            pos[j] = i
-        pairs = []
-        while par[k] is not None:
-            if eng[k] is not None and eng[par[k]] == eng[k] and par[k] not in ops[k]["deps"]:
-                pairs.append((par[k], k))
-            k = par[k]
-        if not pairs:
-            continue
-        z = (z * 1103515245 + 12345) % 2147483648
-        a, b = pairs[(z >> 8) % len(pairs)]
-        new = None
-        early = max([pos[d] for d in ops[b]["deps"]], default=-1) < pos[a]
-        late = min([pos[s] for s in succ[a]], default=N) > pos[b]
-        if early and (not late or (z >> 20) & 1):
-            new = seq[:pos[a]] + [b] + seq[pos[a]:pos[b]] + seq[pos[b] + 1:]
-        elif late:
-            new = seq[:pos[a]] + seq[pos[a] + 1:pos[b] + 1] + [a] + seq[pos[b] + 1:]
-        if new is None:
-            continue
-        s, kp = score(new)
-        if s <= cur + p["temp"] * (1.0 - it / p["iters"]) * ((z >> 4) % 16) / 16.0:
-            cur, keep, seq = s, kp, new
-            if s < best:
-                best, bseq = s, new
-    out = {}
-    for k in bseq:
-        if eng[k] is not None:
-            out.setdefault(eng[k], []).append(k)
-    return out
-
-
 PLAN = {}
 
 
@@ -811,7 +902,7 @@ def plan():
     if not PLAN:
         ops = build(P)
         PLAN["ops"] = ops
-        PLAN["order"] = polish(ops, P, schedule(ops, P))
+        PLAN["order"] = schedule(ops, P)
     return PLAN["ops"], PLAN["order"]
 
 
@@ -819,13 +910,17 @@ def rank_program(g, core, T, topo):
     rank = T.rank_of(core)
     if rank is None:
         return
-    ops, order = plan()
+    ops, both = plan()
+    order = {e: l for e, l in both.items() if e[1] == str(rank % (1 + P["pair"]))}
     peers = [T.cores[(rank + j) % NR] for j in range(NR)]
     mask = topo.mask(core, peers[1])
     for c in peers[2:]:
         mask &= topo.mask(core, c)
-    ne = bin(mask).count("1")
-    X = {"addr": [topo.addr(c) for c in peers], "mask": mask}
+    bits = [1 << e for e in topo.engines(core, peers[1]) if mask >> e & 1]
+    ne = len(bits)
+    low, high = sum(bits[:ne // 2]), sum(bits[ne // 2:])
+    parts = {2: [low, high], 3: [low, sum(bits[ne // 2:3 * ne // 4]), sum(bits[3 * ne // 4:])]}
+    X = {"addr": [topo.addr(c) for c in peers], "mask": mask, "all": mask, "low": low, "high": high, "parts": parts}
     queue = {"V": g.vector, "S": g.scalar, "P": g.tensor, "G": g, "Y": g.sync}
     pos = {}
     for e, l in order.items():
@@ -842,9 +937,11 @@ def rank_program(g, core, T, topo):
                 top = {}
                 for d in ops[k]["deps"]:
                     o = ops[d]
+                    if o["cost"][0] == "r":
+                        continue
                     if o["sem"] is not None:
                         top[("x", d)] = d
-                    elif not (e == "P" and o["eng"] == "P"):
+                    elif not (e[0] == "P" and o["eng"] == e):
                         f = o["eng"]
                         if f not in top or pos[d] > pos[top[f]]:
                             top[f] = d
@@ -870,16 +967,16 @@ def rank_program(g, core, T, topo):
     for e, l in order.items():
         for k in l:
             if k in needed:
-                total["s" + e] = total.get("s" + e, 0) + 1
-                token[k] = ("s" + e, total["s" + e])
+                total[e] = total.get(e, 0) + 1
+                token[k] = ("s" + e[0], total[e])
     for k, o in enumerate(ops):
         if o["eng"] is None:
-            token[k] = (o["sem"], ne * (NR - 1 if o["sem"] == "karr" else 1))
+            token[k] = (o["sem"], ne * (NR - 1) if o["sem"] == "karr" else ne if o["lat"] == "all" else ne // 2)
         elif o["cost"][0] == "d":
             token[k] = (o["sem"], 16)
     nout = nsent = 0
     for e, l in order.items():
-        q = queue[e]
+        q = queue[e[0]]
         for k in l:
             for d in waits[k]:
                 q.wait_ge(T.sem[token[d][0]], token[d][1])
@@ -889,8 +986,8 @@ def rank_program(g, core, T, topo):
                 ins.then_inc(T.sem[o["sem"]], 16)
                 nout += 16 if o["sem"] == "outs" else 0
             elif o["cost"][0] == "r":
-                nsent += ne
+                nsent += ne // 2 if o["lat"] in ("low", "high") else ne
             elif k in needed:
-                ins.then_inc(T.sem["s" + e], 1)
+                ins.then_inc(T.sem["s" + e[0]], 1)
     g.wait_ge(T.sem["sent"], nsent)
     g.sync.wait_ge(T.sem["outs"], nout)

@@ -5,123 +5,88 @@ NR, LN, RO = 4, 256, 6
 NCH = 4
 n = LN // NCH
 HS = 7 * n
-NU = NCH + 2
-TW = 16400
-KW = 2 * LN + 48
-DEAD = -16384.0
+TW = 8192
+XW = 16 * n + 16
+SW = 12 * n
+RM = {2: 0, 3: 2 * n, 4: 5 * n, 5: 9 * n}
+DEAD = -32768.0
 GONE = -2.0 ** 90
 OFS = 240.0
-BIG = 2.0 ** 18
+LOST = 16384.0
 
-P = {"sk": ((0, 2, 1, 3), (1, 3, 0, 2)), "pair": 1, "hf": 1, "nd1": 2, "neg2": "VVVV", "tlate": 1, "x0": 1, "q2": 0, "mv": 1, "neg": "SSSS",
-     "vcols": 16, "spieces": 4, "spieces0": 2, "vp": 2, "scp": 8, "rp": 1,
-     "vc0": 32, "vc1": 24, "vc5": 24,
-     "e_lh": "V", "e_og": "V", "e_sg": "S", "e_msq": "V", "e_ost": "V", "e_su": "S", "e_hist": "G", "e_ms": "G",
-     "e_yc": "S", "e_ya": "S", "e_yl": "V", "e_f0": "G", "e_f1": "G", "e_f2": "G", "e_f3": "V",
-     "g": 1.75, "f": 1.2, "pe": 0.7, "hop": 0.23, "rlat": 2.3, "riss": 0.8, "klat": 5.0, "bw": 350.0, "fix": 0.0,
-     "tq": 4.0, "short": 2.0, "fbi": 6}
+P = {"one": 1, "nd": 2, "m1r": 1, "sel": 1, "sela": 1, "h16": 0, "nep": 1, "jz": 0, "jp": 1, "neg": "SSSV", "negw": 1024, "klate": 4,
+     "cut": ("S", 32, "S", 72, "S", 104, "V", 116, "V", 128),
+     "cut0": ("S", 24, "S", 48, "V", 64), "cuto": ("S", 24, "S", 52, "V", 64), "cutn": ("V", 8, "S", 36, "S", 64),
+     "e_lh": "V", "e_og": "V", "e_msq": "V", "e_ost": "V", "e_su": "V", "e_yc": "V", "e_ya": "S", "e_yl": "V", "e_d1": "GVGV",
+     "g": 1.7, "f": 1.1, "pe": 0.7, "hop": 0.23, "rlat": 2.3, "riss": 0.6, "klat": 3.0, "bw": 400.0, "tq": 3.0, "short": 0.0, "fbi": 6, "up": {}, "sgn": 0, "e_ha": "V", "eq1": 0, "sfirst": 0, "lp": (1, 2, 3, 4),
+     "e_cs": ("king2", "ab", "pk", "nking", "sgh", "m2", "af", "t32", "aw", "q0", "q2", "s0", "g16o", "c0", "cf1")}
+P.update({'one': 1, 'cut0': ('V', 16, 'S', 40, 'S', 64), 'jz': 0, 'jp': 0, 'nep': 0, 'm1r': 1, 'nd': 2, 'e_d1': 'GDD', 'sel': 4, 'sela': 3, 'h16': 0,
+          'g': 2.0, 'f': 1.0, 'hop': 0.25, 'tq': 6, 'short': 1, 'rlat': 1.8, 'e_su': 'S', 'e_ost': 'V', 'e_msq': 'V', 'e_yl': 'V', 'e_ya': 'S',
+          'e_yc': 'S', 'e_lh': 'V', 'klate': 4, 'cut': ('V', 16, 'V', 32, 'S', 80, 'S', 112, 'S', 128),
+          'cut5': ('V', 16, 'V', 28, 'S', 80, 'S', 112, 'S', 128), 'neg': 'SSVV', 'negw': 512, 'cut0_0': ('V', 32, 'S', 64),
+          'cut0_3': ('S', 24, 'S', 48, 'V', 64)})
+P.update({'cut0': ('V', 16, 'S', 48, 'S', 64), 'jz': 0, 'jp': 2, 'nep': 0, 'm1r': 1, 'nd': 2, 'e_d1': 'GDD', 'sel': 3, 'sela': 3, 'h16': 1, 'g': 2.0,
+          'f': 1.0, 'hop': 0.25, 'tq': 6, 'short': 0, 'rlat': 1.8, 'e_su': 'V', 'e_ost': 'V', 'e_msq': 'V', 'e_yl': 'S', 'e_ya': 'S', 'e_yc': 'S',
+          'e_lh': 'S', 'klate': 4, 'eq1': 1, 'sfirst': 0, 'sgn': 0, 'e_ha': 'V', 'pe': 0.7, 'cut': ('V', 16, 'V', 24, 'S', 64, 'S', 96, 'S', 128),
+          'cut1': ('V', 16, 'V', 32, 'S', 96, 'S', 128), 'cut5': ('V', 16, 'S', 48, 'S', 96, 'V', 112, 'S', 128), 'neg': 'SSVV', 'negw': 512,
+          'cut0_0': ('S', 24, 'S', 44, 'V', 64), 'cut0_3': ('V', 16, 'S', 48, 'S', 64)})
 
-P.update({"sk": ((0, 1, 2, 3), (0, 1, 2, 3)), "pair": 0, "spieces0": 3, "e_ms": "V", "e_f3": "G",
-          "up": {}, "klate": 1, "x00": 1, "bor": (99, 0), "xka": 0, "tail": 0, "e_mn": "V", "m1r": 1, "t1": 2, "nship": 1, "ogh": 1, "nep": 0, "lp": ((0, 1), (1, 2), (2, 3), (3, 4))})
-
-P.update({'vcols': 20, 'spieces0': 1, 'vc0': 16, 'vc1': 16, 'vc5': 32, 'e_su': 'V', 'e_f0': 'V', 'e_f2': 'V', 'riss': 1.0, 'bw': 450.0,
-          'fbi': 2, 'lp': ((0, 1), (1, 4)),
-          'up': {'dgx0': 1, 'og0': -8, 'dg0': -1, 'so2': 2, 'poff0': 4, 'tt0': 1, 'x4': 2, 'x2': 1, 'rq0': -1, 'sg0': -1, 'tq0': -2,
-                 'x5': -1, 'so6': -1, 'so0': -8, 'ne0': -4, 'so1': -2, 'offo0': 4, 'h0': 4, 'hl0': 2, 'mn0': 8, 'd0': -2}})
-
-P.update({'up': {}, 'mv': 2, 'spieces': 3, 'vp': 1, 'scp': 4, 'vc0': 24, 'vc5': 24, 'e_sg': 'V', 'e_ms': 'G', 'e_f1': 'V', 'e_f2': 'G',
-          'g': 1.6, 'f': 1.3, 'hop': 0.19, 'bw': 350.0, 'fix': 0.015, 'm1r': 0})
-
-P.update({'mv': 1, 'neg': 'SVSV', 'spieces': 4, 'vp': 2, 'scp': 8, 'vc0': 16, 'vc5': 32, 'e_sg': 'S', 'e_su': 'S', 'e_f1': 'G', 'e_f2': 'S',
-          'g': 1.75, 'f': 1.2, 'hop': 0.23, 'riss': 0.6, 'bw': 300.0, 'fix': 0.0,
-          'up': {'dgx0': 4, 'og0': -8, 'dg0': -1, 'so2': 2, 'poff0': 4, 'tt0': 1, 'x4': 2, 'x2': 1, 'rq0': -1, 'sg0': -1, 'tq0': -2, 'x5': -1,
-                 'so6': 4, 'so0': -8, 'ne0': -4, 'so1': -2, 'offo0': 4, 'h0': -1, 'hl0': 2, 'mn0': 8, 'd0': -2, 'ht0': -4, 'M0': 1, 'suu': -8,
-                 'sws': -1, 'ax': -8, 'ad': 4}})
-
-P.update({'spieces0': 3, 'e_f0': 'S', 'e_f1': 'S', 'e_f2': 'G', 'tq': 6.0, 'bor': (4, 19), 'm1r': 1, 'vc0_1': 8,
-          'up': {'dgx0': 4, 'og0': -8, 'dg0': -1, 'so2': -2, 'tt0': 8, 'x4': 2, 'x2': 1, 'rq0': -2, 'sg0': -1, 'tq0': 1, 'x5': -1, 'so6': 4,
-                 'so0': -8, 'ne0': -4, 'so1': -2, 'offo0': 4, 'h0': -1, 'mn0': 8, 'd0': -2, 'ht0': -8, 'M0': 1, 'suu': -8, 'sws': -1, 'ad': -1,
-                 'so5': 8, 'wr0': -8, 'asu': -8, 'so4': -8, 'dM': -4, 'cfoff': -4, 'so7': -2, 'ost0': -2, 'yb0': -2, 'so3': -2, 'su0': 4}})
-
-P.update({'neg': 'SSSV', 'vcols': 24, 'spieces': 3, 'vc0': 8, 'vc1': 24, 'e_su': 'V', 'e_f0': 'G', 'f': 1.1, 'bw': 450.0, 'bor': (5, 23),
-          'nep': 1, 'vc0_0': 32,
-          'up': {'ahl': -8, 'ost0': 2, 'so5': -4, 'coyc': 8, 'dgx0': -4, 'coya': -4, 'msq0': -4, 'x4': 1, 'xoff0': 4, 'sng': 8, 'ax': -2,
-                 'sws': 8, 'cx': -4, 'so6': -2}})
-
-BF, F32, I32, U16 = "bfloat16", "float32", "int32", "uint16"
+BF, F32, I32, U16, F16 = "bfloat16", "float32", "int32", "uint16", "float16"
 SCRATCH = {
-    "tab": ("sbuf", [128, 2 * TW], BF),
-    "xb": ("sbuf", [128, 32 * LN], BF), "so": ("sbuf", [128, 32 * LN], BF), "d1": ("sbuf", [128, 32 * LN], BF),
-    "hl": ("sbuf", [128, NU * HS], F32), "ha": ("sbuf", [128, NU * HS], F32),
-    "posi": ("sbuf", [128, LN], I32), "ki": ("sbuf", [128, LN], I32), "si": ("sbuf", [128, LN], I32), "dd": ("sbuf", [128, LN], F32),
-    "kall": ("sbuf", [128, NR * KW], BF), "sin": ("sbuf", [128, NU * RO * 2 * n], BF), "sout": ("sbuf", [128, NU * RO * 2 * n], BF),
-    "stepi": ("sbuf", [128, 4], I32), "du": ("sbuf", [128, 64], BF),
-    "dg": ("sbuf", [128, LN], F32), "poff": ("sbuf", [128, 16 * NCH], U16),
-    "og": ("sbuf", [128, LN], F32), "ne": ("sbuf", [128, LN], BF), "off": ("sbuf", [128, 2 * LN], U16),
-    "tt": ("sbuf", [128, LN], BF), "yb": ("sbuf", [128, 9 * n], BF),
-    "selkf": ("sbuf", [128, 128], F32), "eyef": ("sbuf", [128, 128], F32), "cd2": ("sbuf", [128, n], BF), "dg2": ("sbuf", [128, LN], F32),
-    "xoff": ("sbuf", [128, 16 * NCH], U16), "sg": ("sbuf", [128, LN], BF),
-    "rq": ("sbuf", [128, 128 * NCH], BF), "tq": ("sbuf", [128, 128 * NCH], BF),
-    "msq": ("sbuf", [128, LN], BF), "ost": ("sbuf", [128, LN], BF), "wr": ("sbuf", [128, LN], BF),
-    "ht": ("sbuf", [128, LN], BF), "h2": ("sbuf", [128, LN], BF), "mn": ("sbuf", [128, LN], BF),
+    "tab": ("sbuf", [128, 2 * TW], BF), "uu": ("sbuf", [128, 256], BF),
+    "xb": ("sbuf", [128, 2 * NCH * XW], BF), "so": ("sbuf", [128, 32 * LN], F16),
+    "d1b": ("sbuf", [128, 128], BF), "d1": ("sbuf", [128, 32 * LN], F16),
+    "hl": ("sbuf", [128, NCH * HS], F32), "hh": ("sbuf", [128, NCH * HS], F16), "ha": ("sbuf", [128, NCH * HS], BF),
+    "posi": ("sbuf", [128, LN], I32), "ki": ("sbuf", [128, LN], I32), "si": ("sbuf", [128, LN], I32),
+    "dd": ("sbuf", [128, LN], F32), "sq": ("sbuf", [128, LN], F32),
+    "kall": ("sbuf", [128, NR * 2 * LN], BF), "sin": ("sbuf", [128, NCH * SW], BF), "sout": ("sbuf", [128, NCH * SW], BF),
+    "uv": ("sbuf", [128, 32], BF), "stepi": ("sbuf", [128, 4], I32), "du": ("sbuf", [128, 32], BF),
+    "dg": ("sbuf", [128, LN], F32), "poff": ("sbuf", [128, 16 * NCH], U16), "rm": ("sbuf", [128, 14 * n], BF),
+    "og": ("sbuf", [128, LN], F16), "ogs": ("sbuf", [128, 5 * LN], F16), "acc": ("sbuf", [128, 2 * LN], F16),
+    "ne": ("sbuf", [128, LN], BF), "off": ("sbuf", [128, 2 * LN], U16),
+    "yb": ("sbuf", [128, 9 * n], BF), "rq": ("sbuf", [128, 128 * NCH], BF), "tq": ("sbuf", [128, 144 * NCH], BF),
+    "msq": ("sbuf", [128, LN], BF), "ost": ("sbuf", [128, LN], BF), "ht": ("sbuf", [128, LN], BF), "mn": ("sbuf", [128, LN], BF),
     "fm": ("sbuf", [128, 2 * LN], BF), "foff": ("sbuf", [128, 16 * NCH], U16),
     "oyl": ("sbuf", [128, LN], F32), "oya": ("sbuf", [128, 4 * LN], F32), "oyc": ("sbuf", [128, 4 * LN], F32),
-    "ci": ("sbuf", [128, 16], I32), "col": ("sbuf", [128, 64], F32), "thr": ("sbuf", [128, 8], F32), "gm": ("sbuf", [128, 8], F32),
-    "i2t": ("sbuf", [128, 8], F32), "dw": ("sbuf", [128, 160], BF), "c4": ("sbuf", [128, 16], BF), "cd": ("sbuf", [128, n], BF),
-    "cmp": ("sbuf", [128, 8], F32), "wfw": ("sbuf", [128, 144], BF), "ws": ("sbuf", [128, RO * 128], BF),
-    "ogh": ("sbuf", [128, LN], "float16"), "eyeh": ("sbuf", [128, 128], "float16"), "selkh": ("sbuf", [128, 128], "float16"),
-    "tmp": ("sbuf", [128, n], F32), "one": ("sbuf", [128, n], BF),
+    "ci": ("sbuf", [128, 8], I32), "col": ("sbuf", [128, 64], F32), "thr": ("sbuf", [128, 8], F32), "gm": ("sbuf", [128, 8], F32),
+    "gt": ("sbuf", [128, 8], F32), "it": ("sbuf", [128, 8], F32), "cmp": ("sbuf", [128, 8], F32), "wc": ("sbuf", [128, 16], F32),
+    "dw": ("sbuf", [128, 160], BF), "eyew": ("sbuf", [128, 144], BF), "wfw": ("sbuf", [128, 144], BF), "pw": ("sbuf", [128, 130], BF),
+    "c4": ("sbuf", [128, 16], BF), "ws": ("sbuf", [128, RO * 128], BF), "wm": ("sbuf", [128, RO * 128], BF),
+    "eyeh": ("sbuf", [128, 128], F16), "tmp": ("sbuf", [128, n], F32),
 }
-for _m in ("cg", "pw", "tie", "rs", "bmq", "bmh", "eye2", "selk2", "nhalf", "eye", "neye", "selk", "nselk", "wp", "wb", "ee", "ee2", "selk24", "n16", "n24",
-           "dc", "dc2", "eps", "zr", "cp", "cn", "gd"):
+for _m in ("cd", "rs", "one", "bs", "nb", "cb"):
+    SCRATCH[_m] = ("sbuf", [128, n], BF)
+for _m in ("cg", "km", "blk", "bmq", "bmh", "eye2", "selk2", "nhalf", "neye", "nselk", "wp", "wb", "ee", "ee2", "n16", "rt", "eps",
+           "cp", "cn", "gd", "pen", "pa", "pz", "n24", "m16", "neye2"):
     SCRATCH[_m] = ("sbuf", [128, 128], BF)
-for _m in ("uu0", "vv0", "uu1", "vv1", "pen", "pen2"):
-    SCRATCH[_m] = ("sbuf", [128, 144], BF)
 for _b in range(8):
     SCRATCH["pb%d" % _b] = ("psum", [128, 512], F32)
 
-SEMAPHORES = ["sV", "sS", "sP", "sG", "karr", "sent", "outs", "lpos", "lu", "lv", "lstep"] + ["lf%d" % i for i in range(4)] \
-    + ["ar%d_%d" % (t, c) for t in range(1, RO) for c in range(NCH)] + ["tf%d" % i for i in range(4)] \
-    + [x + str(c) for x in ("h0_", "h4_", "mn_") for c in range(NCH)]
+SEMAPHORES = ["sV", "sS", "sP", "sG", "karr", "sarr", "sent", "outs", "lpos", "lu", "lv", "lstep"] + [x + str(i) for x in ("lf", "ld") for i in range(4)] \
+    + ["ar%d_%d" % (t, c) for t in range(1, RO) for c in range(NCH)]
 
 
 def build(p):
     ops = []
     lastw, readers, bank = {}, {}, {}
-    tag, me, cur, count = [None], [0], [None], {}
-    kinds = 1 + p["pair"]
+    tag = [None]
 
-    def kind(eng, nm, rd):
-        if cur[0] is None:
-            return "s" + nm
-        x = "adbbbc"[cur[0][0]] + "".join([ch for ch in nm if ch.isalpha()]).replace("sin", "").replace("sout", "")
-        if eng in ("V", "S", "G"):
-            i = count[me[0], cur[0], x] = count.get((me[0], cur[0], x), -1) + 1
-            x += str(i)
-        elif eng == "P":
-            x += "." + "".join([ch for ch in rd[0][1] + rd[1][1][:3] if ch.isalpha()]).replace("sin", "").replace("sou", "")
-        return x
-
-    def add(eng, fn, r, w, cost, bk=None, sem=None, lat=None, to=None):
+    def add(eng, fn, rd, w, cost, bk=None, sem=None, cnt=0):
         k = len(ops)
         deps = set()
-        at = me[0] if to is None else to
-        nm = (list(w) + [""])[0]
-        r, w = [(me[0], x) for x in r], [(at, x) for x in w]
-        for x in r:
+        for x in rd:
             if x in lastw:
                 deps.add(lastw[x])
         for x in w:
             if x in lastw:
                 deps.add(lastw[x])
             deps.update(readers.get(x, ()))
-        for x in r:
+        for x in rd:
             readers.setdefault(x, []).append(k)
         for x in w:
             lastw[x] = k
             readers[x] = []
         if bk is not None:
-            bk = (at, bk)
             e0, run, prev = bank.get(bk, (None, [], []))
             if e0 == eng:
                 deps.update(prev)
@@ -132,29 +97,30 @@ def build(p):
                 deps.update(run)
                 bank[bk] = (eng, [k], run)
         deps.discard(k)
-        ops.append({"eng": eng and eng + str(at), "fn": fn, "deps": deps, "cost": cost, "sem": sem, "lat": lat, "tag": tag[0],
-                    "w": nm, "core": at, "unit": cur[0], "ty": kind(eng, nm, r)})
-        return k
+        ops.append({"eng": eng, "fn": fn, "deps": deps, "cost": cost, "sem": sem, "cnt": cnt, "tag": tag[0], "w": (list(w) + [""])[0]})
 
-    def ts(out, in0, s1, s2, o0, o1, r, w, m, bk=None):
+    def num(v):
+        return lambda T: v
+
+    def ts(out, in0, s1, s2, o0, o1, rd, w, m, bk=None, kind="c"):
         if o1 is None:
-            add("V", lambda q, T, X: q.tensor_scalar(out(T), in0(T), s1(T), None, o0), r, w, ("c", m), bk)
+            add("V", lambda q, T, X: q.tensor_scalar(out(T), in0(T), s1(T), None, o0), rd, w, (kind, m), bk)
         else:
-            add("V", lambda q, T, X: q.tensor_scalar(out(T), in0(T), s1(T), s2(T), o0, o1), r, w, ("c", m), bk)
+            add("V", lambda q, T, X: q.tensor_scalar(out(T), in0(T), s1(T), s2(T), o0, o1), rd, w, (kind, m), bk)
 
-    def tt(out, a, b, o, r, w, m, bk=None, kind="c"):
-        add("V", lambda q, T, X: q.tensor_tensor(out(T), a(T), b(T), o), r, w, (kind, m), bk)
+    def tt(out, a, b, o, rd, w, m, bk=None, kind="c"):
+        add("V", lambda q, T, X: q.tensor_tensor(out(T), a(T), b(T), o), rd, w, (kind, m), bk)
 
-    def cp(out, a, r, w, m, bk=None, kind="c"):
-        add("V", lambda q, T, X: q.tensor_copy(out(T), a(T)), r, w, (kind, m), bk)
+    def cp(out, a, rd, w, m, bk=None, kind="c"):
+        add("V", lambda q, T, X: q.tensor_copy(out(T), a(T)), rd, w, (kind, m), bk)
 
-    def ms(out, v, w, m, r=()):
-        add("V", lambda q, T, X: q.memset(out(T), v), r, w, ("c", m))
+    def ms(out, v, w, m=64):
+        add("V", lambda q, T, X: q.memset(out(T), v), [], w, ("c", m))
 
-    def scan(out, a, b, o0, o1, r, w, m, bk=None):
-        add("V", lambda q, T, X: q.tensor_tensor_scan(out(T), a(T), b(T), 0.0, o0, o1), r, w, ("c", m), bk)
+    def scan(out, a, b, init, o0, o1, rd, w, m, bk=None):
+        add("V", lambda q, T, X: q.tensor_tensor_scan(out(T), a(T), b(T), init, o0, o1), rd, w, ("c", m), bk)
 
-    def act(out, a, f, r, w, m, bk=None, kind="c", bias=None, scale=None):
+    def act(out, a, f, rd, w, m, bk=None, kind="c", bias=None, scale=None):
         def fn(q, T, X):
             kw = {}
             if bias is not None:
@@ -162,42 +128,44 @@ def build(p):
             if scale is not None:
                 kw["scale"] = scale(T)
             return q.activation(out(T), a(T), f, **kw)
-        add("S", fn, r, w, (kind, m), bk)
+        add("S", fn, rd, w, (kind, m), bk)
 
-    def relu(e, out, a, r, w, m, bk, bias=None):
+    def relu(e, out, a, rd, w, m, bk, bias=None):
         if e == "S":
-            act(out, a, F.Relu, r, w, m, bk, bias=bias)
+            act(out, a, F.Relu, rd, w, m, bk, bias=bias)
         elif bias is None:
-            ts(out, a, num(0.0), None, A.max, None, r, w, m, bk)
+            ts(out, a, num(0.0), None, A.max, None, rd, w, m, bk)
         else:
-            ts(out, a, bias, num(0.0), A.add, A.max, r, w, m, bk)
+            ts(out, a, bias, num(0.0), A.add, A.max, rd, w, m, bk)
 
-    def copy(e, out, a, r, w, m, bk=None, gather=False):
+    def copy(e, out, a, rd, w, m, bk=None, gather=False, neg=False):
         if e == "S":
-            act(out, a, F.Copy, r, w, m, bk, kind="gs" if gather else "c")
+            act(out, a, F.Copy, rd, w, m, bk, kind="gs" if gather else "c", scale=num(-1.0) if neg else None)
+        elif e == "G":
+            add("G", lambda q, T, X: q.affine_select(out(T), a(T), [[0, m]], A.is_ge, 0.0, 0, 0), rd, w, ("ga", m))
+        elif neg:
+            ts(out, a, num(-1.0), None, A.mult, None, rd, w, m, bk, kind="gv" if gather else "c")
         else:
-            cp(out, a, r, w, m, bk, kind="gv" if gather else "c")
+            cp(out, a, rd, w, m, bk, kind="gv" if gather else "c")
 
     def group(out, key, bk, terms, first=True, last=True):
         for i, x in enumerate(terms):
             o, lh, rh, st, sp = x[4] if len(x) > 4 else out, x[0], x[1], first and i == 0, last and i == len(terms) - 1
             add("P", lambda q, T, X, o=o, lh=lh, rh=rh, st=st, sp=sp: q.matmul(o(T), lh(T), rh(T), st, sp), x[2], [key], ("p", x[3]), bk)
 
-    def iota(out, pat, base, cm, w, m, flag=True):
-        if flag:
-            add("G", lambda q, T, X: q.iota(out(T), pat, base, cm, allow_small_or_imprecise_dtypes=True), [], w, ("gi", m))
+    def iota(name, pat, base, cm=0, a=None, b=None, key=None):
+        m = 1
+        for s, c in pat:
+            m *= c
+        if SCRATCH[name][2] == I32:
+            add("G", lambda q, T, X: q.iota(ap(name, a, b)(T), pat, base, cm), [], [name], ("gi", m))
         else:
-            add("G", lambda q, T, X: q.iota(out(T), pat, base, cm), [], w, ("gi", m))
+            add("G", lambda q, T, X: q.iota(ap(name, a, b)(T), pat, base, cm, allow_small_or_imprecise_dtypes=True), [], [key or name], ("gi", m))
 
-    def num(v):
-        return lambda T: v
-
-    def ap(name, a=None, b=None, s=None, p1=None):
+    def ap(name, a=None, b=None, s=None):
         if a is None:
             return lambda T: T[name][:]
-        if p1 is not None:
-            return lambda T: T[name][0:p1, a:b]
-        if s is None:
+        if s is None or s == 1:
             return lambda T: T[name][:, a:b]
         return lambda T: T[name][:, a:b:s]
 
@@ -207,25 +175,15 @@ def build(p):
     def ind(name, a, b, oname, c, d):
         return lambda T: T[name][:, a:b].indirect(T[oname][:, c:d])
 
-    def dma(eng, out, a, r, w, sem, nbytes):
-        add(eng, lambda q, T, X: q.dma_start(out(T), a(T)), r, w, ("d", 0), None, sem, ("dl", nbytes))
+    def dma(eng, out, a, rd, w, sem, nbytes):
+        add(eng, lambda q, T, X: q.dma_start(out(T), a(T)), rd, w, ("d", nbytes), None, sem, 16)
 
-    def send(dst, pieces, rd, wr, sem, cost=("a", 0), mask="all", name=None):
-        d = (dst - me[0]) % NR
+    def lands(after, wr, sem, lat, cnt=1):
+        add(None, None, after, wr, ("a", lat), None, sem, cnt)
 
-        def fn(q, T, X):
-            rid, pid = X["addr"][d][0], X["addr"][d][1]
-            if len(pieces) == 1:
-                b, i, b2, o, w = pieces[0]
-                return q.remote_dma(T[b2][:, o:o + w], T[b][:, i:i + w], T.sem[sem], T.sem["sent"], pid, rid, X[mask])
-            return q.remote_dma_fused([RemoteDMATransfer(dst_ids=[DstId(rid=rid, pnc=pid)], dma_engine_mask=m, remote_sem=T.sem[sem],
-                                                         srcs=[T[b][:, i:i + w]], dsts=[T[b2][:, o:o + w]])
-                                       for (b, i, b2, o, w), m in zip(pieces, X["parts"][len(pieces)])], local_sem=T.sem["sent"])
-        add("G", fn, rd, ["st" + (name or sem)], ("r", 0), None, "sent", mask)
-        add(None, None, ["st" + (name or sem)], wr, cost, None, sem, mask, to=dst % kinds)
-
-    def mat(name, rhs, r, m=n):
-        return (ap(name, 0, 128), rhs, [name] + r, m)
+    def mat(name, rhs, rd, m=n):
+        lh = ap("eyew", 16, 144) if name == "eye" else ap(name, 0, 128)
+        return (lh, rhs, ["eyew" if name == "eye" else name] + rd, m)
 
     names = {}
 
@@ -234,545 +192,477 @@ def build(p):
         return ap("col", j, j + 1)
 
     def cs(name, src, s1, s2, o0, o1=None):
-        r = ["c_" + x for x in (src, s1, s2) if isinstance(x, str)]
+        rd = ["c_" + x for x in (src, s1, s2) if isinstance(x, str)]
         f = [C(x) if isinstance(x, str) else num(x) for x in (src, s1, s2)]
-        ts(C(name), f[0], f[1], f[2], o0, o1, r, ["c_" + name], 64)
-
-    def blk(name, c):
-        r = ["cg", "c_g"] + (["c_" + c] if isinstance(c, str) else [])
-        ts(ap(name), ap("cg"), C("g"), C(c) if isinstance(c, str) else num(c), A.is_equal, A.mult, r, [name], 64)
-
-    def diag(name, v, m=64, at=16, w=128):
-        r = ["dw", "c_p"] + (["c_" + v] if isinstance(v, str) else [])
-        ts(ap(name, 0, w), ap("dw", at, at + w), C("p"), C(v) if isinstance(v, str) else num(v), A.is_equal, A.mult, r, [name], m)
-
-    def marks(name, v, at, w):
-        ms(ap(name), v, [name], 64)
-        ms(ap(name, at, 128, 16), w, [name], 64)
-
-    def fill(e, name, a, b, v, w, half=2):
-        if e == "V":
-            ms(ap(name, a, b), v, w, (b - a) // half)
-        elif e == "S":
-            act(ap(name, a, b), ap("tab", 64, 64 + b - a), F.Identity, ["tab0_0"], w, b - a, bias=num(v), scale=num(0.0))
+        if name in p["e_cs"] and (o0, o1) in ((A.mult, None), (A.add, None), (A.mult, A.add)):
+            act(C(name), f[0], F.Identity, rd, ["c_" + name], 64, scale=f[1] if o0 == A.mult else None,
+                bias=f[1] if o0 == A.add else f[2] if o1 else None)
         else:
-            iota(ap(name, a, b), [[0, b - a]], int(v), 0, w, b - a)
+            ts(C(name), f[0], f[1], f[2], o0, o1, rd, ["c_" + name], 64)
 
-    def weights(w, slot):
-        for i, x in enumerate("uv"):
-            a, b, dst = slot * KW + 2 * LN + 16 * i, 32 * w + 16 * i, "%s%s%d" % (x, x, w)
-            ms(ap("du", b, b + 1), 0.0, [dst + "z"], 64)
-            tt(ap("du", b + 1, b + 16), ap("kall", a, a + 15), ap("kall", a + 1, a + 16), A.subtract, [x + str(slot)], [dst + "d"], 64)
-            if p["q2"]:
-                ms(ap(dst, 128, 144), 0.0, [dst + "_8"], 64)
-            for gi in range(8):
-                act(ap(dst, 16 * gi, 16 * gi + 16), ap("du", b, b + 16), F.Copy, [dst + "z", dst + "d", "gm"], ["%s_%d" % (dst, gi)], 64,
-                    scale=ap("gm", gi, gi + 1))
+    def scaled(name, src, v, at=0):
+        act(ap(name), ap(src, at, at + 128), F.Copy, [src] + (["c_" + v] if isinstance(v, str) else []), [name], 128,
+            scale=C(v) if isinstance(v, str) else num(v))
 
-    negs = []
+    def pay(c, s):
+        return c * SW + 2 * n * s
 
-    def negate(w, engs):
-        for i in range(4):
-            a = w * TW + 2048 * i
-            src, dst, rd, wr = ap("tab", a, a + 2048), ap("tab", 8192 + a, 10240 + a), ["tab%d_%d" % (w, i), "low"], ["neg%d_%d" % (w, i)]
-            if engs[i] == "S":
-                act(dst, src, F.Copy, rd, wr, 2048, scale=num(-1.0))
-            else:
-                for b in range(a, a + 2048, 512):
-                    ts(ap("tab", 8192 + b, 8704 + b), ap("tab", b, b + 512), num(-1.0), None, A.mult, None, rd, ["ng%d" % b], 256)
-                    negs.append("ng%d" % b)
-
-    def setup(r):
-        dma("Y", ap("posi"), ap("pos"), [], ["posi"], "lpos", 131072)
-        for i, (a, b) in enumerate(p["lp"]):
-            dma("Y", ap("tab", 2048 * a, 2048 * b), ap("feat", 2048 * a, 2048 * b), [], ["tab0_%d" % j for j in range(a, b)], "lf%d" % i,
-                131072 + 524288 * b + 100000 * (i + 2))
-        dma("S", ap("kall", 2 * LN, 2 * LN + 16), ap("u"), [], ["u0"], "lu", 4096)
-        dma("S", ap("kall", 2 * LN + 16, 2 * LN + 32), ap("v"), [], ["v0"], "lv", 4096)
-        iota(ap("ci", 0, 1), [[0, 1]], 0, 1, ["ci0"], 1, False)
-        iota(ap("dw"), [[1, 160]], -16, 0, ["dw"], 160)
-        iota(ap("cg"), [[1, 8], [0, 16]], 0, 0, ["cg"], 128)
-        iota(ap("i2t"), [[2, 8]], 0, 0, ["i2t"], 8)
-        iota(ap("tie"), [[0, 8], [-2, 16]], 15, 0, ["tie"], 128)
-        iota(ap("pw"), [[1, 64], [0, 2]], 0, 0, ["pw"], 128)
-        iota(ap("c4"), [[4, 16]], 0, 0, ["c4"], 16)
-        dma("S", ap("stepi", 0, 1), ap("step"), [], ["stepi"], "lstep", 512)
-
-        C("p")
-        for j, (nm, op, v) in enumerate((("k", A.bitwise_and, 15), ("g", A.arith_shift_right, 4), ("odd", A.bitwise_and, 1),
-                                         ("ph", A.arith_shift_right, 1))):
-            C(nm)
-            ts(ap("ci", j + 1, j + 2), ap("ci", 0, 1), num(v), None, op, None, ["ci0"], ["ci%d" % (j + 1)], 64)
-        cp(ap("col", 0, 5), ap("ci", 0, 5), ["ci%d" % j for j in range(5)], ["c_p", "c_k", "c_g", "c_odd", "c_ph"], 64)
-        cs("king", "k", 0.0, None, A.is_equal)
-        cs("ab", "k", 13.0, 2048.0, A.is_ge, A.mult)
-        cs("big12", "k", 12.0, 1.0e6, A.is_le, A.mult)
-        cs("o32", "odd", 32.0, None, A.mult)
-        cs("b0", "k", -12.0, 32.0, A.add, A.mult)
-        cs("base", "b0", "o32", None, A.max)
-        ts(ap("gm"), ap("i2t"), C("k"), C("big12"), A.is_le, A.mult, ["i2t", "c_k", "c_big12"], ["gm"], 64)
-        ts(ap("thr"), ap("gm"), C("base"), num(128.0), A.add, A.add, ["gm", "c_base"], ["thr"], 64)
-        ts(ap("gm"), ap("dw", 16, 24), C("g"), None, A.is_equal, None, ["dw", "c_g"], ["gm"], 64)
-        diag("eye", 1.0)
-        diag("eye2", 2.0)
-        blk("selk", "king")
-        cs("king2", "king", 2.0, None, A.mult)
-        blk("selk2", "king2")
-        blk("wb", "ab")
-        ts(ap("ki"), ap("posi"), num(1920), None, A.bitwise_and, None, ["posi"], ["ki"], 256)
-        ts(ap("si"), ap("posi"), num(127), None, A.bitwise_and, None, ["posi"], ["si"], 256)
-        ts(ap("dd"), ap("posi"), num(0.0), num(GONE), A.is_equal, A.mult, ["posi"], ["dd"], 256)
-        ts(ap("kall", 0, LN), ap("ki"), num(-128.0), None, A.add, None, ["ki"], ["kall0"], 256)
-        ts(ap("og"), ap("si"), num(0.5), num(64.0), A.mult, A.add, ["si"], ["og%d" % j for j in range(NCH)], 256)
-        tt(ap("kall", LN, 2 * LN), ap("og"), ap("dd"), A.add, ["og0", "og1", "og2", "og3", "dd"], ["sall0"], 512)
-        ms(ap("zr"), 0.0, ["zr"], 64)
-        cp(C("step"), ap("stepi", 0, 1), ["stepi"], ["c_step"], 64)
-        ts(ap("kall", 2 * LN + 32, KW), ap("zr", 0, 16), C("step"), num(128.0), A.add, A.add, ["zr", "c_step"], ["step0"], 64)
-
-        def sendk(q, T, X):
-            kw = KW if p["pair"] else 2 * LN
-            tr = RemoteDMATransfer(dst_ids=[DstId(rid=X["addr"][j][0], pnc=X["addr"][j][1]) for j in range(1, NR)],
-                                   dma_engine_mask=X["mask"], remote_sem=T.sem["karr"], srcs=[T["kall"][:, 0:kw]],
-                                   dsts=[T["kall"][:, j * KW:j * KW + kw] for j in range(1, NR)])
-            return q.remote_dma_fused([tr], local_sem=T.sem["sent"])
-        add("G", sendk, ["kall0", "sall0"] + ["tab0_%d" % i for i in range(4 * p["klate"])] + (["u0", "v0", "step0"] if p["pair"] else []), ["ksent"], ("r", 0), None, "sent")
-        add(None, None, ["ksent"], [x + str(j) for x in ("kall", "sall", "u", "v", "step") for j in range(1, NR)], ("a", 1), None, "karr",
-            to=(r + 1) % kinds)
-        if p["pair"] and not p["nship"]:
-            for i in range(4):
-                send(r ^ 1, [("tab", 2048 * i, "tab", TW + 2048 * i, 2048)],
-                     ["tab0_%d" % j for j in (range(4) if p["tlate"] else [i])] + ["sttf%d" % (i - 1)],
-                     ["tab1_%d" % i], "tf%d" % i, ("b", 524288 * (i + 1)))
-
-        marks("rs", 0.0, 0, -2.0 ** 30)
-        fill(p["e_f0"], "yb", 0, 9 * n, 0.0, ["yb%d" % c for c in range(NCH)])
-        for par in range(p["nd1"]):
-            for i in range(4):
-                fill(p["e_f1"] if i < 2 else p["e_f2"], "d1", (32 * par + 8 * i) * n, (32 * par + 8 * i + 8) * n, -OFS, ["d1f%d_%d" % (par, i)])
-        weights(0, 0)
-        diag("pen", -2.0 ** -71, 72, 16, 144)
-        diag("pen2", 2.0 ** -71, 72, 15, 144)
-        tt(ap("pen"), ap("pen"), ap("pen2"), A.add, ["pen", "pen2"], ["pen"], 288)
-        marks("dc", 1.0 / 16, 0, -2.0 ** 22)
-        if p["q2"]:
-            marks("dc2", 1.0 / 16, 15, 2.0 ** 22)
-        else:
-            marks("eps", -2.0 ** -9, 0, 2.0 ** 30)
-        diag("ee", -BIG)
-        diag("ee2", BIG / 2)
-        diag("neye", -1.0)
-        diag("nhalf", -0.5)
-        cs("nking", "king", -1.0, None, A.mult)
-        blk("nselk", "nking")
-        cs("sg", "odd", -2.0, 1.0, A.mult, A.add)
-        cs("kt", "k", -2.0, 15.0, A.mult, A.add)
-        blk("bmq", -0.25)
-        blk("bmh", 0.5)
-        ms(ap("one"), 1.0, ["one"], 64)
-        ms(ap("cp"), 1.5 * 2.0 ** 22, ["cp"], 64)
-        ms(ap("cn"), -1.5 * 2.0 ** 22, ["cn"], 64)
-        cs("gone", "k", 1.0, GONE, A.is_ge, A.mult)
-        diag("gd", "gone")
-        if p["x00"]:
-            ms(ap("tab", 16, 32), -1024.0, ["low"], 64, ["tab0_0"])
-            cs("rest", "k", 1.0, None, A.is_ge)
-            cs("k1", "king", 16.0, None, A.mult)
-        if p["x0"]:
-            cs("k16", "king", 16384.0, None, A.mult)
-            blk("selkh" if p["ogh"] else "selkf", "king")
-            cs("k24", "king", 24576.0, None, A.mult)
-            blk("selk24", "k24")
-            ts(ap("cd2"), ap("tie", 0, n), C("kt"), num(-131072.0), A.not_equal, A.mult, ["tie", "c_kt"], ["cd2"], 64)
-            for w in range(1 + (p["pair"] and not p["nship"])):
-                ms(ap("tab", w * TW + 16384, w * TW + TW), -1024.0, ["tabx%d" % w], 64)
-
-        negate(0, p["neg"])
-        if p["pair"] and p["nship"]:
-            send(r ^ 1, [("tab", 0, "tab", TW, 8192)], ["tab0_%d" % j for j in range(4)], ["tab1_%d" % j for j in range(4)], "tf0",
-                 ("b", 2 * 2097152), "low")
-            send(r ^ 1, [("tab", 8192, "tab", TW + 8192, TW - 8192)], ["neg0_%d" % j for j in range(4)] + ["tabx0", "sttf0"],
-                 ["neg1_%d" % j for j in range(4)] + ["tabx1"], "tf1", ("b", 3 * 2097152), "low")
-        for u in range(NU if p["pair"] else NCH):
-            fill(p["e_f3"], "hl", u * HS, u * HS + n, 0.0, ["hl%d_0" % u], 1)
-            fill(p["e_f3"], "ha", u * HS, u * HS + n, -OFS, ["ha%d_0" % u], 1)
-        cs("le12", "k", 12.0, "sg", A.is_le, A.mult)
-        cs("s1", "k", "odd", 0.5 * n, A.subtract, A.mult)
-        cs("af", "s1", float(n), None, A.add)
-        cs("apx", "af", "le12", None, A.mult)
-        cs("ath", "ab", -1.0 / 64, None, A.mult)
-        cs("aw", "le12", -256.0, "ath", A.mult, A.add)
-        cs("th2", "ab", 1.0 / 4096, None, A.mult)
-        cs("q0", "g", 8.0, "ph", A.mult, A.subtract)
-        cs("q1", "q0", "th2", 2.0, A.mult, A.mult)
-        cs("q2", "q1", "ph", None, A.add)
-        ts(ap("cmp"), ap("i2t"), C("th2"), C("q2"), A.mult, A.add, ["i2t", "c_th2", "c_q2"], ["cmp"], 64)
-        blk("wp", "apx")
-        for s in range(RO):
-            ts(ap("ws", 128 * s, 128 * s + 128), ap("pw"), ap("cmp", s, s + 1), C("aw"), A.is_equal, A.mult, ["pw", "cmp", "c_aw"],
-               ["ws%d" % s], 64)
-        ts(ap("tmp"), ap("tie", 0, n), C("kt"), num(DEAD), A.not_equal, A.mult, ["tie", "c_kt"], ["tmp5"], 64)
-        tt(ap("cd"), ap("tmp"), ap("dw", 16, 16 + n), A.add, ["tmp5", "dw"], ["cd"], 128)
-        diag("eyeh" if p["ogh"] else "eyef", 1.0, 128)
-        diag("n16", 16384.0)
-        diag("n24", 24576.0)
-        cs("g16o", "g", 16.0, "odd", A.mult, A.add)
-        cs("ge12", "k", 12.0, 1.0e6, A.is_ge, A.mult)
-        cs("cf0", "ge12", "o32", None, A.subtract)
-        cs("cf1", "cf0", -64.0, None, A.add)
-        ts(ap("ci", 6, 7), ap("ci", 1, 2), num(2), None, A.arith_shift_right, None, ["ci1"], ["ci8"], 64)
-        cp(C("rf"), ap("ci", 6, 7), ["ci8"], ["c_rf"], 64)
-        ts(ap("wfw"), ap("dw", 0, 144), C("g16o"), C("af"), A.is_equal, A.mult, ["dw", "c_g16o", "c_af"], ["wfw"], 72)
-
-    nc = n // 16
-
-    t1 = p["t1"]
-
-    def away(q, c):
-        return (q - q % 2 + (c // 2 ^ p["hf"])) % NR if p["pair"] else q % NR
-
-    def proc(q, c, t):
-        return away(q, c) if t1 <= t < RO - 1 else q % NR
-
-    def unit(r, q, c):
-        return c if q % NR == r % NR else NCH + c % 2
-
-    slots = {}
-    for t in range(RO):
-        for r in range(NR):
-            here = [(q, c) for c in range(NCH) for q in range(NR) if proc(q, c, t) == r]
-            for q, c in here:
-                if t and proc(q - 1, c, t - 1) == r:
-                    slots[t, q, c] = slots[t - 1, (q - 1) % NR, c]
-            left = [j for j in range(NCH) if j not in [slots.get((t, q, c)) for q, c in here]]
-            for q, c in here:
-                if (t, q, c) not in slots:
-                    slots[t, q, c] = left.pop(0)
-
-    def pay(buf, u, s):
-        return (u * RO + s) * 2 * n
-
-    def flags(buf, u, s):
-        o = pay(buf, u, s) + n
-        return ap(buf, o, o + n), "%sM%d_%d" % (buf, u, s)
-
-    def nextflags(r, q, c, s):
-        if proc(q + 1, c, s) == r:
-            return flags("sin", unit(r, q + 1, c), s)
-        return flags("sout", unit(r, q, c), s)
+    def flags(buf, c, s):
+        o = pay(c, s) + n
+        return ap(buf, o, o + n), "%sM%d_%d" % (buf, c, s)
 
     def struck(fl):
         return [(ap("ws", 128 * s, 128 * s + 128), x[0], ["ws%d" % s, x[1]], n) for s, x in enumerate(fl)]
 
-    def partner(r):
-        sl = (r - (r ^ 1)) % NR
-        weights(1, sl)
-        if not p["nship"]:
-            negate(1, p["neg2"])
+    def flag(out, z, t, rd, w, bk):
+        if p["sgn"]:
+            act(out, z, F.Sign, rd + ["thr"], w, n, bk, bias=ap("thr", t, t + 1))
+        else:
+            ts(out, z, ap("thr", t, t + 1), None, A.is_ge, None, rd + ["thr"], w, n, bk)
+
+    hf = 0.5 if p["sgn"] else 1.0
+    TAB = ["tab%d" % i for i in range(4)]
+    NEG = ["neg%d" % a for a in range(0, TW, p["negw"])]
+
+    def setup():
+        dma("Y", ap("posi"), ap("pos"), [], ["posi"], "lpos", 131072)
+        for i, (a, b) in enumerate(zip((0,) + p["lp"], p["lp"])):
+            dma("Y", ap("tab", 2048 * a, 2048 * b), ap("feat", 2048 * a, 2048 * b), [], TAB[a:b], "lf%d" % i, 131072 + 524288 * b)
+        dma("S", ap("uv", 0, 16), ap("u"), [], ["u"], "lu", 4096)
+        dma("S", ap("uv", 16, 32), ap("v"), [], ["v"], "lv", 4096)
+        dma("S", ap("stepi", 0, 1), ap("step"), [], ["stepi"], "lstep", 512)
+        iota("ci", [[1, 2]], 0, 1, 0, 2)
+        iota("dw", [[1, 160]], -16)
+        iota("cg", [[1, 8], [0, 16]], 0)
+        iota("it", [[1, 8]], 0)
+        iota("km", [[0, 8], [1, 16]], 0)
+        iota("pw", [[1, 65], [0, 2]], 0)
+        iota("d1b", [[512, 8], [0, 16]], -2048)
+        iota("nb", [[0, 8], [-512, 8]], 2048)
+        iota("bs", [[0, 8], [512, 8]], -2048)
+        iota("cb", [[0, 8], [512, 8]], -2048 + int(OFS))
+        iota("c4", [[4, 16]], 0)
+        iota("yb", [[0, 9 * n]], 0)
+
+        for x in ("p", "p1"):
+            C(x)
+        for j, (nm, src, op, v) in enumerate((("k", 0, A.bitwise_and, 15), ("g", 0, A.arith_shift_right, 4), ("od", 1, A.bitwise_and, 1),
+                                              ("ph", 1, A.arith_shift_right, 1), ("rf", 2, A.arith_shift_right, 2))):
+            C(nm)
+            ts(ap("ci", j + 2, j + 3), ap("ci", src, src + 1), num(v), None, op, None, ["ci", "ci%d" % src], ["ci%d" % (j + 2)], 64)
+        cp(ap("col", 0, 7), ap("ci", 0, 7), ["ci"] + ["ci%d" % j for j in range(2, 7)], ["c_" + x for x in names], 64)
+        ts(ap("eyew"), ap("dw", 0, 144), C("p"), None, A.is_equal, None, ["dw", "c_p"], ["eyew"], 72)
+        ts(ap("blk"), ap("cg"), C("g"), None, A.is_equal, None, ["cg", "c_g"], ["blk"], 64)
+        ts(ap("gm"), ap("dw", 16, 24), C("g"), None, A.is_equal, None, ["dw", "c_g"], ["gm"], 64)
+        cs("king", "k", 0.0, None, A.is_equal)
+        cs("top", "k", 13.0, None, A.is_ge)
+        cs("m1", "top", -1.0, 1.0, A.mult, A.add)
+        cs("mid", "m1", "king", None, A.subtract)
+        cs("s1", "g", -8.0, "ph", A.mult, A.add)
+        cs("o32", "od", 32.0, None, A.mult)
+        cs("b0", "k", -12.0, 32.0, A.add, A.mult)
+        cs("b1", "b0", "o32", 128.0, A.max, A.add)
+        cs("b2", "king", -1.0e6, "b1", A.mult, A.add)
+        cs("big", "mid", 1.0e6, None, A.mult)
+        ts(ap("gt"), ap("it"), C("s1"), C("big"), A.is_lt, A.mult, ["it", "c_s1", "c_big"], ["gt"], 64)
+        if p["sgn"]:
+            cs("b3", "b2", -1.0, 0.5, A.mult, A.add)
+            ts(ap("thr"), ap("gt"), num(-1.0), C("b3"), A.mult, A.add, ["gt", "c_b3"], ["thr"], 64)
+        else:
+            ts(ap("thr"), ap("gt"), C("b2"), None, A.add, None, ["gt", "c_b2"], ["thr"], 64)
+        cs("top0", "king", 3.0 * p["sgn"], "top", A.mult, A.add)
+        scaled("eye2", "eyew", 2.0, 16)
+        cs("king2", "king", 2.0, None, A.mult)
+        scaled("selk2", "blk", "king2")
+        cs("ab", "top0", 2048.0 * hf, None, A.mult)
+        scaled("wb", "blk", "ab")
+
+        ts(ap("ki"), ap("posi"), num(1920), None, A.bitwise_and, None, ["posi"], ["ki"], 256)
+        ts(ap("si"), ap("posi"), num(127), None, A.bitwise_and, None, ["posi"], ["si"], 256)
+        ts(ap("dd"), ap("posi"), num(0.0), num(GONE), A.is_equal, A.mult, ["posi"], ["dd"], 256)
+        ts(ap("sq"), ap("si"), num(0.5), num(64.0), A.mult, A.add, ["si"], ["sq"], 256)
+        ts(ap("kall", 0, LN), ap("ki"), num(-128.0), None, A.add, None, ["ki"], ["kall0"], 256)
         for c in range(NCH):
-            if away(r ^ 1, c) == r and t1 == 1:
-                u, j = unit(r, r ^ 1, c), slots[1, r ^ 1, c]
-                a = sl * KW + c * n
-                group(ap("pb%d" % (2 * j), 448, 448 + n), "l0%d" % j, 2 * j,
-                      [mat("eye", ap("kall", a, a + n), ["kall%d" % sl]), mat("eye", ap("kall", LN + a, LN + a + n), ["sall%d" % sl])])
-                relu("S", ap("hl", u * HS + n, u * HS + 2 * n), ap("pb%d" % (2 * j), 448, 448 + n), ["l0%d" % j], ["hl%d_1" % u], n, 2 * j)
+            S0 = ap("sin", pay(c, 0), pay(c, 0) + n)
+            tt(S0, ap("sq", c * n, c * n + n), ap("dd", c * n, c * n + n), A.add, ["sq", "dd"], ["sinS%d_0" % c], 2 * n)
+            copy("S", ap("kall", LN + c * n, LN + c * n + n), S0, ["sinS%d_0" % c], ["sall%d" % c], n)
 
-    uses = {}
+        kw = LN if p["sfirst"] else 2 * LN
+        sall = ["sall%d" % c for c in range(NCH)]
+        if p["sfirst"]:
+            add("G", lambda q, T, X: q.remote_dma(T["kall"][:, 7 * LN:8 * LN], T["kall"][:, LN:2 * LN], T.sem["sarr"], T.sem["sent"], X["addr"][3][1],
+                                                  X["addr"][3][0], X["mask"]), sall, ["ssent"], ("r", 0), None, "sent")
+            lands(["ssent"], ["snext"], "sarr", p["klat"])
 
-    def ply(t, r, q, c):
-        u, j, tw = unit(r, q, c), slots[t, q, c], int(q % NR != r)
-        ba, bb = 2 * j, 2 * j + 1
+        def sendk(q, T, X):
+            tr = RemoteDMATransfer(dst_ids=[DstId(rid=X["addr"][j][0], pnc=X["addr"][j][1]) for j in range(1, NR)],
+                                   dma_engine_mask=X["mask"], remote_sem=T.sem["karr"], srcs=[T["kall"][:, 0:kw]],
+                                   dsts=[T["kall"][:, j * 2 * LN:j * 2 * LN + kw] for j in range(1, NR)])
+            return q.remote_dma_fused([tr], local_sem=T.sem["sent"])
+        add("G", sendk, ["kall0", "ssent"] + sall + TAB[:p["klate"]], ["ksent"], ("r", 0), None, "sent")
+        lands(["ksent"], ["kall%d" % j for j in range(1, NR)] + ["snext"] * (1 - p["sfirst"]), "karr", p["klat"] * (1 - 0.8 * p["sfirst"]), NR - 1)
+
+        ms(ap("du", 0, 32, 16), 0.0, ["duz"])
+        for i, x in enumerate("uv"):
+            tt(ap("du", 16 * i + 1, 16 * i + 16), ap("uv", 16 * i, 16 * i + 15), ap("uv", 16 * i + 1, 16 * i + 16), A.subtract, [x], ["du" + x], 64)
+            for gi in range(8):
+                o = 128 * i + 16 * gi
+                act(ap("uu", o, o + 16), ap("du", 16 * i, 16 * i + 16), F.Copy, ["duz", "du" + x, "gm"], ["uu%d" % (8 * i + gi)], 64,
+                    scale=ap("gm", gi, gi + 1))
+        ms(ap("xb", 15, 2 * NCH * XW, 2 * XW if p["one"] else XW), 0.0, ["xp"])
+        ms(ap("tq", 128, NCH * 144, 144), 0.0, ["tqp"])
+        cs("pk", "king", -2.0 ** 22, -2.0 ** -71, A.mult, A.add)
+        scaled("pa", "eyew", "pk", 16)
+        scaled("pz", "eyew", 2.0 ** -71, 15)
+        tt(ap("pen"), ap("pa"), ap("pz"), A.add, ["pa", "pz"], ["pen"], 256)
+        scaled("rt", "km", -1.0 / 16)
+        ms(ap("eps"), 1.0 / 16, ["eps"])
+        ms(ap("eps", 15, 128, 16), -14.0 / 16, ["eps"])
+        scaled("ee", "eyew", -LOST, 16)
+        scaled("ee2", "eyew", LOST, 16)
+        cs("b15", "k", 15.0, -LOST * 15 / 16, A.is_equal, A.mult)
+        cp(C("step"), ap("stepi", 0, 1), ["stepi"], ["c_step"], 64)
+        cs("st", "step", "b15", 128.0, A.add, A.add)
+        scaled("nhalf", "eyew", -0.5, 16)
+        cs("nking", "king", -1.0, None, A.mult)
+        scaled("nselk", "blk", "nking")
+        scaled("bmq", "blk", -0.25)
+        scaled("bmh", "blk", 0.5)
+        ms(ap("one"), 1.0, ["one"])
+        ms(ap("cp"), 1.5 * 2.0 ** 22, ["cp"])
+        scaled("cn", "cp", -1.0)
+        cs("gone", "k", 1.0, GONE, A.is_ge, A.mult)
+        scaled("gd", "eyew", "gone", 16)
+        cp(ap("eyeh"), ap("eyew", 16, 144), ["eyew"], ["eyeh"], 64)
+
+        for i in range(p["nd"]):
+            o, x = i * 32 * n, ["d1o%d" % i, "d1n%d" % i]
+            if p["e_d1"][i] == "D":
+                dma("Y", ap("d1", o, o + 32 * n), ap("d1", 0, 32 * n), ["d1o0", "d1n0"] + TAB, x, "ld%d" % i, 524288)
+            else:
+                for h in range(2):
+                    iota("d1", [[0, 4], [512, 8], [0, 32]] if p["one"] else [[0, 8], [512, 8], [0, 16]], -2048, 0, o + 16 * n * h, o + 16 * n * (h + 1),
+                         x[h])
+        if p["one"]:
+            for a in range(0, TW, p["negw"]):
+                e = p["neg"][a // 2048]
+                copy(e, ap("tab", TW + a, TW + a + p["negw"]), ap("tab", a, a + p["negw"]), [TAB[a // 2048]], ["neg%d" % a],
+                     p["negw"] // (2 if e == "V" else 1), neg=True)
+        for c in range(NCH):
+            act(ap("hl", c * HS, c * HS + n), ap("bs"), F.Copy, ["bs"], ["hl%d_0" % c], n, scale=num(0.0))
+            act(ap("ha", c * HS, c * HS + n), ap("bs"), F.Identity, ["bs"], ["ha%d_0" % c], n, scale=num(0.0), bias=num(-OFS))
+        cs("sg", "od", -2.0, 1.0, A.mult, A.add)
+        cs("sgm", "sg", "mid", None, A.mult)
+        cs("sgh", "sgm", hf, None, A.mult)
+        cs("m2", "mid", -1.0, 1.0, A.mult, A.add)
+        cs("af", "s1", float(n), None, A.mult)
+        cs("apx", "af", "sgm", hf, A.mult, A.mult)
+        cs("t32", "top0", -32.0 * hf, None, A.mult)
+        cs("aw", "sgm", -256.0 * hf, "t32", A.mult, A.add)
+        cs("q0", "s1", -1.0, 1.0, A.mult, A.add)
+        cs("q2", "q0", "m2", "ph", A.mult, A.add)
+        ts(ap("cmp"), ap("it"), C("m2"), C("q2"), A.mult, A.add, ["it", "c_m2", "c_q2"], ["cmp"], 64)
+        scaled("wp", "blk", "apx")
+        for s in range(RO):
+            ts(ap("ws", 128 * s, 128 * s + 128), ap("pw", 1, 129), ap("cmp", s, s + 1), C("aw"), A.is_equal, A.mult, ["pw", "cmp", "c_aw"],
+               ["ws%d" % s], 64)
+        cs("s0", "s1", -1.0, None, A.add)
+        ts(ap("wc", 0, 8), ap("it"), C("s0"), C("sgh"), A.is_equal, A.mult, ["it", "c_s0", "c_sgh"], ["wc0"], 64)
+        ts(ap("wc", 8, 16), ap("wc", 0, 8), C("king"), num(-DEAD), A.subtract, A.mult, ["wc0", "c_king"], ["wc"], 64)
+        for s in range(max(p["sel"], p["sela"])):
+            act(ap("wm", 128 * s, 128 * s + 128), ap("blk"), F.Copy, ["blk", "wc"], ["wm%d" % s], 128, scale=ap("wc", 8 + s, 9 + s))
+        for t in range(2, p["sel"] + 1):
+            ms(ap("rm", RM[t], RM[t] + t * n), 1.0, ["rm%d" % t], t * n // 2)
+            ms(ap("rm", RM[t], RM[t] + t * n, t), 0.0, ["rm%d" % t])
+        ms(ap("rs"), 0.0, ["rs"])
+        ms(ap("rs", 0, n, 16), -2.0 ** 30, ["rs"])
+        ts(ap("tmp"), ap("km", 0, n), C("k"), num(DEAD), A.not_equal, A.mult, ["km", "c_k"], ["tmp"], 64)
+        tt(ap("cd"), ap("tmp"), ap("dw", 16, 16 + n), A.add, ["tmp", "dw"], ["cd"], 128)
+        scaled("n16", "eyew", -DEAD, 16)
+        scaled("neye", "eyew", -1.0, 16)
+        if p["jp"] == 2:
+            scaled("n24", "eyew", TW - DEAD, 16)
+        if p["eq1"]:
+            scaled("m16", "eyew", DEAD, 16)
+            scaled("neye2", "eyew", -2.0, 16)
+        cs("g16o", "g", 16.0, "od", A.mult, A.add)
+        cs("c0", "big", -1.0, 1.0e6, A.mult, A.add)
+        cs("cf0", "c0", "o32", None, A.subtract)
+        cs("cf1", "cf0", -64.0, None, A.add)
+        ts(ap("wfw"), ap("dw", 0, 144), C("g16o"), C("af"), A.is_equal, A.mult, ["dw", "c_g16o", "c_af"], ["wfw"], 72)
+
+    nc = n // 16
+    uses = [0]
+
+    def ply(t, c):
+        ba, bb = 2 * c, 2 * c + 1
         pa, pb = "pb%d" % ba, "pb%d" % bb
-        cn, h0, t0 = j * n, u * HS, tw * TW
-        par = uses.get(r, 0) % p["nd1"]
-        uses[r] = uses.get(r, 0) + 1
-        o = pay("sin", u, t)
-        S, sk = (ap("sin", o, o + n), "sinS%d_%d" % (u, t)) if t else (ap("kall", LN + c * n, LN + c * n + n), "sall0")
-        ks, ws_ = (r - q + t) % NR, (r - q) % NR
-        K, kk = ap("kall", ks * KW + c * n, ks * KW + c * n + n), "kall%d" % ks
-        step = ap("kall", ws_ * KW + 2 * LN + 32, ws_ * KW + 2 * LN + 33)
-        M, mk = flags("sin", u, t)
-        TAB = ["tab%d_%d" % (tw, i) for i in range(4)]
-        NEG = ["neg%d_%d" % (tw, i) for i in range(4)] + negs
+        cn, h0 = c * n, c * HS
+        o = pay(c, t)
+        S, sk = ap("sin", o, o + n), "sinS%d_%d" % (c, t)
+        M, mk = flags("sin", c, t)
+
+        def kinds(s):
+            a = s % NR * 2 * LN + cn
+            return ap("kall", a, a + n), "kall%d" % (s % NR)
+        K, kk = kinds(t)
 
         def k(x):
-            return "%s%d" % (x, j)
+            return "%s%d" % (x, c)
 
-        def loc(name, w=1):
-            return ap(name, w * cn, w * cn + w * n)
+        def loc(name):
+            return ap(name, cn, cn + n)
 
         def on(name, x):
             return mat(name, loc(x), [k(x)])
-        HL = ["hl%d_%d" % (u, s) for s in range(t + 1)]
-        HA = ["ha%d_%d" % (u, s) for s in range(t + 1)]
-        Lh, lk = ap("hl", h0 + (t + 1) * n, h0 + (t + 2) * n), "hl%d_%d" % (u, t + 1)
+        HL = ["hl%d_%d" % (c, s) for s in range(t + 1)]
+        HA = ["ha%d_%d" % (c, s) for s in range(t + 1)]
+        Lh, lk = ap("hl", h0 + (t + 1) * n, h0 + (t + 2) * n), "hl%d_%d" % (c, t + 1)
         KS = [mat("eye", K, [kk]), mat("eye2", S, [sk])]
         if t <= p["m1r"]:
-            group(ap(pa, 384, 384 + n), k("z0"), ba, struck([flags("sin", u, s) for s in range(t)]) + [mat("selk2", S, [sk])])
-            ts(M, ap(pa, 384, 384 + n), ap("thr", t, t + 1), None, A.is_ge, None, [k("z0"), "thr"], [mk], n, ba)
-        group(ap(pb, 0, n), k("L"), bb, KS)
-        relu(p["e_lh"], Lh, ap(pb, 0, n), [k("L")], [lk], n, bb)
-        st = 32 if t else 16
-        x0 = 32 * cn
-        if t:
-            group(ap(pa, 0, n), k("pt"), ba, [mat("eye", ap("cd"), ["cd"]), mat("wp", M, [mk])])
-            scan(loc("dg"), ap("rs", 0, n), ap(pa, 0, n), A.add, A.max, ["rs", k("pt")], [k("dg")], n, ba)
-            cp(ap("poff", 16 * j, 16 * j + nc), ap("dg", cn + 15, cn + n, 16), [k("dg")], [k("poff")], 64)
-            src = ind("hl", h0, h0 + (t + 1) * n, "poff", 16 * j, 16 * j + nc)
-            og, om = (loc("ogh"), n) if p["ogh"] else (loc("og"), 4 * n)
-            sfx = "h" if p["ogh"] else "f"
-            copy(p["e_og"], og, src, HL + [k("poff")], [k("og")], n, gather=True)
-            if p["nep"]:
-                tt(loc("ne"), og, ap(pb, 0, n), A.not_equal, [k("og"), k("L")], [k("ne")], n, bb)
-            else:
-                tt(loc("ne"), src, Lh, A.not_equal, HL + [k("poff"), lk], [k("ne")], n, kind="gv")
-            group(ap(pa, n, 2 * n), k("pl"), ba, KS + [mat("wb", M, [mk]), on("n16", "ne")])
-            group(ap(pb, n, 2 * n), k("po"), bb, [mat("wb", M, [mk]), mat("eye" + sfx, og, [k("og")], om), on("n24", "ne")])
-            xterms = [mat("eye", ap("cd2"), ["cd2"]), mat("wb", M, [mk]), mat("selk" + sfx, og, [k("og")], om), on("selk24", "ne")]
-            px, bx = (pa, ba) if p["xka"] else (pb, bb)
-            if p["x0"] and not p["xka"]:
-                group(ap(px, 256, 256 + n), k("xk"), bx, xterms)
-            ts(ap("off", 2 * cn + 1, 2 * cn + 2 * n, 2), ap(pa, n, 2 * n), num(DEAD), num(0.0), A.add, A.max, [k("pl")], [k("offl")], n, ba)
-            if p["x0"] and p["xka"]:
-                group(ap(px, 256, 256 + n), k("xk"), bx, xterms)
-            vc = p.get("vc%d" % t, p["vcols"])
-            ncol, sp, win, wk = 2 * n, p["spieces"], 16384, TAB + NEG
-            if p["x0"]:
-                ts(ap("off", 2 * cn, 2 * cn + 2 * n, 2), ap(pb, n, 2 * n), num(DEAD), C("k16"), A.add, A.max, [k("po"), "c_k16"], [k("offo")], n, bb)
-                scan(loc("dg2"), ap("rs", 0, n), ap(px, 256, 256 + n), A.add, A.max, ["rs", k("xk")], [k("dgx")], n, bx)
-                ts(ap("xoff", 16 * j, 16 * j + nc), ap("dg2", cn + 15, cn + n, 16), num(DEAD), num(0.0), A.add, A.max, [k("dgx")], [k("xoff")], 64)
-                copy(p["e_sg"], loc("sg"), ind("ha", h0, h0 + (t + 1) * n, "poff", 16 * j, 16 * j + nc), HA + [k("poff")], [k("sg")], n, gather=True)
-                win, wk = TW, wk + ["tabx%d" % tw]
-            else:
-                ts(ap("off", 2 * cn, 2 * cn + 2 * n, 2), ap(pb, n, 2 * n), num(DEAD), num(0.0), A.add, A.max, [k("po")], [k("offo")], n, bb)
+            z = ap(pa, 384, 384 + n)
+            group(z, k("z0"), ba, struck([flags("sin", c, s) for s in range(t)]) + [mat("selk2", S, [sk])])
+            flag(M, z, t, [k("z0")], [mk], ba)
+        L, PL = ap(pb, 0, n), ap(pb, n, 2 * n)
+        group(L, k("L"), bb, KS)
+        if p["h16"]:
+            Lf, lf = ap("hh", h0 + (t + 1) * n, h0 + (t + 2) * n), "hh%d_%d" % (c, t + 1)
+            relu("V", Lf, L, [k("L")], [lf], n, bb)
+            copy("G", Lh, Lf, [lf], [lk], n)
         else:
-            group(ap(pa, n, 2 * n), k("pl"), ba, KS + [mat("wb", M, [mk])])
-            ncol, vc, sp, win, wk = n, p.get("vc0_%d" % c, p["vc0"]), p["spieces0"], 8192, TAB
-            if p["x00"]:
-                ts(ap("off", 2 * cn, 2 * cn + n), ap(pa, n, 2 * n), C("rest"), C("k1"), A.mult, A.max, [k("pl"), "c_rest", "c_k1"],
-                   [k("offl"), k("offo")], n, ba)
-                group(ap(pb, 256, 256 + n), k("xk"), bb, [mat("eye", ap("cd2"), ["cd2"]), mat("wb", M, [mk]), mat("selk", K, [kk]), mat("selk2", S, [sk])])
-                scan(loc("dg2"), ap("rs", 0, n), ap(pb, 256, 256 + n), A.add, A.max, ["rs", k("xk")], [k("dgx")], n, bb)
-                cp(ap("xoff", 16 * j, 16 * j + nc), ap("dg2", cn + 15, cn + n, 16), [k("dgx")], [k("xoff")], 64)
-                wk = wk + ["low"]
+            Lf, lf = Lh, lk
+        late_l = t and not p["h16"] and (t <= p["sel"] or p["nep"])
+        if not p["h16"] and not late_l:
+            relu(p["e_lh"], Lh, L, [k("L")], [lk], n, bb)
+        one = p["one"] and t > 0
+        oo, on_, st = (2 * cn, 2 * cn + 1, 2) if one else (2 * cn, 2 * cn + n, 1)
+        par = uses[0] % p["nd"]
+        d0 = par * 32 * n
+        do, dn = "d1o%d" % par, "d1n%d" % par
+        if t:
+            uses[0] += 1
+            og = loc("og")
+            pick, picka = t <= p["sel"], t <= p["sela"]
+
+            def mask(s):
+                return (ap("wm", 128 * s, 128 * s + 128), M, ["wm%d" % s, mk], n)
+
+            def slot():
+                group(ap(pa, 0, n), k("pt"), ba, [mat("eye", ap("cd"), ["cd"]), mat("wp", M, [mk])])
+                scan(loc("dg"), ap("rs"), ap(pa, 0, n), 0.0, A.add, A.max, ["rs", k("pt")], [k("dg")], n, ba)
+                cp(ap("poff", 16 * c, 16 * c + nc), ap("dg", cn + 15, cn + n, 16), [k("dg")], [k("poff")], 64)
+            eq1 = t == 1 and p["eq1"]
+            if eq1:
+                old = [mat("eye2", ap("sin", pay(c, 0), pay(c, 0) + n), ["sinS%d_0" % c]), mat("eye", kinds(0)[0], [kinds(0)[1]])]
+                group(ap(pa, 0, n), k("pt"), ba, old + [mat("neye", K, [kk]), mat("neye2", S, [sk]), mask(0)])
+                ts(loc("ne"), ap(pa, 0, n), num(0.0), None, A.is_equal, None, [k("pt")], [k("ne")], n, ba)
+            elif pick:
+                terms = []
+                for s in range(t):
+                    z = ap(pa, s, t * n, t)
+                    if p["h16"]:
+                        terms += [mat("eyeh", ap("hh", h0 + (s + 1) * n, h0 + (s + 2) * n), ["hh%d_%d" % (c, s + 1)]) + (z,)]
+                    else:
+                        terms += [mat("eye", kinds(s)[0], [kinds(s)[1]]) + (z,),
+                                  mat("eye2", ap("sin", pay(c, s), pay(c, s) + n), ["sinS%d_%d" % (c, s)]) + (z,)]
+                group(None, k("pt"), ba, terms + [mask(s) + (ap(pa, s, t * n, t),) for s in range(t)])
+                if t == 1:
+                    relu("V", og, ap(pa, 0, n), [k("pt")], [k("og")], n, ba)
+                else:
+                    a = 5 * cn
+                    scan(ap("ogs", a, a + t * n), ap("rm", RM[t], RM[t] + t * n), ap(pa, 0, t * n), 0.0, A.mult, A.max, ["rm%d" % t, k("pt")],
+                         [k("og")], t * n, ba)
+                    og = ap("ogs", a + t - 1, a + t * n, t)
+                tt(loc("ne"), og, L, A.not_equal, [k("og"), k("L")], [k("ne")], n, bb)
             else:
-                ts(ap("off", 2 * cn, 2 * cn + n), ap(pa, n, 2 * n), num(0.0), None, A.max, None, [k("pl")], [k("offl"), k("offo")], n, ba)
+                slot()
+                src = ind("hl", h0, h0 + t * n + n, "poff", 16 * c, 16 * c + nc)
+                copy(p["e_og"], og, src, HL + [k("poff")], [k("og")], n, gather=True)
+                if p["nep"]:
+                    tt(loc("ne"), og, L, A.not_equal, [k("og"), k("L")], [k("ne")], n, bb)
+                else:
+                    tt(loc("ne"), src, Lf, A.not_equal, HL + [k("poff"), lf], [k("ne")], n, kind="gv")
+            if late_l and p["jp"]:
+                relu(p["e_lh"], Lh, L, [k("L")], [lk], n, bb)
+            PO = ap(pa, 5 * n, 6 * n)
+            new = ([mat("eyeh", Lf, [lf])] if p["h16"] else KS) + [mat("wb", M, [mk])]
+            both = one and p["jp"] == 2 and not eq1
+            old = old + [mask(0), mat("wb", M, [mk])] if eq1 else [mat("wb", M, [mk]), mat("eyeh", og, [k("og")])]
+            same, dead = ("m16", 0.0) if eq1 else ("n16", DEAD)
+            if p["jp"]:
+                PO, PL = (ap(pa, 5 * n, 7 * n, 2), ap(pa, 5 * n + 1, 7 * n, 2)) if both else (PO, ap(pa, 6 * n, 7 * n))
+                group(None, k("po"), ba, [x + (PL,) for x in new] + [x + (PO,) for x in old]
+                      + [on("n24" if both else same, "ne") + (PO,), on(same, "ne") + (PL,)])
+            else:
+                group(PO, k("po"), ba, old + [on(same, "ne")])
+                group(PL, k("pl"), bb, new + [on(same, "ne")])
+            if both:
+                ts(ap("off", oo, oo + 2 * n), ap(pa, 5 * n, 7 * n), num(DEAD), num(0.0), A.add, A.max, [k("po")], [k("offo"), k("offn")], 2 * n, ba)
+            else:
+                ts(ap("off", oo, oo + st * n, st), PO, num(dead + (TW if one else 0)), num(0.0), A.add, A.max, [k("po")], [k("offo")], n, ba)
+                ts(ap("off", on_, 2 * cn + 2 * n, st), PL, num(dead), num(0.0), A.add, A.max, [k("po" if p["jp"] else "pl")], [k("offn")], n,
+                   ba if p["jp"] else bb)
+            if late_l and not p["jp"]:
+                relu(p["e_lh"], Lh, L, [k("L")], [lk], n, bb)
+            start = ap("d1", d0, d0 + 32 * n, 32) if one else ap("d1", d0, d0 + 16 * n, 16)
+            if picka:
+                bk = bb if p["jp"] else ba
+                terms = [[mat("eye", ap("ha", h0 + (s + 1) * n, h0 + (s + 2) * n), [HA[s + 1]]), mat("eye", ap("cb"), ["cb"]), mask(s)]
+                         for s in range(t)]
+                group(None, k("za"), bk, [x + (ap("pb%d" % bk, (s + 2) * n, (s + 3) * n),) for s in range(t) for x in terms[s]])
+                acc, ak = ap("bs"), "bs"
+                for s in range(t):
+                    out, ok = (start, do) if s == t - 1 else (ap("acc", 2 * cn + s % 2 * n, 2 * cn + s % 2 * n + n), k("acc%d_" % (s % 2)))
+                    tt(out, ap("pb%d" % bk, (s + 2) * n, (s + 3) * n), acc, A.max, [k("za"), ak] + [dn] * one, [ok], n, bk)
+                    acc, ak = out, ok
+            else:
+                if pick:
+                    slot()
+                tt(start, ind("ha", h0, h0 + (t + 1) * n, "poff", 16 * c, 16 * c + nc), ap("cb"), A.add, HA + [k("poff"), "cb"] + [dn] * one, [do], n,
+                   kind="gv")
+        else:
+            on_ = 2 * cn + n
+            group(PL, k("pl"), bb, KS + [mat("wb", M, [mk])])
+            ts(ap("off", on_, on_ + n), PL, num(0.0), None, A.max, None, [k("pl")], [k("offn"), k("offo")], n, bb)
         if t == p["m1r"]:
-            a = 3 * KW + LN + c * n
-            kings = [(ap("kall", a, a + n), "sall3"), (ap("sout", pay("sout", u, 1), pay("sout", u, 1) + n), "su%d_1" % u)]
+            a = 3 * 2 * LN + LN + cn
+            kings = [(ap("kall", a, a + n), "snext"), (ap("sout", pay(c, 1), pay(c, 1) + n), "su%d_1" % c)]
             for s in range(t + 1):
-                fl = [nextflags(r, q, c, i) for i in range(s + 1)]
-                group(ap(pa, 448, 448 + n), k("l0"), ba, struck(fl[:s]) + [mat("selk2", kings[s][0], [kings[s][1]])])
-                ts(fl[s][0], ap(pa, 448, 448 + n), ap("thr", s, s + 1), None, A.is_ge, None, [k("l0"), "thr"], [fl[s][1]], n, ba)
-        sc = ncol - vc
-        cuts = [2 * ((sc * i // sp) // 2) for i in range(sp)] + [sc]
-        if t and p["tail"]:
-            e = (sc - p["tail"]) // 16 * 16
-            cuts = [2 * ((e * i // (sp - 1)) // 2) for i in range(sp)] + [sc]
-        vp = p["vp"] if vc else 0
-        cuts += [sc + 2 * ((vc * (i + 1) // vp) // 2) for i in range(vp)]
-        XK = ["x%d_%d" % (j, i) for i in range(64)]
-        ok = wk + [k("offl"), k("offo")]
-        for i in range(sp + vp):
-            a, b = cuts[i], cuts[i + 1]
-            if a < b:
-                copy("S" if i < sp else "V", ap("xb", x0 + 16 * a, x0 + 16 * b), ind("tab", t0, t0 + win, "off", 2 * cn + a, 2 * cn + b),
-                     ok, XK[a // 2:b // 2], 16 * (b - a), gather=True)
+                fl = [flags("sout", c, i) for i in range(s + 1)]
+                group(ap(pb, 448, 448 + n), k("l0"), bb, struck(fl[:s]) + [mat("selk2", kings[s][0], [kings[s][1]])])
+                flag(fl[s][0], ap(pb, 448, 448 + n), s, [k("l0")], [fl[s][1]], bb)
+        s0 = 32 * cn
+        SO = ["so%d_%d" % (c, i) for i in range(8)]
+
+        def phase(x, x0, m, col, keys, cut, d1, dk, a0, neg, win):
+            XK = ["%s%d_%d" % (x, c, i) for i in range(m * n // 2)]
+            a = 0
+            for e, b in zip(cut[0::2], cut[1::2]):
+                copy(e, ap("xb", x0 + 16 * a, x0 + 16 * b), ind("tab", 0, win, "off", col + a, col + b), TAB + keys, XK[a // 2:b // 2],
+                     16 * (b - a), gather=True, neg=neg)
+                a = b
+            w = 128 * m
+            for i in range(8):
+                a = w * i
+                scan(ap("so", s0 + a, s0 + a + w), ap("xb", x0 + a - 1, x0 + a + w - 1), ap(d1, a0 + a, a0 + a + w) if t else ap(d1), -4096.0, A.add, A.max,
+                     XK[max(0, 4 * m * i - 1):4 * m * (i + 1)] + dk + ["xp"], [SO[i]], w // 2)
+            return [mat("eye", ap("xb", x0 + 16 * m - 1, x0 + 16 * m * n, 16 * m), XK),
+                    mat("eyeh", ap("so", s0 + 16 * m - 1, s0 + 16 * m * n, 16 * m), SO)]
+        xo, xn = 2 * c * XW + 16, (2 * c + 1) * XW + 16
+        if one:
+            fin = phase("xn", xo, 2, oo, [k("offo"), k("offn")] + NEG, p.get("cut%d" % t, p["cut"]), "d1", [do, dn], d0, False, 2 * TW)
+        elif t:
+            z = ap(pa, 3 * n, 4 * n)
+            group(z, k("zj"), ba, phase("xo", xo, 1, oo, [k("offo")], p["cuto"], "d1", [do], d0, True, TW))
+            tt(ap("d1", d0 + 16 * n, d0 + 32 * n, 16), z, ap("bs"), A.max, [k("zj"), "bs"], [dn], n, ba)
+            fin = phase("xn", xn, 1, on_, [k("offn")], p["cutn"], "d1", [dn], d0 + 16 * n, False, TW)
+        else:
+            fin = phase("xn", xo if p["one"] else xn, 1, on_, [k("offn")], p.get("cut0_%d" % c, p["cut0"]), "d1b", ["d1b"], 0, False, TW)
         if t == RO - 1:
             final(c, bb)
             outs(c, "yc", "hl", p["e_yc"], 0.0)
-        d0 = par * 32 * n
-        DK = ["d1_%d_%d" % (par, i) for i in range(8)]
-        df = ["d1f%d_%d" % (par, i) for i in range(st // 8)]
-        if t == 1 and uses[r] <= NCH + p["nd1"]:
-            ms(ap("d1", d0 + 16, d0 + 16 * n, 32), -OFS, DK[:4], 64, df)
-        rp = p["rp"] if t else 1
-        h = n // rp
-        if t == 0 and p["x00"]:
-            rp = 0
-            add("V", lambda q, T, X: q.tensor_scalar(T["d1"][:, d0:d0 + st * n:st], T["tab"][:, 0:8192].indirect(T["xoff"][:, 16 * j:16 * j + nc]),
-                                                     -OFS, -OFS, A.add, A.max), wk + [k("xoff")] + df, DK, ("gv", n))
-        if t and p["x0"]:
-            rp = 0
-            tt(loc("tt"), ind("tab", t0, t0 + 16384, "xoff", 16 * j, 16 * j + nc), loc("sg"), A.add, wk + [k("xoff"), k("sg")], [k("tt")], n,
-               kind="gv")
-            ts(ap("d1", d0, d0 + st * n, st), loc("tt"), num(-OFS), None, A.max, None, [k("tt")] + df, DK, 64)
-        for i in range(rp):
-            a, b = st * h * i, st * h * (i + 1)
-            xf, xk, dk = ap("xb", x0 + a, x0 + b, st), XK[a // 32:b // 32], DK[a // 256:b // 256]
-            if t:
-                tb = ap("tt", cn + h * i, cn + h * i + h)
-                tt(tb, ind("ha", h0, h0 + (t + 1) * n, "poff", 16 * j + h * i // 16, 16 * j + (h * i + h) // 16), xf, A.add,
-                   HA + xk + [k("poff")], [k("tt%d_" % i)], h, kind="gv")
-                ts(ap("d1", d0 + a, d0 + b, st), tb, num(-OFS), None, A.max, None, [k("tt%d_" % i)] + df, dk, 64)
-            else:
-                ts(ap("d1", d0 + a, d0 + b, st), xf, num(-OFS), num(-OFS), A.add, A.max, xk + df, dk, 64)
-            if p["e_ms"] == "V":
-                ms(xf, -1024.0, xk, 64)
-            else:
-                iota(xf, [[0, h]], -1024, 0, xk, h)
-        sok = ["so%d_%d" % (j, i) for i in range(8)]
-        scp = max(1, rp, p["scp"] * st // 32)
-        w = st * n // scp
-        for i in range(scp):
-            a = i * w
-            scan(ap("so", x0 + a, x0 + a + w), ap("xb", x0 + a, x0 + a + w), ap("d1", d0 + a, d0 + a + w), A.add, A.max,
-                 XK[a // 32:(a + w) // 32] + DK[a // 256:(a + w) // 256], sok[a // 256:(a + w) // 256], w // 2)
-        fin = ap("so", x0 + st - 1, x0 + st * n, st)
-        ts(ap("yb", 2 * cn + n, 2 * cn + 2 * n), fin, num(OFS), num(127.0), A.add, A.min, sok, [k("yb")], 64)
-        Ah, ak = ap("ha", h0 + (t + 1) * n, h0 + (t + 2) * n), "ha%d_%d" % (u, t + 1)
-        if p["e_hist"] == "G":
-            add("G", lambda q, T, X: q.affine_select(Ah(T), fin(T), [[0, n]], A.is_ge, 0.0, 0, 0), sok, [ak], ("ga", n))
+        z = ap(pa, 4 * n, 5 * n)
+        group(z, k("zf"), ba, [mat("eye", ap("nb"), ["nb"])] + fin)
+        ts(ap("yb", 2 * cn + n, 2 * cn + 2 * n), z, num(0.0), num(127.0), A.max, A.min, [k("zf"), "yb"], [k("yb")], n, ba)
+        Ah, ak = ap("ha", h0 + (t + 1) * n, h0 + (t + 2) * n), "ha%d_%d" % (c, t + 1)
+        if p["sela"] == RO - 1 and p["e_ha"] == "S":
+            act(Ah, z, F.Identity, [k("zf")], [ak], n, ba, bias=num(-OFS))
         else:
-            copy(p["e_hist"], Ah, fin, sok, [ak], 64)
-        if t == t1 - 1 and away(q, c) != r:
-            u2 = unit(away(q, c), q, c)
-            hs = ("ha", "hl") if t else ("ha",)
-            send(away(q, c), [(x, h0 + n, x, u2 * HS + n, t1 * n) for x in hs], [ak, lk] + HL[1:] + HA[1:],
-                 ["%s%d_%d" % (x, u2, s) for x in hs for s in range(1, t1 + 1)], "h0_%d" % c)
-        if t == RO - 2 and q % NR != r:
-            a, m = (t1 + 1) * n, (RO - 1 - t1) * n
-            send(q, [("hl", h0 + a, "hl", c * HS + a, m), ("ha", h0 + a, "ha", c * HS + a, m),
-                     ("sin", pay("sin", u, t1), "sin", pay("sin", c, t1), 2 * m)],
-                 [x % (u, s) for s in range(t1, 5) for x in ("sinS%d_%d", "sinM%d_%d")] + HL[t1 + 1:] + HA[t1 + 1:] + [lk, ak],
-                 [x % (c, s) for s in range(t1 + 1, 6) for x in ("hl%d_%d", "ha%d_%d")] + ["sinM%d_%d" % (c, s) for s in range(t1, 5)],
-                 "h4_%d" % c, ("b", 1536 * m))
-        lo, hi = ap("yb", 2 * cn + n, 2 * cn + 3 * n), ap("yb", 2 * cn, 2 * cn + 2 * n)
-        uu, vv = "uu%d" % tw, "vv%d" % tw
-
-        def keys(pb, bb, at, key, const, sh):
-            group(ap(pb, at, at + 128), key, bb,
-                  [mat("eye", ap(const), [const], 128), (S, ap("pen", sh, sh + 128), [sk, "pen"], 128, ap(pb, at, at + 128, p1=n)),
-                   (lo, ap(uu, sh, sh + 128), [k("yb")] + ["%s_%d" % (uu, i) for i in range(9)], 128),
-                   (hi, ap(vv, sh, sh + 128), [k("yb")] + ["%s_%d" % (vv, i) for i in range(9)], 128)])
-        q0 = 128 * j
-        rq, tq = ap("rq", q0, q0 + 128), ap("tq", q0, q0 + 128)
-        keys(pb, bb, 128, k("key"), "dc", 0)
-        if p["q2"]:
-            keys(pa, ba, 0, k("kez"), "dc2", 1)
-        scan(rq, ap(pb, 128, 256), ap("zr"), A.add, A.max, [k("key"), "zr"], [k("rq")], 128, bb)
-        if p["q2"]:
-            scan(back("tq", q0, q0 + 128), back(pa, 0, 128), ap("zr"), A.add, A.min, [k("kez"), "zr"], [k("tq")], 128, ba)
-        else:
-            scan(back("tq", q0, q0 + 128), ap("eps"), back("rq", q0, q0 + 128), A.add, A.min, [k("rq"), "eps"], [k("tq")], 64)
+            ts(Ah, z, num(0.0), num(-OFS), A.max, A.add, [k("zf")], [ak], n, ba)
+        wk = ["uu%d" % i for i in range(16)]
+        group(ap(pb, 128, 256), k("key"), bb,
+              [(ap("sin", o, o + 2 * n), ap("pen"), [sk, mk, "pen"], 128),
+               (ap("yb", 2 * cn + n, 2 * cn + 3 * n), ap("uu", 0, 128), [k("yb")] + wk, 128),
+               (ap("yb", 2 * cn, 2 * cn + 2 * n), ap("uu", 128, 256), [k("yb")] + wk, 128)])
+        q0, q1 = 128 * c, 144 * c
+        scan(ap("rq", q0, q0 + 128), ap(pb, 128, 256), ap("rt"), 0.0, A.add, A.max, [k("key"), "rt"], [k("rq")], 128, bb)
+        scan(back("tq", q1, q1 + 128), back("eps", 0, 128), back("rq", q0, q0 + 128), 0.0, A.add, A.min, [k("rq"), "eps"], [k("tq")], 64)
 
         def lost(a):
-            return [(rq, ap("ee", a, a + n), ["ee", k("rq")], n), (tq, ap("ee2", a, a + n), ["ee2", k("tq")], n)]
-        group(ap(pa, 192, 192 + n), k("zu"), ba, [mat("eye2", S, [sk])] + lost(0))
-        group(ap(pb, 320, 320 + n), k("zv"), bb, lost(n))
-        relu(p["e_msq"], loc("msq"), ap(pa, 192, 192 + n), [k("zu")], [k("msq")], n, ba)
-        relu(p["e_ost"], loc("ost"), ap(pb, 320, 320 + n), [k("zv"), "step%d" % ws_], [k("ost")], n, bb, step)
-        if p["m1r"] <= t < RO - 1:
-            group(ap(pb, 384, 384 + n), k("zn"), bb,
-                  struck([nextflags(r, q, c, s) for s in range(t + 1)]) + [mat("selk2", S, [sk]), on("nselk", "msq")], last=False)
-        b1 = (ba - 2) % 8 if p["bor"][0] <= t * NCH + c <= p["bor"][1] else ba
-        w1 = ap("pb%d" % b1, 256, 256 + n)
-        group(w1, k("w1"), b1, [on("bmq", "msq"), on("bmq", "ost"), mat("cp", ap("one"), ["one"]), mat("cn", ap("one"), ["one"]),
+            return [(ap("tq", q1, q1 + 128), ap("ee", a, a + n), ["ee", k("tq")], n),
+                    (ap("tq", q1 + 1, q1 + 129), ap("ee2", a, a + n), ["ee2", "tqp", k("tq")], n)]
+        group(ap(pa, 5 * n, 6 * n), k("zu"), ba, [mat("eye2", S, [sk])] + lost(0))
+        group(ap(pb, 4 * n, 5 * n), k("zv"), bb, lost(n))
+        relu(p["e_msq"], loc("msq"), ap(pa, 5 * n, 6 * n), [k("zu"), "c_b15"], [k("msq")], n, ba, C("b15"))
+        relu(p["e_ost"], loc("ost"), ap(pb, 4 * n, 5 * n), [k("zv"), "c_st"], [k("ost")], n, bb, C("st"))
+        zn = p["m1r"] <= t < RO - 1
+        Z = ap(pb, 5 * n, 6 * n)
+        if zn:
+            group(Z, k("zn"), bb, struck([flags("sout", c, s) for s in range(t + 1)]) + [mat("selk2", S, [sk]), on("nselk", "msq")], last=False)
+        early = KS + [on("neye", "msq")] if t == RO - 1 else [mat("eye", S, [sk]), on("nhalf", "msq")]
+        late = [on("eye2" if t == RO - 1 else "eye", "mn"), on("gd", "ht")]
+        bf = bb if p["jz"] or not zn else ba
+        Fn = ap("pb%d" % bf, 6 * n, 7 * n)
+        if bf == bb:
+            group(Fn, k("fin"), bb, early, first=not zn, last=False)
+        w1 = ap(pa, 7 * n, 8 * n)
+        group(w1, k("w1"), ba, [on("bmq", "msq"), on("bmq", "ost"), mat("cp", ap("one"), ["one"]), mat("cn", ap("one"), ["one"]),
                                 on("bmh", "msq"), on("bmh", "ost")])
-        tt(loc("mn"), w1, loc("msq"), A.min, [k("w1"), k("msq")], [k("mn")], n, b1)
-        tt(loc("ht"), w1, S, A.is_equal, [k("w1"), sk], [k("ht")], n, b1)
-        king = [on("selk2", "mn")]
-        last = [on("eye", "mn"), on("gd", "ht")]
-        s2 = [mat("eye", S, [sk]), on("nhalf", "msq")]
+        tt(loc("mn"), w1, loc("msq"), A.min, [k("w1"), k("msq")], [k("mn")], n, ba)
+        tt(loc("ht"), w1, S, A.is_equal, [k("w1"), sk], [k("ht")], n, ba)
+        if zn:
+            group(Z, k("zn"), bb, [on("selk2", "mn")], first=False, last=bf != bb)
+        group(Fn, k("fin"), bf, late if bf == bb else early + late, first=bf != bb)
         if t < RO - 1:
-            r2 = proc(q + 1, c, t + 1)
-            u2 = unit(r2, q + 1, c)
-            Mn, mnk = nextflags(r, q, c, t + 1)
-            o2 = pay("sin", u2, t + 1)
-            buf, o1, su = ("sin", o2, "sinS%d_%d" % (u2, t + 1)) if r2 == r else ("sout", pay("sout", u, t + 1), "su%d_%d" % (u, t + 1))
-            if t >= p["m1r"]:
-                group(ap(pb, 384, 384 + n), k("zn"), bb, king, first=False)
-            group(ap(pa, 320, 320 + n), k("fin"), ba, s2 + last)
-            if t >= p["m1r"]:
-                ts(Mn, ap(pb, 384, 384 + n), ap("thr", t + 1, t + 2), None, A.is_ge, None, [k("zn"), "thr"], [mnk], n, bb)
-            copy(p["e_su"], ap(buf, o1, o1 + n), ap(pa, 320, 320 + n), [k("fin")], [su], n, ba)
-            if t < p["m1r"]:
-                send(r2, [("sout", o1, "sin", o2, n)], [su], ["sinS%d_%d" % (u2, t + 1)], "ar%d_%d" % (t + 1, c), name=su)
-            elif r2 != r:
-                send(r2, [("sout", o1, "sin", o2, 2 * n)], [su, mnk], ["sinS%d_%d" % (u2, t + 1), "sinM%d_%d" % (u2, t + 1)],
-                     "ar%d_%d" % (t + 1, slots[t + 1, (q + 1) % NR, c]), mask="high" if p["pair"] and p["nship"] and t < 2 else "all", name=su)
-            r3 = proc(q, c, t1)
-            if t == t1 - 1 and r3 != r and r3 != r2:
-                u3 = unit(r3, q, c)
-                send(r3, [("sout", pay("sout", u, 0) + n, "sout", pay("sout", u3, 0) + n, (2 * t1 + 1) * n)],
-                     ["su%d_%d" % (u, s) for s in range(1, t1 + 1)] + ["soutM%d_%d" % (u, s) for s in range(t1 + 1)],
-                     ["soutM%d_%d" % (u3, s) for s in range(t1 + 1)], "mn_%d" % c)
+            o2 = pay(c, t + 1)
+            su = "su%d_%d" % (c, t + 1)
+            Mn, mnk = flags("sout", c, t + 1)
+            if zn:
+                flag(Mn, Z, t + 1, [k("zn")], [mnk], bb)
+            copy(p["e_su"], ap("sout", o2, o2 + n), Fn, [k("fin")], [su], n, bf)
+            w = 2 * n if zn else n
+            sem = "ar%d_%d" % (t + 1, c)
+            add("G", lambda q, T, X: q.remote_dma(T["sin"][:, o2:o2 + w], T["sout"][:, o2:o2 + w], T.sem[sem], T.sem["sent"], X["addr"][1][1],
+                                                  X["addr"][1][0], X["mask"]), [su] + ([mnk] if zn else []), ["st" + sem], ("r", 0), None, "sent")
+            lands(["st" + sem], ["sinS%d_%d" % (c, t + 1)] + (["sinM%d_%d" % (c, t + 1)] if zn else []), sem, 0.0)
         else:
-            group(ap(pa, 320, 320 + n), k("fin"), ba, KS + [on("neye", "msq"), on("eye2", "mn"), on("gd", "ht")])
-            relu(p["e_yl"], loc("oyl"), ap(pa, 320, 320 + n), [k("fin")], [k("oyl")], n, ba)
-            dma("Y", ap("yl", c * n, c * n + n), loc("oyl"), [k("oyl")], [], "outs", 32768)
+            outs(c, "ya", "ha", p["e_ya"], OFS)
+            relu(p["e_yl"], loc("oyl"), Fn, [k("fin")], [k("oyl")], n, bf)
+            dma("Y", ap("yl", cn, cn + n), loc("oyl"), [k("oyl")], [], "outs", 32768)
 
     def final(c, bb):
         pb = "pb%d" % bb
         cn, n4 = c * n, n // 4
-        group(ap(pb, 448, 448 + n), "zf%d" % c, bb, struck([flags("sin", c, s) for s in range(RO)]))
+        group(ap(pb, 448, 448 + n), "zf%d" % bb, bb, struck([flags("sin", c, s) for s in range(RO)]))
         for h in range(2):
             ts(ap("fm", 2 * cn + h * n, 2 * cn + h * n + n), ap(pb, 448, 448 + n), C("cf%d" % h), None, A.is_equal, None,
-               ["zf%d" % c, "c_cf%d" % h], ["fm%d_%d" % (c, h)], n, bb)
+               ["zf%d" % bb, "c_cf%d" % h], ["fm%d_%d" % (c, h)], n, bb)
         terms = [mat("eye", ap("c4", 0, n4), ["c4"], 64)]
         for h in range(2):
-            for r in range(4):
-                d = 4 * r + 2 * h
-                terms.append((ap("wfw", 16 - d, 144 - d), ap("fm", 2 * cn + h * n + r, 2 * cn + h * n + n, 4), ["wfw", "fm%d_%d" % (c, h)], 64))
-        group(ap(pb, 448, 448 + n4), "zf%d" % c, bb, terms)
-        ts(ap("foff", 16 * c, 16 * c + n4), ap(pb, 448, 448 + n4), C("rf"), None, A.add, None, ["zf%d" % c, "c_rf"], ["foff%d" % c], 64, bb)
+            for i in range(4):
+                d = 4 * i + 2 * h
+                terms.append((ap("wfw", 16 - d, 144 - d), ap("fm", 2 * cn + h * n + i, 2 * cn + h * n + n, 4), ["wfw", "fm%d_%d" % (c, h)], 64))
+        group(ap(pb, 448, 448 + n4), "zf%d" % bb, bb, terms)
+        ts(ap("foff", 16 * c, 16 * c + n4), ap(pb, 448, 448 + n4), C("rf"), None, A.add, None, ["zf%d" % bb, "c_rf"], ["foff%d" % c], 64, bb)
 
     def outs(c, nm, hn, e, bias):
-        cn, h0, n4 = c * n, c * HS, n // 4
+        h0, n4 = c * HS, n // 4
         src = ind(hn, h0, h0 + HS, "foff", 16 * c, 16 * c + n4)
-        r = ["%s%d_%d" % (hn, c, s) for s in range(7)] + ["foff%d" % c]
-        dst = ap("o" + nm, 4 * cn, 4 * cn + 4 * n)
+        rd = ["%s%d_%d" % (hn, c, s) for s in range(7)] + ["foff%d" % c]
+        dst = ap("o" + nm, 4 * n * c, 4 * n * c + 4 * n)
         if e == "S":
-            act(dst, src, F.Identity, r, ["o%s%d" % (nm, c)], 4 * n, kind="gs", bias=num(bias))
+            act(dst, src, F.Relu, rd, ["o%s%d" % (nm, c)], 4 * n, kind="gs", bias=num(bias))
         else:
-            add("V", lambda q, T, X: q.tensor_scalar(dst(T), src(T), bias, None, A.add), r, ["o%s%d" % (nm, c)], ("gv", 4 * n))
-        dma("Y", ap(nm, 4 * cn, 4 * cn + 4 * n), dst, ["o%s%d" % (nm, c)], [], "outs", 131072)
+            ts(dst, src, num(bias), num(0.0), A.add, A.max, rd, ["o%s%d" % (nm, c)], 4 * n, kind="gv")
+        dma("Y", ap(nm, 4 * n * c, 4 * n * c + 4 * n), dst, ["o%s%d" % (nm, c)], [], "outs", 131072)
 
-    for r in range(kinds):
-        me[0] = r
-        setup(r)
+    setup()
     for t in range(RO):
-        if t == 1 and p["pair"]:
-            tag[0] = cur[0] = None
-            for r in range(2):
-                me[0] = r
-                partner(r)
         for c in range(NCH):
             tag[0] = t * NCH + c
-            for r in range(kinds):
-                me[0] = r
-                for q in (r, r ^ 1):
-                    if proc(q, c, t) == r:
-                        tag[0] = t * NCH + p["sk"][(q - t) % 2][c]
-                        cur[0] = (t, (q - t) % 2 if p["pair"] else 0, c)
-                        ply(t, r, q, c)
-                        if t == RO - 1:
-                            outs(c, "ya", "ha", p["e_ya"], OFS)
+            ply(t, c)
     return ops
 
 
 def times(op, p):
     kind, m = op["cost"]
     cy = 0.00083 * p["f"]
-    if kind == "c":
-        d = max(64, m) * cy + p["fix"]
-    elif kind == "p":
-        d = max(64, m) * cy * p["pe"]
-    elif kind == "gv":
-        d = 0.05 + m * cy * p["g"]
-    elif kind == "gs":
-        d = 0.065 + m * cy * p["g"]
-    elif kind == "gi":
-        d = 0.13 + 2 * m * cy
-    elif kind == "ga":
-        d = 0.17 + 2 * m * cy
-    elif kind == "r":
-        d = p["riss"]
-    elif kind == "a":
-        return 0.0, p["rlat"] + p["klat"] * m
-    elif kind == "b":
-        return 0.0, p["rlat"] + m / p["bw"] / 1000.0
-    else:
-        return 0.1, 2.0 + op["lat"][1] / p["bw"] / 1000.0
+    if kind == "a":
+        return 0.0, p["rlat"] + m
+    if kind == "d":
+        return 0.1, 2.0 + m / p["bw"] / 1000.0
+    d = {"c": max(64, m) * cy, "p": max(64, m) * cy * p["pe"], "gv": 0.05 + m * cy * p["g"], "gs": 0.065 + m * cy * p["g"],
+         "gi": 0.13 + 2 * m * cy, "ga": 0.17 + 2 * m * cy, "r": p["riss"]}[kind]
     return d, d
 
 
@@ -788,18 +678,16 @@ def schedule(ops, p):
         own = -p["tq"] * ops[k]["tag"] if ops[k]["tag"] is not None else -1.0e3
         pr[k] = tm[k][1] + max([pr[s] + p["hop"] for s in succ[k]] + [own])
     for k in range(N):
-        pr[k] += p["up"].get(ops[k]["ty"][1:], 0.0) + p["up"].get(ops[k]["ty"].rstrip("0123456789_"), 0.0) - p["short"] * tm[k][0]
+        pr[k] += 1.0e4 if ops[k]["cost"][0] == "r" else p["up"].get(ops[k]["w"].rstrip("0123456789_"), 0.0) - p["short"] * tm[k][0]
     left = [len(o["deps"]) for o in ops]
     rdy = [0.0] * N
     free, order, ready = {}, {}, {}
     stack = [k for k in range(N) if not left[k]]
-    done = 0
-    while done < N:
+    while True:
         while stack:
             k = stack.pop()
             e = ops[k]["eng"]
             if e is None:
-                done += 1
                 for s in succ[k]:
                     rdy[s] = max(rdy[s], rdy[k] + tm[k][1])
                     left[s] -= 1
@@ -820,17 +708,16 @@ def schedule(ops, p):
         st = max(bt, rdy[k])
         free[be] = st + tm[k][0]
         order.setdefault(be, []).append(k)
-        done += 1
         for s in succ[k]:
-            hop = 0.0 if (be[0] == "P" and ops[s]["eng"] == be) else p["hop"]
+            hop = 0.0 if (be == "P" and ops[s]["eng"] == be) else p["hop"]
             rdy[s] = max(rdy[s], st + tm[k][1] + hop)
             left[s] -= 1
             if not left[s]:
                 stack.append(s)
     order = improve(ops, p, order)
-    for e, l in order.items():
-        if e[0] == "Y":
-            order[e] = sorted([k for k in l if not ops[k]["deps"]]) + [k for k in l if ops[k]["deps"]]
+    for e in "YG":
+        l = order[e]
+        order[e] = sorted([k for k in l if not ops[k]["deps"]]) + [k for k in l if ops[k]["deps"]]
     return order
 
 
@@ -861,7 +748,7 @@ def improve(ops, p, order):
     fw, bw = [[] for _ in range(N)], [[] for _ in range(N)]
     for k, o in enumerate(ops):
         for d in o["deps"]:
-            h = 0.0 if (ops[d]["eng"] is None or (o["eng"] == ops[d]["eng"] and o["eng"][0] == "P")) else p["hop"]
+            h = 0.0 if (ops[d]["eng"] is None or (o["eng"] == ops[d]["eng"] and o["eng"] == "P")) else p["hop"]
             fw[k].append((d, tm[d][1] + h))
             bw[d].append((k, tm[k][0] + h + tm[d][1] - tm[d][0]))
     nxt = {e: 0 for e in order}
@@ -899,28 +786,24 @@ PLAN = {}
 
 
 def plan():
-    if not PLAN:
+    key = str(P)
+    if key not in PLAN:
         ops = build(P)
-        PLAN["ops"] = ops
-        PLAN["order"] = schedule(ops, P)
-    return PLAN["ops"], PLAN["order"]
+        PLAN[key] = (ops, schedule(ops, P))
+    return PLAN[key]
 
 
 def rank_program(g, core, T, topo):
     rank = T.rank_of(core)
     if rank is None:
         return
-    ops, both = plan()
-    order = {e: l for e, l in both.items() if e[1] == str(rank % (1 + P["pair"]))}
+    ops, order = plan()
     peers = [T.cores[(rank + j) % NR] for j in range(NR)]
     mask = topo.mask(core, peers[1])
     for c in peers[2:]:
         mask &= topo.mask(core, c)
-    bits = [1 << e for e in topo.engines(core, peers[1]) if mask >> e & 1]
-    ne = len(bits)
-    low, high = sum(bits[:ne // 2]), sum(bits[ne // 2:])
-    parts = {2: [low, high], 3: [low, sum(bits[ne // 2:3 * ne // 4]), sum(bits[3 * ne // 4:])]}
-    X = {"addr": [topo.addr(c) for c in peers], "mask": mask, "all": mask, "low": low, "high": high, "parts": parts}
+    ne = len([e for e in topo.engines(core, peers[1]) if mask >> e & 1])
+    X = {"addr": [topo.addr(c) for c in peers], "mask": mask}
     queue = {"V": g.vector, "S": g.scalar, "P": g.tensor, "G": g, "Y": g.sync}
     pos = {}
     for e, l in order.items():
@@ -941,7 +824,7 @@ def rank_program(g, core, T, topo):
                         continue
                     if o["sem"] is not None:
                         top[("x", d)] = d
-                    elif not (e[0] == "P" and o["eng"] == e):
+                    elif not (e == "P" and o["eng"] == e):
                         f = o["eng"]
                         if f not in top or pos[d] > pos[top[f]]:
                             top[f] = d
@@ -968,15 +851,15 @@ def rank_program(g, core, T, topo):
         for k in l:
             if k in needed:
                 total[e] = total.get(e, 0) + 1
-                token[k] = ("s" + e[0], total[e])
+                token[k] = ("s" + e, total[e])
     for k, o in enumerate(ops):
         if o["eng"] is None:
-            token[k] = (o["sem"], ne * (NR - 1) if o["sem"] == "karr" else ne if o["lat"] == "all" else ne // 2)
+            token[k] = (o["sem"], ne * o["cnt"])
         elif o["cost"][0] == "d":
             token[k] = (o["sem"], 16)
     nout = nsent = 0
     for e, l in order.items():
-        q = queue[e[0]]
+        q = queue[e]
         for k in l:
             for d in waits[k]:
                 q.wait_ge(T.sem[token[d][0]], token[d][1])
@@ -986,8 +869,8 @@ def rank_program(g, core, T, topo):
                 ins.then_inc(T.sem[o["sem"]], 16)
                 nout += 16 if o["sem"] == "outs" else 0
             elif o["cost"][0] == "r":
-                nsent += ne // 2 if o["lat"] in ("low", "high") else ne
+                nsent += ne
             elif k in needed:
-                ins.then_inc(T.sem["s" + e[0]], 1)
+                ins.then_inc(T.sem["s" + e], 1)
     g.wait_ge(T.sem["sent"], nsent)
     g.sync.wait_ge(T.sem["outs"], nout)

@@ -6,40 +6,35 @@ NCH = 4
 n = LN // NCH
 HS = 7 * n
 TW = 8192
-XW = 16 * n + 16
+XW = 32 * n + 16
 SW = 12 * n
 RM = {2: 0, 3: 2 * n, 4: 5 * n, 5: 9 * n}
-DEAD = -32768.0
+BIG = 32768.0
 GONE = -2.0 ** 90
 OFS = 240.0
-LOST = 16384.0
 
-P = {"one": 1, "nd": 2, "m1r": 1, "sel": 1, "sela": 1, "h16": 0, "nep": 1, "jz": 0, "jp": 1, "neg": "SSSV", "negw": 1024, "klate": 4,
-     "cut": ("S", 32, "S", 72, "S", 104, "V", 116, "V", 128),
-     "cut0": ("S", 24, "S", 48, "V", 64), "cuto": ("S", 24, "S", 52, "V", 64), "cutn": ("V", 8, "S", 36, "S", 64),
-     "e_lh": "V", "e_og": "V", "e_msq": "V", "e_ost": "V", "e_su": "V", "e_yc": "V", "e_ya": "S", "e_yl": "V", "e_d1": "GVGV",
-     "g": 1.7, "f": 1.1, "pe": 0.7, "hop": 0.23, "rlat": 2.3, "riss": 0.6, "klat": 3.0, "bw": 400.0, "tq": 3.0, "short": 0.0, "fbi": 6, "up": {}, "sgn": 0, "e_ha": "V", "eq1": 0, "sfirst": 0, "lp": (1, 2, 3, 4),
-     "e_cs": ("king2", "ab", "pk", "nking", "sgh", "m2", "af", "t32", "aw", "q0", "q2", "s0", "g16o", "c0", "cf1")}
-P.update({'one': 1, 'cut0': ('V', 16, 'S', 40, 'S', 64), 'jz': 0, 'jp': 0, 'nep': 0, 'm1r': 1, 'nd': 2, 'e_d1': 'GDD', 'sel': 4, 'sela': 3, 'h16': 0,
-          'g': 2.0, 'f': 1.0, 'hop': 0.25, 'tq': 6, 'short': 1, 'rlat': 1.8, 'e_su': 'S', 'e_ost': 'V', 'e_msq': 'V', 'e_yl': 'V', 'e_ya': 'S',
-          'e_yc': 'S', 'e_lh': 'V', 'klate': 4, 'cut': ('V', 16, 'V', 32, 'S', 80, 'S', 112, 'S', 128),
-          'cut5': ('V', 16, 'V', 28, 'S', 80, 'S', 112, 'S', 128), 'neg': 'SSVV', 'negw': 512, 'cut0_0': ('V', 32, 'S', 64),
-          'cut0_3': ('S', 24, 'S', 48, 'V', 64)})
-P.update({'cut0': ('V', 16, 'S', 48, 'S', 64), 'jz': 0, 'jp': 2, 'nep': 0, 'm1r': 1, 'nd': 2, 'e_d1': 'GDD', 'sel': 3, 'sela': 3, 'h16': 1, 'g': 2.0,
-          'f': 1.0, 'hop': 0.25, 'tq': 6, 'short': 0, 'rlat': 1.8, 'e_su': 'V', 'e_ost': 'V', 'e_msq': 'V', 'e_yl': 'S', 'e_ya': 'S', 'e_yc': 'S',
-          'e_lh': 'S', 'klate': 4, 'eq1': 1, 'sfirst': 0, 'sgn': 0, 'e_ha': 'V', 'pe': 0.7, 'cut': ('V', 16, 'V', 24, 'S', 64, 'S', 96, 'S', 128),
-          'cut1': ('V', 16, 'V', 32, 'S', 96, 'S', 128), 'cut5': ('V', 16, 'S', 48, 'S', 96, 'V', 112, 'S', 128), 'neg': 'SSVV', 'negw': 512,
-          'cut0_0': ('S', 24, 'S', 44, 'V', 64), 'cut0_3': ('V', 16, 'S', 48, 'S', 64)})
+P = {"nd": 2, "sel": 3, "sela": 3, "nep": 0, "jz": 0, "eq1": 1, "neg": "SSSS", "negw": 512, "e_uv": "Y",
+     "cut": ("V", 16, "V", 24, "S", 64, "S", 96, "S", 128), "cut1": ("V", 16, "V", 32, "S", 96, "S", 128),
+     "cut5": ("V", 16, "S", 48, "S", 96, "V", 112, "S", 128),
+     "cut0": ("V", 16, "S", 48, "S", 64), "cut0_0": ("S", 24, "S", 44, "V", 64),
+     "e_msq": "V", "e_ost": "V", "e_su": "V", "e_yc": "S", "e_ya": "S", "e_yl": "S",
+     "g": 2.0, "f": 1.0, "pe": 0.7, "hop": 0.25, "rlat": 1.8, "riss": 0.6, "klat": 2.0, "bw": 400.0, "tq": 6.0, "short": 0.0, "fbi": 6, "up": {},
+     "moves": 0, "cases": ((1.0, 1.56, 0.25, 1.6), (1.5, 1.3, 0.2, 1.6), (1.4, 2.0, 0.2, 2.3))}
+P.update({'cut0': ('V', 16, 'S', 48, 'S', 64), 'cut0_0': ('V', 32, 'S', 48, 'S', 64), 'cut0_3': ('V', 16, 'V', 24, 'S', 48, 'S', 64),
+          'cut': ('V', 16, 'V', 24, 'S', 56, 'S', 80, 'S', 112, 'S', 128), 'cut1': ('V', 16, 'V', 32, 'S', 96, 'S', 128),
+          'cut5': ('V', 16, 'V', 28, 'S', 112, 'S', 128), 'cut5_3': ('V', 48, 'S', 112, 'S', 128), 'jz': 1, 'nep': 0, 'nd': 2, 'sel': 3, 'sela': 3,
+          'eq1': 0, 'g': 2.0, 'f': 1.1, 'e_yl': 'V', 'neg': 'SVSV', 'moves': 8000,
+          'cases': ((1.0, 1.56, 0.25, 1.6), (1.4, 1.4, 0.22, 1.8), (1.3, 2.0, 0.22, 2.0))})
 
 BF, F32, I32, U16, F16 = "bfloat16", "float32", "int32", "uint16", "float16"
 SCRATCH = {
     "tab": ("sbuf", [128, 2 * TW], BF), "uu": ("sbuf", [128, 256], BF),
-    "xb": ("sbuf", [128, 2 * NCH * XW], BF), "so": ("sbuf", [128, 32 * LN], F16),
+    "xb": ("sbuf", [128, NCH * XW], BF), "so": ("sbuf", [128, 32 * LN], F16),
     "d1b": ("sbuf", [128, 128], BF), "d1": ("sbuf", [128, 32 * LN], F16),
     "hl": ("sbuf", [128, NCH * HS], F32), "hh": ("sbuf", [128, NCH * HS], F16), "ha": ("sbuf", [128, NCH * HS], BF),
     "posi": ("sbuf", [128, LN], I32), "ki": ("sbuf", [128, LN], I32), "si": ("sbuf", [128, LN], I32),
-    "dd": ("sbuf", [128, LN], F32), "sq": ("sbuf", [128, LN], F32),
-    "kall": ("sbuf", [128, NR * 2 * LN], BF), "sin": ("sbuf", [128, NCH * SW], BF), "sout": ("sbuf", [128, NCH * SW], BF),
+    "dd": ("sbuf", [128, LN], BF), "sq": ("sbuf", [128, LN], BF),
+    "kall": ("sbuf", [128, NR * LN], BF), "sin": ("sbuf", [128, NCH * SW], BF), "sout": ("sbuf", [128, NCH * SW], BF),
     "uv": ("sbuf", [128, 32], BF), "stepi": ("sbuf", [128, 4], I32), "du": ("sbuf", [128, 32], BF),
     "dg": ("sbuf", [128, LN], F32), "poff": ("sbuf", [128, 16 * NCH], U16), "rm": ("sbuf", [128, 14 * n], BF),
     "og": ("sbuf", [128, LN], F16), "ogs": ("sbuf", [128, 5 * LN], F16), "acc": ("sbuf", [128, 2 * LN], F16),
@@ -48,7 +43,7 @@ SCRATCH = {
     "msq": ("sbuf", [128, LN], BF), "ost": ("sbuf", [128, LN], BF), "ht": ("sbuf", [128, LN], BF), "mn": ("sbuf", [128, LN], BF),
     "fm": ("sbuf", [128, 2 * LN], BF), "foff": ("sbuf", [128, 16 * NCH], U16),
     "oyl": ("sbuf", [128, LN], F32), "oya": ("sbuf", [128, 4 * LN], F32), "oyc": ("sbuf", [128, 4 * LN], F32),
-    "ci": ("sbuf", [128, 8], I32), "col": ("sbuf", [128, 64], F32), "thr": ("sbuf", [128, 8], F32), "gm": ("sbuf", [128, 8], F32),
+    "ci": ("sbuf", [128, 8], I32), "col": ("sbuf", [128, 64], F32), "thr": ("sbuf", [128, 8], F32),
     "gt": ("sbuf", [128, 8], F32), "it": ("sbuf", [128, 8], F32), "cmp": ("sbuf", [128, 8], F32), "wc": ("sbuf", [128, 16], F32),
     "dw": ("sbuf", [128, 160], BF), "eyew": ("sbuf", [128, 144], BF), "wfw": ("sbuf", [128, 144], BF), "pw": ("sbuf", [128, 130], BF),
     "c4": ("sbuf", [128, 16], BF), "ws": ("sbuf", [128, RO * 128], BF), "wm": ("sbuf", [128, RO * 128], BF),
@@ -56,14 +51,14 @@ SCRATCH = {
 }
 for _m in ("cd", "rs", "one", "bs", "nb", "cb"):
     SCRATCH[_m] = ("sbuf", [128, n], BF)
-for _m in ("cg", "km", "blk", "bmq", "bmh", "eye2", "selk2", "nhalf", "neye", "nselk", "wp", "wb", "ee", "ee2", "n16", "rt", "eps",
-           "cp", "cn", "gd", "pen", "pa", "pz", "n24", "m16", "neye2"):
+for _m in ("cg", "km", "blk", "bmq", "bmh", "eye2", "selh", "selq", "neye", "neye2", "wp", "wb", "up", "down", "upt", "rt", "eps",
+           "cp", "cn", "gd", "pen", "pa", "pz"):
     SCRATCH[_m] = ("sbuf", [128, 128], BF)
 for _b in range(8):
     SCRATCH["pb%d" % _b] = ("psum", [128, 512], F32)
 
-SEMAPHORES = ["sV", "sS", "sP", "sG", "karr", "sarr", "sent", "outs", "lpos", "lu", "lv", "lstep"] + [x + str(i) for x in ("lf", "ld") for i in range(4)] \
-    + ["ar%d_%d" % (t, c) for t in range(1, RO) for c in range(NCH)]
+SEMAPHORES = ["sV", "sS", "sP", "sG", "karr", "marr", "sent", "outs", "lpos", "lu", "lv", "lstep"] \
+    + [x + str(i) for x in ("lf", "ld") for i in range(4)] + ["ar%d_%d" % (t, c) for t in range(1, RO) for c in range(NCH)]
 
 
 def build(p):
@@ -130,21 +125,21 @@ def build(p):
             return q.activation(out(T), a(T), f, **kw)
         add("S", fn, rd, w, (kind, m), bk)
 
-    def relu(e, out, a, rd, w, m, bk, bias=None):
+    def relu(e, out, a, rd, w, m, bk, bias=None, kind="c"):
         if e == "S":
-            act(out, a, F.Relu, rd, w, m, bk, bias=bias)
+            act(out, a, F.Relu, rd, w, m, bk, "gs" if kind == "g" else kind, bias)
         elif bias is None:
             ts(out, a, num(0.0), None, A.max, None, rd, w, m, bk)
         else:
-            ts(out, a, bias, num(0.0), A.add, A.max, rd, w, m, bk)
+            ts(out, a, bias, num(0.0), A.add, A.max, rd, w, m, bk, "gv" if kind == "g" else kind)
 
-    def copy(e, out, a, rd, w, m, bk=None, gather=False, neg=False):
+    def copy(e, out, a, rd, w, m, bk=None, gather=False, by=None):
         if e == "S":
-            act(out, a, F.Copy, rd, w, m, bk, kind="gs" if gather else "c", scale=num(-1.0) if neg else None)
+            act(out, a, F.Copy, rd, w, m, bk, kind="gs" if gather else "c", scale=num(by) if by else None)
         elif e == "G":
             add("G", lambda q, T, X: q.affine_select(out(T), a(T), [[0, m]], A.is_ge, 0.0, 0, 0), rd, w, ("ga", m))
-        elif neg:
-            ts(out, a, num(-1.0), None, A.mult, None, rd, w, m, bk, kind="gv" if gather else "c")
+        elif by:
+            ts(out, a, num(by), None, A.mult, None, rd, w, m, bk)
         else:
             cp(out, a, rd, w, m, bk, kind="gv" if gather else "c")
 
@@ -153,14 +148,14 @@ def build(p):
             o, lh, rh, st, sp = x[4] if len(x) > 4 else out, x[0], x[1], first and i == 0, last and i == len(terms) - 1
             add("P", lambda q, T, X, o=o, lh=lh, rh=rh, st=st, sp=sp: q.matmul(o(T), lh(T), rh(T), st, sp), x[2], [key], ("p", x[3]), bk)
 
-    def iota(name, pat, base, cm=0, a=None, b=None, key=None):
+    def iota(name, pat, base, cm=0, a=None, b=None, key=None, after=()):
         m = 1
         for s, c in pat:
             m *= c
         if SCRATCH[name][2] == I32:
             add("G", lambda q, T, X: q.iota(ap(name, a, b)(T), pat, base, cm), [], [name], ("gi", m))
         else:
-            add("G", lambda q, T, X: q.iota(ap(name, a, b)(T), pat, base, cm, allow_small_or_imprecise_dtypes=True), [], [key or name], ("gi", m))
+            add("G", lambda q, T, X: q.iota(ap(name, a, b)(T), pat, base, cm, allow_small_or_imprecise_dtypes=True), after, [key or name], ("gi", m))
 
     def ap(name, a=None, b=None, s=None):
         if a is None:
@@ -194,15 +189,22 @@ def build(p):
     def cs(name, src, s1, s2, o0, o1=None):
         rd = ["c_" + x for x in (src, s1, s2) if isinstance(x, str)]
         f = [C(x) if isinstance(x, str) else num(x) for x in (src, s1, s2)]
-        if name in p["e_cs"] and (o0, o1) in ((A.mult, None), (A.add, None), (A.mult, A.add)):
-            act(C(name), f[0], F.Identity, rd, ["c_" + name], 64, scale=f[1] if o0 == A.mult else None,
-                bias=f[1] if o0 == A.add else f[2] if o1 else None)
+        if (o0, o1) == (A.mult, A.add):
+            act(C(name), f[0], F.Identity, rd, ["c_" + name], 64, scale=f[1], bias=f[2])
         else:
             ts(C(name), f[0], f[1], f[2], o0, o1, rd, ["c_" + name], 64)
 
-    def scaled(name, src, v, at=0):
-        act(ap(name), ap(src, at, at + 128), F.Copy, [src] + (["c_" + v] if isinstance(v, str) else []), [name], 128,
-            scale=C(v) if isinstance(v, str) else num(v))
+    def scaled(name, src, v, w=None, at=0):
+        rd = [src] + ["c_" + x for x in (v, w) if isinstance(x, str)]
+        f = [C(x) if isinstance(x, str) else num(x) for x in (v, w)]
+        if w is None:
+            act(ap(name), ap(src, at, at + 128), F.Copy, rd, [name], 128, scale=f[0])
+        else:
+            ts(ap(name), ap(src, at, at + 128), f[0], f[1], A.mult, A.mult, rd, [name], 64)
+
+    def fill(name, v, a=None, b=None, s=None):
+        m = len(range(a, b, s)) if s else SCRATCH[name][1][1]
+        act(ap(name, a, b, s), ap("dw", 0, m), F.Identity, ["dw"], [name], m, scale=num(0.0), bias=num(v))
 
     def pay(c, s):
         return c * SW + 2 * n * s
@@ -214,23 +216,17 @@ def build(p):
     def struck(fl):
         return [(ap("ws", 128 * s, 128 * s + 128), x[0], ["ws%d" % s, x[1]], n) for s, x in enumerate(fl)]
 
-    def flag(out, z, t, rd, w, bk):
-        if p["sgn"]:
-            act(out, z, F.Sign, rd + ["thr"], w, n, bk, bias=ap("thr", t, t + 1))
-        else:
-            ts(out, z, ap("thr", t, t + 1), None, A.is_ge, None, rd + ["thr"], w, n, bk)
-
-    hf = 0.5 if p["sgn"] else 1.0
     TAB = ["tab%d" % i for i in range(4)]
     NEG = ["neg%d" % a for a in range(0, TW, p["negw"])]
 
     def setup():
         dma("Y", ap("posi"), ap("pos"), [], ["posi"], "lpos", 131072)
-        for i, (a, b) in enumerate(zip((0,) + p["lp"], p["lp"])):
-            dma("Y", ap("tab", 2048 * a, 2048 * b), ap("feat", 2048 * a, 2048 * b), [], TAB[a:b], "lf%d" % i, 131072 + 524288 * b)
-        dma("S", ap("uv", 0, 16), ap("u"), [], ["u"], "lu", 4096)
-        dma("S", ap("uv", 16, 32), ap("v"), [], ["v"], "lv", 4096)
-        dma("S", ap("stepi", 0, 1), ap("step"), [], ["stepi"], "lstep", 512)
+        for i in range(4):
+            a, b = 2048 * i + 128, 2048 * i + 2048
+            dma("Y", ap("tab", a, b), ap("feat", a, b), [], [TAB[i]], "lf%d" % i, 131072 + 491520 * (i + 1))
+            ms(ap("tab", a - 128, a), 0.0, ["tabz%d" % i])
+        for i, (x, src) in enumerate(((ap("uv", 0, 16), "u"), (ap("uv", 16, 32), "v"), (ap("stepi", 0, 1), "step"))):
+            dma(p["e_uv"], x, ap(src), [], [src], "l" + src, (2200000 + 80000 * i) * (p["e_uv"] == "Y"))
         iota("ci", [[1, 2]], 0, 1, 0, 2)
         iota("dw", [[1, 160]], -16)
         iota("cg", [[1, 8], [0, 16]], 0)
@@ -239,9 +235,6 @@ def build(p):
         iota("pw", [[1, 65], [0, 2]], 0)
         iota("d1b", [[512, 8], [0, 16]], -2048)
         iota("nb", [[0, 8], [-512, 8]], 2048)
-        iota("bs", [[0, 8], [512, 8]], -2048)
-        iota("cb", [[0, 8], [512, 8]], -2048 + int(OFS))
-        iota("c4", [[4, 16]], 0)
         iota("yb", [[0, 9 * n]], 0)
 
         for x in ("p", "p1"):
@@ -253,146 +246,130 @@ def build(p):
         cp(ap("col", 0, 7), ap("ci", 0, 7), ["ci"] + ["ci%d" % j for j in range(2, 7)], ["c_" + x for x in names], 64)
         ts(ap("eyew"), ap("dw", 0, 144), C("p"), None, A.is_equal, None, ["dw", "c_p"], ["eyew"], 72)
         ts(ap("blk"), ap("cg"), C("g"), None, A.is_equal, None, ["cg", "c_g"], ["blk"], 64)
-        ts(ap("gm"), ap("dw", 16, 24), C("g"), None, A.is_equal, None, ["dw", "c_g"], ["gm"], 64)
         cs("king", "k", 0.0, None, A.is_equal)
         cs("top", "k", 13.0, None, A.is_ge)
-        cs("m1", "top", -1.0, 1.0, A.mult, A.add)
-        cs("mid", "m1", "king", None, A.subtract)
+        cs("mid", "k", 1.0, "top", A.is_ge, A.subtract)
         cs("s1", "g", -8.0, "ph", A.mult, A.add)
-        cs("o32", "od", 32.0, None, A.mult)
-        cs("b0", "k", -12.0, 32.0, A.add, A.mult)
-        cs("b1", "b0", "o32", 128.0, A.max, A.add)
-        cs("b2", "king", -1.0e6, "b1", A.mult, A.add)
-        cs("big", "mid", 1.0e6, None, A.mult)
+        cs("o8", "od", 8.0, 32.0, A.mult, A.add)
+        cs("b0", "k", 8.0, -64.0, A.mult, A.add)
+        cs("b1", "king", -1.0e6, 0.0, A.mult, A.add)
+        cs("b2", "b0", "o8", "b1", A.max, A.add)
+        cs("big", "mid", 1.0e6, 0.0, A.mult, A.add)
         ts(ap("gt"), ap("it"), C("s1"), C("big"), A.is_lt, A.mult, ["it", "c_s1", "c_big"], ["gt"], 64)
-        if p["sgn"]:
-            cs("b3", "b2", -1.0, 0.5, A.mult, A.add)
-            ts(ap("thr"), ap("gt"), num(-1.0), C("b3"), A.mult, A.add, ["gt", "c_b3"], ["thr"], 64)
-        else:
-            ts(ap("thr"), ap("gt"), C("b2"), None, A.add, None, ["gt", "c_b2"], ["thr"], 64)
-        cs("top0", "king", 3.0 * p["sgn"], "top", A.mult, A.add)
-        scaled("eye2", "eyew", 2.0, 16)
-        cs("king2", "king", 2.0, None, A.mult)
-        scaled("selk2", "blk", "king2")
-        cs("ab", "top0", 2048.0 * hf, None, A.mult)
-        scaled("wb", "blk", "ab")
+        act(ap("thr"), ap("gt"), F.Identity, ["gt", "c_b2"], ["thr"], 64, bias=C("b2"))
+        scaled("eye2", "eyew", 2.0, at=16)
+        scaled("bmq", "blk", -0.25)
+        scaled("bmh", "blk", 0.5)
+        scaled("selh", "bmh", "king")
+        scaled("wb", "blk", "top", 2048.0)
 
-        ts(ap("ki"), ap("posi"), num(1920), None, A.bitwise_and, None, ["posi"], ["ki"], 256)
         ts(ap("si"), ap("posi"), num(127), None, A.bitwise_and, None, ["posi"], ["si"], 256)
         ts(ap("dd"), ap("posi"), num(0.0), num(GONE), A.is_equal, A.mult, ["posi"], ["dd"], 256)
         ts(ap("sq"), ap("si"), num(0.5), num(64.0), A.mult, A.add, ["si"], ["sq"], 256)
+        ts(ap("ki"), ap("posi"), num(1920), None, A.bitwise_and, None, ["posi"], ["ki"], 256)
         ts(ap("kall", 0, LN), ap("ki"), num(-128.0), None, A.add, None, ["ki"], ["kall0"], 256)
         for c in range(NCH):
-            S0 = ap("sin", pay(c, 0), pay(c, 0) + n)
-            tt(S0, ap("sq", c * n, c * n + n), ap("dd", c * n, c * n + n), A.add, ["sq", "dd"], ["sinS%d_0" % c], 2 * n)
-            copy("S", ap("kall", LN + c * n, LN + c * n + n), S0, ["sinS%d_0" % c], ["sall%d" % c], n)
+            S0, sk, z = ap("sin", pay(c, 0), pay(c, 0) + n), "sinS%d_0" % c, ap("pb%d" % (2 * c), 0, n)
+            group(z, "z0%d" % c, 2 * c, [mat("eye", ap(x, c * n, c * n + n), [x]) for x in ("dd", "sq")])
+            copy("S", S0, z, ["z0%d" % c], [sk], n, 2 * c)
+            group(z, "z0%d" % c, 2 * c, [mat("selh", ap("sq", c * n, c * n + n), ["sq"])])
+            M, mk = flags("sin", c, 0)
+            ts(M, z, ap("thr", 0, 1), None, A.is_ge, None, ["z0%d" % c, "thr"], [mk], n, 2 * c)
 
-        kw = LN if p["sfirst"] else 2 * LN
-        sall = ["sall%d" % c for c in range(NCH)]
-        if p["sfirst"]:
-            add("G", lambda q, T, X: q.remote_dma(T["kall"][:, 7 * LN:8 * LN], T["kall"][:, LN:2 * LN], T.sem["sarr"], T.sem["sent"], X["addr"][3][1],
-                                                  X["addr"][3][0], X["mask"]), sall, ["ssent"], ("r", 0), None, "sent")
-            lands(["ssent"], ["snext"], "sarr", p["klat"])
+        def sendm(q, T, X):
+            return q.remote_dma_fused([RemoteDMATransfer(
+                dst_ids=[DstId(rid=X["addr"][NR - 1][0], pnc=X["addr"][NR - 1][1])], dma_engine_mask=X["parts"][c], remote_sem=T.sem["marr"],
+                srcs=[flags("sin", c, 0)[0](T)], dsts=[flags("sout", c, 0)[0](T)]) for c in range(NCH)], local_sem=T.sem["sent"])
+        add("G", sendm, [flags("sin", c, 0)[1] for c in range(NCH)], ["msent"], ("r", 0), None, "sent")
+        lands(["msent"], [flags("sout", c, 0)[1] for c in range(NCH)], "marr", p["klat"])
 
         def sendk(q, T, X):
             tr = RemoteDMATransfer(dst_ids=[DstId(rid=X["addr"][j][0], pnc=X["addr"][j][1]) for j in range(1, NR)],
-                                   dma_engine_mask=X["mask"], remote_sem=T.sem["karr"], srcs=[T["kall"][:, 0:kw]],
-                                   dsts=[T["kall"][:, j * 2 * LN:j * 2 * LN + kw] for j in range(1, NR)])
+                                   dma_engine_mask=X["mask"], remote_sem=T.sem["karr"], srcs=[T["kall"][:, 0:LN]],
+                                   dsts=[T["kall"][:, j * LN:(j + 1) * LN] for j in range(1, NR)])
             return q.remote_dma_fused([tr], local_sem=T.sem["sent"])
-        add("G", sendk, ["kall0", "ssent"] + sall + TAB[:p["klate"]], ["ksent"], ("r", 0), None, "sent")
-        lands(["ksent"], ["kall%d" % j for j in range(1, NR)] + ["snext"] * (1 - p["sfirst"]), "karr", p["klat"] * (1 - 0.8 * p["sfirst"]), NR - 1)
+        add("G", sendk, ["kall0", "msent"] + TAB, ["ksent"], ("r", 0), None, "sent")
+        lands(["ksent"], ["kall%d" % j for j in range(1, NR)], "karr", 0.6, NR - 1)
 
         ms(ap("du", 0, 32, 16), 0.0, ["duz"])
         for i, x in enumerate("uv"):
             tt(ap("du", 16 * i + 1, 16 * i + 16), ap("uv", 16 * i, 16 * i + 15), ap("uv", 16 * i + 1, 16 * i + 16), A.subtract, [x], ["du" + x], 64)
-            for gi in range(8):
-                o = 128 * i + 16 * gi
-                act(ap("uu", o, o + 16), ap("du", 16 * i, 16 * i + 16), F.Copy, ["duz", "du" + x, "gm"], ["uu%d" % (8 * i + gi)], 64,
-                    scale=ap("gm", gi, gi + 1))
-        ms(ap("xb", 15, 2 * NCH * XW, 2 * XW if p["one"] else XW), 0.0, ["xp"])
+            group(None, "z" + x, 7, [mat("eye", ap("du", 16 * i, 16 * i + 16), ["duz", "du" + x]) + (ap("pb7", 256 + 16 * j, 272 + 16 * j),)
+                                     for j in range(8)])
+            tt(ap("uu", 128 * i, 128 * i + 128), ap("pb7", 256, 384), ap("blk"), A.mult, ["z" + x, "blk"], ["uu" + x], 128, 7)
+        ms(ap("xb", 15, NCH * XW, XW), 0.0, ["xp"])
         ms(ap("tq", 128, NCH * 144, 144), 0.0, ["tqp"])
         cs("pk", "king", -2.0 ** 22, -2.0 ** -71, A.mult, A.add)
-        scaled("pa", "eyew", "pk", 16)
-        scaled("pz", "eyew", 2.0 ** -71, 15)
+        scaled("pa", "eyew", "pk", at=16)
+        scaled("pz", "eyew", 2.0 ** -71, at=15)
         tt(ap("pen"), ap("pa"), ap("pz"), A.add, ["pa", "pz"], ["pen"], 256)
         scaled("rt", "km", -1.0 / 16)
-        ms(ap("eps"), 1.0 / 16, ["eps"])
-        ms(ap("eps", 15, 128, 16), -14.0 / 16, ["eps"])
-        scaled("ee", "eyew", -LOST, 16)
-        scaled("ee2", "eyew", LOST, 16)
-        cs("b15", "k", 15.0, -LOST * 15 / 16, A.is_equal, A.mult)
-        cp(C("step"), ap("stepi", 0, 1), ["stepi"], ["c_step"], 64)
+        fill("eps", 1.0 / 16)
+        fill("eps", -14.0 / 16, 15, 128, 16)
+        scaled("down", "eyew", -BIG, at=16)
+        scaled("up", "eyew", BIG, at=16)
+        cs("b15", "k", 15.0, -BIG * 15 / 16, A.is_equal, A.mult)
+        cp(C("step"), ap("stepi", 0, 1), ["step"], ["c_step"], 64)
         cs("st", "step", "b15", 128.0, A.add, A.add)
-        scaled("nhalf", "eyew", -0.5, 16)
-        cs("nking", "king", -1.0, None, A.mult)
-        scaled("nselk", "blk", "nking")
-        scaled("bmq", "blk", -0.25)
-        scaled("bmh", "blk", 0.5)
-        ms(ap("one"), 1.0, ["one"])
-        ms(ap("cp"), 1.5 * 2.0 ** 22, ["cp"])
-        scaled("cn", "cp", -1.0)
-        cs("gone", "k", 1.0, GONE, A.is_ge, A.mult)
-        scaled("gd", "eyew", "gone", 16)
+        scaled("neye", "eyew", -1.0, at=16)
+        scaled("selq", "bmq", "king")
+        fill("one", 1.0)
+        fill("cp", 1.5 * 2.0 ** 22)
+        fill("cn", -1.5 * 2.0 ** 22)
+        cs("rest", "king", -2 * GONE, 2 * GONE, A.mult, A.add)
+        scaled("gd", "eyew", "rest", at=16)
         cp(ap("eyeh"), ap("eyew", 16, 144), ["eyew"], ["eyeh"], 64)
 
-        for i in range(p["nd"]):
-            o, x = i * 32 * n, ["d1o%d" % i, "d1n%d" % i]
-            if p["e_d1"][i] == "D":
-                dma("Y", ap("d1", o, o + 32 * n), ap("d1", 0, 32 * n), ["d1o0", "d1n0"] + TAB, x, "ld%d" % i, 524288)
-            else:
-                for h in range(2):
-                    iota("d1", [[0, 4], [512, 8], [0, 32]] if p["one"] else [[0, 8], [512, 8], [0, 16]], -2048, 0, o + 16 * n * h, o + 16 * n * (h + 1),
-                         x[h])
-        if p["one"]:
-            for a in range(0, TW, p["negw"]):
-                e = p["neg"][a // 2048]
-                copy(e, ap("tab", TW + a, TW + a + p["negw"]), ap("tab", a, a + p["negw"]), [TAB[a // 2048]], ["neg%d" % a],
-                     p["negw"] // (2 if e == "V" else 1), neg=True)
-        for c in range(NCH):
-            act(ap("hl", c * HS, c * HS + n), ap("bs"), F.Copy, ["bs"], ["hl%d_0" % c], n, scale=num(0.0))
-            act(ap("ha", c * HS, c * HS + n), ap("bs"), F.Identity, ["bs"], ["ha%d_0" % c], n, scale=num(0.0), bias=num(-OFS))
+        iota("bs", [[0, 8], [512, 8]], -2048)
+        iota("cb", [[0, 8], [512, 8]], -2048 + int(OFS))
+        for h in range(2):
+            iota("d1", [[0, 4], [512, 8], [0, 32]], -2048, 0, 16 * n * h, 16 * n * (h + 1), "d1_0" + "ab"[h], [("msent", "ksent")[h]])
+        for i in range(1, p["nd"]):
+            dma("Y", ap("d1", 32 * n * i, 32 * n * (i + 1)), ap("d1", 0, 32 * n), ["d1_0a", "d1_0b"], ["d1_%da" % i, "d1_%db" % i], "ld%d" % i, 524288)
+        for a in range(0, TW, p["negw"]):
+            e = p["neg"][a // 2048]
+            copy(e, ap("tab", TW + a, TW + a + p["negw"]), ap("tab", a, a + p["negw"]), [TAB[a // 2048], "tabz%d" % (a // 2048)], ["neg%d" % a],
+                 p["negw"] // (2 if e == "V" else 1), by=-1.0)
         cs("sg", "od", -2.0, 1.0, A.mult, A.add)
-        cs("sgm", "sg", "mid", None, A.mult)
-        cs("sgh", "sgm", hf, None, A.mult)
-        cs("m2", "mid", -1.0, 1.0, A.mult, A.add)
-        cs("af", "s1", float(n), None, A.mult)
-        cs("apx", "af", "sgm", hf, A.mult, A.mult)
-        cs("t32", "top0", -32.0 * hf, None, A.mult)
-        cs("aw", "sgm", -256.0 * hf, "t32", A.mult, A.add)
+        cs("sgm", "sg", "mid", 0.0, A.mult, A.add)
+        cs("af", "s1", float(n), 0.0, A.mult, A.add)
+        cs("t8", "top", -8.0, 0.0, A.mult, A.add)
+        cs("aw", "sgm", -64.0, "t8", A.mult, A.add)
         cs("q0", "s1", -1.0, 1.0, A.mult, A.add)
-        cs("q2", "q0", "m2", "ph", A.mult, A.add)
-        ts(ap("cmp"), ap("it"), C("m2"), C("q2"), A.mult, A.add, ["it", "c_m2", "c_q2"], ["cmp"], 64)
-        scaled("wp", "blk", "apx")
+        cs("q2", "q0", "top", "ph", A.mult, A.add)
+        act(ap("cmp"), ap("it"), F.Identity, ["it", "c_top", "c_q2"], ["cmp"], 64, scale=C("top"), bias=C("q2"))
+        scaled("wp", "blk", "af", "sgm")
         for s in range(RO):
             ts(ap("ws", 128 * s, 128 * s + 128), ap("pw", 1, 129), ap("cmp", s, s + 1), C("aw"), A.is_equal, A.mult, ["pw", "cmp", "c_aw"],
                ["ws%d" % s], 64)
-        cs("s0", "s1", -1.0, None, A.add)
-        ts(ap("wc", 0, 8), ap("it"), C("s0"), C("sgh"), A.is_equal, A.mult, ["it", "c_s0", "c_sgh"], ["wc0"], 64)
-        ts(ap("wc", 8, 16), ap("wc", 0, 8), C("king"), num(-DEAD), A.subtract, A.mult, ["wc0", "c_king"], ["wc"], 64)
+        cs("s0", "s1", 1.0, -1.0, A.mult, A.add)
+        cs("kb", "king", -BIG, 0.0, A.mult, A.add)
+        ts(ap("wc", 0, 8), ap("it"), C("s0"), C("sgm"), A.is_equal, A.mult, ["it", "c_s0", "c_sgm"], ["wc0"], 64)
+        act(ap("wc", 8, 16), ap("wc", 0, 8), F.Identity, ["wc0", "c_kb"], ["wc"], 64, scale=num(BIG), bias=C("kb"))
         for s in range(max(p["sel"], p["sela"])):
             act(ap("wm", 128 * s, 128 * s + 128), ap("blk"), F.Copy, ["blk", "wc"], ["wm%d" % s], 128, scale=ap("wc", 8 + s, 9 + s))
-        for t in range(2, p["sel"] + 1):
-            ms(ap("rm", RM[t], RM[t] + t * n), 1.0, ["rm%d" % t], t * n // 2)
-            ms(ap("rm", RM[t], RM[t] + t * n, t), 0.0, ["rm%d" % t])
-        ms(ap("rs"), 0.0, ["rs"])
-        ms(ap("rs", 0, n, 16), -2.0 ** 30, ["rs"])
-        ts(ap("tmp"), ap("km", 0, n), C("k"), num(DEAD), A.not_equal, A.mult, ["km", "c_k"], ["tmp"], 64)
+        ts(ap("tmp"), ap("km", 0, n), C("k"), num(-BIG), A.not_equal, A.mult, ["km", "c_k"], ["tmp"], 64)
         tt(ap("cd"), ap("tmp"), ap("dw", 16, 16 + n), A.add, ["tmp", "dw"], ["cd"], 128)
-        scaled("n16", "eyew", -DEAD, 16)
-        scaled("neye", "eyew", -1.0, 16)
-        if p["jp"] == 2:
-            scaled("n24", "eyew", TW - DEAD, 16)
+        scaled("upt", "eyew", TW + BIG, at=16)
         if p["eq1"]:
-            scaled("m16", "eyew", DEAD, 16)
-            scaled("neye2", "eyew", -2.0, 16)
+            scaled("neye2", "eyew", -2.0, at=16)
         cs("g16o", "g", 16.0, "od", A.mult, A.add)
         cs("c0", "big", -1.0, 1.0e6, A.mult, A.add)
-        cs("cf0", "c0", "o32", None, A.subtract)
-        cs("cf1", "cf0", -64.0, None, A.add)
+        cs("cf0", "od", -8.0, "c0", A.mult, A.add)
+        cs("cf1", "cf0", 1.0, -16.0, A.mult, A.add)
         ts(ap("wfw"), ap("dw", 0, 144), C("g16o"), C("af"), A.is_equal, A.mult, ["dw", "c_g16o", "c_af"], ["wfw"], 72)
 
+    def patterns(t, c, after):
+        if t == 1:
+            iota("hl", [[0, n]], 0, 0, c * HS, c * HS + n, "hl%d_0" % c, after)
+            iota("ha", [[0, n]], -int(OFS), 0, c * HS, c * HS + n, "ha%d_0" % c, after)
+        if c == NCH - 1 and t + 2 <= p["sel"]:
+            iota("rm", [[0, n], [4096, t + 2]], 0, 0, RM[t + 2], RM[t + 2] + (t + 2) * n, "rm%d" % (t + 2), after)
+        if (t, c) == (0, NCH - 1):
+            iota("rs", [[0, 4], [4096, 16]], 0, after=after)
+            iota("c4", [[4, 16]], 0, after=after)
+
     nc = n // 16
-    uses = [0]
 
     def ply(t, c):
         ba, bb = 2 * c, 2 * c + 1
@@ -401,11 +378,7 @@ def build(p):
         o = pay(c, t)
         S, sk = ap("sin", o, o + n), "sinS%d_%d" % (c, t)
         M, mk = flags("sin", c, t)
-
-        def kinds(s):
-            a = s % NR * 2 * LN + cn
-            return ap("kall", a, a + n), "kall%d" % (s % NR)
-        K, kk = kinds(t)
+        K, kk = ap("kall", t % NR * LN + cn, t % NR * LN + cn + n), "kall%d" % (t % NR)
 
         def k(x):
             return "%s%d" % (x, c)
@@ -415,182 +388,118 @@ def build(p):
 
         def on(name, x):
             return mat(name, loc(x), [k(x)])
+
+        def lists(s):
+            return mat("eyeh", ap("hh", h0 + (s + 1) * n, h0 + (s + 2) * n), ["hh%d_%d" % (c, s + 1)])
+
+        def mask(s):
+            return (ap("wm", 128 * s, 128 * s + 128), M, ["wm%d" % s, mk], n)
+
+        def slot():
+            group(ap(pa, 0, n), k("pt"), ba, [mat("eye", ap("cd"), ["cd"]), mat("wp", M, [mk])])
+            scan(loc("dg"), ap("rs"), ap(pa, 0, n), 0.0, A.min, A.max, ["rs", k("pt")], [k("dg")], n, ba)
+            cp(ap("poff", 16 * c, 16 * c + nc), ap("dg", cn + 15, cn + n, 16), [k("dg")], [k("poff")], 64)
         HL = ["hl%d_%d" % (c, s) for s in range(t + 1)]
         HA = ["ha%d_%d" % (c, s) for s in range(t + 1)]
-        Lh, lk = ap("hl", h0 + (t + 1) * n, h0 + (t + 2) * n), "hl%d_%d" % (c, t + 1)
         KS = [mat("eye", K, [kk]), mat("eye2", S, [sk])]
-        if t <= p["m1r"]:
-            z = ap(pa, 384, 384 + n)
-            group(z, k("z0"), ba, struck([flags("sin", c, s) for s in range(t)]) + [mat("selk2", S, [sk])])
-            flag(M, z, t, [k("z0")], [mk], ba)
-        L, PL = ap(pb, 0, n), ap(pb, n, 2 * n)
+        L = ap(pb, 0, n)
         group(L, k("L"), bb, KS)
-        if p["h16"]:
-            Lf, lf = ap("hh", h0 + (t + 1) * n, h0 + (t + 2) * n), "hh%d_%d" % (c, t + 1)
-            relu("V", Lf, L, [k("L")], [lf], n, bb)
-            copy("G", Lh, Lf, [lf], [lk], n)
+        Lf, lf = ap("hh", h0 + (t + 1) * n, h0 + (t + 2) * n), "hh%d_%d" % (c, t + 1)
+        relu("V", Lf, L, [k("L")], [lf], n, bb)
+        if t == RO - 1:
+            copy("G", ap("hl", h0 + (t + 1) * n, h0 + (t + 2) * n), Lf, [lf], ["hl%d_%d" % (c, t + 1)], n)
+        par = (t * NCH + c) % p["nd"]
+        d0, do, dn = par * 32 * n, "d1_%da" % par, "d1_%db" % par
+        bucket = mat("wb", M, [mk])
+        PO, PL = ap(pa, 5 * n, 7 * n, 2), ap(pa, 5 * n + 1, 7 * n, 2)
+        if t == 0:
+            group(ap(pa, 0, n), k("po"), ba, KS + [bucket])
+            ts(ap("off", 2 * cn, 2 * cn + n), ap(pa, 0, n), num(0.0), None, A.max, None, [k("po")], [k("off")], n, ba)
+        elif t == 1 and p["eq1"]:
+            group(ap(pa, 0, n), k("pt"), ba, [lists(0), mat("neye", K, [kk]), mat("neye2", S, [sk]), mask(0)])
+            ts(loc("ne"), ap(pa, 0, n), num(0.0), None, A.is_equal, None, [k("pt")], [k("ne")], n, ba)
+            group(None, k("po"), ba, [x + (PL,) for x in KS + [bucket]] + [x + (PO,) for x in (lists(0), mask(0), bucket)]
+                  + [on("down", "ne") + (PO,), on("down", "ne") + (PL,)])
+            for i in range(2):
+                ts(ap("off", 2 * cn + i, 2 * cn + 2 * n, 2), (PO, PL)[i], num(float(TW - TW * i)), num(0.0), A.add, A.max, [k("po")],
+                   [k(("off", "offn")[i])], n, ba)
         else:
-            Lf, lf = Lh, lk
-        late_l = t and not p["h16"] and (t <= p["sel"] or p["nep"])
-        if not p["h16"] and not late_l:
-            relu(p["e_lh"], Lh, L, [k("L")], [lk], n, bb)
-        one = p["one"] and t > 0
-        oo, on_, st = (2 * cn, 2 * cn + 1, 2) if one else (2 * cn, 2 * cn + n, 1)
-        par = uses[0] % p["nd"]
-        d0 = par * 32 * n
-        do, dn = "d1o%d" % par, "d1n%d" % par
-        if t:
-            uses[0] += 1
             og = loc("og")
-            pick, picka = t <= p["sel"], t <= p["sela"]
-
-            def mask(s):
-                return (ap("wm", 128 * s, 128 * s + 128), M, ["wm%d" % s, mk], n)
-
-            def slot():
-                group(ap(pa, 0, n), k("pt"), ba, [mat("eye", ap("cd"), ["cd"]), mat("wp", M, [mk])])
-                scan(loc("dg"), ap("rs"), ap(pa, 0, n), 0.0, A.add, A.max, ["rs", k("pt")], [k("dg")], n, ba)
-                cp(ap("poff", 16 * c, 16 * c + nc), ap("dg", cn + 15, cn + n, 16), [k("dg")], [k("poff")], 64)
-            eq1 = t == 1 and p["eq1"]
-            if eq1:
-                old = [mat("eye2", ap("sin", pay(c, 0), pay(c, 0) + n), ["sinS%d_0" % c]), mat("eye", kinds(0)[0], [kinds(0)[1]])]
-                group(ap(pa, 0, n), k("pt"), ba, old + [mat("neye", K, [kk]), mat("neye2", S, [sk]), mask(0)])
-                ts(loc("ne"), ap(pa, 0, n), num(0.0), None, A.is_equal, None, [k("pt")], [k("ne")], n, ba)
-            elif pick:
-                terms = []
-                for s in range(t):
-                    z = ap(pa, s, t * n, t)
-                    if p["h16"]:
-                        terms += [mat("eyeh", ap("hh", h0 + (s + 1) * n, h0 + (s + 2) * n), ["hh%d_%d" % (c, s + 1)]) + (z,)]
-                    else:
-                        terms += [mat("eye", kinds(s)[0], [kinds(s)[1]]) + (z,),
-                                  mat("eye2", ap("sin", pay(c, s), pay(c, s) + n), ["sinS%d_%d" % (c, s)]) + (z,)]
-                group(None, k("pt"), ba, terms + [mask(s) + (ap(pa, s, t * n, t),) for s in range(t)])
+            if t <= p["sel"]:
+                group(None, k("pt"), ba, [x(s) + (ap(pa, s, t * n, t),) for x in (lists, mask) for s in range(t)])
                 if t == 1:
                     relu("V", og, ap(pa, 0, n), [k("pt")], [k("og")], n, ba)
                 else:
                     a = 5 * cn
-                    scan(ap("ogs", a, a + t * n), ap("rm", RM[t], RM[t] + t * n), ap(pa, 0, t * n), 0.0, A.mult, A.max, ["rm%d" % t, k("pt")],
+                    scan(ap("ogs", a, a + t * n), ap("rm", RM[t], RM[t] + t * n), ap(pa, 0, t * n), 0.0, A.min, A.max, ["rm%d" % t, k("pt")],
                          [k("og")], t * n, ba)
                     og = ap("ogs", a + t - 1, a + t * n, t)
                 tt(loc("ne"), og, L, A.not_equal, [k("og"), k("L")], [k("ne")], n, bb)
             else:
                 slot()
                 src = ind("hl", h0, h0 + t * n + n, "poff", 16 * c, 16 * c + nc)
-                copy(p["e_og"], og, src, HL + [k("poff")], [k("og")], n, gather=True)
+                copy("V", og, src, HL + [k("poff")], [k("og")], n, gather=True)
                 if p["nep"]:
                     tt(loc("ne"), og, L, A.not_equal, [k("og"), k("L")], [k("ne")], n, bb)
                 else:
                     tt(loc("ne"), src, Lf, A.not_equal, HL + [k("poff"), lf], [k("ne")], n, kind="gv")
-            if late_l and p["jp"]:
-                relu(p["e_lh"], Lh, L, [k("L")], [lk], n, bb)
-            PO = ap(pa, 5 * n, 6 * n)
-            new = ([mat("eyeh", Lf, [lf])] if p["h16"] else KS) + [mat("wb", M, [mk])]
-            both = one and p["jp"] == 2 and not eq1
-            old = old + [mask(0), mat("wb", M, [mk])] if eq1 else [mat("wb", M, [mk]), mat("eyeh", og, [k("og")])]
-            same, dead = ("m16", 0.0) if eq1 else ("n16", DEAD)
-            if p["jp"]:
-                PO, PL = (ap(pa, 5 * n, 7 * n, 2), ap(pa, 5 * n + 1, 7 * n, 2)) if both else (PO, ap(pa, 6 * n, 7 * n))
-                group(None, k("po"), ba, [x + (PL,) for x in new] + [x + (PO,) for x in old]
-                      + [on("n24" if both else same, "ne") + (PO,), on(same, "ne") + (PL,)])
-            else:
-                group(PO, k("po"), ba, old + [on(same, "ne")])
-                group(PL, k("pl"), bb, new + [on(same, "ne")])
-            if both:
-                ts(ap("off", oo, oo + 2 * n), ap(pa, 5 * n, 7 * n), num(DEAD), num(0.0), A.add, A.max, [k("po")], [k("offo"), k("offn")], 2 * n, ba)
-            else:
-                ts(ap("off", oo, oo + st * n, st), PO, num(dead + (TW if one else 0)), num(0.0), A.add, A.max, [k("po")], [k("offo")], n, ba)
-                ts(ap("off", on_, 2 * cn + 2 * n, st), PL, num(dead), num(0.0), A.add, A.max, [k("po" if p["jp"] else "pl")], [k("offn")], n,
-                   ba if p["jp"] else bb)
-            if late_l and not p["jp"]:
-                relu(p["e_lh"], Lh, L, [k("L")], [lk], n, bb)
-            start = ap("d1", d0, d0 + 32 * n, 32) if one else ap("d1", d0, d0 + 16 * n, 16)
-            if picka:
-                bk = bb if p["jp"] else ba
-                terms = [[mat("eye", ap("ha", h0 + (s + 1) * n, h0 + (s + 2) * n), [HA[s + 1]]), mat("eye", ap("cb"), ["cb"]), mask(s)]
-                         for s in range(t)]
-                group(None, k("za"), bk, [x + (ap("pb%d" % bk, (s + 2) * n, (s + 3) * n),) for s in range(t) for x in terms[s]])
-                acc, ak = ap("bs"), "bs"
-                for s in range(t):
-                    out, ok = (start, do) if s == t - 1 else (ap("acc", 2 * cn + s % 2 * n, 2 * cn + s % 2 * n + n), k("acc%d_" % (s % 2)))
-                    tt(out, ap("pb%d" % bk, (s + 2) * n, (s + 3) * n), acc, A.max, [k("za"), ak] + [dn] * one, [ok], n, bk)
-                    acc, ak = out, ok
-            else:
-                if pick:
-                    slot()
-                tt(start, ind("ha", h0, h0 + (t + 1) * n, "poff", 16 * c, 16 * c + nc), ap("cb"), A.add, HA + [k("poff"), "cb"] + [dn] * one, [do], n,
-                   kind="gv")
-        else:
-            on_ = 2 * cn + n
-            group(PL, k("pl"), bb, KS + [mat("wb", M, [mk])])
-            ts(ap("off", on_, on_ + n), PL, num(0.0), None, A.max, None, [k("pl")], [k("offn"), k("offo")], n, bb)
-        if t == p["m1r"]:
-            a = 3 * 2 * LN + LN + cn
-            kings = [(ap("kall", a, a + n), "snext"), (ap("sout", pay(c, 1), pay(c, 1) + n), "su%d_1" % c)]
-            for s in range(t + 1):
-                fl = [flags("sout", c, i) for i in range(s + 1)]
-                group(ap(pb, 448, 448 + n), k("l0"), bb, struck(fl[:s]) + [mat("selk2", kings[s][0], [kings[s][1]])])
-                flag(fl[s][0], ap(pb, 448, 448 + n), s, [k("l0")], [fl[s][1]], bb)
-        s0 = 32 * cn
-        SO = ["so%d_%d" % (c, i) for i in range(8)]
-
-        def phase(x, x0, m, col, keys, cut, d1, dk, a0, neg, win):
-            XK = ["%s%d_%d" % (x, c, i) for i in range(m * n // 2)]
-            a = 0
-            for e, b in zip(cut[0::2], cut[1::2]):
-                copy(e, ap("xb", x0 + 16 * a, x0 + 16 * b), ind("tab", 0, win, "off", col + a, col + b), TAB + keys, XK[a // 2:b // 2],
-                     16 * (b - a), gather=True, neg=neg)
-                a = b
-            w = 128 * m
-            for i in range(8):
-                a = w * i
-                scan(ap("so", s0 + a, s0 + a + w), ap("xb", x0 + a - 1, x0 + a + w - 1), ap(d1, a0 + a, a0 + a + w) if t else ap(d1), -4096.0, A.add, A.max,
-                     XK[max(0, 4 * m * i - 1):4 * m * (i + 1)] + dk + ["xp"], [SO[i]], w // 2)
-            return [mat("eye", ap("xb", x0 + 16 * m - 1, x0 + 16 * m * n, 16 * m), XK),
-                    mat("eyeh", ap("so", s0 + 16 * m - 1, s0 + 16 * m * n, 16 * m), SO)]
-        xo, xn = 2 * c * XW + 16, (2 * c + 1) * XW + 16
-        if one:
-            fin = phase("xn", xo, 2, oo, [k("offo"), k("offn")] + NEG, p.get("cut%d" % t, p["cut"]), "d1", [do, dn], d0, False, 2 * TW)
+            group(None, k("po"), ba, [x + (PL,) for x in (lists(t), bucket)] + [x + (PO,) for x in (bucket, mat("eyeh", og, [k("og")]))]
+                  + [on("upt", "ne") + (PO,), on("up", "ne") + (PL,)])
+            ts(ap("off", 2 * cn, 2 * cn + 2 * n), ap(pa, 5 * n, 7 * n), num(-BIG), num(0.0), A.add, A.max, [k("po")], [k("off"), k("offn")], 2 * n, ba)
+        start = ap("d1", d0, d0 + 32 * n, 32)
+        if 0 < t <= p["sela"]:
+            terms = [[mat("eye", ap("ha", h0 + (s + 1) * n, h0 + (s + 2) * n), [HA[s + 1]]), mat("eye", ap("cb"), ["cb"]), mask(s)] for s in range(t)]
+            group(None, k("za"), bb, [x + (ap(pb, (s + 2) * n, (s + 3) * n),) for s in range(t) for x in terms[s]])
+            acc, ak = ap("bs"), "bs"
+            for s in range(t):
+                out, ok = (start, do) if s == t - 1 else (ap("acc", 2 * cn + s % 2 * n, 2 * cn + s % 2 * n + n), k("acc%d_" % (s % 2)))
+                tt(out, ap(pb, (s + 2) * n, (s + 3) * n), acc, A.max, [k("za"), ak, dn], [ok], n, bb)
+                acc, ak = out, ok
         elif t:
-            z = ap(pa, 3 * n, 4 * n)
-            group(z, k("zj"), ba, phase("xo", xo, 1, oo, [k("offo")], p["cuto"], "d1", [do], d0, True, TW))
-            tt(ap("d1", d0 + 16 * n, d0 + 32 * n, 16), z, ap("bs"), A.max, [k("zj"), "bs"], [dn], n, ba)
-            fin = phase("xn", xn, 1, on_, [k("offn")], p["cutn"], "d1", [dn], d0 + 16 * n, False, TW)
-        else:
-            fin = phase("xn", xo if p["one"] else xn, 1, on_, [k("offn")], p.get("cut0_%d" % c, p["cut0"]), "d1b", ["d1b"], 0, False, TW)
+            if t <= p["sel"]:
+                slot()
+            tt(start, ind("ha", h0, h0 + (t + 1) * n, "poff", 16 * c, 16 * c + nc), ap("cb"), A.add, HA + [k("poff"), "cb", dn], [do], n, kind="gv")
+        m = 2 if t else 1
+        x0, s0, w = c * XW + 16, 32 * cn, 128 * m
+        SO = ["so%d_%d" % (c, i) for i in range(8)]
+        XK = ["x%d_%d" % (c, i) for i in range(m * n // 2)]
+        cut = p.get("cut%d_%d" % (t, c), p.get("cut%d" % t, p["cut"]))
+        for e, a, b in zip(cut[0::2], (0,) + cut[1::2], cut[1::2]):
+            copy(e, ap("xb", x0 + 16 * a, x0 + 16 * b), ind("tab", 0, m * TW, "off", 2 * cn + a, 2 * cn + b),
+                 TAB + [k("off"), k("offn")] + (NEG if t else ["tabz%d" % i for i in range(4)]), XK[a // 2:b // 2], 16 * (b - a), gather=True)
+        for i in range(8):
+            a = w * i
+            scan(ap("so", s0 + a, s0 + a + w), ap("xb", x0 + a - 1, x0 + a + w - 1), ap("d1", d0 + a, d0 + a + w) if t else ap("d1b"), -4096.0,
+                 A.add, A.max, XK[max(0, 4 * m * i - 1):4 * m * (i + 1)] + ([do, dn] if t else ["d1b"]) + ["xp"], [SO[i]], w // 2)
         if t == RO - 1:
             final(c, bb)
             outs(c, "yc", "hl", p["e_yc"], 0.0)
         z = ap(pa, 4 * n, 5 * n)
-        group(z, k("zf"), ba, [mat("eye", ap("nb"), ["nb"])] + fin)
+        group(z, k("zf"), ba, [mat("eye", ap("nb"), ["nb"]), mat("eye", ap("xb", x0 + 16 * m - 1, x0 + 16 * m * n, 16 * m), XK),
+                               mat("eyeh", ap("so", s0 + 16 * m - 1, s0 + 16 * m * n, 16 * m), SO)])
         ts(ap("yb", 2 * cn + n, 2 * cn + 2 * n), z, num(0.0), num(127.0), A.max, A.min, [k("zf"), "yb"], [k("yb")], n, ba)
-        Ah, ak = ap("ha", h0 + (t + 1) * n, h0 + (t + 2) * n), "ha%d_%d" % (c, t + 1)
-        if p["sela"] == RO - 1 and p["e_ha"] == "S":
-            act(Ah, z, F.Identity, [k("zf")], [ak], n, ba, bias=num(-OFS))
-        else:
-            ts(Ah, z, num(0.0), num(-OFS), A.max, A.add, [k("zf")], [ak], n, ba)
-        wk = ["uu%d" % i for i in range(16)]
+        ts(ap("ha", h0 + (t + 1) * n, h0 + (t + 2) * n), z, num(0.0), num(-OFS), A.max, A.add, [k("zf")], ["ha%d_%d" % (c, t + 1)], n, ba)
         group(ap(pb, 128, 256), k("key"), bb,
               [(ap("sin", o, o + 2 * n), ap("pen"), [sk, mk, "pen"], 128),
-               (ap("yb", 2 * cn + n, 2 * cn + 3 * n), ap("uu", 0, 128), [k("yb")] + wk, 128),
-               (ap("yb", 2 * cn, 2 * cn + 2 * n), ap("uu", 128, 256), [k("yb")] + wk, 128)])
+               (ap("yb", 2 * cn + n, 2 * cn + 3 * n), ap("uu", 0, 128), [k("yb"), "uuu"], 128),
+               (ap("yb", 2 * cn, 2 * cn + 2 * n), ap("uu", 128, 256), [k("yb"), "uuv"], 128)])
         q0, q1 = 128 * c, 144 * c
         scan(ap("rq", q0, q0 + 128), ap(pb, 128, 256), ap("rt"), 0.0, A.add, A.max, [k("key"), "rt"], [k("rq")], 128, bb)
         scan(back("tq", q1, q1 + 128), back("eps", 0, 128), back("rq", q0, q0 + 128), 0.0, A.add, A.min, [k("rq"), "eps"], [k("tq")], 64)
 
         def lost(a):
-            return [(ap("tq", q1, q1 + 128), ap("ee", a, a + n), ["ee", k("tq")], n),
-                    (ap("tq", q1 + 1, q1 + 129), ap("ee2", a, a + n), ["ee2", "tqp", k("tq")], n)]
+            return [(ap("tq", q1, q1 + 128), ap("down", a, a + n), ["down", k("tq")], n),
+                    (ap("tq", q1 + 1, q1 + 129), ap("up", a, a + n), ["up", "tqp", k("tq")], n)]
         group(ap(pa, 5 * n, 6 * n), k("zu"), ba, [mat("eye2", S, [sk])] + lost(0))
         group(ap(pb, 4 * n, 5 * n), k("zv"), bb, lost(n))
         relu(p["e_msq"], loc("msq"), ap(pa, 5 * n, 6 * n), [k("zu"), "c_b15"], [k("msq")], n, ba, C("b15"))
         relu(p["e_ost"], loc("ost"), ap(pb, 4 * n, 5 * n), [k("zv"), "c_st"], [k("ost")], n, bb, C("st"))
-        zn = p["m1r"] <= t < RO - 1
+        zn = t < RO - 1
         Z = ap(pb, 5 * n, 6 * n)
         if zn:
-            group(Z, k("zn"), bb, struck([flags("sout", c, s) for s in range(t + 1)]) + [mat("selk2", S, [sk]), on("nselk", "msq")], last=False)
-        early = KS + [on("neye", "msq")] if t == RO - 1 else [mat("eye", S, [sk]), on("nhalf", "msq")]
-        late = [on("eye2" if t == RO - 1 else "eye", "mn"), on("gd", "ht")]
+            group(Z, k("zn"), bb, struck([flags("sout", c, s) for s in range(t + 1)]) + [mat("selh", S, [sk]), on("selq", "msq")], last=False)
+        early = (KS[1:] if zn else KS) + [on("neye", "msq")]
+        late = [on("eye2", "mn"), on("gd", "ht")]
         bf = bb if p["jz"] or not zn else ba
         Fn = ap("pb%d" % bf, 6 * n, 7 * n)
         if bf == bb:
@@ -601,20 +510,18 @@ def build(p):
         tt(loc("mn"), w1, loc("msq"), A.min, [k("w1"), k("msq")], [k("mn")], n, ba)
         tt(loc("ht"), w1, S, A.is_equal, [k("w1"), sk], [k("ht")], n, ba)
         if zn:
-            group(Z, k("zn"), bb, [on("selk2", "mn")], first=False, last=bf != bb)
+            group(Z, k("zn"), bb, [on("selh", "mn")], first=False, last=bf != bb)
         group(Fn, k("fin"), bf, late if bf == bb else early + late, first=bf != bb)
-        if t < RO - 1:
-            o2 = pay(c, t + 1)
-            su = "su%d_%d" % (c, t + 1)
+        if zn:
+            o2, su, sem = pay(c, t + 1), "su%d_%d" % (c, t + 1), "ar%d_%d" % (t + 1, c)
             Mn, mnk = flags("sout", c, t + 1)
-            if zn:
-                flag(Mn, Z, t + 1, [k("zn")], [mnk], bb)
-            copy(p["e_su"], ap("sout", o2, o2 + n), Fn, [k("fin")], [su], n, bf)
-            w = 2 * n if zn else n
-            sem = "ar%d_%d" % (t + 1, c)
-            add("G", lambda q, T, X: q.remote_dma(T["sin"][:, o2:o2 + w], T["sout"][:, o2:o2 + w], T.sem[sem], T.sem["sent"], X["addr"][1][1],
-                                                  X["addr"][1][0], X["mask"]), [su] + ([mnk] if zn else []), ["st" + sem], ("r", 0), None, "sent")
-            lands(["st" + sem], ["sinS%d_%d" % (c, t + 1)] + (["sinM%d_%d" % (c, t + 1)] if zn else []), sem, 0.0)
+            ts(Mn, Z, ap("thr", t + 1, t + 2), None, A.is_ge, None, [k("zn"), "thr"], [mnk], n, bb)
+            copy(p["e_su"], ap("sout", o2, o2 + n), Fn, [k("fin")], [su], n, bf, by=0.5)
+            add("G", lambda q, T, X: q.remote_dma(T["sin"][:, o2:o2 + 2 * n], T["sout"][:, o2:o2 + 2 * n], T.sem[sem], T.sem["sent"],
+                                                  X["addr"][1][1], X["addr"][1][0], X["mask"]), [su, mnk], ["st" + sem], ("r", 0), None, "sent")
+            lands(["st" + sem], ["sinS%d_%d" % (c, t + 1), "sinM%d_%d" % (c, t + 1)], sem, 0.0)
+            copy("G", ap("hl", h0 + (t + 1) * n, h0 + (t + 2) * n), Lf, [lf, "st" + sem], ["hl%d_%d" % (c, t + 1)], n)
+            patterns(t, c, ["st" + sem])
         else:
             outs(c, "ya", "ha", p["e_ya"], OFS)
             relu(p["e_yl"], loc("oyl"), Fn, [k("fin")], [k("oyl")], n, bf)
@@ -623,27 +530,23 @@ def build(p):
     def final(c, bb):
         pb = "pb%d" % bb
         cn, n4 = c * n, n // 4
-        group(ap(pb, 448, 448 + n), "zf%d" % bb, bb, struck([flags("sin", c, s) for s in range(RO)]))
+        group(ap(pb, 448, 448 + n), "zl%d" % c, bb, struck([flags("sin", c, s) for s in range(RO)]))
         for h in range(2):
             ts(ap("fm", 2 * cn + h * n, 2 * cn + h * n + n), ap(pb, 448, 448 + n), C("cf%d" % h), None, A.is_equal, None,
-               ["zf%d" % bb, "c_cf%d" % h], ["fm%d_%d" % (c, h)], n, bb)
+               ["zl%d" % c, "c_cf%d" % h], ["fm%d_%d" % (c, h)], n, bb)
         terms = [mat("eye", ap("c4", 0, n4), ["c4"], 64)]
         for h in range(2):
             for i in range(4):
                 d = 4 * i + 2 * h
                 terms.append((ap("wfw", 16 - d, 144 - d), ap("fm", 2 * cn + h * n + i, 2 * cn + h * n + n, 4), ["wfw", "fm%d_%d" % (c, h)], 64))
-        group(ap(pb, 448, 448 + n4), "zf%d" % bb, bb, terms)
-        ts(ap("foff", 16 * c, 16 * c + n4), ap(pb, 448, 448 + n4), C("rf"), None, A.add, None, ["zf%d" % bb, "c_rf"], ["foff%d" % c], 64, bb)
+        group(ap(pb, 448, 448 + n4), "zl%d" % c, bb, terms)
+        ts(ap("foff", 16 * c, 16 * c + n4), ap(pb, 448, 448 + n4), C("rf"), None, A.add, None, ["zl%d" % c, "c_rf"], ["foff%d" % c], 64, bb)
 
     def outs(c, nm, hn, e, bias):
         h0, n4 = c * HS, n // 4
-        src = ind(hn, h0, h0 + HS, "foff", 16 * c, 16 * c + n4)
-        rd = ["%s%d_%d" % (hn, c, s) for s in range(7)] + ["foff%d" % c]
         dst = ap("o" + nm, 4 * n * c, 4 * n * c + 4 * n)
-        if e == "S":
-            act(dst, src, F.Relu, rd, ["o%s%d" % (nm, c)], 4 * n, kind="gs", bias=num(bias))
-        else:
-            ts(dst, src, num(bias), num(0.0), A.add, A.max, rd, ["o%s%d" % (nm, c)], 4 * n, kind="gv")
+        relu(e, dst, ind(hn, h0, h0 + HS, "foff", 16 * c, 16 * c + n4), ["%s%d_%d" % (hn, c, s) for s in range(7)] + ["foff%d" % c],
+             ["o%s%d" % (nm, c)], 4 * n, None, num(bias), "g")
         dma("Y", ap(nm, 4 * n * c, 4 * n * c + 4 * n), dst, ["o%s%d" % (nm, c)], [], "outs", 131072)
 
     setup()
@@ -666,58 +569,67 @@ def times(op, p):
     return d, d
 
 
+def lags(ops, p):
+    tm = [times(o, p) for o in ops]
+    return tm, [[(d, tm[d][1] + (0.0 if ops[d]["eng"] is None or o["eng"] == ops[d]["eng"] == "P" or (o["eng"], ops[d]["sem"]) == ("G", "sent")
+                                 else p["hop"])) for d in sorted(o["deps"])]
+                for o in ops]
+
+
 def schedule(ops, p):
     N = len(ops)
-    tm = [times(o, p) for o in ops]
+    tm, fw = lags(ops, p)
     succ = [[] for _ in range(N)]
-    for k, o in enumerate(ops):
-        for d in o["deps"]:
-            succ[d].append(k)
+    for k in range(N):
+        for d, w in fw[k]:
+            succ[d].append((k, w))
     pr = [0.0] * N
     for k in range(N - 1, -1, -1):
         own = -p["tq"] * ops[k]["tag"] if ops[k]["tag"] is not None else -1.0e3
-        pr[k] = tm[k][1] + max([pr[s] + p["hop"] for s in succ[k]] + [own])
+        pr[k] = tm[k][1] + max([pr[s] + p["hop"] for s, w in succ[k]] + [own])
     for k in range(N):
         pr[k] += 1.0e4 if ops[k]["cost"][0] == "r" else p["up"].get(ops[k]["w"].rstrip("0123456789_"), 0.0) - p["short"] * tm[k][0]
     left = [len(o["deps"]) for o in ops]
-    rdy = [0.0] * N
-    free, order, ready = {}, {}, {}
+    rdy, st = [0.0] * N, [0.0] * N
+    free, ready = {}, {}
     stack = [k for k in range(N) if not left[k]]
     while True:
-        while stack:
+        if stack:
             k = stack.pop()
-            e = ops[k]["eng"]
-            if e is None:
-                for s in succ[k]:
-                    rdy[s] = max(rdy[s], rdy[k] + tm[k][1])
-                    left[s] -= 1
-                    if not left[s]:
-                        stack.append(s)
-            else:
-                ready.setdefault(e, []).append(k)
-        be, bt = None, 0.0
-        for e, l in ready.items():
-            if l:
-                t0 = max(free.get(e, 0.0), min([rdy[k] for k in l]))
-                if be is None or t0 < bt:
-                    be, bt = e, t0
-        if be is None:
-            break
-        k = max([k for k in ready[be] if rdy[k] <= bt], key=lambda j: (pr[j], -j))
-        ready[be].remove(k)
-        st = max(bt, rdy[k])
-        free[be] = st + tm[k][0]
-        order.setdefault(be, []).append(k)
-        for s in succ[k]:
-            hop = 0.0 if (be == "P" and ops[s]["eng"] == be) else p["hop"]
-            rdy[s] = max(rdy[s], st + tm[k][1] + hop)
+            if ops[k]["eng"] is not None:
+                ready.setdefault(ops[k]["eng"], []).append(k)
+                continue
+            st[k] = rdy[k]
+        else:
+            soon = [(max(free.get(e, 0.0), min([rdy[j] for j in l])), i, e) for i, (e, l) in enumerate(ready.items()) if l]
+            if not soon:
+                break
+            bt, i, e = min(soon)
+            k = max([j for j in ready[e] if rdy[j] <= bt], key=lambda j: (pr[j], -j))
+            ready[e].remove(k)
+            st[k] = bt
+            free[e] = bt + tm[k][0]
+        for s, w in succ[k]:
+            rdy[s] = max(rdy[s], st[k] + w)
             left[s] -= 1
             if not left[s]:
                 stack.append(s)
-    order = improve(ops, p, order)
-    for e in "YG":
-        l = order[e]
-        order[e] = sorted([k for k in l if not ops[k]["deps"]]) + [k for k in l if ops[k]["deps"]]
+    bw = [[(s, tm[s][0] + w - tm[k][0]) for s, w in succ[k]] for k in range(N)]
+    best = None
+    for it in range(p["fbi"] + 1):
+        if it:
+            sb = place(ops, tm, bw, [(-round(st[k] + tm[k][0], 6), -k) for k in range(N)])
+            st = place(ops, tm, fw, [(-round(sb[k] + tm[k][0], 6), k) for k in range(N)])
+        end = max([st[k] + tm[k][1] for k in range(N)])
+        if best is None or end < best:
+            best, seq = end, sorted(range(N), key=lambda j: (round(st[j], 6), j))
+    seq = [k for k in range(N) if ops[k]["eng"] in ("Y", "G") and not ops[k]["deps"]] \
+        + [k for k in seq if ops[k]["eng"] not in ("Y", "G") or ops[k]["deps"]]
+    seq = refine(ops, p, seq)
+    order = {}
+    for k in seq:
+        if ops[k]["eng"] is not None:
+            order.setdefault(ops[k]["eng"], []).append(k)
     return order
 
 
@@ -742,44 +654,81 @@ def place(ops, tm, pred, key):
     return start
 
 
-def improve(ops, p, order):
+def refine(ops, p, seq):
     N = len(ops)
-    tm = [times(o, p) for o in ops]
-    fw, bw = [[] for _ in range(N)], [[] for _ in range(N)]
-    for k, o in enumerate(ops):
-        for d in o["deps"]:
-            h = 0.0 if (ops[d]["eng"] is None or (o["eng"] == ops[d]["eng"] and o["eng"] == "P")) else p["hop"]
-            fw[k].append((d, tm[d][1] + h))
-            bw[d].append((k, tm[k][0] + h + tm[d][1] - tm[d][0]))
-    nxt = {e: 0 for e in order}
-    fin, free = [None] * N, {e: 0.0 for e in order}
-    todo = [k for k in range(N) if ops[k]["eng"] is None]
-    moved = True
-    while moved:
-        moved = False
-        for k in todo:
-            if fin[k] is None and all([fin[d] is not None for d, w in fw[k]]):
-                fin[k] = max([fin[d] + w for d, w in fw[k]])
-                moved = True
-        for e, l in order.items():
-            while nxt[e] < len(l) and all([fin[d] is not None for d, w in fw[l[nxt[e]]]]):
-                k = l[nxt[e]]
-                fin[k] = max([free[e]] + [fin[d] + w for d, w in fw[k]])
-                free[e] = fin[k] + tm[k][0]
-                nxt[e] += 1
-                moved = True
-    st = fin
-    best, bo = max([st[k] + tm[k][1] for k in range(N)]), order
-    for it in range(p["fbi"]):
-        sb = place(ops, tm, bw, [(-round(st[k] + tm[k][0], 6), -k) for k in range(N)])
-        st = place(ops, tm, fw, [(-round(sb[k] + tm[k][0], 6), k) for k in range(N)])
-        end = max([st[k] + tm[k][1] for k in range(N)])
-        if end < best:
-            best, bo = end, {}
-            for k in sorted(range(N), key=lambda j: (round(st[j], 6), j)):
-                if ops[k]["eng"] is not None:
-                    bo.setdefault(ops[k]["eng"], []).append(k)
-    return bo
+    prev, nxt, last, pos = [-1] * N, [-1] * N, {}, [0] * N
+    for i, k in enumerate(seq):
+        pos[k], e = i, ops[k]["eng"]
+        if e in last and e is not None:
+            prev[k], nxt[last[e]] = last[e], k
+        last[e] = k
+    cases = [lags(ops, dict(p, f=f, g=g, hop=hop, rlat=rl)) for f, g, hop, rl in p["cases"]]
+    ends = [k for k in range(N) if ops[k]["cost"][0] == "d" and ops[k]["tag"] is not None]
+    marks = ends + [k for k in range(N) if ops[k]["cost"][0] == "r"]
+
+    def heads(case, st, i0):
+        tm, fw = case
+        for k in seq[i0:]:
+            t = st[prev[k]] + tm[prev[k]][0] if prev[k] >= 0 else 0.0
+            for d, w in fw[k]:
+                if st[d] + w > t:
+                    t = st[d] + w
+            st[k] = t
+        return max([st[k] + tm[k][1] for k in ends]) + 0.3 * sum([st[k] for k in marks]) / len(marks)
+    starts = [[0.0] * N for _ in cases]
+    base = [heads(x, st, 0) for x, st in zip(cases, starts)]
+    cur, seed, todo = float(len(cases)), [1], []
+
+    def rnd(m):
+        seed[0] = seed[0] * 48271 % 2147483647
+        return seed[0] % m
+    for it in range(p["moves"]):
+        while not todo:
+            i = rnd(len(cases))
+            (tm, fw), st = cases[i], starts[i]
+            k = marks[rnd(len(marks))] if rnd(2) else max(ends, key=lambda j: st[j])
+            way = []
+            while k >= 0:
+                up = [d for d, w in fw[k] if st[d] + w > st[k] - 1e-9]
+                if prev[k] >= 0 and st[prev[k]] + tm[prev[k]][0] > st[k] - 1e-9 and (not up or rnd(2)):
+                    if prev[k] not in ops[k]["deps"] and ops[k]["eng"] in "VSP":
+                        way.append(k)
+                    up = [prev[k]]
+                k = up[-1] if up else -1
+            todo = [way[rnd(len(way))] for j in range(12 if way else 0)]
+        c = todo.pop()
+        a = prev[c]
+        for j in range((0, 0, 0, 1, 2, 4)[rnd(6)]):
+            a = prev[a] if a >= 0 and prev[a] >= 0 else a
+        if a < 0:
+            continue
+        i0, i1 = pos[a], pos[c]
+        seg, need = seq[i0:i1 + 1], {c}
+        for k in seg[::-1]:
+            if k in need:
+                need.update(ops[k]["deps"])
+                need.add(prev[k] if k != c else c)
+        if any([k in need and k != c and ops[k]["eng"] == ops[c]["eng"] for k in seg]):
+            continue
+        links = [(x, prev[x], nxt[x]) for x in (prev[a], a, prev[c], c, nxt[c]) if x >= 0]
+        pa, pc, nc = prev[a], prev[c], nxt[c]
+        nxt[pc], prev[c], nxt[c], prev[a] = nc, pa, a, c
+        if nc >= 0:
+            prev[nc] = pc
+        if pa >= 0:
+            nxt[pa] = c
+        seq[i0:i1 + 1] = [k for k in seg if k in need] + [k for k in seg if k not in need]
+        new = [list(st) for st in starts]
+        val = sum([heads(x, st, i0) / b for x, st, b in zip(cases, new, base)])
+        if val <= cur:
+            cur, starts = val, new
+            for i in range(i0, i1 + 1):
+                pos[seq[i]] = i
+        else:
+            seq[i0:i1 + 1] = seg
+            for x, u, v in links:
+                prev[x], nxt[x] = u, v
+    return seq
 
 
 PLAN = {}
@@ -802,8 +751,9 @@ def rank_program(g, core, T, topo):
     mask = topo.mask(core, peers[1])
     for c in peers[2:]:
         mask &= topo.mask(core, c)
-    ne = len([e for e in topo.engines(core, peers[1]) if mask >> e & 1])
-    X = {"addr": [topo.addr(c) for c in peers], "mask": mask}
+    bits = [1 << e for e in topo.engines(core, peers[1]) if mask >> e & 1]
+    ne = len(bits)
+    X = {"addr": [topo.addr(c) for c in peers], "mask": mask, "parts": [sum(bits[c * ne // NCH:(c + 1) * ne // NCH]) for c in range(NCH)]}
     queue = {"V": g.vector, "S": g.scalar, "P": g.tensor, "G": g, "Y": g.sync}
     pos = {}
     for e, l in order.items():

from concourse.bass import DstId, RemoteDMATransfer
from concourse.mybir import AluOpType as A, ActivationFunctionType as F

NR, LN, RO = 4, 256, 6
NCH = 4
n = LN // NCH
HS = 7 * n
TW = 8192
XW = 32 * n + 16
SW = 12 * n
RM = {2: 0, 3: 2 * n, 4: 5 * n, 5: 9 * n}
BIG = 32768.0
GONE = -2.0 ** 90
OFS = 240.0

P = {"nd": 2, "sel": 3, "sela": 3, "nep": 0, "jz": 0, "eq1": 1, "neg": "SSSS", "negw": 512, "e_uv": "Y",
     "cut": ("V", 16, "V", 24, "S", 64, "S", 96, "S", 128), "cut1": ("V", 16, "V", 32, "S", 96, "S", 128),
     "cut5": ("V", 16, "S", 48, "S", 96, "V", 112, "S", 128),
     "cut0": ("V", 16, "S", 48, "S", 64), "cut0_0": ("S", 24, "S", 44, "V", 64),
     "e_msq": "V", "e_ost": "V", "e_su": "V", "e_yc": "S", "e_ya": "S", "e_yl": "S",
     "g": 2.0, "f": 1.0, "pe": 0.7, "hop": 0.25, "rlat": 1.8, "riss": 0.6, "klat": 2.0, "bw": 400.0, "tq": 6.0, "short": 0.0, "fbi": 6, "up": {},
     "moves": 0, "cases": ((1.0, 1.56, 0.25, 1.6), (1.5, 1.3, 0.2, 1.6), (1.4, 2.0, 0.2, 2.3))}
P.update({'cut0': ('V', 16, 'S', 48, 'S', 64), 'cut0_0': ('V', 32, 'S', 48, 'S', 64), 'cut0_3': ('V', 16, 'V', 24, 'S', 48, 'S', 64),
          'cut': ('V', 16, 'V', 24, 'S', 56, 'S', 80, 'S', 112, 'S', 128), 'cut1': ('V', 16, 'V', 32, 'S', 96, 'S', 128),
          'cut5': ('V', 16, 'V', 28, 'S', 112, 'S', 128), 'cut5_3': ('V', 48, 'S', 112, 'S', 128), 'jz': 1, 'nep': 0, 'nd': 2, 'sel': 3, 'sela': 3,
          'eq1': 0, 'g': 2.0, 'f': 1.1, 'e_yl': 'V', 'neg': 'SVSV', 'moves': 8000,
          'cases': ((1.0, 1.56, 0.25, 1.6), (1.4, 1.4, 0.22, 1.8), (1.3, 2.0, 0.22, 2.0))})

BF, F32, I32, U16, F16 = "bfloat16", "float32", "int32", "uint16", "float16"
SCRATCH = {
    "tab": ("sbuf", [128, 2 * TW], BF), "uu": ("sbuf", [128, 256], BF),
    "xb": ("sbuf", [128, NCH * XW], BF), "so": ("sbuf", [128, 32 * LN], F16),
    "d1b": ("sbuf", [128, 128], BF), "d1": ("sbuf", [128, 32 * LN], F16),
    "hl": ("sbuf", [128, NCH * HS], F32), "hh": ("sbuf", [128, NCH * HS], F16), "ha": ("sbuf", [128, NCH * HS], BF),
    "posi": ("sbuf", [128, LN], I32), "ki": ("sbuf", [128, LN], I32), "si": ("sbuf", [128, LN], I32),
    "dd": ("sbuf", [128, LN], BF), "sq": ("sbuf", [128, LN], BF),
    "kall": ("sbuf", [128, NR * LN], BF), "sin": ("sbuf", [128, NCH * SW], BF), "sout": ("sbuf", [128, NCH * SW], BF),
    "uv": ("sbuf", [128, 32], BF), "stepi": ("sbuf", [128, 4], I32), "du": ("sbuf", [128, 32], BF),
    "dg": ("sbuf", [128, LN], F32), "poff": ("sbuf", [128, 16 * NCH], U16), "rm": ("sbuf", [128, 14 * n], BF),
    "og": ("sbuf", [128, LN], F16), "ogs": ("sbuf", [128, 5 * LN], F16), "acc": ("sbuf", [128, 2 * LN], F16),
    "ne": ("sbuf", [128, LN], BF), "off": ("sbuf", [128, 2 * LN], U16),
    "yb": ("sbuf", [128, 9 * n], BF), "rq": ("sbuf", [128, 128 * NCH], BF), "tq": ("sbuf", [128, 144 * NCH], BF),
    "msq": ("sbuf", [128, LN], BF), "ost": ("sbuf", [128, LN], BF), "ht": ("sbuf", [128, LN], BF), "mn": ("sbuf", [128, LN], BF),
    "fm": ("sbuf", [128, 2 * LN], BF), "foff": ("sbuf", [128, 16 * NCH], U16),
    "oyl": ("sbuf", [128, LN], F32), "oya": ("sbuf", [128, 4 * LN], F32), "oyc": ("sbuf", [128, 4 * LN], F32),
    "ci": ("sbuf", [128, 8], I32), "col": ("sbuf", [128, 64], F32), "thr": ("sbuf", [128, 8], F32),
    "gt": ("sbuf", [128, 8], F32), "it": ("sbuf", [128, 8], F32), "cmp": ("sbuf", [128, 8], F32), "wc": ("sbuf", [128, 16], F32),
    "dw": ("sbuf", [128, 160], BF), "eyew": ("sbuf", [128, 144], BF), "wfw": ("sbuf", [128, 144], BF), "pw": ("sbuf", [128, 130], BF),
    "c4": ("sbuf", [128, 16], BF), "ws": ("sbuf", [128, RO * 128], BF), "wm": ("sbuf", [128, RO * 128], BF),
    "eyeh": ("sbuf", [128, 128], F16), "tmp": ("sbuf", [128, n], F32),
}
for _m in ("cd", "rs", "one", "bs", "nb", "cb"):
    SCRATCH[_m] = ("sbuf", [128, n], BF)
for _m in ("cg", "km", "blk", "bmq", "bmh", "eye2", "selh", "selq", "neye", "neye2", "wp", "wb", "up", "down", "upt", "rt", "eps",
           "cp", "cn", "gd", "pen", "pa", "pz"):
    SCRATCH[_m] = ("sbuf", [128, 128], BF)
for _b in range(8):
    SCRATCH["pb%d" % _b] = ("psum", [128, 512], F32)

SEMAPHORES = ["sV", "sS", "sP", "sG", "karr", "marr", "sent", "outs", "lpos", "lu", "lv", "lstep"] \
    + [x + str(i) for x in ("lf", "ld") for i in range(4)] + ["ar%d_%d" % (t, c) for t in range(1, RO) for c in range(NCH)]


def build(p):
    ops = []
    lastw, readers, bank = {}, {}, {}
    tag = [None]

    def add(eng, fn, rd, w, cost, bk=None, sem=None, cnt=0):
        k = len(ops)
        deps = set()
        for x in rd:
            if x in lastw:
                deps.add(lastw[x])
        for x in w:
            if x in lastw:
                deps.add(lastw[x])
            deps.update(readers.get(x, ()))
        for x in rd:
            readers.setdefault(x, []).append(k)
        for x in w:
            lastw[x] = k
            readers[x] = []
        if bk is not None:
            e0, run, prev = bank.get(bk, (None, [], []))
            if e0 == eng:
                deps.update(prev)
                if eng == "P":
                    deps.add(run[-1])
                run.append(k)
            else:
                deps.update(run)
                bank[bk] = (eng, [k], run)
        deps.discard(k)
        ops.append({"eng": eng, "fn": fn, "deps": deps, "cost": cost, "sem": sem, "cnt": cnt, "tag": tag[0], "w": (list(w) + [""])[0]})

    def num(v):
        return lambda T: v

    def ts(out, in0, s1, s2, o0, o1, rd, w, m, bk=None, kind="c"):
        if o1 is None:
            add("V", lambda q, T, X: q.tensor_scalar(out(T), in0(T), s1(T), None, o0), rd, w, (kind, m), bk)
        else:
            add("V", lambda q, T, X: q.tensor_scalar(out(T), in0(T), s1(T), s2(T), o0, o1), rd, w, (kind, m), bk)

    def tt(out, a, b, o, rd, w, m, bk=None, kind="c"):
        add("V", lambda q, T, X: q.tensor_tensor(out(T), a(T), b(T), o), rd, w, (kind, m), bk)

    def cp(out, a, rd, w, m, bk=None, kind="c"):
        add("V", lambda q, T, X: q.tensor_copy(out(T), a(T)), rd, w, (kind, m), bk)

    def ms(out, v, w, m=64):
        add("V", lambda q, T, X: q.memset(out(T), v), [], w, ("c", m))

    def scan(out, a, b, init, o0, o1, rd, w, m, bk=None):
        add("V", lambda q, T, X: q.tensor_tensor_scan(out(T), a(T), b(T), init, o0, o1), rd, w, ("c", m), bk)

    def act(out, a, f, rd, w, m, bk=None, kind="c", bias=None, scale=None):
        def fn(q, T, X):
            kw = {}
            if bias is not None:
                kw["bias"] = bias(T)
            if scale is not None:
                kw["scale"] = scale(T)
            return q.activation(out(T), a(T), f, **kw)
        add("S", fn, rd, w, (kind, m), bk)

    def relu(e, out, a, rd, w, m, bk, bias=None, kind="c"):
        if e == "S":
            act(out, a, F.Relu, rd, w, m, bk, "gs" if kind == "g" else kind, bias)
        elif bias is None:
            ts(out, a, num(0.0), None, A.max, None, rd, w, m, bk)
        else:
            ts(out, a, bias, num(0.0), A.add, A.max, rd, w, m, bk, "gv" if kind == "g" else kind)

    def copy(e, out, a, rd, w, m, bk=None, gather=False, by=None):
        if e == "S":
            act(out, a, F.Copy, rd, w, m, bk, kind="gs" if gather else "c", scale=num(by) if by else None)
        elif e == "G":
            add("G", lambda q, T, X: q.affine_select(out(T), a(T), [[0, m]], A.is_ge, 0.0, 0, 0), rd, w, ("ga", m))
        elif by:
            ts(out, a, num(by), None, A.mult, None, rd, w, m, bk)
        else:
            cp(out, a, rd, w, m, bk, kind="gv" if gather else "c")

    def group(out, key, bk, terms, first=True, last=True):
        for i, x in enumerate(terms):
            o, lh, rh, st, sp = x[4] if len(x) > 4 else out, x[0], x[1], first and i == 0, last and i == len(terms) - 1
            add("P", lambda q, T, X, o=o, lh=lh, rh=rh, st=st, sp=sp: q.matmul(o(T), lh(T), rh(T), st, sp), x[2], [key], ("p", x[3]), bk)

    def iota(name, pat, base, cm=0, a=None, b=None, key=None, after=()):
        m = 1
        for s, c in pat:
            m *= c
        if SCRATCH[name][2] == I32:
            add("G", lambda q, T, X: q.iota(ap(name, a, b)(T), pat, base, cm), [], [name], ("gi", m))
        else:
            add("G", lambda q, T, X: q.iota(ap(name, a, b)(T), pat, base, cm, allow_small_or_imprecise_dtypes=True), after, [key or name], ("gi", m))

    def ap(name, a=None, b=None, s=None):
        if a is None:
            return lambda T: T[name][:]
        if s is None or s == 1:
            return lambda T: T[name][:, a:b]
        return lambda T: T[name][:, a:b:s]

    def back(name, a, b):
        return (lambda T: T[name][:, b - 1:a - 1:-1]) if a else (lambda T: T[name][:, b - 1::-1])

    def ind(name, a, b, oname, c, d):
        return lambda T: T[name][:, a:b].indirect(T[oname][:, c:d])

    def dma(eng, out, a, rd, w, sem, nbytes):
        add(eng, lambda q, T, X: q.dma_start(out(T), a(T)), rd, w, ("d", nbytes), None, sem, 16)

    def lands(after, wr, sem, lat, cnt=1):
        add(None, None, after, wr, ("a", lat), None, sem, cnt)

    def mat(name, rhs, rd, m=n):
        lh = ap("eyew", 16, 144) if name == "eye" else ap(name, 0, 128)
        return (lh, rhs, ["eyew" if name == "eye" else name] + rd, m)

    names = {}

    def C(name):
        j = names.setdefault(name, len(names))
        return ap("col", j, j + 1)

    def cs(name, src, s1, s2, o0, o1=None):
        rd = ["c_" + x for x in (src, s1, s2) if isinstance(x, str)]
        f = [C(x) if isinstance(x, str) else num(x) for x in (src, s1, s2)]
        if (o0, o1) == (A.mult, A.add):
            act(C(name), f[0], F.Identity, rd, ["c_" + name], 64, scale=f[1], bias=f[2])
        else:
            ts(C(name), f[0], f[1], f[2], o0, o1, rd, ["c_" + name], 64)

    def scaled(name, src, v, w=None, at=0):
        rd = [src] + ["c_" + x for x in (v, w) if isinstance(x, str)]
        f = [C(x) if isinstance(x, str) else num(x) for x in (v, w)]
        if w is None:
            act(ap(name), ap(src, at, at + 128), F.Copy, rd, [name], 128, scale=f[0])
        else:
            ts(ap(name), ap(src, at, at + 128), f[0], f[1], A.mult, A.mult, rd, [name], 64)

    def fill(name, v, a=None, b=None, s=None):
        m = len(range(a, b, s)) if s else SCRATCH[name][1][1]
        act(ap(name, a, b, s), ap("dw", 0, m), F.Identity, ["dw"], [name], m, scale=num(0.0), bias=num(v))

    def pay(c, s):
        return c * SW + 2 * n * s

    def flags(buf, c, s):
        o = pay(c, s) + n
        return ap(buf, o, o + n), "%sM%d_%d" % (buf, c, s)

    def struck(fl):
        return [(ap("ws", 128 * s, 128 * s + 128), x[0], ["ws%d" % s, x[1]], n) for s, x in enumerate(fl)]

    TAB = ["tab%d" % i for i in range(4)]
    NEG = ["neg%d" % a for a in range(0, TW, p["negw"])]

    def setup():
        dma("Y", ap("posi"), ap("pos"), [], ["posi"], "lpos", 131072)
        for i in range(4):
            a, b = 2048 * i + 128, 2048 * i + 2048
            dma("Y", ap("tab", a, b), ap("feat", a, b), [], [TAB[i]], "lf%d" % i, 131072 + 491520 * (i + 1))
            ms(ap("tab", a - 128, a), 0.0, ["tabz%d" % i])
        for i, (x, src) in enumerate(((ap("uv", 0, 16), "u"), (ap("uv", 16, 32), "v"), (ap("stepi", 0, 1), "step"))):
            dma(p["e_uv"], x, ap(src), [], [src], "l" + src, (2200000 + 80000 * i) * (p["e_uv"] == "Y"))
        iota("ci", [[1, 2]], 0, 1, 0, 2)
        iota("dw", [[1, 160]], -16)
        iota("cg", [[1, 8], [0, 16]], 0)
        iota("it", [[1, 8]], 0)
        iota("km", [[0, 8], [1, 16]], 0)
        iota("pw", [[1, 65], [0, 2]], 0)
        iota("d1b", [[512, 8], [0, 16]], -2048)
        iota("nb", [[0, 8], [-512, 8]], 2048)
        iota("yb", [[0, 9 * n]], 0)

        for x in ("p", "p1"):
            C(x)
        for j, (nm, src, op, v) in enumerate((("k", 0, A.bitwise_and, 15), ("g", 0, A.arith_shift_right, 4), ("od", 1, A.bitwise_and, 1),
                                              ("ph", 1, A.arith_shift_right, 1), ("rf", 2, A.arith_shift_right, 2))):
            C(nm)
            ts(ap("ci", j + 2, j + 3), ap("ci", src, src + 1), num(v), None, op, None, ["ci", "ci%d" % src], ["ci%d" % (j + 2)], 64)
        cp(ap("col", 0, 7), ap("ci", 0, 7), ["ci"] + ["ci%d" % j for j in range(2, 7)], ["c_" + x for x in names], 64)
        ts(ap("eyew"), ap("dw", 0, 144), C("p"), None, A.is_equal, None, ["dw", "c_p"], ["eyew"], 72)
        ts(ap("blk"), ap("cg"), C("g"), None, A.is_equal, None, ["cg", "c_g"], ["blk"], 64)
        cs("king", "k", 0.0, None, A.is_equal)
        cs("top", "k", 13.0, None, A.is_ge)
        cs("mid", "k", 1.0, "top", A.is_ge, A.subtract)
        cs("s1", "g", -8.0, "ph", A.mult, A.add)
        cs("o8", "od", 8.0, 32.0, A.mult, A.add)
        cs("b0", "k", 8.0, -64.0, A.mult, A.add)
        cs("b1", "king", -1.0e6, 0.0, A.mult, A.add)
        cs("b2", "b0", "o8", "b1", A.max, A.add)
        cs("big", "mid", 1.0e6, 0.0, A.mult, A.add)
        ts(ap("gt"), ap("it"), C("s1"), C("big"), A.is_lt, A.mult, ["it", "c_s1", "c_big"], ["gt"], 64)
        act(ap("thr"), ap("gt"), F.Identity, ["gt", "c_b2"], ["thr"], 64, bias=C("b2"))
        scaled("eye2", "eyew", 2.0, at=16)
        scaled("bmq", "blk", -0.25)
        scaled("bmh", "blk", 0.5)
        scaled("selh", "bmh", "king")
        scaled("wb", "blk", "top", 2048.0)

        ts(ap("si"), ap("posi"), num(127), None, A.bitwise_and, None, ["posi"], ["si"], 256)
        ts(ap("dd"), ap("posi"), num(0.0), num(GONE), A.is_equal, A.mult, ["posi"], ["dd"], 256)
        ts(ap("sq"), ap("si"), num(0.5), num(64.0), A.mult, A.add, ["si"], ["sq"], 256)
        ts(ap("ki"), ap("posi"), num(1920), None, A.bitwise_and, None, ["posi"], ["ki"], 256)
        ts(ap("kall", 0, LN), ap("ki"), num(-128.0), None, A.add, None, ["ki"], ["kall0"], 256)
        for c in range(NCH):
            S0, sk, z = ap("sin", pay(c, 0), pay(c, 0) + n), "sinS%d_0" % c, ap("pb%d" % (2 * c), 0, n)
            group(z, "z0%d" % c, 2 * c, [mat("eye", ap(x, c * n, c * n + n), [x]) for x in ("dd", "sq")])
            copy("S", S0, z, ["z0%d" % c], [sk], n, 2 * c)
            group(z, "z0%d" % c, 2 * c, [mat("selh", ap("sq", c * n, c * n + n), ["sq"])])
            M, mk = flags("sin", c, 0)
            ts(M, z, ap("thr", 0, 1), None, A.is_ge, None, ["z0%d" % c, "thr"], [mk], n, 2 * c)

        def sendm(q, T, X):
            return q.remote_dma_fused([RemoteDMATransfer(
                dst_ids=[DstId(rid=X["addr"][NR - 1][0], pnc=X["addr"][NR - 1][1])], dma_engine_mask=X["parts"][c], remote_sem=T.sem["marr"],
                srcs=[flags("sin", c, 0)[0](T)], dsts=[flags("sout", c, 0)[0](T)]) for c in range(NCH)], local_sem=T.sem["sent"])
        add("G", sendm, [flags("sin", c, 0)[1] for c in range(NCH)], ["msent"], ("r", 0), None, "sent")
        lands(["msent"], [flags("sout", c, 0)[1] for c in range(NCH)], "marr", p["klat"])

        def sendk(q, T, X):
            tr = RemoteDMATransfer(dst_ids=[DstId(rid=X["addr"][j][0], pnc=X["addr"][j][1]) for j in range(1, NR)],
                                   dma_engine_mask=X["mask"], remote_sem=T.sem["karr"], srcs=[T["kall"][:, 0:LN]],
                                   dsts=[T["kall"][:, j * LN:(j + 1) * LN] for j in range(1, NR)])
            return q.remote_dma_fused([tr], local_sem=T.sem["sent"])
        add("G", sendk, ["kall0", "msent"] + TAB, ["ksent"], ("r", 0), None, "sent")
        lands(["ksent"], ["kall%d" % j for j in range(1, NR)], "karr", 0.6, NR - 1)

        ms(ap("du", 0, 32, 16), 0.0, ["duz"])
        for i, x in enumerate("uv"):
            tt(ap("du", 16 * i + 1, 16 * i + 16), ap("uv", 16 * i, 16 * i + 15), ap("uv", 16 * i + 1, 16 * i + 16), A.subtract, [x], ["du" + x], 64)
            group(None, "z" + x, 7, [mat("eye", ap("du", 16 * i, 16 * i + 16), ["duz", "du" + x]) + (ap("pb7", 256 + 16 * j, 272 + 16 * j),)
                                     for j in range(8)])
            tt(ap("uu", 128 * i, 128 * i + 128), ap("pb7", 256, 384), ap("blk"), A.mult, ["z" + x, "blk"], ["uu" + x], 128, 7)
        ms(ap("xb", 15, NCH * XW, XW), 0.0, ["xp"])
        ms(ap("tq", 128, NCH * 144, 144), 0.0, ["tqp"])
        cs("pk", "king", -2.0 ** 22, -2.0 ** -71, A.mult, A.add)
        scaled("pa", "eyew", "pk", at=16)
        scaled("pz", "eyew", 2.0 ** -71, at=15)
        tt(ap("pen"), ap("pa"), ap("pz"), A.add, ["pa", "pz"], ["pen"], 256)
        scaled("rt", "km", -1.0 / 16)
        fill("eps", 1.0 / 16)
        fill("eps", -14.0 / 16, 15, 128, 16)
        scaled("down", "eyew", -BIG, at=16)
        scaled("up", "eyew", BIG, at=16)
        cs("b15", "k", 15.0, -BIG * 15 / 16, A.is_equal, A.mult)
        cp(C("step"), ap("stepi", 0, 1), ["step"], ["c_step"], 64)
        cs("st", "step", "b15", 128.0, A.add, A.add)
        scaled("neye", "eyew", -1.0, at=16)
        scaled("selq", "bmq", "king")
        fill("one", 1.0)
        fill("cp", 1.5 * 2.0 ** 22)
        fill("cn", -1.5 * 2.0 ** 22)
        cs("rest", "king", -2 * GONE, 2 * GONE, A.mult, A.add)
        scaled("gd", "eyew", "rest", at=16)
        cp(ap("eyeh"), ap("eyew", 16, 144), ["eyew"], ["eyeh"], 64)

        iota("bs", [[0, 8], [512, 8]], -2048)
        iota("cb", [[0, 8], [512, 8]], -2048 + int(OFS))
        for h in range(2):
            iota("d1", [[0, 4], [512, 8], [0, 32]], -2048, 0, 16 * n * h, 16 * n * (h + 1), "d1_0" + "ab"[h], [("msent", "ksent")[h]])
        for i in range(1, p["nd"]):
            dma("Y", ap("d1", 32 * n * i, 32 * n * (i + 1)), ap("d1", 0, 32 * n), ["d1_0a", "d1_0b"], ["d1_%da" % i, "d1_%db" % i], "ld%d" % i, 524288)
        for a in range(0, TW, p["negw"]):
            e = p["neg"][a // 2048]
            copy(e, ap("tab", TW + a, TW + a + p["negw"]), ap("tab", a, a + p["negw"]), [TAB[a // 2048], "tabz%d" % (a // 2048)], ["neg%d" % a],
                 p["negw"] // (2 if e == "V" else 1), by=-1.0)
        cs("sg", "od", -2.0, 1.0, A.mult, A.add)
        cs("sgm", "sg", "mid", 0.0, A.mult, A.add)
        cs("af", "s1", float(n), 0.0, A.mult, A.add)
        cs("t8", "top", -8.0, 0.0, A.mult, A.add)
        cs("aw", "sgm", -64.0, "t8", A.mult, A.add)
        cs("q0", "s1", -1.0, 1.0, A.mult, A.add)
        cs("q2", "q0", "top", "ph", A.mult, A.add)
        act(ap("cmp"), ap("it"), F.Identity, ["it", "c_top", "c_q2"], ["cmp"], 64, scale=C("top"), bias=C("q2"))
        scaled("wp", "blk", "af", "sgm")
        for s in range(RO):
            ts(ap("ws", 128 * s, 128 * s + 128), ap("pw", 1, 129), ap("cmp", s, s + 1), C("aw"), A.is_equal, A.mult, ["pw", "cmp", "c_aw"],
               ["ws%d" % s], 64)
        cs("s0", "s1", 1.0, -1.0, A.mult, A.add)
        cs("kb", "king", -BIG, 0.0, A.mult, A.add)
        ts(ap("wc", 0, 8), ap("it"), C("s0"), C("sgm"), A.is_equal, A.mult, ["it", "c_s0", "c_sgm"], ["wc0"], 64)
        act(ap("wc", 8, 16), ap("wc", 0, 8), F.Identity, ["wc0", "c_kb"], ["wc"], 64, scale=num(BIG), bias=C("kb"))
        for s in range(max(p["sel"], p["sela"])):
            act(ap("wm", 128 * s, 128 * s + 128), ap("blk"), F.Copy, ["blk", "wc"], ["wm%d" % s], 128, scale=ap("wc", 8 + s, 9 + s))
        ts(ap("tmp"), ap("km", 0, n), C("k"), num(-BIG), A.not_equal, A.mult, ["km", "c_k"], ["tmp"], 64)
        tt(ap("cd"), ap("tmp"), ap("dw", 16, 16 + n), A.add, ["tmp", "dw"], ["cd"], 128)
        scaled("upt", "eyew", TW + BIG, at=16)
        if p["eq1"]:
            scaled("neye2", "eyew", -2.0, at=16)
        cs("g16o", "g", 16.0, "od", A.mult, A.add)
        cs("c0", "big", -1.0, 1.0e6, A.mult, A.add)
        cs("cf0", "od", -8.0, "c0", A.mult, A.add)
        cs("cf1", "cf0", 1.0, -16.0, A.mult, A.add)
        ts(ap("wfw"), ap("dw", 0, 144), C("g16o"), C("af"), A.is_equal, A.mult, ["dw", "c_g16o", "c_af"], ["wfw"], 72)

    def patterns(t, c, after):
        if t == 1:
            iota("hl", [[0, n]], 0, 0, c * HS, c * HS + n, "hl%d_0" % c, after)
            iota("ha", [[0, n]], -int(OFS), 0, c * HS, c * HS + n, "ha%d_0" % c, after)
        if c == NCH - 1 and t + 2 <= p["sel"]:
            iota("rm", [[0, n], [4096, t + 2]], 0, 0, RM[t + 2], RM[t + 2] + (t + 2) * n, "rm%d" % (t + 2), after)
        if (t, c) == (0, NCH - 1):
            iota("rs", [[0, 4], [4096, 16]], 0, after=after)
            iota("c4", [[4, 16]], 0, after=after)

    nc = n // 16

    def ply(t, c):
        ba, bb = 2 * c, 2 * c + 1
        pa, pb = "pb%d" % ba, "pb%d" % bb
        cn, h0 = c * n, c * HS
        o = pay(c, t)
        S, sk = ap("sin", o, o + n), "sinS%d_%d" % (c, t)
        M, mk = flags("sin", c, t)
        K, kk = ap("kall", t % NR * LN + cn, t % NR * LN + cn + n), "kall%d" % (t % NR)

        def k(x):
            return "%s%d" % (x, c)

        def loc(name):
            return ap(name, cn, cn + n)

        def on(name, x):
            return mat(name, loc(x), [k(x)])

        def lists(s):
            return mat("eyeh", ap("hh", h0 + (s + 1) * n, h0 + (s + 2) * n), ["hh%d_%d" % (c, s + 1)])

        def mask(s):
            return (ap("wm", 128 * s, 128 * s + 128), M, ["wm%d" % s, mk], n)

        def slot():
            group(ap(pa, 0, n), k("pt"), ba, [mat("eye", ap("cd"), ["cd"]), mat("wp", M, [mk])])
            scan(loc("dg"), ap("rs"), ap(pa, 0, n), 0.0, A.min, A.max, ["rs", k("pt")], [k("dg")], n, ba)
            cp(ap("poff", 16 * c, 16 * c + nc), ap("dg", cn + 15, cn + n, 16), [k("dg")], [k("poff")], 64)
        HL = ["hl%d_%d" % (c, s) for s in range(t + 1)]
        HA = ["ha%d_%d" % (c, s) for s in range(t + 1)]
        KS = [mat("eye", K, [kk]), mat("eye2", S, [sk])]
        L = ap(pb, 0, n)
        group(L, k("L"), bb, KS)
        Lf, lf = ap("hh", h0 + (t + 1) * n, h0 + (t + 2) * n), "hh%d_%d" % (c, t + 1)
        relu("V", Lf, L, [k("L")], [lf], n, bb)
        if t == RO - 1:
            copy("G", ap("hl", h0 + (t + 1) * n, h0 + (t + 2) * n), Lf, [lf], ["hl%d_%d" % (c, t + 1)], n)
        par = (t * NCH + c) % p["nd"]
        d0, do, dn = par * 32 * n, "d1_%da" % par, "d1_%db" % par
        bucket = mat("wb", M, [mk])
        PO, PL = ap(pa, 5 * n, 7 * n, 2), ap(pa, 5 * n + 1, 7 * n, 2)
        if t == 0:
            group(ap(pa, 0, n), k("po"), ba, KS + [bucket])
            ts(ap("off", 2 * cn, 2 * cn + n), ap(pa, 0, n), num(0.0), None, A.max, None, [k("po")], [k("off")], n, ba)
        elif t == 1 and p["eq1"]:
            group(ap(pa, 0, n), k("pt"), ba, [lists(0), mat("neye", K, [kk]), mat("neye2", S, [sk]), mask(0)])
            ts(loc("ne"), ap(pa, 0, n), num(0.0), None, A.is_equal, None, [k("pt")], [k("ne")], n, ba)
            group(None, k("po"), ba, [x + (PL,) for x in KS + [bucket]] + [x + (PO,) for x in (lists(0), mask(0), bucket)]
                  + [on("down", "ne") + (PO,), on("down", "ne") + (PL,)])
            for i in range(2):
                ts(ap("off", 2 * cn + i, 2 * cn + 2 * n, 2), (PO, PL)[i], num(float(TW - TW * i)), num(0.0), A.add, A.max, [k("po")],
                   [k(("off", "offn")[i])], n, ba)
        else:
            og = loc("og")
            if t <= p["sel"]:
                group(None, k("pt"), ba, [x(s) + (ap(pa, s, t * n, t),) for x in (lists, mask) for s in range(t)])
                if t == 1:
                    relu("V", og, ap(pa, 0, n), [k("pt")], [k("og")], n, ba)
                else:
                    a = 5 * cn
                    scan(ap("ogs", a, a + t * n), ap("rm", RM[t], RM[t] + t * n), ap(pa, 0, t * n), 0.0, A.min, A.max, ["rm%d" % t, k("pt")],
                         [k("og")], t * n, ba)
                    og = ap("ogs", a + t - 1, a + t * n, t)
                tt(loc("ne"), og, L, A.not_equal, [k("og"), k("L")], [k("ne")], n, bb)
            else:
                slot()
                src = ind("hl", h0, h0 + t * n + n, "poff", 16 * c, 16 * c + nc)
                copy("V", og, src, HL + [k("poff")], [k("og")], n, gather=True)
                if p["nep"]:
                    tt(loc("ne"), og, L, A.not_equal, [k("og"), k("L")], [k("ne")], n, bb)
                else:
                    tt(loc("ne"), src, Lf, A.not_equal, HL + [k("poff"), lf], [k("ne")], n, kind="gv")
            group(None, k("po"), ba, [x + (PL,) for x in (lists(t), bucket)] + [x + (PO,) for x in (bucket, mat("eyeh", og, [k("og")]))]
                  + [on("upt", "ne") + (PO,), on("up", "ne") + (PL,)])
            ts(ap("off", 2 * cn, 2 * cn + 2 * n), ap(pa, 5 * n, 7 * n), num(-BIG), num(0.0), A.add, A.max, [k("po")], [k("off"), k("offn")], 2 * n, ba)
        start = ap("d1", d0, d0 + 32 * n, 32)
        if 0 < t <= p["sela"]:
            terms = [[mat("eye", ap("ha", h0 + (s + 1) * n, h0 + (s + 2) * n), [HA[s + 1]]), mat("eye", ap("cb"), ["cb"]), mask(s)] for s in range(t)]
            group(None, k("za"), bb, [x + (ap(pb, (s + 2) * n, (s + 3) * n),) for s in range(t) for x in terms[s]])
            acc, ak = ap("bs"), "bs"
            for s in range(t):
                out, ok = (start, do) if s == t - 1 else (ap("acc", 2 * cn + s % 2 * n, 2 * cn + s % 2 * n + n), k("acc%d_" % (s % 2)))
                tt(out, ap(pb, (s + 2) * n, (s + 3) * n), acc, A.max, [k("za"), ak, dn], [ok], n, bb)
                acc, ak = out, ok
        elif t:
            if t <= p["sel"]:
                slot()
            tt(start, ind("ha", h0, h0 + (t + 1) * n, "poff", 16 * c, 16 * c + nc), ap("cb"), A.add, HA + [k("poff"), "cb", dn], [do], n, kind="gv")
        m = 2 if t else 1
        x0, s0, w = c * XW + 16, 32 * cn, 128 * m
        SO = ["so%d_%d" % (c, i) for i in range(8)]
        XK = ["x%d_%d" % (c, i) for i in range(m * n // 2)]
        cut = p.get("cut%d_%d" % (t, c), p.get("cut%d" % t, p["cut"]))
        for e, a, b in zip(cut[0::2], (0,) + cut[1::2], cut[1::2]):
            copy(e, ap("xb", x0 + 16 * a, x0 + 16 * b), ind("tab", 0, m * TW, "off", 2 * cn + a, 2 * cn + b),
                 TAB + [k("off"), k("offn")] + (NEG if t else ["tabz%d" % i for i in range(4)]), XK[a // 2:b // 2], 16 * (b - a), gather=True)
        for i in range(8):
            a = w * i
            scan(ap("so", s0 + a, s0 + a + w), ap("xb", x0 + a - 1, x0 + a + w - 1), ap("d1", d0 + a, d0 + a + w) if t else ap("d1b"), -4096.0,
                 A.add, A.max, XK[max(0, 4 * m * i - 1):4 * m * (i + 1)] + ([do, dn] if t else ["d1b"]) + ["xp"], [SO[i]], w // 2)
        if t == RO - 1:
            final(c, bb)
            outs(c, "yc", "hl", p["e_yc"], 0.0)
        z = ap(pa, 4 * n, 5 * n)
        group(z, k("zf"), ba, [mat("eye", ap("nb"), ["nb"]), mat("eye", ap("xb", x0 + 16 * m - 1, x0 + 16 * m * n, 16 * m), XK),
                               mat("eyeh", ap("so", s0 + 16 * m - 1, s0 + 16 * m * n, 16 * m), SO)])
        ts(ap("yb", 2 * cn + n, 2 * cn + 2 * n), z, num(0.0), num(127.0), A.max, A.min, [k("zf"), "yb"], [k("yb")], n, ba)
        ts(ap("ha", h0 + (t + 1) * n, h0 + (t + 2) * n), z, num(0.0), num(-OFS), A.max, A.add, [k("zf")], ["ha%d_%d" % (c, t + 1)], n, ba)
        group(ap(pb, 128, 256), k("key"), bb,
              [(ap("sin", o, o + 2 * n), ap("pen"), [sk, mk, "pen"], 128),
               (ap("yb", 2 * cn + n, 2 * cn + 3 * n), ap("uu", 0, 128), [k("yb"), "uuu"], 128),
               (ap("yb", 2 * cn, 2 * cn + 2 * n), ap("uu", 128, 256), [k("yb"), "uuv"], 128)])
        q0, q1 = 128 * c, 144 * c
        scan(ap("rq", q0, q0 + 128), ap(pb, 128, 256), ap("rt"), 0.0, A.add, A.max, [k("key"), "rt"], [k("rq")], 128, bb)
        scan(back("tq", q1, q1 + 128), back("eps", 0, 128), back("rq", q0, q0 + 128), 0.0, A.add, A.min, [k("rq"), "eps"], [k("tq")], 64)

        def lost(a):
            return [(ap("tq", q1, q1 + 128), ap("down", a, a + n), ["down", k("tq")], n),
                    (ap("tq", q1 + 1, q1 + 129), ap("up", a, a + n), ["up", "tqp", k("tq")], n)]
        group(ap(pa, 5 * n, 6 * n), k("zu"), ba, [mat("eye2", S, [sk])] + lost(0))
        group(ap(pb, 4 * n, 5 * n), k("zv"), bb, lost(n))
        relu(p["e_msq"], loc("msq"), ap(pa, 5 * n, 6 * n), [k("zu"), "c_b15"], [k("msq")], n, ba, C("b15"))
        relu(p["e_ost"], loc("ost"), ap(pb, 4 * n, 5 * n), [k("zv"), "c_st"], [k("ost")], n, bb, C("st"))
        zn = t < RO - 1
        Z = ap(pb, 5 * n, 6 * n)
        if zn:
            group(Z, k("zn"), bb, struck([flags("sout", c, s) for s in range(t + 1)]) + [mat("selh", S, [sk]), on("selq", "msq")], last=False)
        early = (KS[1:] if zn else KS) + [on("neye", "msq")]
        late = [on("eye2", "mn"), on("gd", "ht")]
        bf = bb if p["jz"] or not zn else ba
        Fn = ap("pb%d" % bf, 6 * n, 7 * n)
        if bf == bb:
            group(Fn, k("fin"), bb, early, first=not zn, last=False)
        w1 = ap(pa, 7 * n, 8 * n)
        group(w1, k("w1"), ba, [on("bmq", "msq"), on("bmq", "ost"), mat("cp", ap("one"), ["one"]), mat("cn", ap("one"), ["one"]),
                                on("bmh", "msq"), on("bmh", "ost")])
        tt(loc("mn"), w1, loc("msq"), A.min, [k("w1"), k("msq")], [k("mn")], n, ba)
        tt(loc("ht"), w1, S, A.is_equal, [k("w1"), sk], [k("ht")], n, ba)
        if zn:
            group(Z, k("zn"), bb, [on("selh", "mn")], first=False, last=bf != bb)
        group(Fn, k("fin"), bf, late if bf == bb else early + late, first=bf != bb)
        if zn:
            o2, su, sem = pay(c, t + 1), "su%d_%d" % (c, t + 1), "ar%d_%d" % (t + 1, c)
            Mn, mnk = flags("sout", c, t + 1)
            ts(Mn, Z, ap("thr", t + 1, t + 2), None, A.is_ge, None, [k("zn"), "thr"], [mnk], n, bb)
            copy(p["e_su"], ap("sout", o2, o2 + n), Fn, [k("fin")], [su], n, bf, by=0.5)
            add("G", lambda q, T, X: q.remote_dma(T["sin"][:, o2:o2 + 2 * n], T["sout"][:, o2:o2 + 2 * n], T.sem[sem], T.sem["sent"],
                                                  X["addr"][1][1], X["addr"][1][0], X["mask"]), [su, mnk], ["st" + sem], ("r", 0), None, "sent")
            lands(["st" + sem], ["sinS%d_%d" % (c, t + 1), "sinM%d_%d" % (c, t + 1)], sem, 0.0)
            copy("G", ap("hl", h0 + (t + 1) * n, h0 + (t + 2) * n), Lf, [lf, "st" + sem], ["hl%d_%d" % (c, t + 1)], n)
            patterns(t, c, ["st" + sem])
        else:
            outs(c, "ya", "ha", p["e_ya"], OFS)
            relu(p["e_yl"], loc("oyl"), Fn, [k("fin")], [k("oyl")], n, bf)
            dma("Y", ap("yl", cn, cn + n), loc("oyl"), [k("oyl")], [], "outs", 32768)

    def final(c, bb):
        pb = "pb%d" % bb
        cn, n4 = c * n, n // 4
        group(ap(pb, 448, 448 + n), "zl%d" % c, bb, struck([flags("sin", c, s) for s in range(RO)]))
        for h in range(2):
            ts(ap("fm", 2 * cn + h * n, 2 * cn + h * n + n), ap(pb, 448, 448 + n), C("cf%d" % h), None, A.is_equal, None,
               ["zl%d" % c, "c_cf%d" % h], ["fm%d_%d" % (c, h)], n, bb)
        terms = [mat("eye", ap("c4", 0, n4), ["c4"], 64)]
        for h in range(2):
            for i in range(4):
                d = 4 * i + 2 * h
                terms.append((ap("wfw", 16 - d, 144 - d), ap("fm", 2 * cn + h * n + i, 2 * cn + h * n + n, 4), ["wfw", "fm%d_%d" % (c, h)], 64))
        group(ap(pb, 448, 448 + n4), "zl%d" % c, bb, terms)
        ts(ap("foff", 16 * c, 16 * c + n4), ap(pb, 448, 448 + n4), C("rf"), None, A.add, None, ["zl%d" % c, "c_rf"], ["foff%d" % c], 64, bb)

    def outs(c, nm, hn, e, bias):
        h0, n4 = c * HS, n // 4
        dst = ap("o" + nm, 4 * n * c, 4 * n * c + 4 * n)
        relu(e, dst, ind(hn, h0, h0 + HS, "foff", 16 * c, 16 * c + n4), ["%s%d_%d" % (hn, c, s) for s in range(7)] + ["foff%d" % c],
             ["o%s%d" % (nm, c)], 4 * n, None, num(bias), "g")
        dma("Y", ap(nm, 4 * n * c, 4 * n * c + 4 * n), dst, ["o%s%d" % (nm, c)], [], "outs", 131072)

    setup()
    for t in range(RO):
        for c in range(NCH):
            tag[0] = t * NCH + c
            ply(t, c)
    return ops


def times(op, p):
    kind, m = op["cost"]
    cy = 0.00083 * p["f"]
    if kind == "a":
        return 0.0, p["rlat"] + m
    if kind == "d":
        return 0.1, 2.0 + m / p["bw"] / 1000.0
    d = {"c": max(64, m) * cy, "p": max(64, m) * cy * p["pe"], "gv": 0.05 + m * cy * p["g"], "gs": 0.065 + m * cy * p["g"],
         "gi": 0.13 + 2 * m * cy, "ga": 0.17 + 2 * m * cy, "r": p["riss"]}[kind]
    return d, d


def lags(ops, p):
    tm = [times(o, p) for o in ops]
    return tm, [[(d, tm[d][1] + (0.0 if ops[d]["eng"] is None or o["eng"] == ops[d]["eng"] == "P" or (o["eng"], ops[d]["sem"]) == ("G", "sent")
                                 else p["hop"])) for d in sorted(o["deps"])]
                for o in ops]


def schedule(ops, p):
    N = len(ops)
    tm, fw = lags(ops, p)
    succ = [[] for _ in range(N)]
    for k in range(N):
        for d, w in fw[k]:
            succ[d].append((k, w))
    pr = [0.0] * N
    for k in range(N - 1, -1, -1):
        own = -p["tq"] * ops[k]["tag"] if ops[k]["tag"] is not None else -1.0e3
        pr[k] = tm[k][1] + max([pr[s] + p["hop"] for s, w in succ[k]] + [own])
    for k in range(N):
        pr[k] += 1.0e4 if ops[k]["cost"][0] == "r" else p["up"].get(ops[k]["w"].rstrip("0123456789_"), 0.0) - p["short"] * tm[k][0]
    left = [len(o["deps"]) for o in ops]
    rdy, st = [0.0] * N, [0.0] * N
    free, ready = {}, {}
    stack = [k for k in range(N) if not left[k]]
    while True:
        if stack:
            k = stack.pop()
            if ops[k]["eng"] is not None:
                ready.setdefault(ops[k]["eng"], []).append(k)
                continue
            st[k] = rdy[k]
        else:
            soon = [(max(free.get(e, 0.0), min([rdy[j] for j in l])), i, e) for i, (e, l) in enumerate(ready.items()) if l]
            if not soon:
                break
            bt, i, e = min(soon)
            k = max([j for j in ready[e] if rdy[j] <= bt], key=lambda j: (pr[j], -j))
            ready[e].remove(k)
            st[k] = bt
            free[e] = bt + tm[k][0]
        for s, w in succ[k]:
            rdy[s] = max(rdy[s], st[k] + w)
            left[s] -= 1
            if not left[s]:
                stack.append(s)
    bw = [[(s, tm[s][0] + w - tm[k][0]) for s, w in succ[k]] for k in range(N)]
    best = None
    for it in range(p["fbi"] + 1):
        if it:
            sb = place(ops, tm, bw, [(-round(st[k] + tm[k][0], 6), -k) for k in range(N)])
            st = place(ops, tm, fw, [(-round(sb[k] + tm[k][0], 6), k) for k in range(N)])
        end = max([st[k] + tm[k][1] for k in range(N)])
        if best is None or end < best:
            best, seq = end, sorted(range(N), key=lambda j: (round(st[j], 6), j))
    seq = [k for k in range(N) if ops[k]["eng"] in ("Y", "G") and not ops[k]["deps"]] \
        + [k for k in seq if ops[k]["eng"] not in ("Y", "G") or ops[k]["deps"]]
    seq = refine(ops, p, seq)
    order = {}
    for k in seq:
        if ops[k]["eng"] is not None:
            order.setdefault(ops[k]["eng"], []).append(k)
    return order


def place(ops, tm, pred, key):
    N = len(ops)
    start, busy = [0.0] * N, {}
    for k in sorted(range(N), key=lambda j: key[j]):
        e = ops[k]["eng"]
        t0 = 0.0
        for d, w in pred[k]:
            t0 = max(t0, start[d] + w)
        if e is not None:
            l, du = busy.setdefault(e, []), tm[k][0]
            i = len(l)
            while i > 0 and l[i - 1][1] > t0:
                i -= 1
            while i < len(l) and l[i][0] < t0 + du - 1e-9:
                t0 = max(t0, l[i][1])
                i += 1
            l.insert(i, (t0, t0 + du))
        start[k] = t0
    return start


def refine(ops, p, seq):
    N = len(ops)
    prev, nxt, last, pos = [-1] * N, [-1] * N, {}, [0] * N
    for i, k in enumerate(seq):
        pos[k], e = i, ops[k]["eng"]
        if e in last and e is not None:
            prev[k], nxt[last[e]] = last[e], k
        last[e] = k
    cases = [lags(ops, dict(p, f=f, g=g, hop=hop, rlat=rl)) for f, g, hop, rl in p["cases"]]
    ends = [k for k in range(N) if ops[k]["cost"][0] == "d" and ops[k]["tag"] is not None]
    marks = ends + [k for k in range(N) if ops[k]["cost"][0] == "r"]

    def heads(case, st, i0):
        tm, fw = case
        for k in seq[i0:]:
            t = st[prev[k]] + tm[prev[k]][0] if prev[k] >= 0 else 0.0
            for d, w in fw[k]:
                if st[d] + w > t:
                    t = st[d] + w
            st[k] = t
        return max([st[k] + tm[k][1] for k in ends]) + 0.3 * sum([st[k] for k in marks]) / len(marks)
    starts = [[0.0] * N for _ in cases]
    base = [heads(x, st, 0) for x, st in zip(cases, starts)]
    cur, seed, todo = float(len(cases)), [1], []

    def rnd(m):
        seed[0] = seed[0] * 48271 % 2147483647
        return seed[0] % m
    for it in range(p["moves"]):
        while not todo:
            i = rnd(len(cases))
            (tm, fw), st = cases[i], starts[i]
            k = marks[rnd(len(marks))] if rnd(2) else max(ends, key=lambda j: st[j])
            way = []
            while k >= 0:
                up = [d for d, w in fw[k] if st[d] + w > st[k] - 1e-9]
                if prev[k] >= 0 and st[prev[k]] + tm[prev[k]][0] > st[k] - 1e-9 and (not up or rnd(2)):
                    if prev[k] not in ops[k]["deps"] and ops[k]["eng"] in "VSP":
                        way.append(k)
                    up = [prev[k]]
                k = up[-1] if up else -1
            todo = [way[rnd(len(way))] for j in range(12 if way else 0)]
        c = todo.pop()
        a = prev[c]
        for j in range((0, 0, 0, 1, 2, 4)[rnd(6)]):
            a = prev[a] if a >= 0 and prev[a] >= 0 else a
        if a < 0:
            continue
        i0, i1 = pos[a], pos[c]
        seg, need = seq[i0:i1 + 1], {c}
        for k in seg[::-1]:
            if k in need:
                need.update(ops[k]["deps"])
                need.add(prev[k] if k != c else c)
        if any([k in need and k != c and ops[k]["eng"] == ops[c]["eng"] for k in seg]):
            continue
        links = [(x, prev[x], nxt[x]) for x in (prev[a], a, prev[c], c, nxt[c]) if x >= 0]
        pa, pc, nc = prev[a], prev[c], nxt[c]
        nxt[pc], prev[c], nxt[c], prev[a] = nc, pa, a, c
        if nc >= 0:
            prev[nc] = pc
        if pa >= 0:
            nxt[pa] = c
        seq[i0:i1 + 1] = [k for k in seg if k in need] + [k for k in seg if k not in need]
        new = [list(st) for st in starts]
        val = sum([heads(x, st, i0) / b for x, st, b in zip(cases, new, base)])
        if val <= cur:
            cur, starts = val, new
            for i in range(i0, i1 + 1):
                pos[seq[i]] = i
        else:
            seq[i0:i1 + 1] = seg
            for x, u, v in links:
                prev[x], nxt[x] = u, v
    return seq


PLAN = {}


def plan():
    key = str(P)
    if key not in PLAN:
        ops = build(P)
        PLAN[key] = (ops, schedule(ops, P))
    return PLAN[key]


def rank_program(g, core, T, topo):
    rank = T.rank_of(core)
    if rank is None:
        return
    ops, order = plan()
    peers = [T.cores[(rank + j) % NR] for j in range(NR)]
    mask = topo.mask(core, peers[1])
    for c in peers[2:]:
        mask &= topo.mask(core, c)
    bits = [1 << e for e in topo.engines(core, peers[1]) if mask >> e & 1]
    ne = len(bits)
    X = {"addr": [topo.addr(c) for c in peers], "mask": mask, "parts": [sum(bits[c * ne // NCH:(c + 1) * ne // NCH]) for c in range(NCH)]}
    queue = {"V": g.vector, "S": g.scalar, "P": g.tensor, "G": g, "Y": g.sync}
    pos = {}
    for e, l in order.items():
        for i, k in enumerate(l):
            pos[k] = i
    waits, needed, known = {}, set(), {}
    seen, nxt = {e: {} for e in order}, {e: 0 for e in order}
    moved = True
    while moved:
        moved = False
        for e, l in order.items():
            while nxt[e] < len(l) and all([ops[d]["eng"] is None or d in known for d in ops[l[nxt[e]]]["deps"]]):
                k = l[nxt[e]]
                top = {}
                for d in ops[k]["deps"]:
                    o = ops[d]
                    if o["cost"][0] == "r":
                        continue
                    if o["sem"] is not None:
                        top[("x", d)] = d
                    elif not (e == "P" and o["eng"] == e):
                        f = o["eng"]
                        if f not in top or pos[d] > pos[top[f]]:
                            top[f] = d
                w = []
                for f, d in top.items():
                    at = 0 if ops[d]["sem"] is not None else pos[d]
                    if seen[e].get(f, -1) >= at:
                        continue
                    if any([d2 != d and known.get(d2, {}).get(f, -1) >= at for d2 in top.values()]):
                        continue
                    w.append(d)
                for f, d in top.items():
                    at = 0 if ops[d]["sem"] is not None else pos[d]
                    seen[e][f] = max(seen[e].get(f, -1), at)
                    for f2, a2 in known.get(d, {}).items():
                        seen[e][f2] = max(seen[e].get(f2, -1), a2)
                needed.update([d for d in w if ops[d]["sem"] is None])
                waits[k] = sorted(w)
                known[k] = dict(seen[e])
                nxt[e] += 1
                moved = True
    token, total = {}, {}
    for e, l in order.items():
        for k in l:
            if k in needed:
                total[e] = total.get(e, 0) + 1
                token[k] = ("s" + e, total[e])
    for k, o in enumerate(ops):
        if o["eng"] is None:
            token[k] = (o["sem"], ne * o["cnt"])
        elif o["cost"][0] == "d":
            token[k] = (o["sem"], 16)
    nout = nsent = 0
    for e, l in order.items():
        q = queue[e]
        for k in l:
            for d in waits[k]:
                q.wait_ge(T.sem[token[d][0]], token[d][1])
            o = ops[k]
            ins = o["fn"](q, T, X)
            if o["cost"][0] == "d":
                ins.then_inc(T.sem[o["sem"]], 16)
                nout += 16 if o["sem"] == "outs" else 0
            elif o["cost"][0] == "r":
                nsent += ne
            elif k in needed:
                ins.then_inc(T.sem["s" + e], 1)
    g.wait_ge(T.sem["sent"], nsent)
    g.sync.wait_ge(T.sem["outs"], nout)
